import numpy as np, ml_dtypes
CORES = [23,119,17,113]
N = 4
BF = ml_dtypes.bfloat16
def gentries(a):
    return np.ascontiguousarray(a.reshape(8, 16, -1).transpose(0, 2, 1)).reshape(8, -1)
def gtable(e):
    e = np.asarray(e); return np.ascontiguousarray(e.reshape(8, -1, 16).transpose(0, 2, 1)).reshape(128, -1).astype(np.int32)
def f(rng, *shape):
    return (rng.standard_normal(shape, dtype=np.float32) * np.exp2(rng.integers(-2, 3, shape[:-1] + (1,)))).astype(BF)
def wide(rng, *shape):
    v = f(rng, *shape).astype(np.float32); k = shape[:-2] + (1, shape[-1])
    return (v * np.exp2(rng.integers(-6, 7, k)) * (rng.random(k) > 0.0625)).astype(BF)
V, G, S, P, RO, VO = 1792, 256, 512, 4, 4, 9
def parts(rng):
    sd = (rng.random((N, 8, V)) < 0.3 + 0.4 * rng.random((N, 8, 1))).astype(np.int64)
    nr = rng.integers(0, S, (N, 8, V)); hs = np.ascontiguousarray(np.argsort(rng.random((N, 8, V)), axis=-1)[..., :S])
    tl = rng.integers(0, V, (N, 8, 16, V)); tl = np.where(rng.random(tl.shape) < 0.2, V + rng.integers(0, G, tl.shape), tl)
    u = 0.6 * rng.standard_normal((N, 8, 16, V)) + np.where(sd == 0, 0.5, -0.5)[:, :, None, :]
    c = 0.5 * rng.standard_normal((N, 8, 16, S)); lean = 0.4 * rng.choice(np.array([-1.0, -0.5, 0.0, 0.5, 1.0]), (N, 8, 1, S))
    w = np.stack([c + lean + 0.3 * rng.standard_normal(c.shape), c - lean + 0.3 * rng.standard_normal(c.shape)], axis=-1)
    th = rng.integers(0, 48, (N, 8, 16, 1)) * 0.015625
    return sd, nr, hs, tl, u, w, th
def pack(sd, nr, hs, tl, u, w, th):
    def cut(a, n): return np.where(np.abs(a) < 2.0 ** -20, 0.0, np.clip(a, -2.0, 2.0)).reshape(N, 128, n).astype(np.float32).astype(BF)
    return {"tl": np.ascontiguousarray(tl.reshape(N, 128, V)).astype(np.int32), "u0": cut(u, V), "w0": cut(w, 2 * S), "sd": sd.astype(np.int32), "nr": nr.astype(np.int32),
            "hs": hs.astype(np.int32), "th": th.reshape(N, 128, 1).astype(np.float32)}
def still(rng, p, r, g, up, fine):
    sd, nr, hs, tl, u, w, th = p
    a1 = rng.integers(-48, 49, (16, 1)) * 0.015625; gap = rng.integers(1, 65, (16, 1)) * 0.015625; sign = 1.0 if up else -1.0; a0 = a1 + sign * gap
    tl[r, g] = tl[r, g] % V; u[r, g] = np.where(sd[r, g] == 0, a0, a1)
    n = rng.choice(np.array([0, 1, VO - 1, VO - 1, VO, VO, 15, 16]), S); m = np.argsort(rng.random((16, S)), axis=0) < n
    w[r, g, :, :, 0] = a0 + sign * np.where(m, 0.0078125, 0.0); w[r, g, :, :, 1] = a1
    th[r, g] = gap + (0.0078125 - 0.000244140625 if fine else 0.0)
def hang(rng, p, r, g, up):
    sd, nr, hs, tl, u, w, th = p; z = 0 if up else 1
    kind = rng.permutation(np.arange(16) % 3)[:, None]; m = 1 + rng.integers(1, 64, (16, 1)) * 0.0078125; j = rng.integers(1, 17, (16, 1)) * 0.0078125
    base = np.where(kind == 0, -2.0 ** -20 - 2.0 ** -27, np.where(kind == 1, m, (2 * rng.integers(64, 128, (16, 1)) + 1) * 2.0 ** -17))
    at = np.where(kind == 1, m + j, m); dif = (at - base).astype(np.float32)
    th[r, g] = np.where(kind == 0, dif, np.nextafter(dif, np.float32(0)))
    o = np.argsort(rng.random((16, S)), axis=0); step = rng.integers(1, 33, (16, S)) * 0.0078125
    w[r, g, :, :, z] = at + np.where(o < VO - 1, step, np.where(o == VO - 1, 0.0, -step)); w[r, g, :, :, 1 - z] = base
    sd[r, g] = 1 - z; tl[r, g] = tl[r, g] % V; u[r, g] = base
def full(rng, p, r, g, c):
    sd, nr, hs, tl, u, w, th = p; E = S // 2; z = int(rng.integers(0, 2))
    v = np.arange(V)
    if c in (1, 3, 6): v = np.roll(v, E - G)
    if c in (4, 7): v = rng.permutation(V)
    to = np.zeros(S, np.int64); to[0::2] = rng.permutation(v[:E]); to[1::2] = rng.permutation(v[E:S]); sd[r, g, to] = 1 - z
    if c < 2: to[S - 2] = to[0]
    k = np.arange(16)[:, None]; k0 = rng.integers(0, 4, S); own = rng.integers(0, V, (16, S)); gh = V + rng.integers(0, G, (16, S))
    nm = np.where(k < k0, gh, np.where(k == k0, to, own))
    if c in (2, 3, 4): nm[:, 1::2] = gh[:, 1::2]
    tl[r, g][:, hs[r, g]] = nm
    h = 1.25 if z == 0 else -1.25
    u[r, g] = np.where(sd[r, g] == 0, h, -h) + 0.25 * (2 * rng.random((16, V)) - 1)
    w[r, g] = np.array([h, -h]) + 0.25 * (2 * rng.random((16, S, 2)) - 1)
    th[r, g] = rng.integers(0, 33, (16, 1)) * 0.015625
def setup_inputs(rng):
    return pack(*parts(rng))
def setup_inputs_spread(rng):
    sd, nr, hs, tl, u, w, th = parts(rng)
    u = wide(rng, N, 128, V).astype(np.float64).reshape(N, 8, 16, V) * 0.0625
    w = wide(rng, N, 128, 2 * S).astype(np.float64).reshape(N, 8, 16, S, 2) * 0.0625
    b = rng.integers(0, 3, (N, 8, 1, S, 1)); z = np.array([1.0, -1.0])
    w = np.where(b == 0, w, np.where(b == 1, np.abs(w) * z, -np.abs(w) * z))
    th = np.exp2(rng.integers(-10, 2, (N, 8, 16, 1))) * (rng.random((N, 8, 16, 1)) > 0.125)
    return pack(sd, nr, hs, tl, u, w, th)
def setup_inputs_ends(rng):
    sd, nr, hs, tl, u, w, th = parts(rng)
    def ends(shape, hi, share): return np.where(rng.random(shape) < share, hi * rng.integers(0, 2, shape), rng.integers(0, hi + 1, shape))
    nr = ends((N, 8, V), S - 1, 0.75); hs = ends((N, 8, S), V - 1, 0.75); tl = ends((N, 8, 16, V), V + G - 1, 0.75)
    u = np.where(rng.random((N, 8, 1, V)) < 0.5, 4.0 * rng.integers(0, 2, (N, 8, 1, V)) - 2, 4.0 * rng.integers(0, 2, (N, 8, 16, V)) - 2)
    z = np.array([2.0, -2.0]); b = rng.integers(0, 4, (N, 8, 1, S, 1)); free = 4.0 * rng.integers(0, 2, (N, 8, 16, S, 2)) - 2
    n = VO - rng.integers(0, 2, (N, 8, 1, S)); m = (np.argsort(rng.random((N, 8, 16, S)), axis=2) < n)[..., None]
    w = np.where(b == 0, z, np.where(b == 1, -z, np.where(b == 2, free, np.where(m, z, -2.0))))
    th = 2.0 * rng.integers(0, 2, (N, 8, 16, 1))
    tl = np.where(tl == G - 1, G - 2, np.where(tl == V - 1, V - 2, tl)); hs = np.where(hs == G - 1, G - 2, hs)
    for g in range(8):
        far = 2.0 if g % 2 == 0 else -2.0
        sd[:, g, G - 1] = 0; u[:, g, :, G - 1] = far; tl[:, g, :, G - 1] = G - 1
        if g in (0, 7):
            for v in (0, V - 1): sd[:, g, v] = 0; u[:, g, :, v] = far; tl[:, g, :, v] = V + G - 1
    return pack(sd, nr, hs, tl, u, w, th)
def setup_inputs_corners(rng):
    p = parts(rng); sd, nr, hs, tl, u, w, th = p
    for r in range(N):
        o = rng.permutation(8)
        for g in range(8):
            c = int(o[g])
            if c < 2: sd[r, g] = c
            elif c == 2: tl[r, g] = V + tl[r, g] % G
            elif c == 3: tl[r, g] = np.arange(V)
            elif c == 4:
                tl[r, g] = rng.choice(np.array([0, V - 1, V, V + G - 1]), (16, V)); hs[r, g] = np.where(rng.random(S) < 0.5, rng.choice(np.array([0, V - 1]), S), hs[r, g])
            elif c == 5:
                hs[r, g, 0::2] = int(rng.integers(0, V)); hs[r, g, 1::4] = V - 1; hs[r, g, 3::4] = 0; nr[r, g] = rng.choice(np.array([0, S - 1]), V)
            elif c == 6:
                own = rng.integers(0, V, (16, V)); gh = V + rng.integers(0, G, (16, V)); k = np.arange(16)[:, None]; v = np.arange(V)
                tl[r, g] = np.where(k == np.where(v % 2 == 0, 15, 0), own, gh)
            else: still(rng, p, r, g, r % 2 == 0, False)
    return pack(*p)
def setup_inputs_crowd(rng):
    p = parts(rng); sd, nr, hs, tl, u, w, th = p; most = rng.permutation(N)[:N // 2]
    for r in range(N):
        o = rng.permutation(8)
        for g in range(8):
            c = int(o[g])
            if r in most:
                full(rng, p, r, g, c); continue
            if c > 3: continue
            z = int(rng.integers(0, 2)); q = 1 + rng.permutation(V - 2)[:16]
            if c == 0: q[0] = V - 1
            if c == 1: q[0] = 0
            sd[r, g, q] = 1 - z; tl[r, g] = q[:, None]
            if c == 1:
                for j in (0, 1): tl[r, g, :, hs[r, g, 2 * int(rng.integers(0, S // 2)) + j]] = rng.integers(0, V, 16)
            if c == 2: tl[r, g] = q[(np.arange(16)[:, None] + np.arange(V) % 3) % 16]
            if c == 3: tl[r, g] = np.where(rng.random(V) < 0.5, rng.integers(0, V, (16, V)), tl[r, g])
            h = 1.25 if z == 0 else -1.25
            u[r, g] = np.where(sd[r, g] == 0, h, -h) + 0.25 * (2 * rng.random((16, V)) - 1)
            w[r, g] = np.array([h, -h]) + 0.25 * (2 * rng.random((16, S, 2)) - 1)
            th[r, g] = rng.integers(0, 33, (16, 1)) * 0.015625
    return pack(*p)
def setup_inputs_calm(rng):
    p = parts(rng)
    for r in range(N):
        o = rng.permutation(8)
        for g in range(8):
            c = int(o[g])
            if c < 4: still(rng, p, r, g, c % 2 == 0, c > 1)
            elif c < 6: hang(rng, p, r, g, c == 4)
    return pack(*p)
def check_inputs(d):
    bad = []
    for k, lo, hi in (("tl", 0, V + G - 1), ("u0", -2, 2), ("w0", -2, 2), ("sd", 0, 1), ("nr", 0, S - 1), ("hs", 0, V - 1), ("th", 0, 2)):
        a = np.asarray(d[k]).astype(np.float64)
        if not (np.min(a) >= lo and np.max(a) <= hi): bad.append("range of " + k)
        if k in ("u0", "w0", "th") and np.any((a != 0) & (np.abs(a) < 2.0 ** -20)): bad.append("least size of " + k)
    return bad
def tree(q):
    for h in (8, 4, 2, 1): q = q[..., :h, :] + q[..., h:, :]
    return q[..., 0, :]
def ext(a):
    b = np.roll(a, -1, axis=0)
    return np.concatenate([a, b[..., :G // 2], np.roll(b, -1, axis=1)[..., G // 2:G]], axis=-1)
def reference(tl, u0, w0, sd, nr, hs, th):
    t = tl.astype(np.int64).reshape(N, 8, 16, V); u = np.array(u0.astype(np.float32).reshape(N, 8, 16, V)); w = np.array(w0.astype(np.float32).reshape(N, 8, 16, S, 2))
    side = sd.astype(np.int64); near = nr.astype(np.int64); host = hs.astype(np.int64); lim = th.astype(np.float32).reshape(N, 8, 16, 1); c = np.float32(0.015625)
    for rnd in range(RO):
        view = [ext(np.where((side == z)[:, :, None, :], u, np.take_along_axis(w[..., z], near[:, :, None, :], 3))) for z in (0, 1)]
        es = ext(side)
        v = np.arange(rnd % P, V, P); ix = t[..., v] + (V + G) * side[..., v][:, :, None, :]
        x = np.take_along_axis(np.concatenate(view, axis=3), ix.reshape(N, 8, 1, -1), 3).reshape(N, 8, 16, 16, len(v))
        d = x - u[..., v][..., None, :]; nu = u.copy(); nu[..., v] = u[..., v] + tree(d * np.abs(d)) * c
        s = np.arange(rnd % 2, S, 2); name = np.take_along_axis(t, host[..., s][:, :, None, :], 3)
        flat = name.reshape(N, 8, -1); e = np.take_along_axis(es, flat, 2).reshape(name.shape)
        x = np.take_along_axis(np.where((es == 0)[:, :, None, :], view[0], view[1]), flat[:, :, None, :], 3).reshape(N, 8, 16, 16, len(s))
        new = []
        for z in (0, 1):
            old = w[..., z][..., s]; d = np.where((e == z)[:, :, None], x - old[..., None, :], np.float32(0))
            new.append(old + tree(d * np.abs(d)) * c)
        diff = new[0] - new[1]
        up = np.count_nonzero(diff > lim, axis=2) >= VO; dn = np.count_nonzero(diff < -lim, axis=2) >= VO
        sg = np.where(up, 0, 1); fit = (up | dn)[:, :, None] & (name < V) & (e == 1 - sg[:, :, None])
        k = np.argmax(fit, axis=2); ok = np.any(fit, axis=2)
        claim = np.where(ok, np.take_along_axis(name, k[:, :, None], 2)[:, :, 0], V)
        a, b, i = np.nonzero(ok); first = np.full((N, 8, V + 1), S, np.int64); np.minimum.at(first, (a, b, claim[a, b, i]), i)
        a, b, i = np.nonzero(ok & (np.take_along_axis(first, claim, 2) == np.arange(len(s))))
        n = claim[a, b, i]; z = sg[a, b, i]
        w[..., s, 0] = new[0]; w[..., s, 1] = new[1]; u = nu
        u[a, b, :, n] = w[a, b, :, s[i], z]; side[a, b, n] = z; near[a, b, n] = s[i]; host[a, b, s[i]] = n
    return {"yu": u.reshape(N, 128, V), "ys": w.reshape(N, 128, 2 * S), "yc": (2 * near + side).astype(np.float32), "yh": host.astype(np.float32)}

@@ -1,0 +1,713 @@
+import numpy as np
+from concourse.bass import DstId, RemoteDMATransfer
+from concourse.mybir import dt, AluOpType, AxisListType, ActivationFunctionType
+A = AluOpType
+F = ActivationFunctionType
+
+NV, NG, NS, RO = 1792, 256, 512, 4
+U0 = 256
+G0 = U0 + NV
+W0 = G0 + NG
+OPT = {"pair_pe": False, "tree_pe": True, "lvl_pe": True, "c1_pe": True, "dd_pe": False, "tree_dma": True,
+       "tail": "sv", "s1un": ((), ()), "s1pe": ((), ()), "vwv": (), "gvv": False,
+       "boost": {"s2": 36.3, "s3": 27.1, "sides": 174.9, "cand": -43.1, "gv": 33.3, "vw": 1.1, "ue": 5.6, "prep": 1.1, "A": -3.8, "B": -7.4}}
+f32, f16, i32, u16, bf = "float32", "float16", "int32", "uint16", "bfloat16"
+SB = {
+    "uw": ([128, W0 + 1024], f32), "cc": ([128, W0], f32), "vw0": ([128, 4096], f32), "vw1": ([128, 4096], f32),
+    "tli": ([128, NV], i32), "lsw": ([128, 2, 896], i32), "ftr": ([128, 14, 32], f16), "tlt": ([128, 14, 32], f16),
+    "tt": ([128, 12288], f32), "d2": ([128, 3584], f32), "uu": ([128, 4096], f32), "gg": ([128, 4096], f16),
+    "rb": ([128, 5888], f32), "c1": ([128, 512], f32), "uexp": ([128, 2, 448], f32),
+    "sdi": ([128, 112], i32), "nri": ([128, 112], i32), "sdf": ([128, 112], f32), "nrf": ([128, 112], f32), "cb": ([128, 112], f16),
+    "hsi": ([128, 512], i32), "hsf": ([128, 16, 32], f16), "thr": ([128, 4], f32), "nth": ([128, 4], f32),
+    "hw": ([128, 32], f32), "hix": ([128, 32], u16), "hw16": ([128, 32], f16),
+    "nmf": ([128, 256], f32), "nix": ([128, 2, 256], u16), "j2k": ([128, 16], f32), "n32m": ([128, 128], f32), "n1": ([128, 256], f16),
+    "uix": ([128, 256], u16), "sg": ([128, 256], f16), "lix": ([128, 256], u16), "ts": ([128, 256], f16), "cab": ([128, 512], f16),
+    "sel": ([128, 512], f16), "cand": ([128, 512], f32),
+    "dd": ([128, 256], f32), "ud": ([128, 512], f16), "rab": ([128, 512], f16), "cz": ([128, 2, 256], f16), "zs": ([128, 256], f32),
+    "cw": ([128, 16], f32), "cwm": ([128, 16], f16), "cwp": ([128, 16], f16), "vlx": ([128, 16], u16),
+    "neg": ([128, 256], f16), "tgf": ([128, 16], f32), "tgx": ([128, 16], u16), "val": ([128, 256], f32),
+    "h1": ([128, 16], f32), "h2": ([128, 16], f32),
+    "f0": ([128, 224], f32), "f1": ([128, 112], f32), "vix": ([128, 224], u16), "sgw": ([128, 28], f16), "six0": ([128, 448], u16), "six1": ([128, 448], u16),
+    "sc": ([128, 128], f32), "su": ([128, 128], f32), "sv": ([128, 256], f32),
+    "yc1": ([128, 112], f32), "yc2": ([128, 112], f32),
+    "pi": ([128, 4], i32), "pj": ([128, 4], i32), "col": ([128, 16], f32), "xr": ([128, 144], f32), "x16": ([128, 16], f32),
+    "ce": ([128, 16], f32), "cl": ([128, 16], f32), "md": ([128, 128], f32), "kk": ([128, 128], f32), "tz": ([128, 128], f32),
+    "i32m": ([128, 128], f32), "i16m": ([128, 128], f16), "k16m": ([128, 128], f16), "pm": ([128, 128], f32), "b32": ([128, 144], f32), "b162": ([128, 144], f16), "cch": ([128, NV], f16),
+    "b16": ([128, 144], f16), "b4k": ([128, 144], f16), "b8": ([128, 144], f16), "blk": ([128, 128], f16), "blk2k": ([128, 128], f16),
+    "ym": ([128, 128], f16), "t1": ([128, 128], f32), "t2": ([128, 128], f32), "t3": ([128, 8, 16], f32), "z16": ([128, 128], f16),
+    "rowb": ([128, 2048], f16), "tri": ([128, 2048], f16), "mm": ([128, 4, 8, 16], f16),
+    "tab8": ([128, 256], f32), "tab8h": ([128, 256], f16), "tab32": ([128, 128], f32), "tab32h": ([128, 128], f16),
+    "tabs": ([128, 512], f32), "jw": ([128, 112], f32), "t128": ([128, 16], f32), "t128h": ([128, 16], f16),
+}
+SCRATCH = {k: ("sbuf", s, d) for k, (s, d) in SB.items()}
+SCRATCH["ps"] = ("psum", [128, 4096], f32)
+IO = {"tl": [128, NV], "sd": [8, NV], "nr": [8, NV], "hs": [8, NS], "u0": [128, NV], "w0": [128, 1024], "th": [128, 1],
+      "yu": [128, NV], "ys": [128, 1024], "yc": [8, NV], "yh": [8, NS]}
+SEMAPHORES = (["v", "s", "p", "gq"] + ["d%d" % i for i in range(112)] + ["a%d" % i for i in range(16)] + ["l%d" % i for i in range(16)])
+
+CY, PCY, GAM, SIG = 0.83e-3 * 1.2, 0.417e-3 * 1.2, 1.5, 3.5
+GI, DL, DR = 1.0, 2.0, 120e3
+LOOK, PASSES = 0.0, 8
+
+
+def V_(name, *idx):
+    shape = SB[name][0] if name in SB else (IO[name] if name in IO else [128, 4096])
+    if not idx:
+        idx = (slice(None),)
+    ar = np.arange(int(np.prod(shape[1:]))).reshape(shape[1:])[idx[1:]].ravel()
+    pr = range(shape[0])[idx[0]]
+    n = int(ar.size)
+    if name == "ps":
+        m = 0
+        for b in set((ar // 512).tolist()):
+            m |= 1 << b
+        box = m
+    else:
+        bits = np.zeros(int(np.prod(shape[1:])), np.uint8); bits[ar] = 1
+        m = int.from_bytes(np.packbits(bits, bitorder="little").tobytes(), "little")
+        lo, hi = int(ar.min()) // 8 * 8, int(ar.max()) // 8 * 8 + 8
+        box = ((1 << (hi - lo)) - 1) << lo
+    return {"n": name, "i": idx, "m": m, "box": box, "p": (pr[0], pr[-1] + 1), "c": n, "off": None}
+
+
+S_ = slice
+AL = slice(None)
+
+
+def c2(name, a, b, s=None):
+    return V_(name, AL, slice(a, b, s))
+
+
+def ind(win, off):
+    w = dict(win); w["off"] = off; w["c"] = off["c"] * 16
+    return w
+
+
+def two(v):
+    return v["n"] != "ps" and SB[v["n"]][1] in (f16, u16, bf)
+
+
+def build(opt):
+    cl = ["setup"]; ops = []; hist = {}; nd = [0]; na = [0]
+
+    def add(eng, emit, rd, wr, cost, lat=0.08, kind="c", ninc=1, sem=None, after=(), ext=None):
+        me = len(ops); deps = set(after); acc = []
+        for v in rd:
+            acc.append((v, v["n"] == "ps"))
+            if v["off"] is not None:
+                acc.append((v["off"], False))
+        for v in wr:
+            acc.append((v, True))
+            if v["off"] is not None:
+                acc.append((v["off"], False))
+        dma = kind != "c"
+        for v, w in acc:
+            if v["n"] in IO:
+                continue
+            for (o, m, box, p, w0, d0) in hist.get(v["n"], []):
+                if (w or w0) and o != me and p[0] < v["p"][1] and v["p"][0] < p[1] and ((box & v["box"]) if (dma or d0) else (m & v["m"])):
+                    deps.add(o)
+        for v, w in acc:
+            if v["n"] in IO:
+                continue
+            h = hist.setdefault(v["n"], [])
+            if w:
+                h[:] = [e for e in h if not (e[3][0] >= v["p"][0] and e[3][1] <= v["p"][1] and (e[1] & ~v["m"]) == 0)]
+            h.append((me, v["m"], v["box"], v["p"], w, dma))
+        ops.append({"cl": cl[0], "up": opt["boost"].get(cl[0], 0.0), "tag": wr[0]["n"] if wr else "send", "e": eng, "f": emit, "deps": deps, "cost": cost, "lat": lat, "k": kind, "ninc": ninc, "sem": sem, "ext": ext})
+        return me
+
+    def ap(c, v):
+        if not isinstance(v, dict):
+            return v
+        a = c["T"][v["n"]][v["i"]]
+        return a if v["off"] is None else a.indirect(ap(c, v["off"]))
+
+    def vs(*xs):
+        return [x for x in xs if isinstance(x, dict)]
+
+    def vcost(out, ins, k):
+        if out["off"] is not None:
+            return 0.06 + out["c"] * SIG * CY
+        if ins and ins[0]["off"] is not None:
+            return 0.06 + out["c"] * GAM * CY
+        if all(two(x) for x in [out] + ins):
+            k = k * 0.5
+        return 0.03 + max(64, out["c"] * k) * CY
+
+    def cp(out, a):
+        return add("v", lambda c: [c["g"].vector.tensor_copy(ap(c, out), ap(c, a))], [a], [out], vcost(out, [a], 1))
+
+    def tt(out, a, b, op):
+        k = 1 if "ps" in (a["n"], b["n"]) else 2
+        return add("v", lambda c: [c["g"].vector.tensor_tensor(ap(c, out), ap(c, a), ap(c, b), op)], [a, b], [out], vcost(out, [a, b], k))
+
+    def ts(out, a, s1, op0, s2=None, op1=None):
+        if op1 is None:
+            f = lambda c: [c["g"].vector.tensor_scalar(ap(c, out), ap(c, a), ap(c, s1), None, op0)]
+        else:
+            f = lambda c: [c["g"].vector.tensor_scalar(ap(c, out), ap(c, a), ap(c, s1), ap(c, s2), op0, op1)]
+        return add("v", f, vs(a, s1, s2), [out], vcost(out, [a], 1))
+
+    def ms(out, x):
+        return add("v", lambda c: [c["g"].vector.memset(ap(c, out), x)], [], [out], vcost(out, [], 1))
+
+    def tr(out, a):
+        return add("v", lambda c: [c["g"].vector.transpose(ap(c, out), ap(c, a))], [a], [out], vcost(out, [a], 1))
+
+    def act(out, a, fn, scale=1.0, bias=0.0):
+        k = GAM if a["off"] is not None else 1
+        return add("s", lambda c: [c["g"].scalar.activation(ap(c, out), ap(c, a), fn, bias=ap(c, bias), scale=ap(c, scale))],
+                   vs(a, scale, bias), [out], 0.06 + max(64, out["c"] * k) * CY)
+
+    def dadd(out, a):
+        s = "d%d" % nd[0]; nd[0] += 1
+        return add("g", lambda c: [c["g"].dma_start(ap(c, out), ap(c, a), accum_op=A.add)], [a, out], [out], GI,
+                   lat=DL + out["c"] * 512 / DR, kind="d", sem=(s, 16))
+
+    def mm(lst):
+        cost = 0.02
+        for o, l, r, a, b in lst:
+            cost += max(min(64, l["c"]), r["c"]) * (1 if two(r) else 4) * PCY
+        return add("p", lambda c: [c["g"].tensor.matmul(ap(c, o), ap(c, l), ap(c, r), a, b) for o, l, r, a, b in lst],
+                   [x[1] for x in lst] + [x[2] for x in lst], [x[0] for x in lst], cost, lat=0.15, ninc=len(lst))
+
+    def mmg(lst, per=4):
+        full = [(o, l, r, j == 0, j == len(lst) - 1) for j, (o, l, r) in enumerate(lst)]
+        for j in range(0, len(full), per):
+            mm(full[j:j + per])
+
+    def iota(out, pat, base, cm):
+        isf = SB[out["n"]][1] != i32
+        if isf:
+            f = lambda c: [c["g"].iota(ap(c, out), pat, base, cm, allow_small_or_imprecise_dtypes=True)]
+        else:
+            f = lambda c: [c["g"].iota(ap(c, out), pat, base, cm)]
+        return add("g", f, [], [out], 0.13 + 2 * out["c"] * CY)
+
+    def dma(q, out, a, nbytes):
+        s = "d%d" % nd[0]; nd[0] += 1
+        def f(c):
+            e = {"y": c["g"].sync, "s": c["g"].scalar, "g": c["g"]}[q]
+            return [e.dma_start(ap(c, out), ap(c, a))]
+        return add(q, f, [a], [out], 1.0 if q == "g" else 0.1, lat=1.8 + nbytes / 200e3, kind="d", sem=(s, 16))
+
+    def send(pairs, credit):
+        k = na[0]; na[0] += 1
+        def f(c):
+            en = c["en"]; per = len(en) // len(pairs); trs = []
+            for j, (a, b) in enumerate(pairs):
+                trs.append(RemoteDMATransfer(dst_ids=[c["dst"]], dma_engine_mask=sum(1 << e for e in en[j * per:(j + 1) * per]),
+                                             remote_sem=c["T"].sem["a%d" % k], src=ap(c, a), dst=ap(c, b)))
+            c["g"].remote_dma_fused(trs, local_sem=c["T"].sem["l%d" % k])
+            return []
+        nb = len(pairs) * 65536
+        o = add("g", f, [a for a, b in pairs], [], 1.0, lat=1.5 + nb / 80e3, kind="r", sem=("l%d" % k, "en"),
+                after=[credit[0]] if credit else [], ext=credit[1] if credit else None)
+        add(None, None, [], [b for a, b in pairs], 0.0, lat=0.5, kind="x", sem=("a%d" % k, "en"), after=[o])
+
+    def credit(views):
+        k = na[0]; na[0] += 1
+        def f(c):
+            c["g"].remote_sem_update(c["T"].sem["a%d" % k], c["T"].sem["l%d" % k], c["up"][1], c["up"][0], c["upm"])
+            return []
+        o = add("g", f, [], views, 1.0, lat=2.0, kind="r", sem=("l%d" % k, 1))
+        return (o, ("a%d" % k, 1))
+
+    def ps(a, b, s=None):
+        return c2("ps", a, b, s)
+
+    def sel(name, i):
+        return c2(name, 16 - i, 144 - i)
+
+    def colv(j):
+        return c2("col", j, j + 1)
+
+    B4, B5, B6, B7 = 2048, 2560, 3072, 3584
+    I32, I16 = V_("i32m"), V_("i16m")
+
+    dma("y", V_("sdi"), V_("sd"), 57344); dma("s", V_("nri"), V_("nr"), 57344)
+    dma("y", V_("hsi", S_(0, 8), AL), V_("hs"), 16384)
+    dma("s", V_("tli"), V_("tl"), 917504)
+    dma("g", c2("uw", U0, G0), V_("u0"), 917504); dma("g", c2("uw", W0, W0 + 1024), V_("w0"), 524288)
+    dma("y", c2("thr", 0, 1), V_("th"), 4096)
+    iota(c2("pi", 0, 1), [[0, 1]], 0, 1)
+    iota(V_("xr"), [[1, 144]], -16, 0); iota(V_("md"), [[1, 8], [0, 16]], 0, 0); iota(V_("x16"), [[1, 16]], 0, 0)
+    P_, PM, PD, E0, P16, KV, KS, ZV0, ZV1, M0, M1, M2, M3, JL, KQ = [colv(j) for j in range(15)]
+    cp(P_, c2("pi", 0, 1))
+    ts(c2("pj", 0, 1), c2("pi", 0, 1), 15, A.bitwise_and); cp(PM, c2("pj", 0, 1))
+    ts(c2("pj", 1, 2), c2("pi", 0, 1), 4, A.arith_shift_right); cp(PD, c2("pj", 1, 2))
+    ts(V_("blk"), V_("md"), PD, A.is_equal)
+    ts(V_("ce"), V_("x16"), PM, A.is_equal)
+    for i in range(16):
+        if i % 2:
+            ts(c2("rowb", 128 * i, 128 * i + 128), V_("blk"), c2("ce", i, i + 1), A.mult)
+        else:
+            act(c2("rowb", 128 * i, 128 * i + 128), V_("blk"), F.Copy, c2("ce", i, i + 1))
+    ts(c2("pm", 0, 112), c2("xr", 32, 144), P_, A.is_equal); ts(c2("pm", 112, 128), c2("xr", 16, 32), P_, A.is_equal)
+    ts(P16, P_, 16.0, A.mult); ts(V_("b8"), V_("xr"), P16, A.is_equal)
+    ts(V_("b32"), V_("xr"), P_, A.is_equal, c2("ce", 0, 1), A.mult)
+    act(V_("b16"), V_("b32"), F.Copy); act(V_("b4k"), V_("b32"), F.Copy, 4096.0); act(V_("b162"), V_("b32"), F.Copy, 2.0)
+    ts(I32, c2("xr", 16, 144), P_, A.is_equal); act(I16, I32, F.Copy); act(V_("k16m"), I32, F.Copy, 1024.0)
+    ts(V_("sdf"), V_("sdi"), 2.0, A.mult, -1.0, A.add); ts(V_("nrf"), V_("nri"), 1024.0, A.add)
+    tt(V_("cb"), V_("sdf"), V_("nrf"), A.mult)
+    for b in range(4):
+        mm([(ps(512 * b + 112 * j, 512 * b + 112 * j + 112), c2("rowb", 128 * (4 * b + j), 128 * (4 * b + j) + 128), V_("cb"), True, True) for j in range(4)])
+        if b % 2:
+            cp(c2("cc", U0 + 448 * b, U0 + 448 * b + 448), ps(512 * b, 512 * b + 448))
+        else:
+            act(c2("cc", U0 + 448 * b, U0 + 448 * b + 448), ps(512 * b, 512 * b + 448), F.Copy)
+        cp(c2("cch", 448 * b, 448 * b + 448), ps(512 * b, 512 * b + 448))
+
+    def send_shifted(name, stage, bank, cr):
+        mm([(ps(bank, bank + 128), V_("pm"), c2(name, U0 + 128, U0 + 256), True, True)])
+        act(V_(stage), ps(bank, bank + 128), F.Copy)
+        send([(c2(name, U0, U0 + 128), c2(name, G0, G0 + 128)), (V_(stage), c2(name, G0 + 128, G0 + 256))], cr)
+
+    send_shifted("cc", "sc", B6, None)
+    send_shifted("uw", "su", B7, None)
+    cp(V_("hsf", S_(0, 8)), V_("hsi", S_(0, 8), AL))
+    for par in range(2):
+        mmg([(ps(B6 + 16 * par, B6 + 16 * par + 16), V_("b8", S_(0, 8), S_(16 - i, 144 - i)), V_("hsf", S_(0, 8), AL, 2 * i + par)) for i in range(16)], 16)
+    cp(V_("hix"), ps(B6, B6 + 32)); cp(V_("hw"), ps(B6, B6 + 32))
+    iota(V_("tab8"), [[8, 256]], 0, 0); act(V_("tab8h"), V_("tab8"), F.Copy)
+    iota(V_("jw"), [[16, 112]], 0, 0); ts(V_("jw"), V_("jw"), PM, A.add)
+    iota(V_("kk"), [[0, 32], [1, 4]], 0, 0); iota(V_("tz"), [[0, 16], [2, 2], [0, 4]], -1, 0)
+    iota(V_("tab32"), [[0, 2], [32, 64]], 0, 0); act(V_("tab32h"), V_("tab32"), F.Copy)
+    iota(V_("t128"), [[128, 16]], 0, 0); act(V_("t128h"), V_("t128"), F.Copy)
+    iota(V_("tabs"), [[1, 2], [2, 256]], 1024, 0)
+    iota(c2("uw", 0, U0), [[0, 256]], 0, 0); iota(c2("cc", 0, U0), [[0, 256]], 0, 0)
+    for h in range(2):
+        for j in range(2):
+            iota(c2("tt", 6144 * h + 1024 * j, 6144 * h + 1024 * j + 1024), [[0, 1024]], 0, 0)
+            iota(c2("tt", 6144 * h + 4096 + 1024 * j, 6144 * h + 5120 + 1024 * j), [[0, 1024]], 0, 0)
+    ms(V_("z16"), 0.0); ms(V_("mm"), 0.0)
+    act(V_("blk2k"), V_("blk"), F.Copy, 2048.0)
+    ts(c2("nth", 0, 1), c2("thr", 0, 1), -1.0, A.mult)
+    ts(V_("t1"), c2("xr", 16, 144), P_, A.is_gt, -2048.0, A.mult); tt(V_("t1"), V_("t1"), V_("blk"), A.mult); tt(V_("ym"), V_("t1"), I32, A.add)
+    ts(V_("cl"), V_("x16"), PM, A.is_gt)
+    for i in range(1, 16):
+        act(c2("tri", 128 * i, 128 * i + 128), V_("blk"), F.Copy, c2("cl", i, i + 1))
+    tt(V_("tz"), V_("tz"), V_("blk"), A.mult)
+    for L in range(2):
+        ts(M0, PM, -4.0 * L, A.add); ts(M1, PM, -4.0 * L - 8, A.add)
+        ts(V_("t1"), V_("kk"), M0, A.is_equal, 1024.0, A.mult); ts(V_("t2"), V_("kk"), M1, A.is_equal, 1028.0, A.mult)
+        tt(V_("t1"), V_("t1"), V_("t2"), A.add); tt(V_("t3"), V_("t1"), V_("tz"), A.mult)
+        for jl in range(2):
+            cp(V_("mm", AL, 2 * L + jl, AL, S_(8 * jl, 8 * jl + 8)), V_("t3", AL, AL, S_(8 * jl, 8 * jl + 8)))
+    ts(c2("pj", 2, 3), c2("pi", 0, 1), 3, A.bitwise_and); cp(KQ, c2("pj", 2, 3))
+    ts(JL, PM, 8.0, A.is_ge, 16.0, A.mult); tt(KV, JL, KQ, A.add); ts(KS, KV, 2056.0, A.add); ts(KV, KV, 2052.0, A.add)
+    ts(ZV0, PM, 8.0, A.mult, 1.0, A.add); ts(ZV1, PM, 8.0, A.mult, 5.0, A.add)
+    ms(KQ, 1792.0); ts(V_("j2k"), c2("jw", 0, 16), 2048.0, A.add); act(V_("n32m"), I32, F.Copy, -1.0)
+    q = 0
+    for a in range(4):
+        for r1 in range(2):
+            for h in range(2):
+                dma("y", V_("lsw", S_(32 * a + 16 * r1, 32 * a + 16 * r1 + 16), h, AL),
+                    V_("tl", S_(32 * a + 16 * h, 32 * a + 16 * h + 16), S_(896 * r1, 896 * r1 + 896)), 57344 * 4)
+
+    def turn(t):
+        for h in range(2):
+            cp(V_("ftr", AL, AL, S_(16 * h, 16 * h + 16)), V_("lsw", AL, h, S_(t, 896, 4)))
+        tr(V_("tlt"), V_("ftr"))
+
+    def names(t):
+        par = t % 2
+        cp(V_("nmf"), ind(c2("tli", 0, NV), c2("hix", 16 * par, 16 * par + 16)))
+        cp(V_("nix", AL, par, AL), V_("nmf"))
+        act(V_("n1"), V_("nmf"), F.Relu, -1.0, KQ)
+
+    def nixv(t, a, b):
+        return V_("nix", AL, t % 2, S_(a, b))
+
+    def view_lists(t):
+        mmg([(ps(B6, B6 + 112), sel("b162", i), c2("cch", i, NV, 16)) for i in range(16)], 8)
+        tt(c2("f0", 0, 112), ps(B6, B6 + 112), V_("jw"), A.max)
+        ts(V_("f1"), ps(B6, B6 + 112), -1.0, A.mult, 1.0, A.add)
+        tt(c2("f0", 112, 224), V_("f1"), V_("jw"), A.max)
+        cp(V_("vix"), V_("f0"))
+
+    def node_lists(t):
+        if t:
+            for j in range(2):
+                act(c2("cch", 896 * j, 896 * j + 896), c2("cc", U0 + 896 * j, U0 + 896 * j + 896), F.Copy)
+        mmg([(ps(B7, B7 + 28), sel("b16", i), c2("cch", 4 * i + t, NV, 64)) for i in range(16)], 16)
+        act(V_("sgw"), ps(B7, B7 + 28), F.Sign)
+        lst = [(ps(B7, B7 + 448), V_("z16"), c2("rowb", 0, 448))]
+        for r in range(2):
+            for k in range(16):
+                o = ps(B7 + 224 * r + 14 * k, B7 + 224 * r + 14 * k + 14)
+                lst.append((o, I16, V_("tlt", AL, AL, 16 * r + k)))
+                lst.append((o, V_("k16m"), c2("sgw", 14 * r, 14 * r + 14)))
+        mmg(lst, 16)
+        ts(V_("six%d" % (t % 2)), ps(B7, B7 + 448), 1024.0, A.add)
+
+    def sides(t):
+        par = t % 2
+        for c in range(4):
+            bk = (B6, B7)[c % 2]
+            act(c2("gg", 1024 * c, 1024 * c + 1024), ind(c2("cc", U0, W0), nixv(t, 64 * c, 64 * c + 64)), F.Sign)
+            mmg([(ps(bk, bk + 64), c2("rowb", 0, 128), c2("tab8h", 64 * c, 64 * c + 64))] +
+                [(ps(bk, bk + 64), sel("b16", k), c2("gg", 1024 * c + k, 1024 * c + 1024, 16)) for k in range(16)], 17)
+            ts(c2("uix", 64 * c, 64 * c + 64), ps(bk, bk + 64), 1.0 + 4 * par, A.add, 0.5, A.mult)
+            tt(c2("sg", 64 * c, 64 * c + 64), ps(bk, bk + 64), c2("tab8", 64 * c, 64 * c + 64), A.subtract)
+
+    def pair_lists(t):
+        for L in range(2):
+            o = ps(B6 + 128 * L, B6 + 128 * L + 128)
+            mmg([(o, c2("rowb", 0, 128), V_("tab32h"))] + [(o, V_("mm", AL, 2 * L + jl), c2("sg", jl, 256, 2)) for jl in range(2)])
+        ts(c2("lix", 0, 128), ps(B6, B6 + 128), KV, A.add); ts(c2("lix", 128, 256), ps(B6 + 128, B6 + 256), KS, A.add)
+
+    def candidates(t):
+        tt(V_("ts"), V_("n1"), V_("sg"), A.mult)
+        act(c2("cab", 0, 256), V_("ts"), F.Relu); act(c2("cab", 256, 512), V_("ts"), F.Relu, -1.0)
+        mm([(ps(B7, B7 + 512), V_("ym"), V_("cab"), True, True)])
+        act(V_("sel"), ps(B7, B7 + 512), F.Relu)
+        mm([(ps(B7, B7 + 512), V_("blk"), V_("sel"), True, True)])
+        act(V_("cand"), ps(B7, B7 + 512), F.Copy)
+
+    def step1(t, r):
+        vw = "vw%d" % (t % 2); win = c2(vw, 0, 4096); ue = V_("uexp", AL, r, AL)
+        def d(k, n=1): return c2("d2", 448 * k, 448 * (k + n))
+        def qq(k, n=1): return c2("rb", 448 * k, 448 * (k + n))
+        def gat(k):
+            x = ind(win, c2("six%d" % (t % 2), 224 * r + 28 * k, 224 * r + 28 * k + 28))
+            if k in opt["s1un"][r]:
+                act(d(k), x, F.Copy); dadd(d(k), ue)
+            else:
+                tt(d(k), x, ue, A.add)
+        s1, s2 = ps(B4, B4 + 448), ps(B5, B5 + 448)
+        lo, hi = ps(B4, B4 + 224), ps(B4 + 224, B4 + 448)
+        cc1 = c2("rb", 448 * 8, 448 * 8 + 224)
+        unew = c2("uw", U0 + 896 * r + t, U0 + 896 * r + 896, 4); uold = V_("uexp", AL, r, S_(0, 224))
+        if opt["tree_dma"]:
+            sq = (1, 5, 3, 7, 0, 4, 2, 6); q0 = 448 * (0, 4)[r]
+            def qq(k, n=1):
+                k = ((0, 1, 2, 3, 4, 5, 6, 7), (4, 5, 6, 7, 2, 3, 0, 1))[r][k]
+                return c2("rb", 448 * k, 448 * (k + n))
+            def one(j, n):
+                for i in range(j, j + n):
+                    x = ind(win, c2("six%d" % (t % 2), 224 * r + 28 * sq[i], 224 * r + 28 * sq[i] + 28))
+                    if i in opt["s1un"][r]:
+                        act(d(i), x, F.Copy); dadd(d(i), ue)
+                    else:
+                        tt(d(i), x, ue, A.add)
+            for j in (0, 2, 4):
+                bk = 1024 * ((j // 2) % 2)
+                if j in opt["s1pe"][r]:
+                    for i in (j, j + 1):
+                        o = ps(bk + 512 * (i - j), bk + 512 * (i - j) + 448)
+                        act(d(i), ind(win, c2("six%d" % (t % 2), 224 * r + 28 * sq[i], 224 * r + 28 * sq[i] + 28)), F.Copy)
+                        mm([(o, I32, ue, True, False)]); mm([(o, I32, d(i), False, True)])
+                        act(d(i), o, F.Abs); tt(qq(i), d(i), o, A.mult)
+                else:
+                    one(j, 2); act(ps(bk, bk + 896), d(j, 2), F.Abs); tt(qq(j, 2), d(j, 2), ps(bk, bk + 896), A.mult)
+                if j < 4:
+                    dadd(qq(j), qq(j + 1))
+                if j == 2:
+                    dadd(qq(0), qq(2))
+            mm([(s1, I32, qq(4), True, False)]); mm([(s1, I32, qq(5), False, opt["tail"][r] == "v")])
+            a, b = ps(1024, 1472), ps(1536, 1984)
+            one(6, 1); act(a, d(6), F.Abs); tt(a, d(6), a, A.mult)
+            one(7, 1); act(b, d(7), F.Abs); tt(qq(7), d(7), b, A.mult)
+            tt(qq(6), a, qq(7), A.add)
+            if opt["tail"][r] == "v":
+                tt(s1, s1, qq(6), A.add)
+                tt(cc1, hi, c2("rb", q0 + 224, q0 + 448), A.add); tt(lo, lo, c2("rb", q0, q0 + 224), A.add)
+                tt(lo, lo, cc1, A.add); ts(lo, lo, 0.015625, A.mult)
+            else:
+                mm([(s1, I32, qq(6), False, False)]); mm([(s1, I32, qq(0), False, True)])
+                act(cc1, hi, F.Copy); tt(lo, lo, cc1, A.add); act(lo, lo, F.Copy, 0.015625)
+            tt(unew, lo, uold, A.subtract)
+            return
+        if opt["tree_pe"]:
+            for k, bk in ((0, 0), (4, 1024)):
+                gat(k); gat(k + 1)
+                act(ps(bk, bk + 896), d(k, 2), F.Abs)
+                tt(qq(k, 2), d(k, 2), ps(bk, bk + 896), A.mult)
+                mm([(s1, I32, qq(k), k == 0, False)]); mm([(s2, I32, qq(k + 1), k == 0, k == 4)])
+        else:
+            for k, bk, s in ((0, 0, s1), (1, 512, s2)):
+                gat(k); act(s, d(k), F.Abs); tt(s, d(k), s, A.mult)
+                gat(k + 4); act(ps(bk, bk + 448), d(k + 4), F.Abs); tt(qq(k + 4), d(k + 4), ps(bk, bk + 448), A.mult)
+                tt(s, s, qq(k + 4), A.add)
+        for k, bk in ((2, 0), (3, 1024)):
+            a, b = ps(bk, bk + 448), ps(bk + 512, bk + 960)
+            gat(k); act(a, d(k), F.Abs); tt(a, d(k), a, A.mult)
+            gat(k + 4); act(b, d(k + 4), F.Abs); tt(qq(k + 4), d(k + 4), b, A.mult)
+            tt(qq(k), a, qq(k + 4), A.add)
+            if k == 2:
+                if opt["tree_pe"]:
+                    mm([(s1, I32, qq(2), False, True)])
+                else:
+                    tt(s1, s1, qq(2), A.add)
+        tt(qq(7), s2, qq(3), A.add)
+        tt(cc1, hi, c2("rb", 448 * 7 + 224, 448 * 8), A.add)
+        tt(lo, lo, c2("rb", 448 * 7, 448 * 7 + 224), A.add)
+        tt(lo, lo, cc1, A.add)
+        if opt["tail"][r] == "v":
+            ts(lo, lo, 0.015625, A.mult)
+        else:
+            act(lo, lo, F.Copy, 0.015625)
+        tt(unew, lo, uold, A.subtract)
+
+    turn(0); names(0); view_lists(0); sides(0); node_lists(0); pair_lists(0); candidates(0)
+    cr = None
+    for t in range(RO):
+        par = t % 2; last = t == RO - 1; vw = "vw%d" % par
+        vwin = c2("uw", U0, W0 + 1024); cl[0] = "gv"
+        for z in range(2):
+            o = c2(vw, 2048 * z, 2048 * z + 256); x = ind(vwin, c2("vix", 112 * z, 112 * z + 16))
+            if opt["gvv"]:
+                cp(o, x)
+            else:
+                act(o, x, F.Copy)
+        mm([(ps(B6 + 128 * z, B6 + 128 * z + 128), V_("pm"), c2(vw, 2048 * z + 128, 2048 * z + 256), True, True) for z in range(2)])
+        act(V_("sv"), ps(B6, B6 + 256), F.Copy)
+        send([(c2(vw, 0, 128), c2(vw, NV, NV + 128)), (c2("sv", 0, 128), c2(vw, NV + 128, NV + 256)),
+              (c2(vw, 2048, 2176), c2(vw, 2048 + NV, 2048 + NV + 128)), (c2("sv", 128, 256), c2(vw, 2048 + NV + 128, 4096))], cr)
+        cl[0] = "s2"
+        for c in range(4):
+            a, b = 1024 * c, 1024 * c + 1024; bk = 1024 * (c % 2); h = c // 2
+            act(c2("uu", a, b), ind(c2("uw", W0, W0 + 1024), c2("uix", 64 * c, 64 * c + 64)), F.Copy, -1.0)
+            x = ind(c2("uw", U0, W0), nixv(t, 64 * c, 64 * c + 64))
+            tt(c2("uu", a, b), x, c2("uu", a, b), A.add)
+            act(ps(bk, bk + 1024), c2("uu", a, b), F.Abs)
+            q0 = 6144 * h + 2048 + 1024 * (c % 2)
+            tt(c2("tt", q0, q0 + 1024), c2("uu", a, b), ps(bk, bk + 1024), A.mult)
+            if c < 2:
+                z = c
+                for j in range(2):
+                    cl[0] = "vw"
+                    o = c2(vw, 2048 * z + 256 + 768 * j, 2048 * z + 1024 + 768 * j); x = ind(vwin, c2("vix", 112 * z + 16 + 48 * j, 112 * z + 64 + 48 * j))
+                    if 2 * z + j in opt["vwv"]:
+                        cp(o, x)
+                    else:
+                        act(o, x, F.Copy)
+            if c == 2:
+                cl[0] = "ue"
+                for r in range(2):
+                    for j in range(2):
+                        act(V_("uexp", AL, r, S_(224 * j, 224 * j + 224)), c2("uw", U0 + 896 * r + t, U0 + 896 * r + 896, 4), F.Copy, -1.0)
+            cl[0] = "s2"
+            if c % 2:
+                q0 = 6144 * h + 2048
+                for k in range(8):
+                    o = c2("tt", q0 + 2056 + k, q0 + 4096, 16); x = c2("tt", q0 + k, q0 + 2048, 16); y = c2("tt", q0 + 8 + k, q0 + 2048, 16)
+                    if opt["pair_pe"]:
+                        pb = ps(B4 + 128 * k, B4 + 128 * k + 128)
+                        mm([(pb, I32, x, True, False), (pb, I32, y, False, True)])
+                        if k % 4 == 3:
+                            for k2 in range(k - 3, k + 1):
+                                act(c2("tt", q0 + 2056 + k2, q0 + 4096, 16), ps(B4 + 128 * k2, B4 + 128 * k2 + 128), F.Copy)
+                    else:
+                        tt(o, x, y, A.add)
+        if not last:
+            other = "vw%d" % (1 - par)
+            cr = credit([c2("uw", G0, W0), c2("cc", G0, W0), c2(other, NV, 2048), c2(other, 2048 + NV, 4096)])
+        for h in range(2):
+            win = c2("tt", 6144 * h, 6144 * h + 6144); a, b = 1024 * h, 1024 * h + 1024
+            a, b = a + 3840, b + 3840; rr = c2("rb", a, b)
+            act(rr, ind(win, c2("lix", 128 + 64 * h, 192 + 64 * h)), F.Copy)
+            tt(c2("rb", a, b), ind(win, c2("lix", 64 * h, 64 * h + 64)), rr, A.add)
+            bk = (B4, B5)[h]; o = ps(bk, bk + 256); cc1 = c2("c1", 256 * h, 256 * h + 256)
+            if opt["c1_pe"]:
+                o1 = ps(B7, B7 + 256)
+                mm([(o1, I32, c2("rb", a + 1, b, 4), True, False), (o1, I32, c2("rb", a + 3, b, 4), False, True)])
+                act(cc1, o1, F.Copy)
+            else:
+                tt(cc1, c2("rb", a + 1, b, 4), c2("rb", a + 3, b, 4), A.add)
+            if opt["lvl_pe"]:
+                mm([(o, I32, c2("rb", a, b, 4), True, False), (o, I32, c2("rb", a + 2, b, 4), False, False)])
+                mm([(o, I32, cc1, False, True)])
+            else:
+                tt(o, c2("rb", a, b, 4), c2("rb", a + 2, b, 4), A.add); tt(o, o, cc1, A.add)
+            act(o, o, F.Copy, 0.015625)
+            for z in range(2):
+                w = c2("uw", W0 + 512 * h + 2 * par + z, W0 + 512 * h + 512, 4)
+                tt(w, ps(bk + z, bk + 256, 2), w, A.add)
+        if last:
+            dma("y", V_("ys"), c2("uw", W0, W0 + 1024), 524288)
+        cl[0] = "s3"
+        n0, n1 = c2("uw", W0 + 2 * par, W0 + 1024, 4), c2("uw", W0 + 2 * par + 1, W0 + 1024, 4)
+        if opt["dd_pe"]:
+            dd = ps(B7, B7 + 256)
+            mm([(dd, I32, n0, True, False), (dd, V_("n32m"), n1, False, True)])
+        else:
+            dd = V_("dd"); tt(dd, n0, n1, A.subtract)
+        ts(c2("ud", 0, 256), dd, c2("thr", 0, 1), A.is_gt, 0.5, A.subtract)
+        ts(c2("ud", 256, 512), dd, c2("nth", 0, 1), A.is_lt, 0.5, A.subtract)
+        mm([(ps(B6, B6 + 512), V_("blk2k"), V_("ud"), True, True)])
+        tt(V_("rab"), ps(B6, B6 + 512), V_("cand"), A.min)
+        act(V_("cz", AL, 1, AL), ps(B6 + 256, B6 + 512), F.Sign); act(V_("zs"), ps(B6 + 256, B6 + 512), F.Sign)
+        tt(V_("cz", AL, 0, AL), c2("rab", 0, 256), c2("rab", 256, 512), A.max)
+        mmg([(ps(B7, B7 + 16), sel("b16", i), V_("cz", AL, 0, S_(i, 256, 16))) for i in range(16)], 16)
+        cp(V_("cw"), ps(B7, B7 + 16))
+        mmg([(ps(B7, B7 + 16), c2("rowb", 0, 128), V_("t128h"))] + [(ps(B7, B7 + 16), sel("b16", i), V_("cz", AL, 1, S_(i, 256, 16))) for i in range(16)], 17)
+        mm([(ps(B6, B6 + 256), V_("z16"), c2("rowb", 0, 256), True, False)])
+        for a in range(16):
+            ts(c2("gg", 256 * a, 256 * a + 256 - 16 * a), V_("cz", AL, 0, S_(16 * a, 256)), c2("cw", a, a + 1), A.is_equal)
+            if a < 15:
+                mm([(ps(B6 + 16 * a + 16, B6 + 256), V_("blk"), c2("gg", 256 * a + 16, 256 * a + 256 - 16 * a), False, False)])
+        mm([(ps(B6 + i, B6 + 256, 16), c2("tri", 128 * i, 128 * i + 128), c2("gg", i, 4096, 256), False, i == 15) for i in range(1, 16)])
+        ts(V_("vlx"), ps(B7, B7 + 16), (ZV0, ZV1)[par], A.add, 0.5, A.mult)
+        act(V_("val"), ind(c2("uw", W0, W0 + 1024), V_("vlx")), F.Copy)
+        ts(V_("cwm"), V_("cw"), 0.0, A.is_gt, 4.0, A.mult); ts(V_("cwp"), V_("cw"), -1.0, A.mult, 0.0, A.min)
+        act(V_("neg"), ps(B6, B6 + 256), F.Sign, -1.0)
+        mmg([(ps(B7, B7 + 16), I16, V_("cwp")), (ps(B7, B7 + 16), V_("k16m"), V_("cwm"))] +
+            [(ps(B7, B7 + 16), sel("b4k", i), c2("neg", i, 256, 16)) for i in range(16)], 18)
+        tt(V_("tgf"), ps(B7, B7 + 16), V_("j2k"), A.max); ts(V_("tgx"), V_("tgf"), -2048.0, A.add)
+        tt(ind(c2("cc", 0, G0), V_("tgx")), V_("zs"), c2("tabs", 256 * par, 256 * par + 256), A.mult)
+        if not last:
+            send_shifted("cc", "sc", B6, cr)
+            names(t + 1); cl[0] = "prep"; turn(t + 1)
+        cl[0] = "prep"
+        hw = c2("hw", 16 * par, 16 * par + 16)
+        ts(V_("h1"), V_("tgf"), 2304.0, A.is_ge, -4096.0, A.mult); ts(V_("h2"), V_("tgf"), -2304.0, A.add)
+        tt(V_("h1"), V_("h1"), hw, A.add); tt(hw, V_("h1"), V_("h2"), A.max)
+        if t < 2:
+            cp(c2("hix", 16 * par, 16 * par + 16), hw)
+        if not last:
+            node_lists(t + 1); view_lists(t + 1); cl[0] = "sides"; sides(t + 1); cl[0] = "cand"; pair_lists(t + 1); candidates(t + 1)
+        else:
+            for j in range(2):
+                act(c2("cch", 896 * j, 896 * j + 896), c2("cc", U0 + 896 * j, U0 + 896 * j + 896), F.Copy)
+            mmg([(ps(B6, B6 + 112), sel("b162", i), c2("cch", 112 * i, 112 * i + 112)) for i in range(16)], 8)
+            ts(V_("yc1"), ps(B6, B6 + 112), -2047.0, A.add); ts(V_("yc2"), ps(B6, B6 + 112), -1.0, A.mult, -2048.0, A.add)
+            tt(V_("yc1"), V_("yc1"), V_("yc2"), A.max)
+            dma("y", V_("yc"), V_("yc1"), 57344)
+            cp(V_("hw16"), V_("hw"))
+            mm([(V_("ps", S_(0, 8), S_(B7 + 2 * i + p2, B7 + 512, 32)), c2("rowb", 128 * i, 128 * i + 128, 16), c2("hw16", 16 * p2, 16 * p2 + 16), True, True)
+                for i in range(16) for p2 in range(2)])
+            act(V_("cand", S_(0, 8), AL), V_("ps", S_(0, 8), S_(B7, B7 + 512)), F.Copy)
+            dma("y", V_("yh"), V_("cand", S_(0, 8), AL), 16384)
+        cl[0] = "A"
+        step1(t, 0)
+        cp(ind(c2("uw", 0, G0), V_("tgx")), V_("val"))
+        if not last:
+            send_shifted("uw", "su", B5, cr)
+        else:
+            dma("y", c2("yu", 0, 896), c2("uw", U0, U0 + 896), 458752)
+        cl[0] = "B"
+        step1(t, 1)
+        cp(ind(c2("uw", 0, G0), V_("tgx")), V_("val"))
+    dma("y", c2("yu", 896, 1344), c2("uw", U0 + 896, U0 + 1344), 229376)
+    dma("s", c2("yu", 1344, NV), c2("uw", U0 + 1344, G0), 229376)
+    return ops
+
+
+def plan(ops):
+    n = len(ops); succ = [[] for _ in ops]
+    for j, o in enumerate(ops):
+        for d in o["deps"]:
+            succ[d].append(j)
+    def gap(d, j):
+        return 0.0 if (ops[d]["e"] == "p" and ops[j]["e"] == "p") else ops[d]["lat"]
+    pri = [0.0] * n
+    for j in range(n - 1, -1, -1):
+        pri[j] = ops[j]["cost"] + max([gap(j, s) + pri[s] for s in succ[j]] + [ops[j]["lat"]])
+    left = [len(o["deps"]) for o in ops]; rdy = [0.0] * n; end = [0.0] * n; start = [0.0] * n
+    free = {e: 0.0 for e in "vspgy"}; pool = {e: [] for e in "vspgy"}; order = []
+    def release(j):
+        for s in succ[j]:
+            rdy[s] = max(rdy[s], end[j] + gap(j, s)); left[s] -= 1
+            if left[s] == 0:
+                if ops[s]["e"] is None:
+                    start[s] = end[s] = rdy[s]; order.append(s); release(s)
+                else:
+                    pool[ops[s]["e"]].append(s)
+    for j in range(n):
+        if left[j] == 0:
+            pool[ops[j]["e"]].append(j)
+    while len(order) < n:
+        best = None
+        for e in pool:
+            if pool[e]:
+                tnow = max(free[e], min(rdy[j] for j in pool[e]))
+                if best is None or tnow < best[0]:
+                    best = (tnow, e)
+        tnow, e = best
+        j = max([x for x in pool[e] if rdy[x] <= tnow + 0.05], key=lambda x: (pri[x] + ops[x]["up"], -x))
+        soon = [x for x in pool[e] if rdy[x] <= tnow + LOOK * ops[j]["cost"]]
+        j = max(soon + [j], key=lambda x: (pri[x] + ops[x]["up"], -x))
+        pool[e].remove(j); start[j] = max(tnow, rdy[j]); end[j] = start[j] + ops[j]["cost"]; free[e] = end[j]
+        order.append(j); release(j)
+
+    def place(seq, links):
+        st = [0.0] * n; busy = {e: [] for e in "vspgy"}
+        for j in seq:
+            o = ops[j]; r = 0.0; w = o["cost"]
+            for d, gp in links[j]:
+                r = max(r, st[d] + ops[d]["cost"] + gp)
+            if o["e"] is not None:
+                b = busy[o["e"]]; k = len(b)
+                while k > 0 and b[k - 1][1] > r:
+                    k -= 1
+                while k < len(b) and b[k][0] < r + w - 1e-9:
+                    r = max(r, b[k][1]); k += 1
+                b.insert(k, (r, r + w))
+            st[j] = r
+        return st
+    fw = [[(d, gap(d, j)) for d in ops[j]["deps"]] for j in range(n)]
+    bw = [[(s, gap(j, s)) for s in succ[j]] for j in range(n)]
+    span = lambda st: max(st[j] + ops[j]["cost"] + ops[j]["lat"] for j in range(n))
+    best = span(start); st = start
+    for it in range(PASSES):
+        sb = place(sorted(range(n), key=lambda j: (-(st[j] + ops[j]["cost"]), -j)), bw)
+        st = place(sorted(range(n), key=lambda j: (-(sb[j] + ops[j]["cost"]), j)), fw)
+        if span(st) < best:
+            best = span(st); start = st
+    order = sorted(range(n), key=lambda j: (start[j], j))
+    return order, start, [start[j] + ops[j]["cost"] for j in range(n)]
+
+
+CACHE = {}
+
+
+def rank_program(g, core, T, topo):
+    rank = T.rank_of(core)
+    if rank is None:
+        return
+    if "ops" not in CACHE:
+        CACHE["ops"] = build(OPT); CACHE["plan"] = plan(CACHE["ops"])
+    ops = CACHE["ops"]; order = CACHE["plan"][0]
+    nr = len(T.cores); dst = T.cores[(rank - 1) % nr]; up = T.cores[(rank + 1) % nr]
+    rid, pid = topo.addr(dst)[:2]
+    en = topo.engines(core, dst); inn = len(topo.engines(up, core))
+    c = {"g": g, "T": T, "dst": DstId(rid=rid, pnc=pid), "en": en, "up": topo.addr(up)[:2], "upm": 1 << topo.engines(core, up)[0]}
+    queue = {"v": g.vector, "s": g.scalar, "p": g.tensor, "g": g, "y": g.sync}
+    own = {"v": "v", "s": "s", "p": "p", "g": "gq"}
+    count = {}; token = {}; known = {e: {} for e in queue}; total = {}
+
+    def wait(e, s, k):
+        if known[e].get(s, 0) < k:
+            queue[e].wait_ge(T.sem[s], k); known[e][s] = k
+
+    for j in order:
+        o = ops[j]; e = o["e"]
+        if o["k"] == "x":
+            token[j] = (o["sem"][0], inn); total[o["sem"][0]] = inn
+            continue
+        need = {}
+        for d in o["deps"]:
+            if (e == "p" and ops[d]["e"] == "p") or (o["k"] == "r" and ops[d]["k"] == "r" and ops[d]["sem"][1] == 1):
+                continue
+            s, k = token[d]; need[s] = max(need.get(s, 0), k)
+        if o["ext"]:
+            need[o["ext"][0]] = o["ext"][1]; total[o["ext"][0]] = o["ext"][1]
+        for s in sorted(need):
+            wait(e, s, need[s])
+        ins = o["f"](c)
+        if o["k"] == "c":
+            s = own[e]
+            for x in ins:
+                x.then_inc(T.sem[s], 1)
+            count[s] = count.get(s, 0) + len(ins); token[j] = (s, count[s]); total[s] = count[s]
+        elif o["k"] == "d":
+            ins[0].then_inc(T.sem[o["sem"][0]], 16); token[j] = o["sem"]; total[o["sem"][0]] = 16
+        else:
+            k = len(en) if o["sem"][1] == "en" else 1
+            token[j] = (o["sem"][0], k); total[o["sem"][0]] = k
+    for s in sorted(total):
+        if max(known[e].get(s, 0) for e in known) < total[s]:
+            wait("y", s, total[s])

@@ -5,39 +5,66 @@ A = AluOpType
 F = ActivationFunctionType
 
 NV, NG, NS, RO = 1792, 256, 512, 4
-U0 = 256
+D0 = 1024
+U0 = D0 + 256
 G0 = U0 + NV
-W0 = G0 + NG
-OPT = {"pair_pe": False, "tree_pe": True, "lvl_pe": True, "c1_pe": True, "dd_pe": False, "tree_dma": True,
-       "tail": "sv", "s1un": ((), ()), "s1pe": ((), ()), "vwv": (), "gvv": False,
-       "boost": {"s2": 36.3, "s3": 27.1, "sides": 174.9, "cand": -43.1, "gv": 33.3, "vw": 1.1, "ue": 5.6, "prep": 1.1, "A": -3.8, "B": -7.4}}
+UE = G0 + NG
+C0 = 256
+SLOT = (4, 0, 6, 2, 5, 1, 7, 3)
+OPT = {"pair": "pppp", "val": "ab", "dd": "p", "c1": "ppv", "scale2": "sss", "grp": ((0, 2), (2, 3), (3, 4)), "fine": (3,), "cch": "gggg", "ue": "g", "const": "g", "nm": "s", "cab": "p",
+       "sides": "ssss", "ucol": "ssss", "rr": "ssss", "gv": "ss", "vA": "ss", "vB": "ss", "vAearly": True,
+       "treeA": "dddv", "treeB": "ddvv", "tail": "ps", "scale1": "ss", "eng": {}, "once": False, "wide": True, "peA": (), "peB": (), "dmaA": (), "dmaB": (),
+       "boost": {"uc0": -2, "uc1": 0, "uc2": 3, "uc3": 5, "x0": 0, "x1": 1.5, "x2": 4.5, "x3": 6.5, "vB": 1, "m0": 2, "m1": 4, "m2": 7, "m3": 9,
+                 "l0": 7, "l1": 8, "l2": 11, "l3": 12, "w0": 10, "w1": 13, "w2": 14, "s3": 16, "A0": 8, "A1": 10, "A2": 14, "A3": 17, "At": 22,
+                 "names": 18, "turn": 20, "host": 27, "cch": 26.5, "vl": 27.5, "nl": 38, "B0": 26, "B1": 28, "B2": 31, "B3": 33, "Bt": 36,
+                 "gv": 29, "vA": 30, "sd0": 31, "sd1": 32.5, "sd2": 34, "sd3": 35.5, "pl": 38, "cand": 40, "ue": 30, "uf": 44}}
+OPT.update({"pair": "pppx", "val": "g", "dd": "v", "treeA": "dddd", "treeB": "ddpv", "tail": "pp", "dmaA": (2, 3), "dmaB": (2,),
+            "sides@0": "svsv", "vA@0": "sv", "vB@0": "sv", "pair@3": "pppv", "dmaB@3": (2, 3), "treeB@3": "ddvv",
+            "boost": {'uc0': -3.0, 'uc1': -1.5, 'uc2': 3.0, 'uc3': 2.5, 'x0': -0.5, 'x1': 1.0, 'x2': 2.5, 'x3': 4.0, 'vB': 8.5, 'm0': 2.0, 'm1': 3.5,
+                      'm2': 10.0, 'm3': 10.5, 'l0': 7.5, 'l1': -2.0, 'l2': 14.0, 'l3': -4.0, 'w0': 10.5, 'w1': 11.0, 'w2': 17.0, 's3': -13.5,
+                      'A0': -23.5, 'A1': 13.0, 'A2': 16.0, 'A3': 20.0, 'At': 22.0, 'names': -18.5, 'turn': 15.0, 'host': 11.0, 'cch': 25.5,
+                      'vl': 27.0, 'nl': 57.5, 'B0': 22.0, 'B1': 28.5, 'B2': 32.0, 'B3': 29.5, 'Bt': 40.5, 'gv': 19.5, 'vA': 30.0, 'sd0': 9.0,
+                      'sd1': 11.5, 'sd2': 38.5, 'sd3': 36.0, 'pl': 23.0, 'cand': 23.0, 'ue': 16.0, 'uf': 43.0, 'B@3': -4.5, 'A@3': -2.0,
+                      'v@-1': -1.0, 's@-1': 6.5}})
+OPT.update({"dmaA": (), "dmaB": (), "peA": (3,), "peB": (2,), "dmaB@3": (), "peA@3": (2, 3), "peB@3": (0, 2), "treeA": "dddd", "treeB": "ddvv",
+            "ucol": "svss", "sides": "vsss", "gv": "vs", "eng": {"nl.sgw": "v", "Bt.ps": "v", "Bt.hi1": "v", "s3.cw": "s"},
+            "boost": {'vB': 4.5, 'uc0': -4.0, 'x0': 0.0, 'm0': 3.5, 'uc1': -5.0, 'x1': 1.5, 'm1': 4.5, 'uc2': 0.0, 'x2': 6.0, 'm2': 9.0, 'uc3': 0.0,
+                      'x3': 5.0, 'm3': 8.5, 'l0': 10.5, 'l1': 10.0, 'l2': 14.5, 'l3': 14.5, 'w0': 15.0, 'w1': 17.0, 'w2': 17.5, 's3': 23.5,
+                      'names': 12, 'turn': 5, 'host': 28.5, 'cch': 30.5, 'vl': 34.5, 'nl': 41.5, 'sd0': 36, 'sd1': 36.5, 'sd2': 41.0,
+                      'sd3': 37.0, 'pl': 46.5, 'cand': 50.0, 'A0': 12.0, 'A1': 14.5, 'A2': 17.5, 'A3': 17.0, 'At': 29.5, 'gv': 41.0,
+                      'vA': 40.0, 'ue': 36.0, 'B0': 26.5, 'B1': 26.0, 'B2': 31.0, 'B3': 30.5, 'Bt': 39.0, 'uf': 44.5}})
+OPT.update({"dmaA": (2, 3), "dmaB": (2,), "peA": (), "peB": (), "dmaB@3": (2, 3), "peA@3": (), "peB@3": (), "treeA": "dddd", "treeB": "dddv",
+            "treeB@3": "ddvv", "wide": False, "pair": "ddxx", "pair@3": "ddxx",
+            "dmaA": (0, 1, 3), "dmaB": (2,), "treeB": "ddvv", "c1": "vvv", "tail": "ss", "cab": "v"})
 f32, f16, i32, u16, bf = "float32", "float16", "int32", "uint16", "bfloat16"
 SB = {
-    "uw": ([128, W0 + 1024], f32), "cc": ([128, W0], f32), "vw0": ([128, 4096], f32), "vw1": ([128, 4096], f32),
+    "uw": ([128, UE], f32), "cc": ([128, C0 + NV + NG], f32), "vw0": ([128, 4096], f32), "vw1": ([128, 4096], f32),
     "tli": ([128, NV], i32), "lsw": ([128, 2, 896], i32), "ftr": ([128, 14, 32], f16), "tlt": ([128, 14, 32], f16),
-    "tt": ([128, 12288], f32), "d2": ([128, 3584], f32), "uu": ([128, 4096], f32), "gg": ([128, 4096], f16),
-    "rb": ([128, 5888], f32), "c1": ([128, 512], f32), "uexp": ([128, 2, 448], f32),
+    "tt": ([128, 8192], f32), "d2": ([128, 3584], f32), "uu": ([128, 4096], f32), "gg": ([128, 4096], f16),
+    "q0": ([128, 3584], f32), "q1": ([128, 3584], f32), "c1": ([128, 512], f32), "hi1": ([128, 448], f32),
+    "uexp": ([128, 2, 896], f32),
     "sdi": ([128, 112], i32), "nri": ([128, 112], i32), "sdf": ([128, 112], f32), "nrf": ([128, 112], f32), "cb": ([128, 112], f16),
     "hsi": ([128, 512], i32), "hsf": ([128, 16, 32], f16), "thr": ([128, 4], f32), "nth": ([128, 4], f32),
     "hw": ([128, 32], f32), "hix": ([128, 32], u16), "hw16": ([128, 32], f16),
-    "nmf": ([128, 256], f32), "nix": ([128, 2, 256], u16), "j2k": ([128, 16], f32), "n32m": ([128, 128], f32), "n1": ([128, 256], f16),
-    "uix": ([128, 256], u16), "sg": ([128, 256], f16), "lix": ([128, 256], u16), "ts": ([128, 256], f16), "cab": ([128, 512], f16),
+    "nmh": ([128, 256], f16), "nix": ([128, 2, 256], u16), "jm": ([128, 16], f32), "n32m": ([128, 128], f32), "n1": ([128, 256], f16),
+    "uix": ([128, 256], u16), "sg": ([128, 256], f16), "lix": ([128, 256], u16), "cab": ([128, 512], f16),
     "sel": ([128, 512], f16), "cand": ([128, 512], f32),
     "dd": ([128, 256], f32), "ud": ([128, 512], f16), "rab": ([128, 512], f16), "cz": ([128, 2, 256], f16), "zs": ([128, 256], f32),
     "cw": ([128, 16], f32), "cwm": ([128, 16], f16), "cwp": ([128, 16], f16), "vlx": ([128, 16], u16),
-    "neg": ([128, 256], f16), "tgf": ([128, 16], f32), "tgx": ([128, 16], u16), "val": ([128, 256], f32),
-    "h1": ([128, 16], f32), "h2": ([128, 16], f32),
-    "f0": ([128, 224], f32), "f1": ([128, 112], f32), "vix": ([128, 224], u16), "sgw": ([128, 28], f16), "six0": ([128, 448], u16), "six1": ([128, 448], u16),
-    "sc": ([128, 128], f32), "su": ([128, 128], f32), "sv": ([128, 256], f32),
+    "neg": ([128, 256], f16), "tgf": ([128, 16], f32), "tgx": ([128, 16], u16), "val": ([128, 512], f32),
+    "h1": ([128, 16], f32),
+    "f0": ([128, 224], f32), "vix": ([128, 224], u16), "sgw": ([128, 28], f16), "six0": ([128, 448], u16), "six1": ([128, 448], u16),
+    "sc": ([128, 256], f32), "su": ([128, 256], f32), "sv": ([128, 256], f32),
     "yc1": ([128, 112], f32), "yc2": ([128, 112], f32),
-    "pi": ([128, 4], i32), "pj": ([128, 4], i32), "col": ([128, 16], f32), "xr": ([128, 144], f32), "x16": ([128, 16], f32),
-    "ce": ([128, 16], f32), "cl": ([128, 16], f32), "md": ([128, 128], f32), "kk": ([128, 128], f32), "tz": ([128, 128], f32),
-    "i32m": ([128, 128], f32), "i16m": ([128, 128], f16), "k16m": ([128, 128], f16), "pm": ([128, 128], f32), "b32": ([128, 144], f32), "b162": ([128, 144], f16), "cch": ([128, NV], f16),
-    "b16": ([128, 144], f16), "b4k": ([128, 144], f16), "b8": ([128, 144], f16), "blk": ([128, 128], f16), "blk2k": ([128, 128], f16),
-    "ym": ([128, 128], f16), "t1": ([128, 128], f32), "t2": ([128, 128], f32), "t3": ([128, 8, 16], f32), "z16": ([128, 128], f16),
-    "rowb": ([128, 2048], f16), "tri": ([128, 2048], f16), "mm": ([128, 4, 8, 16], f16),
-    "tab8": ([128, 256], f32), "tab8h": ([128, 256], f16), "tab32": ([128, 128], f32), "tab32h": ([128, 128], f16),
-    "tabs": ([128, 512], f32), "jw": ([128, 112], f32), "t128": ([128, 16], f32), "t128h": ([128, 16], f16),
+    "pi": ([128, 4], i32), "pj": ([128, 4], i32), "col": ([128, 16], f32), "xr": ([128, 152], f32), "x16": ([128, 16], f32),
+    "ce": ([128, 16], f32), "md": ([128, 128], f32), "tz": ([128, 256], f32), "c2k": ([128, 128], f32),
+    "i32m": ([128, 128], f32), "i16m": ([128, 128], f16), "bz": ([128, 144], f16), "pk": ([128, 4], i32), "pm": ([128, 128], f32), "b32": ([128, 144], f32),
+    "b162": ([128, 144], f16), "cch": ([128, NV], f16), "b16": ([128, 144], f16), "b16h": ([128, 144], f16), "b4k": ([128, 144], f16),
+    "b8": ([128, 144], f16), "blk": ([128, 128], f16), "blk2k": ([128, 128], f16), "lo8": ([128, 152], f16), "hi8": ([128, 152], f16),
+    "y8": ([128, 6, 128], f16), "ee": ([128, 2, 128], f16), "t1": ([128, 128], f32), "t2": ([128, 128], f32), "z16": ([128, 128], f16),
+    "rowb": ([128, 2048], f16), "tri": ([128, 2048], f16), "mm": ([128, 4, 128], f16),
+    "tab8": ([128, 128], f32), "tab8h": ([128, 128], f16), "tab16": ([128, 128], f32), "tab16h": ([128, 128], f16),
+    "tabs": ([128, 512], f32), "jw": ([128, 224], f32), "t128": ([128, 16], f32), "t128h": ([128, 16], f16),
 }
 SCRATCH = {k: ("sbuf", s, d) for k, (s, d) in SB.items()}
 SCRATCH["ps"] = ("psum", [128, 4096], f32)
@@ -45,29 +72,25 @@ IO = {"tl": [128, NV], "sd": [8, NV], "nr": [8, NV], "hs": [8, NS], "u0": [128, 
       "yu": [128, NV], "ys": [128, 1024], "yc": [8, NV], "yh": [8, NS]}
 SEMAPHORES = (["v", "s", "p", "gq"] + ["d%d" % i for i in range(112)] + ["a%d" % i for i in range(16)] + ["l%d" % i for i in range(16)])
 
-CY, PCY, GAM, SIG = 0.83e-3 * 1.2, 0.417e-3 * 1.2, 1.5, 3.5
-GI, DL, DR = 1.0, 2.0, 120e3
-LOOK, PASSES = 0.0, 8
+PLAN = {"cy": 0.83e-3 * 1.1, "gam": 1.5, "sig": 3.5, "gi": 1.0, "dl": 2.0, "dr": 120e3, "hop": 0.1, "rl": 1.8, "rr": 80e3, "first": 3.0, "row": 0.03, "pe": 1.0}
+PLANS = [dict(PLAN, cy=0.87e-3, dr=180e3, rr=100e3), dict(PLAN, cy=0.9e-3, dl=2.3, dr=150e3, rl=2.3, rr=80e3, row=0.04, gi=1.1, hop=0.12, first=4.0, pe=2.0)]
+PHASES = ((22000, 1.5), (26000, 0.6), (14000, 0.3))
+PASSES = [1, 2]
+ROUND = 45.0
+LEAN = 0.1
+WIDE, NARROW, ANY = ((0, 1), (2, 3)), ((4,), (5,), (6,), (7,)), ((4,), (5,), (6,), (7,), (0,), (1,), (2,), (3,))
 
 
 def V_(name, *idx):
-    shape = SB[name][0] if name in SB else (IO[name] if name in IO else [128, 4096])
+    shape = SB[name][0] if name in SB else IO[name]
     if not idx:
         idx = (slice(None),)
     ar = np.arange(int(np.prod(shape[1:]))).reshape(shape[1:])[idx[1:]].ravel()
     pr = range(shape[0])[idx[0]]
-    n = int(ar.size)
-    if name == "ps":
-        m = 0
-        for b in set((ar // 512).tolist()):
-            m |= 1 << b
-        box = m
-    else:
-        bits = np.zeros(int(np.prod(shape[1:])), np.uint8); bits[ar] = 1
-        m = int.from_bytes(np.packbits(bits, bitorder="little").tobytes(), "little")
-        lo, hi = int(ar.min()) // 8 * 8, int(ar.max()) // 8 * 8 + 8
-        box = ((1 << (hi - lo)) - 1) << lo
-    return {"n": name, "i": idx, "m": m, "box": box, "p": (pr[0], pr[-1] + 1), "c": n, "off": None}
+    bits = np.zeros(int(np.prod(shape[1:])), np.uint8); bits[ar] = 1
+    m = int.from_bytes(np.packbits(bits, bitorder="little").tobytes(), "little")
+    lo, hi = int(ar.min()) // 8 * 8, int(ar.max()) // 8 * 8 + 8
+    return {"n": name, "key": name, "i": idx, "m": m, "box": ((1 << (hi - lo)) - 1) << lo, "p": (pr[0], pr[-1] + 1), "c": int(ar.size), "off": None}
 
 
 S_ = slice
@@ -76,6 +99,13 @@ AL = slice(None)
 
 def c2(name, a, b, s=None):
     return V_(name, AL, slice(a, b, s))
+
+
+def ps(h, a, b, s=None, p=AL):
+    cols = range(a, b, s or 1); m = 0
+    for k in range(cols[0] // 512, cols[-1] // 512 + 1):
+        m |= 1 << k
+    return {"n": "ps", "key": h, "i": (p, a, b, s), "m": m, "box": m, "p": (0, 128), "c": len(cols), "off": None}
 
 
 def ind(win, off):
@@ -87,11 +117,21 @@ def two(v):
     return v["n"] != "ps" and SB[v["n"]][1] in (f16, u16, bf)
 
 
-def build(opt):
-    cl = ["setup"]; ops = []; hist = {}; nd = [0]; na = [0]
+def build(opt, P):
+    cl = ["setup", -1]; ops = []; hist = {}; nd = [0]; na = [0]; pieces = []; mark = {}; probe = [False]
+    CY = P["cy"]; PCY = CY / 2 * P["pe"]; GAM = P["gam"]
 
-    def add(eng, emit, rd, wr, cost, lat=0.08, kind="c", ninc=1, sem=None, after=(), ext=None):
-        me = len(ops); deps = set(after); acc = []
+    def O(name, t):
+        return opt.get("%s@%d" % (name, t), opt[name])
+
+    def H(pool=NARROW):
+        pieces.append({"pool": pool, "ops": []})
+        return len(pieces) - 1
+
+    def add(eng, emit, rd, wr, cost, lat=None, kind="c", ninc=1, sem=None, after=(), ext=None, xf=0.0):
+        if probe[0]:
+            return emit, cost
+        me = len(ops); deps = set(after); acc = []; new = []
         for v in rd:
             acc.append((v, v["n"] == "ps"))
             if v["off"] is not None:
@@ -104,22 +144,38 @@ def build(opt):
         for v, w in acc:
             if v["n"] in IO:
                 continue
-            for (o, m, box, p, w0, d0) in hist.get(v["n"], []):
+            if v["n"] == "ps":
+                po = pieces[v["key"]]["ops"]
+                if not po:
+                    new.append(v["key"])
+                elif po[0] != me:
+                    deps.add(po[0])
+                if me not in po:
+                    po.append(me)
+            for (o, m, box, p, w0, d0) in hist.get(v["key"], []):
                 if (w or w0) and o != me and p[0] < v["p"][1] and v["p"][0] < p[1] and ((box & v["box"]) if (dma or d0) else (m & v["m"])):
                     deps.add(o)
         for v, w in acc:
             if v["n"] in IO:
                 continue
-            h = hist.setdefault(v["n"], [])
+            h = hist.setdefault(v["key"], [])
             if w:
                 h[:] = [e for e in h if not (e[3][0] >= v["p"][0] and e[3][1] <= v["p"][1] and (e[1] & ~v["m"]) == 0)]
             h.append((me, v["m"], v["box"], v["p"], w, dma))
-        ops.append({"cl": cl[0], "up": opt["boost"].get(cl[0], 0.0), "tag": wr[0]["n"] if wr else "send", "e": eng, "f": emit, "deps": deps, "cost": cost, "lat": lat, "k": kind, "ninc": ninc, "sem": sem, "ext": ext})
+        ops.append({"cl": cl[0], "rd": cl[1], "tag": wr[0]["n"] if wr else "send", "e": eng, "f": emit, "deps": deps,
+                    "cost": cost, "lat": P["hop"] if lat is None else lat + xf, "xf": xf, "k": kind, "ninc": ninc, "sem": sem, "ext": ext, "new": new, "soft": set(), "alt": None})
         return me
+
+    def hold(j, d):
+        if d is not None and d not in ops[j]["deps"]:
+            ops[j]["deps"].add(d); ops[j]["soft"].add(d)
 
     def ap(c, v):
         if not isinstance(v, dict):
             return v
+        if v["n"] == "ps":
+            p, a, b, s = v["i"]; o = 512 * c["bank"][v["key"]]
+            return c["T"]["ps"][p, slice(o + a, o + b, s)]
         a = c["T"][v["n"]][v["i"]]
         return a if v["off"] is None else a.indirect(ap(c, v["off"]))
 
@@ -128,7 +184,7 @@ def build(opt):
 
     def vcost(out, ins, k):
         if out["off"] is not None:
-            return 0.06 + out["c"] * SIG * CY
+            return 0.06 + out["c"] * P["sig"] * CY
         if ins and ins[0]["off"] is not None:
             return 0.06 + out["c"] * GAM * CY
         if all(two(x) for x in [out] + ins):
@@ -160,17 +216,38 @@ def build(opt):
         return add("s", lambda c: [c["g"].scalar.activation(ap(c, out), ap(c, a), fn, bias=ap(c, bias), scale=ap(c, scale))],
                    vs(a, scale, bias), [out], 0.06 + max(64, out["c"] * k) * CY)
 
+    def asel(out, a, pat, op, fill, base, cm):
+        return add("g", lambda c: [c["g"].affine_select(ap(c, out), ap(c, a), pat, op, fill, base, cm)], [a], [out], 0.17 + 2 * out["c"] * CY)
+
+    def mov(e, out, a, scale=None):
+        ways = {"s": lambda: act(out, a, F.Copy, 1.0 if scale is None else scale),
+                "v": lambda: cp(out, a) if scale is None else ts(out, a, scale, A.mult)}
+        if e == "g":
+            ways["g"] = lambda: asel(out, a, [[0, out["c"]]], A.is_ge, 0.0, 0, 0)
+        return either(e, ways)
+
+    def either(e, ways):
+        me = ways[e](); o = ops[me]; o["alt"] = {}
+        for k in ways:
+            probe[0] = True; o["alt"][k] = ways[k](); probe[0] = False
+        o["e"] = opt["eng"].get("%s.%s" % (o["cl"], o["tag"]), e); o["f"], o["cost"] = o["alt"][o["e"]]
+        return me
+
+    def sign(e, out, a, k=1.0):
+        return either(e, {"s": lambda: act(out, a, F.Sign, k),
+                          "v": lambda: ts(out, a, -1.0, A.max, 1.0, A.min) if k > 0 else ts(out, a, 0.0, A.is_gt, -1.0, A.mult)})
+
     def dadd(out, a):
         s = "d%d" % nd[0]; nd[0] += 1
-        return add("g", lambda c: [c["g"].dma_start(ap(c, out), ap(c, a), accum_op=A.add)], [a, out], [out], GI,
-                   lat=DL + out["c"] * 512 / DR, kind="d", sem=(s, 16))
+        return add("g", lambda c: [c["g"].dma_start(ap(c, out), ap(c, a), accum_op=A.add)], [a, out], [out], P["gi"],
+                   lat=P["dl"], xf=out["c"] * 512 / P["dr"], kind="d", sem=(s, 16))
 
     def mm(lst):
         cost = 0.02
         for o, l, r, a, b in lst:
             cost += max(min(64, l["c"]), r["c"]) * (1 if two(r) else 4) * PCY
         return add("p", lambda c: [c["g"].tensor.matmul(ap(c, o), ap(c, l), ap(c, r), a, b) for o, l, r, a, b in lst],
-                   [x[1] for x in lst] + [x[2] for x in lst], [x[0] for x in lst], cost, lat=0.15, ninc=len(lst))
+                   [x[1] for x in lst] + [x[2] for x in lst], [x[0] for x in lst], cost, lat=P["hop"] + 0.07, ninc=len(lst))
 
     def mmg(lst, per=4):
         full = [(o, l, r, j == 0, j == len(lst) - 1) for j, (o, l, r) in enumerate(lst)]
@@ -178,19 +255,18 @@ def build(opt):
             mm(full[j:j + per])
 
     def iota(out, pat, base, cm):
-        isf = SB[out["n"]][1] != i32
-        if isf:
+        if SB[out["n"]][1] != i32:
             f = lambda c: [c["g"].iota(ap(c, out), pat, base, cm, allow_small_or_imprecise_dtypes=True)]
         else:
             f = lambda c: [c["g"].iota(ap(c, out), pat, base, cm)]
         return add("g", f, [], [out], 0.13 + 2 * out["c"] * CY)
 
-    def dma(q, out, a, nbytes):
+    def dma(q, out, a, nbytes, after=()):
         s = "d%d" % nd[0]; nd[0] += 1
         def f(c):
             e = {"y": c["g"].sync, "s": c["g"].scalar, "g": c["g"]}[q]
             return [e.dma_start(ap(c, out), ap(c, a))]
-        return add(q, f, [a], [out], 1.0 if q == "g" else 0.1, lat=1.8 + nbytes / 200e3, kind="d", sem=(s, 16))
+        return add(q, f, [a], [out], P["gi"] if q == "g" else 0.1, lat=P["dl"], xf=nbytes / (2 * P["dr"]), kind="d", sem=(s, 16), after=after)
 
     def send(pairs, credit):
         k = na[0]; na[0] += 1
@@ -201,8 +277,8 @@ def build(opt):
                                              remote_sem=c["T"].sem["a%d" % k], src=ap(c, a), dst=ap(c, b)))
             c["g"].remote_dma_fused(trs, local_sem=c["T"].sem["l%d" % k])
             return []
-        nb = len(pairs) * 65536
-        o = add("g", f, [a for a, b in pairs], [], 1.0, lat=1.5 + nb / 80e3, kind="r", sem=("l%d" % k, "en"),
+        nb = sum(a["c"] * 512 + 16 * P["row"] * P["rr"] for a, b in pairs)
+        o = add("g", f, [a for a, b in pairs], [], P["gi"], lat=P["rl"] + (P["first"] if k == 0 else 0.0), xf=nb / P["rr"], kind="r", sem=("l%d" % k, "en"),
                 after=[credit[0]] if credit else [], ext=credit[1] if credit else None)
         add(None, None, [], [b for a, b in pairs], 0.0, lat=0.5, kind="x", sem=("a%d" % k, "en"), after=[o])
 
@@ -211,11 +287,8 @@ def build(opt):
         def f(c):
             c["g"].remote_sem_update(c["T"].sem["a%d" % k], c["T"].sem["l%d" % k], c["up"][1], c["up"][0], c["upm"])
             return []
-        o = add("g", f, [], views, 1.0, lat=2.0, kind="r", sem=("l%d" % k, 1))
+        o = add("g", f, [], views, P["gi"], lat=P["rl"], kind="r", sem=("l%d" % k, 1))
         return (o, ("a%d" % k, 1))
-
-    def ps(a, b, s=None):
-        return c2("ps", a, b, s)
 
     def sel(name, i):
         return c2(name, 16 - i, 144 - i)
@@ -223,380 +296,415 @@ def build(opt):
     def colv(j):
         return c2("col", j, j + 1)
 
-    B4, B5, B6, B7 = 2048, 2560, 3072, 3584
-    I32, I16 = V_("i32m"), V_("i16m")
+    I32, I16, ROW0 = V_("i32m"), V_("i16m"), c2("rowb", 0, 128)
+    WW = c2("uw", 0, D0); CE = opt["const"]
 
     dma("y", V_("sdi"), V_("sd"), 57344); dma("s", V_("nri"), V_("nr"), 57344)
     dma("y", V_("hsi", S_(0, 8), AL), V_("hs"), 16384)
     dma("s", V_("tli"), V_("tl"), 917504)
-    dma("g", c2("uw", U0, G0), V_("u0"), 917504); dma("g", c2("uw", W0, W0 + 1024), V_("w0"), 524288)
+    dma("g", c2("uw", U0, G0), V_("u0"), 917504); dma("g", WW, V_("w0"), 524288)
     dma("y", c2("thr", 0, 1), V_("th"), 4096)
     iota(c2("pi", 0, 1), [[0, 1]], 0, 1)
-    iota(V_("xr"), [[1, 144]], -16, 0); iota(V_("md"), [[1, 8], [0, 16]], 0, 0); iota(V_("x16"), [[1, 16]], 0, 0)
-    P_, PM, PD, E0, P16, KV, KS, ZV0, ZV1, M0, M1, M2, M3, JL, KQ = [colv(j) for j in range(15)]
+    iota(V_("xr"), [[1, 152]], -16, 0); iota(V_("md"), [[1, 8], [0, 16]], 0, 0); iota(V_("x16"), [[1, 16]], 0, 0)
+    P_, PM, PD, P16, KV, E4, ZV, ZB, LO, HI, KQ, KZ, KR = [colv(j) for j in range(13)]
     cp(P_, c2("pi", 0, 1))
     ts(c2("pj", 0, 1), c2("pi", 0, 1), 15, A.bitwise_and); cp(PM, c2("pj", 0, 1))
     ts(c2("pj", 1, 2), c2("pi", 0, 1), 4, A.arith_shift_right); cp(PD, c2("pj", 1, 2))
     ts(V_("blk"), V_("md"), PD, A.is_equal)
     ts(V_("ce"), V_("x16"), PM, A.is_equal)
     for i in range(16):
-        if i % 2:
-            ts(c2("rowb", 128 * i, 128 * i + 128), V_("blk"), c2("ce", i, i + 1), A.mult)
-        else:
-            act(c2("rowb", 128 * i, 128 * i + 128), V_("blk"), F.Copy, c2("ce", i, i + 1))
+        mov("vs"[i % 3 == 2], c2("rowb", 128 * i, 128 * i + 128), V_("blk"), c2("ce", i, i + 1))
     ts(c2("pm", 0, 112), c2("xr", 32, 144), P_, A.is_equal); ts(c2("pm", 112, 128), c2("xr", 16, 32), P_, A.is_equal)
-    ts(P16, P_, 16.0, A.mult); ts(V_("b8"), V_("xr"), P16, A.is_equal)
-    ts(V_("b32"), V_("xr"), P_, A.is_equal, c2("ce", 0, 1), A.mult)
-    act(V_("b16"), V_("b32"), F.Copy); act(V_("b4k"), V_("b32"), F.Copy, 4096.0); act(V_("b162"), V_("b32"), F.Copy, 2.0)
-    ts(I32, c2("xr", 16, 144), P_, A.is_equal); act(I16, I32, F.Copy); act(V_("k16m"), I32, F.Copy, 1024.0)
-    ts(V_("sdf"), V_("sdi"), 2.0, A.mult, -1.0, A.add); ts(V_("nrf"), V_("nri"), 1024.0, A.add)
+    ts(P16, P_, 16.0, A.mult); ts(V_("b8"), c2("xr", 0, 144), P16, A.is_equal)
+    ts(V_("b32"), c2("xr", 0, 144), P_, A.is_equal, c2("ce", 0, 1), A.mult)
+    for name, k in (("b16", 1.0), ("b16h", 0.5), ("b162", 2.0), ("b4k", 4096.0)):
+        act(V_(name), V_("b32"), F.Copy, k)
+    ts(HI, PM, 8.0, A.is_ge); ts(LO, PM, 8.0, A.is_lt); ts(E4, PM, 8.0, A.is_ge, 4.0, A.mult)
+    ts(V_("lo8"), V_("xr"), P_, A.is_equal, LO, A.mult); ts(V_("hi8"), V_("xr"), P_, A.is_equal, HI, A.mult)
+    ts(I32, c2("xr", 16, 144), P_, A.is_equal); act(I16, I32, F.Copy)
+    ts(V_("sdf"), V_("sdi"), 2.0, A.mult, -1.0, A.add); ts(V_("nrf"), V_("nri"), -1.0, A.mult, 1024.0, A.add)
     tt(V_("cb"), V_("sdf"), V_("nrf"), A.mult)
     for b in range(4):
-        mm([(ps(512 * b + 112 * j, 512 * b + 112 * j + 112), c2("rowb", 128 * (4 * b + j), 128 * (4 * b + j) + 128), V_("cb"), True, True) for j in range(4)])
-        if b % 2:
-            cp(c2("cc", U0 + 448 * b, U0 + 448 * b + 448), ps(512 * b, 512 * b + 448))
-        else:
-            act(c2("cc", U0 + 448 * b, U0 + 448 * b + 448), ps(512 * b, 512 * b + 448), F.Copy)
-        cp(c2("cch", 448 * b, 448 * b + 448), ps(512 * b, 512 * b + 448))
+        h = H(ANY)
+        mm([(ps(h, 112 * j, 112 * j + 112), c2("rowb", 128 * (4 * b + j), 128 * (4 * b + j) + 128), V_("cb"), True, True) for j in range(4)])
+        mov("sv"[b % 2], c2("cc", C0 + 448 * b, C0 + 448 * b + 448), ps(h, 0, 448))
+        mov("vs"[b % 2], c2("cch", 448 * b, 448 * b + 448), ps(h, 0, 448))
 
-    def send_shifted(name, stage, bank, cr):
-        mm([(ps(bank, bank + 128), V_("pm"), c2(name, U0 + 128, U0 + 256), True, True)])
-        act(V_(stage), ps(bank, bank + 128), F.Copy)
-        send([(c2(name, U0, U0 + 128), c2(name, G0, G0 + 128)), (V_(stage), c2(name, G0 + 128, G0 + 256))], cr)
+    def send_shifted(name, own, ghost, stage, cr):
+        h = H()
+        if opt["wide"]:
+            mm([(ps(h, 128 * k, 128 * k + 128), (I32, V_("pm"))[k], c2(name, own + 128 * k, own + 128 * k + 128), True, True) for k in range(2)])
+            j = mov("s", V_(stage), ps(h, 0, 256))
+            send([(V_(stage), c2(name, ghost, ghost + 256))], cr)
+            return j
+        mm([(ps(h, 0, 128), V_("pm"), c2(name, own + 128, own + 256), True, True)])
+        j = mov("s", c2(stage, 0, 128), ps(h, 0, 128))
+        send([(c2(name, own, own + 128), c2(name, ghost, ghost + 128)), (c2(stage, 0, 128), c2(name, ghost + 128, ghost + 256))], cr)
+        return j
 
-    send_shifted("cc", "sc", B6, None)
-    send_shifted("uw", "su", B7, None)
+    first = send_shifted("cc", C0, C0 + NV, "sc", None)
+    send_shifted("uw", U0, G0, "su", None)
     cp(V_("hsf", S_(0, 8)), V_("hsi", S_(0, 8), AL))
+    h = H()
     for par in range(2):
-        mmg([(ps(B6 + 16 * par, B6 + 16 * par + 16), V_("b8", S_(0, 8), S_(16 - i, 144 - i)), V_("hsf", S_(0, 8), AL, 2 * i + par)) for i in range(16)], 16)
-    cp(V_("hix"), ps(B6, B6 + 32)); cp(V_("hw"), ps(B6, B6 + 32))
-    iota(V_("tab8"), [[8, 256]], 0, 0); act(V_("tab8h"), V_("tab8"), F.Copy)
-    iota(V_("jw"), [[16, 112]], 0, 0); ts(V_("jw"), V_("jw"), PM, A.add)
-    iota(V_("kk"), [[0, 32], [1, 4]], 0, 0); iota(V_("tz"), [[0, 16], [2, 2], [0, 4]], -1, 0)
-    iota(V_("tab32"), [[0, 2], [32, 64]], 0, 0); act(V_("tab32h"), V_("tab32"), F.Copy)
-    iota(V_("t128"), [[128, 16]], 0, 0); act(V_("t128h"), V_("t128"), F.Copy)
-    iota(V_("tabs"), [[1, 2], [2, 256]], 1024, 0)
-    iota(c2("uw", 0, U0), [[0, 256]], 0, 0); iota(c2("cc", 0, U0), [[0, 256]], 0, 0)
-    for h in range(2):
-        for j in range(2):
-            iota(c2("tt", 6144 * h + 1024 * j, 6144 * h + 1024 * j + 1024), [[0, 1024]], 0, 0)
-            iota(c2("tt", 6144 * h + 4096 + 1024 * j, 6144 * h + 5120 + 1024 * j), [[0, 1024]], 0, 0)
-    ms(V_("z16"), 0.0); ms(V_("mm"), 0.0)
+        mmg([(ps(h, 16 * par, 16 * par + 16), V_("b8", S_(0, 8), S_(16 - i, 144 - i)), V_("hsf", S_(0, 8), AL, 2 * i + par)) for i in range(16)], 16)
+    cp(V_("hix"), ps(h, 0, 32)); cp(V_("hw"), ps(h, 0, 32))
+    iota(V_("t2"), [[8, 128]], 0, 0); mov(CE, V_("tab8h"), V_("t2")); ts(V_("tab8"), V_("t2"), -0.5, A.add)
+    iota(V_("jw"), [[-8, 224]], 2048 - U0, 0)
+    ts(c2("pk", 0, 1), c2("pi", 0, 1), 1, A.bitwise_and); ts(KZ, c2("pk", 0, 1), 2048.0, A.add)
+    ts(c2("pk", 1, 2), c2("pi", 0, 1), 1, A.arith_shift_right, 7, A.bitwise_and); ts(KR, c2("pk", 1, 2), 2048.0, A.add)
+    ts(V_("jw"), V_("jw"), KZ, A.add, KR, A.subtract)
+    tt(c2("bz", 1, 144), c2("b162", 1, 144), c2("b162", 0, 143), A.subtract)
+    iota(V_("jm"), [[16, 16]], -256, 0); ts(V_("jm"), V_("jm"), PM, A.add)
+    iota(V_("tab16"), [[0, 4], [16, 32]], 0, 0); mov(CE, V_("tab16h"), V_("tab16"))
+    iota(V_("tabs"), [[-1, 2], [-2, 256]], 1024, 0)
+    iota(c2("uw", D0, U0), [[0, 256]], 0, 0); iota(c2("cc", 0, C0), [[0, 256]], 0, 0)
+    for j in range(4):
+        iota(c2("tt", 2048 * j, 2048 * j + 512), [[0, 512]], 0, 0)
+    ms(V_("z16"), 0.0); ms(KQ, 1792.0)
     act(V_("blk2k"), V_("blk"), F.Copy, 2048.0)
     ts(c2("nth", 0, 1), c2("thr", 0, 1), -1.0, A.mult)
-    ts(V_("t1"), c2("xr", 16, 144), P_, A.is_gt, -2048.0, A.mult); tt(V_("t1"), V_("t1"), V_("blk"), A.mult); tt(V_("ym"), V_("t1"), I32, A.add)
-    ts(V_("cl"), V_("x16"), PM, A.is_gt)
+    ts(c2("pj", 2, 3), c2("pi", 0, 1), 2, A.arith_shift_right, 1, A.bitwise_and); cp(ZB, c2("pj", 2, 3))
+    ts(KV, ZB, -1540.0, A.mult, PM, A.add)
+    if opt["val"] == "g":
+        iota(V_("t128"), [[64, 16]], 0, 0); mov(CE, V_("t128h"), V_("t128")); ts(ZV, PM, 4.0, A.mult, 0.5, A.add)
+    act(V_("n32m"), I32, F.Copy, -1.0)
+    for part in range(2):
+        iota(c2("tz", 128 * part, 128 * part + 128), [[0, 16], [1024 << part, 2], [0, 4]], -(512 << part), 0)
+        for L in range(2):
+            asel(V_("mm", AL, 2 * L + part, AL), c2("tz", 128 * part, 128 * part + 128), [[-8, 16], [0, 2], [-1, 4]], A.is_equal, 0.0, -4 * L, 1)
+    iota(V_("c2k"), [[0, 128]], -2048, 0)
+    asel(V_("t1"), V_("c2k"), [[-8, 16], [0, 8]], A.is_ge, 0.0, 0, 1)
+    asel(V_("y8", AL, 1, AL), V_("t1"), [[8, 16], [0, 8]], A.is_ge, 0.0, 7, -1)
+    asel(V_("t1"), V_("t1"), [[1, 128]], A.is_gt, 0.0, 0, -1)
+    asel(V_("y8", AL, 4, AL), V_("t1"), [[-1, 128]], A.not_equal, 1.0, 0, 1)
+    if opt["cab"] == "p":
+        mov(CE, V_("y8", AL, 0, AL), V_("t1")); act(V_("y8", AL, 5, AL), I32, F.Copy, -1.0)
+        act(V_("y8", AL, S_(2, 4), AL), V_("y8", AL, S_(0, 2), AL), F.Copy, -1.0)
+    asel(V_("ee", AL, 0, AL), V_("blk"), [[16, 8], [0, 16]], A.is_ge, 0.0, 7, -1)
+    asel(V_("ee", AL, 1, AL), V_("blk"), [[-16, 8], [0, 16]], A.is_ge, 0.0, -8, 1)
     for i in range(1, 16):
-        act(c2("tri", 128 * i, 128 * i + 128), V_("blk"), F.Copy, c2("cl", i, i + 1))
-    tt(V_("tz"), V_("tz"), V_("blk"), A.mult)
-    for L in range(2):
-        ts(M0, PM, -4.0 * L, A.add); ts(M1, PM, -4.0 * L - 8, A.add)
-        ts(V_("t1"), V_("kk"), M0, A.is_equal, 1024.0, A.mult); ts(V_("t2"), V_("kk"), M1, A.is_equal, 1028.0, A.mult)
-        tt(V_("t1"), V_("t1"), V_("t2"), A.add); tt(V_("t3"), V_("t1"), V_("tz"), A.mult)
-        for jl in range(2):
-            cp(V_("mm", AL, 2 * L + jl, AL, S_(8 * jl, 8 * jl + 8)), V_("t3", AL, AL, S_(8 * jl, 8 * jl + 8)))
-    ts(c2("pj", 2, 3), c2("pi", 0, 1), 3, A.bitwise_and); cp(KQ, c2("pj", 2, 3))
-    ts(JL, PM, 8.0, A.is_ge, 16.0, A.mult); tt(KV, JL, KQ, A.add); ts(KS, KV, 2056.0, A.add); ts(KV, KV, 2052.0, A.add)
-    ts(ZV0, PM, 8.0, A.mult, 1.0, A.add); ts(ZV1, PM, 8.0, A.mult, 5.0, A.add)
-    ms(KQ, 1792.0); ts(V_("j2k"), c2("jw", 0, 16), 2048.0, A.add); act(V_("n32m"), I32, F.Copy, -1.0)
-    q = 0
+        asel(c2("tri", 128 * i, 128 * i + 128), V_("blk"), [[16, 8], [0, 16]], A.is_ge, 0.0, i - 1, -1)
     for a in range(4):
         for r1 in range(2):
             for h in range(2):
                 dma("y", V_("lsw", S_(32 * a + 16 * r1, 32 * a + 16 * r1 + 16), h, AL),
-                    V_("tl", S_(32 * a + 16 * h, 32 * a + 16 * h + 16), S_(896 * r1, 896 * r1 + 896)), 57344 * 4)
+                    V_("tl", S_(32 * a + 16 * h, 32 * a + 16 * h + 16), S_(896 * r1, 896 * r1 + 896)), 57344, [first])
 
     def turn(t):
         for h in range(2):
-            cp(V_("ftr", AL, AL, S_(16 * h, 16 * h + 16)), V_("lsw", AL, h, S_(t, 896, 4)))
+            ts(V_("ftr", AL, AL, S_(16 * h, 16 * h + 16)), V_("lsw", AL, h, S_(t, 896, 4)), 4.0, A.mult)
         tr(V_("tlt"), V_("ftr"))
 
     def names(t):
-        par = t % 2
-        cp(V_("nmf"), ind(c2("tli", 0, NV), c2("hix", 16 * par, 16 * par + 16)))
-        cp(V_("nix", AL, par, AL), V_("nmf"))
-        act(V_("n1"), V_("nmf"), F.Relu, -1.0, KQ)
+        par = t % 2; h = H()
+        mov(opt["nm"], V_("nmh"), ind(c2("tli", 0, NV), c2("hix", 16 * par, 16 * par + 16)))
+        for part in range(2):
+            mmg([(ps(h, 128 * part, 128 * part + 128), sel(("lo8", "hi8")[part], 8 * (e - part)), c2("nmh", e, 256, 2)) for e in range(2)])
+        cp(V_("nix", AL, par, AL), ps(h, 0, 256))
+        act(V_("n1"), ps(h, 0, 256), F.Relu, -1.0, KQ)
 
-    def nixv(t, a, b):
-        return V_("nix", AL, t % 2, S_(a, b))
+    def half_codes():
+        for j in range(4):
+            mov(opt["cch"][j], c2("cch", 448 * j, 448 * j + 448), c2("cc", C0 + 448 * j, C0 + 448 * j + 448))
 
-    def view_lists(t):
-        mmg([(ps(B6, B6 + 112), sel("b162", i), c2("cch", i, NV, 16)) for i in range(16)], 8)
-        tt(c2("f0", 0, 112), ps(B6, B6 + 112), V_("jw"), A.max)
-        ts(V_("f1"), ps(B6, B6 + 112), -1.0, A.mult, 1.0, A.add)
-        tt(c2("f0", 112, 224), V_("f1"), V_("jw"), A.max)
-        cp(V_("vix"), V_("f0"))
+    def view_lists():
+        h = H(); x = ps(h, 0, 224)
+        mmg([(x, sel("bz", 2 * i), c2("cch", i, NV, 8)) for i in range(8)], 4)
+        tt(V_("f0"), x, V_("jw"), A.max); ts(V_("vix"), V_("f0"), -1.0, A.mult, KZ, A.add)
 
     def node_lists(t):
-        if t:
-            for j in range(2):
-                act(c2("cch", 896 * j, 896 * j + 896), c2("cc", U0 + 896 * j, U0 + 896 * j + 896), F.Copy)
-        mmg([(ps(B7, B7 + 28), sel("b16", i), c2("cch", 4 * i + t, NV, 64)) for i in range(16)], 16)
-        act(V_("sgw"), ps(B7, B7 + 28), F.Sign)
-        lst = [(ps(B7, B7 + 448), V_("z16"), c2("rowb", 0, 448))]
+        h = H()
+        mmg([(ps(h, 0, 28), sel("b16", i), c2("cch", 4 * i + t, NV, 64)) for i in range(16)], 16)
+        sign("s", V_("sgw"), ps(h, 0, 28))
+        h = H(); lst = []
         for r in range(2):
             for k in range(16):
-                o = ps(B7 + 224 * r + 14 * k, B7 + 224 * r + 14 * k + 14)
-                lst.append((o, I16, V_("tlt", AL, AL, 16 * r + k)))
-                lst.append((o, V_("k16m"), c2("sgw", 14 * r, 14 * r + 14)))
-        mmg(lst, 16)
-        ts(V_("six%d" % (t % 2)), ps(B7, B7 + 448), 1024.0, A.add)
+                a = 224 * r + 28 * SLOT[k // 2] + 14 * (k % 2); o = ps(h, a, a + 14)
+                lst.append((o, I16, c2("sgw", 14 * r, 14 * r + 14), True, False))
+                lst.append((o, I16, V_("tlt", AL, AL, 16 * r + k), False, True))
+        for j in range(0, 64, 16):
+            mm(lst[j:j + 16])
+        ts(V_("six%d" % (t % 2)), ps(h, 0, 448), 1.0, A.add, 0.5, A.mult)
+
+    CH = ((0, 0), (1, 0), (0, 1), (1, 1))
 
     def sides(t):
-        par = t % 2
-        for c in range(4):
-            bk = (B6, B7)[c % 2]
-            act(c2("gg", 1024 * c, 1024 * c + 1024), ind(c2("cc", U0, W0), nixv(t, 64 * c, 64 * c + 64)), F.Sign)
-            mmg([(ps(bk, bk + 64), c2("rowb", 0, 128), c2("tab8h", 64 * c, 64 * c + 64))] +
-                [(ps(bk, bk + 64), sel("b16", k), c2("gg", 1024 * c + k, 1024 * c + 1024, 16)) for k in range(16)], 17)
-            ts(c2("uix", 64 * c, 64 * c + 64), ps(bk, bk + 64), 1.0 + 4 * par, A.add, 0.5, A.mult)
-            tt(c2("sg", 64 * c, 64 * c + 64), ps(bk, bk + 64), c2("tab8", 64 * c, 64 * c + 64), A.subtract)
+        for j, (part, hf) in enumerate(CH):
+            cl[0] = "sd%d" % j
+            a = 128 * part + 64 * hf; h = H(); o = ps(h, 0, 64); gq = c2("gg", 16 * a, 16 * a + 1024)
+            x = ind(c2("cc", C0, C0 + NV + NG), V_("nix", AL, t % 2, S_(a, a + 64)))
+            sign(O("sides", t)[j], gq, x)
+            mmg([(o, sel("b16h", k), c2("gg", 16 * a + k, 16 * a + 1024, 16)) for k in range(16)] + [(o, ROW0, c2("tab8h", 64 * hf, 64 * hf + 64))], 17)
+            ts(c2("uix", a, a + 64), o, E4, A.add, 0.5 + 2 * (t % 2), A.add)
+            tt(c2("sg", a, a + 64), o, c2("tab8", 64 * hf, 64 * hf + 64), A.subtract)
 
-    def pair_lists(t):
+    def pair_lists():
+        h = H()
         for L in range(2):
-            o = ps(B6 + 128 * L, B6 + 128 * L + 128)
-            mmg([(o, c2("rowb", 0, 128), V_("tab32h"))] + [(o, V_("mm", AL, 2 * L + jl), c2("sg", jl, 256, 2)) for jl in range(2)])
-        ts(c2("lix", 0, 128), ps(B6, B6 + 128), KV, A.add); ts(c2("lix", 128, 256), ps(B6 + 128, B6 + 256), KS, A.add)
+            o = ps(h, 128 * L, 128 * L + 128)
+            mmg([(o, V_("mm", AL, 2 * L + part, AL), c2("sg", 128 * part, 128 * part + 128)) for part in range(2)] + [(o, ROW0, V_("tab16h"))])
+        for L in range(2):
+            ts(c2("lix", 128 * L, 128 * L + 128), ps(h, 128 * L, 128 * L + 128), KV, A.add, 1536.0 + 4 * L, A.add)
 
-    def candidates(t):
-        tt(V_("ts"), V_("n1"), V_("sg"), A.mult)
-        act(c2("cab", 0, 256), V_("ts"), F.Relu); act(c2("cab", 256, 512), V_("ts"), F.Relu, -1.0)
-        mm([(ps(B7, B7 + 512), V_("ym"), V_("cab"), True, True)])
-        act(V_("sel"), ps(B7, B7 + 512), F.Relu)
-        mm([(ps(B7, B7 + 512), V_("blk"), V_("sel"), True, True)])
-        act(V_("cand"), ps(B7, B7 + 512), F.Copy)
+    def candidates():
+        cab = c2("cab", 0, 256)
+        tt(cab, V_("n1"), V_("sg"), A.mult)
+        h = H(); Y = [V_("y8", AL, j, AL) for j in range(6)]
+        if opt["cab"] == "v":
+            tt(c2("cab", 256, 512), V_("n1"), cab, A.subtract)
+            mmg([(ps(h, 0, 512), Y[4], V_("cab"))] + [(ps(h, 256 * z + 128, 256 * z + 256), Y[1], c2("cab", 256 * z, 256 * z + 128)) for z in range(2)])
+        else:
+            mmg([(ps(h, 0, 256), Y[4], cab), (ps(h, 128, 256), Y[1], c2("cab", 0, 128))])
+            mmg([(ps(h, 256, 512), Y[0], V_("n1")), (ps(h, 256, 512), Y[2], cab), (ps(h, 384, 512), Y[1], c2("n1", 0, 128)),
+                 (ps(h, 384, 512), Y[3], c2("cab", 0, 128)), (ps(h, 256, 512), I16, V_("n1")), (ps(h, 256, 512), Y[5], cab)], 6)
+        x = ps(h, 0, 512)
+        either("s", {"s": lambda: act(V_("sel"), x, F.Relu), "v": lambda: ts(V_("sel"), x, 0.0, A.max)})
+        h = H()
+        mm([(ps(h, 256 * z + e, 256 * z + 256, 2), V_("ee", AL, e, AL), c2("sel", 256 * z + 128 * part, 256 * z + 128 * part + 128), part == 0, part == 1)
+            for z in range(2) for e in range(2) for part in range(2)])
+        mov("s", V_("cand"), ps(h, 0, 512))
+
+    def views(t, a, b, eng):
+        for e, lo, hi in ((eng[0], a, (a + b) // 2), (eng[1], (a + b) // 2, b)):
+            mov(e, c2("vw%d" % (t % 2), 2 * lo, 2 * hi), ind(c2("uw", 0, U0 + b), c2("vix", lo // 8, hi // 8)))
+
+    def ghost_views(t, cr):
+        vw = "vw%d" % (t % 2); cl[0] = "gv"; h = H()
+        views(t, 0, 256, O("gv", t))
+        mm([(ps(h, 0, 256), V_("pm"), c2(vw, 256, 512), True, True)])
+        mov("s", V_("sv"), ps(h, 0, 256))
+        send([(c2(vw, 0, 256), c2(vw, 2 * NV, 2 * NV + 256)), (V_("sv"), c2(vw, 2 * NV + 256, 4096))], cr)
+
+    def old_values(t, r):
+        for j in range(4 if O("dma" + "AB"[r], t) else 2):
+            mov(opt["ue"], V_("uexp", AL, r, S_(224 * j, 224 * j + 224)), c2("uw", U0 + 896 * r + t, U0 + 896 * r + 896, 4))
 
     def step1(t, r):
-        vw = "vw%d" % (t % 2); win = c2(vw, 0, 4096); ue = V_("uexp", AL, r, AL)
+        win = c2("vw%d" % (t % 2), 0, 4096); ue = V_("uexp", AL, r, S_(0, 448))
+        m15, m37, m4, m26 = O("tree" + "AB"[r], t); onpe = O("pe" + "AB"[r], t); ondma = O("dma" + "AB"[r], t)
+        assert (0 in ondma) == (1 in ondma) or m4 == "v"
         def d(k, n=1): return c2("d2", 448 * k, 448 * (k + n))
-        def qq(k, n=1): return c2("rb", 448 * k, 448 * (k + n))
-        def gat(k):
-            x = ind(win, c2("six%d" % (t % 2), 224 * r + 28 * k, 224 * r + 28 * k + 28))
-            if k in opt["s1un"][r]:
-                act(d(k), x, F.Copy); dadd(d(k), ue)
+        def q(k, n=1, a=0, b=448): return c2("q%d" % r, 448 * k + a, 448 * (k + n - 1) + b)
+        def x(k): return ind(win, c2("six%d" % (t % 2), 224 * r + 28 * k, 224 * r + 28 * k + 28))
+        def one(k): return V_("n32m") if k // 2 in ondma else I32
+        def pair(j, mode):
+            h = H(WIDE); cl[0] = "AB"[r] + str(j // 2)
+            if j // 2 in onpe:
+                a, b = ps(h, 0, 448), ps(h, 512, 960)
+                for i, o in ((j, a), (j + 1, b)):
+                    mov("s", d(i), x(i))
+                    mmg([(o, I32, d(i)), (o, V_("n32m"), ue)], 1)
+                    act(d(i), o, F.Abs)
             else:
-                tt(d(k), x, ue, A.add)
-        s1, s2 = ps(B4, B4 + 448), ps(B5, B5 + 448)
-        lo, hi = ps(B4, B4 + 224), ps(B4 + 224, B4 + 448)
-        cc1 = c2("rb", 448 * 8, 448 * 8 + 224)
-        unew = c2("uw", U0 + 896 * r + t, U0 + 896 * r + 896, 4); uold = V_("uexp", AL, r, S_(0, 224))
-        if opt["tree_dma"]:
-            sq = (1, 5, 3, 7, 0, 4, 2, 6); q0 = 448 * (0, 4)[r]
-            def qq(k, n=1):
-                k = ((0, 1, 2, 3, 4, 5, 6, 7), (4, 5, 6, 7, 2, 3, 0, 1))[r][k]
-                return c2("rb", 448 * k, 448 * (k + n))
-            def one(j, n):
-                for i in range(j, j + n):
-                    x = ind(win, c2("six%d" % (t % 2), 224 * r + 28 * sq[i], 224 * r + 28 * sq[i] + 28))
-                    if i in opt["s1un"][r]:
-                        act(d(i), x, F.Copy); dadd(d(i), ue)
-                    else:
-                        tt(d(i), x, ue, A.add)
-            for j in (0, 2, 4):
-                bk = 1024 * ((j // 2) % 2)
-                if j in opt["s1pe"][r]:
-                    for i in (j, j + 1):
-                        o = ps(bk + 512 * (i - j), bk + 512 * (i - j) + 448)
-                        act(d(i), ind(win, c2("six%d" % (t % 2), 224 * r + 28 * sq[i], 224 * r + 28 * sq[i] + 28)), F.Copy)
-                        mm([(o, I32, ue, True, False)]); mm([(o, I32, d(i), False, True)])
-                        act(d(i), o, F.Abs); tt(qq(i), d(i), o, A.mult)
+                a, b = ps(h, 0, 448), ps(h, 448, 896)
+                if j // 2 in ondma:
+                    act(d(j, 2), ind(win, c2("six%d" % (t % 2), 224 * r + 28 * j, 224 * r + 28 * j + 56)), F.Copy, -1.0)
+                    dadd(d(j, 2), V_("uexp", AL, r, AL))
                 else:
-                    one(j, 2); act(ps(bk, bk + 896), d(j, 2), F.Abs); tt(qq(j, 2), d(j, 2), ps(bk, bk + 896), A.mult)
-                if j < 4:
-                    dadd(qq(j), qq(j + 1))
-                if j == 2:
-                    dadd(qq(0), qq(2))
-            mm([(s1, I32, qq(4), True, False)]); mm([(s1, I32, qq(5), False, opt["tail"][r] == "v")])
-            a, b = ps(1024, 1472), ps(1536, 1984)
-            one(6, 1); act(a, d(6), F.Abs); tt(a, d(6), a, A.mult)
-            one(7, 1); act(b, d(7), F.Abs); tt(qq(7), d(7), b, A.mult)
-            tt(qq(6), a, qq(7), A.add)
-            if opt["tail"][r] == "v":
-                tt(s1, s1, qq(6), A.add)
-                tt(cc1, hi, c2("rb", q0 + 224, q0 + 448), A.add); tt(lo, lo, c2("rb", q0, q0 + 224), A.add)
-                tt(lo, lo, cc1, A.add); ts(lo, lo, 0.015625, A.mult)
+                    tt(d(j), x(j), ue, A.subtract); tt(d(j + 1), x(j + 1), ue, A.subtract)
+                act(ps(h, 0, 896), d(j, 2), F.Abs)
+            if mode == "v":
+                tt(q(j + 1), d(j + 1), b, A.mult); tt(a, d(j), a, A.mult); tt(q(j), a, q(j + 1), A.add)
+            elif j // 2 in onpe:
+                tt(q(j), d(j), a, A.mult); tt(q(j + 1), d(j + 1), b, A.mult)
             else:
-                mm([(s1, I32, qq(6), False, False)]); mm([(s1, I32, qq(0), False, True)])
-                act(cc1, hi, F.Copy); tt(lo, lo, cc1, A.add); act(lo, lo, F.Copy, 0.015625)
-            tt(unew, lo, uold, A.subtract)
-            return
-        if opt["tree_pe"]:
-            for k, bk in ((0, 0), (4, 1024)):
-                gat(k); gat(k + 1)
-                act(ps(bk, bk + 896), d(k, 2), F.Abs)
-                tt(qq(k, 2), d(k, 2), ps(bk, bk + 896), A.mult)
-                mm([(s1, I32, qq(k), k == 0, False)]); mm([(s2, I32, qq(k + 1), k == 0, k == 4)])
+                tt(q(j, 2), d(j, 2), ps(h, 0, 896), A.mult)
+            if mode == "d":
+                dadd(q(j), q(j + 1))
+        def onpe_sum(slots):
+            h = H()
+            mmg([(ps(h, 0, 448), I32, q(k)) for k in slots], 1)
+            mov("s", q(slots[0]), ps(h, 0, 448))
+        pair(0, m15)
+        if m15 == "p" and m4 != "p":
+            onpe_sum((0, 1))
+        pair(2, m37)
+        if m37 == "p":
+            onpe_sum((2, 3))
+        if m4 == "d":
+            dadd(q(0), q(2))
+        elif m4 == "v":
+            tt(q(0), q(0), q(2), A.add if (0 in ondma) == (1 in ondma) else A.subtract)
         else:
-            for k, bk, s in ((0, 0, s1), (1, 512, s2)):
-                gat(k); act(s, d(k), F.Abs); tt(s, d(k), s, A.mult)
-                gat(k + 4); act(ps(bk, bk + 448), d(k + 4), F.Abs); tt(qq(k + 4), d(k + 4), ps(bk, bk + 448), A.mult)
-                tt(s, s, qq(k + 4), A.add)
-        for k, bk in ((2, 0), (3, 1024)):
-            a, b = ps(bk, bk + 448), ps(bk + 512, bk + 960)
-            gat(k); act(a, d(k), F.Abs); tt(a, d(k), a, A.mult)
-            gat(k + 4); act(b, d(k + 4), F.Abs); tt(qq(k + 4), d(k + 4), b, A.mult)
-            tt(qq(k), a, qq(k + 4), A.add)
-            if k == 2:
-                if opt["tree_pe"]:
-                    mm([(s1, I32, qq(2), False, True)])
-                else:
-                    tt(s1, s1, qq(2), A.add)
-        tt(qq(7), s2, qq(3), A.add)
-        tt(cc1, hi, c2("rb", 448 * 7 + 224, 448 * 8), A.add)
-        tt(lo, lo, c2("rb", 448 * 7, 448 * 7 + 224), A.add)
-        tt(lo, lo, cc1, A.add)
-        if opt["tail"][r] == "v":
-            ts(lo, lo, 0.015625, A.mult)
+            onpe_sum((0, 1, 2) if m15 == "p" else (0, 2))
+        pair(4, "p"); pair(6, m26)
+        if m26 == "p":
+            onpe_sum((6, 7))
+        hi = c2("hi1", 224 * r, 224 * r + 224); cl[0] = "AB"[r] + "t"
+        if O("tail", t)[r] == "p":
+            h = H()
+            mmg([(ps(h, 0, 224), one(k), q(k, 1, 224, 448)) for k in (4, 5, 6, 0)], 2)
+            mov("s", hi, ps(h, 0, 224))
+            h = H(); lo = ps(h, 0, 224)
+            mmg([(lo, one(k), q(k, 1, 0, 224)) for k in (4, 5, 6, 0)] + [(lo, I32, hi)], 2)
         else:
-            act(lo, lo, F.Copy, 0.015625)
-        tt(unew, lo, uold, A.subtract)
+            h = H(); lo = ps(h, 0, 224)
+            mmg([(ps(h, 0, 448), one(k), q(k)) for k in (4, 5, 6, 0)], 1)
+            mov("s", hi, ps(h, 224, 448)); tt(lo, lo, hi, A.add)
+        mov(opt["scale1"][r], lo, lo, 0.015625)
+        tt(c2("uw", U0 + 896 * r + t, U0 + 896 * r + 896, 4), lo, V_("uexp", AL, r, S_(0, 224)), A.add)
 
-    turn(0); names(0); view_lists(0); sides(0); node_lists(0); pair_lists(0); candidates(0)
+    def claimed_values():
+        o = ind(c2("uw", D0, G0), V_("tgx"))
+        if opt["val"] == "ab":
+            tt(o, c2("val", 0, 256), c2("val", 256, 512), A.max)
+        else:
+            cp(o, c2("val", 0, 256))
+
+    def lists(t):
+        cl[0] = "vl"; view_lists(); cl[0] = "nl"; node_lists(t); sides(t); cl[0] = "pl"; pair_lists(); cl[0] = "cand"; candidates()
+
+    names(0); turn(0); lists(0)
+    ghost_views(0, None); cl[0] = "vA"; views(0, 256, 896, O("vA", 0)); cl[0] = "ue"; old_values(0, 0); old_values(0, 1)
     cr = None
     for t in range(RO):
-        par = t % 2; last = t == RO - 1; vw = "vw%d" % par
-        vwin = c2("uw", U0, W0 + 1024); cl[0] = "gv"
-        for z in range(2):
-            o = c2(vw, 2048 * z, 2048 * z + 256); x = ind(vwin, c2("vix", 112 * z, 112 * z + 16))
-            if opt["gvv"]:
-                cp(o, x)
-            else:
-                act(o, x, F.Copy)
-        mm([(ps(B6 + 128 * z, B6 + 128 * z + 128), V_("pm"), c2(vw, 2048 * z + 128, 2048 * z + 256), True, True) for z in range(2)])
-        act(V_("sv"), ps(B6, B6 + 256), F.Copy)
-        send([(c2(vw, 0, 128), c2(vw, NV, NV + 128)), (c2("sv", 0, 128), c2(vw, NV + 128, NV + 256)),
-              (c2(vw, 2048, 2176), c2(vw, 2048 + NV, 2048 + NV + 128)), (c2("sv", 128, 256), c2(vw, 2048 + NV + 128, 4096))], cr)
-        cl[0] = "s2"
-        for c in range(4):
-            a, b = 1024 * c, 1024 * c + 1024; bk = 1024 * (c % 2); h = c // 2
-            act(c2("uu", a, b), ind(c2("uw", W0, W0 + 1024), c2("uix", 64 * c, 64 * c + 64)), F.Copy, -1.0)
-            x = ind(c2("uw", U0, W0), nixv(t, 64 * c, 64 * c + 64))
-            tt(c2("uu", a, b), x, c2("uu", a, b), A.add)
-            act(ps(bk, bk + 1024), c2("uu", a, b), F.Abs)
-            q0 = 6144 * h + 2048 + 1024 * (c % 2)
-            tt(c2("tt", q0, q0 + 1024), c2("uu", a, b), ps(bk, bk + 1024), A.mult)
-            if c < 2:
-                z = c
-                for j in range(2):
-                    cl[0] = "vw"
-                    o = c2(vw, 2048 * z + 256 + 768 * j, 2048 * z + 1024 + 768 * j); x = ind(vwin, c2("vix", 112 * z + 16 + 48 * j, 112 * z + 64 + 48 * j))
-                    if 2 * z + j in opt["vwv"]:
-                        cp(o, x)
+        par = t % 2; last = t == RO - 1; cl[1] = t
+        if t and not opt["vAearly"]:
+            cl[0] = "vA"; views(t, 256, 896, opt["vA"])
+        cl[0] = "vB"; views(t, 896, NV, O("vB", t))
+        for j, (part, hf) in enumerate(CH):
+            a = 128 * part + 64 * hf; h = H(WIDE); w = 32 if j in opt["fine"] else 64
+            for b in range(a, a + 64, w):
+                uu = c2("uu", 16 * b, 16 * (b + w))
+                cl[0] = "uc%d" % j
+                mov(O("ucol", t)[j], uu, ind(WW, c2("uix", b, b + w)))
+                cl[0] = "x%d" % j
+                mark["x"] = tt(uu, ind(c2("uw", U0, UE), V_("nix", AL, par, S_(b, b + w))), uu, A.subtract)
+                act(ps(h, 16 * (b - a), 16 * (b - a + w)), uu, F.Abs)
+            for i in range(2):
+                t0 = 2048 * (2 * hf + i); mode = O("pair", t)[2 * hf + i]; cl[0] = "m%d" % j
+                lo, hi, sm = [c2("tt", t0 + 512 * k, t0 + 512 * k + 512) for k in (1, 2, 3)]
+                st = ps(h, 512 * i, 512 * i + 512); di = c2("uu", 16 * a + 512 * i, 16 * a + 512 * i + 512)
+                if part == 0:
+                    tt(lo, di, st, A.mult)
+                    if mode == "d":
+                        dma("y", sm, lo, 262144)
+                elif mode == "x":
+                    tt(st, di, st, A.mult); tt(sm, st, lo, A.add); mov("s", hi, st)
+                else:
+                    tt(hi, di, st, A.mult)
+                    if mode == "v":
+                        tt(sm, lo, hi, A.add)
+                    elif mode == "d":
+                        dadd(sm, hi)
                     else:
-                        act(o, x, F.Copy)
-            if c == 2:
-                cl[0] = "ue"
-                for r in range(2):
-                    for j in range(2):
-                        act(V_("uexp", AL, r, S_(224 * j, 224 * j + 224)), c2("uw", U0 + 896 * r + t, U0 + 896 * r + 896, 4), F.Copy, -1.0)
-            cl[0] = "s2"
-            if c % 2:
-                q0 = 6144 * h + 2048
-                for k in range(8):
-                    o = c2("tt", q0 + 2056 + k, q0 + 4096, 16); x = c2("tt", q0 + k, q0 + 2048, 16); y = c2("tt", q0 + 8 + k, q0 + 2048, 16)
-                    if opt["pair_pe"]:
-                        pb = ps(B4 + 128 * k, B4 + 128 * k + 128)
-                        mm([(pb, I32, x, True, False), (pb, I32, y, False, True)])
-                        if k % 4 == 3:
-                            for k2 in range(k - 3, k + 1):
-                                act(c2("tt", q0 + 2056 + k2, q0 + 4096, 16), ps(B4 + 128 * k2, B4 + 128 * k2 + 128), F.Copy)
-                    else:
-                        tt(o, x, y, A.add)
+                        h2 = H(ANY)
+                        mmg([(ps(h2, 0, 512), I32, lo), (ps(h2, 0, 512), I32, hi)], 1)
+                        mov("s", sm, ps(h2, 0, 512))
         if not last:
             other = "vw%d" % (1 - par)
-            cr = credit([c2("uw", G0, W0), c2("cc", G0, W0), c2(other, NV, 2048), c2(other, 2048 + NV, 4096)])
-        for h in range(2):
-            win = c2("tt", 6144 * h, 6144 * h + 6144); a, b = 1024 * h, 1024 * h + 1024
-            a, b = a + 3840, b + 3840; rr = c2("rb", a, b)
-            act(rr, ind(win, c2("lix", 128 + 64 * h, 192 + 64 * h)), F.Copy)
-            tt(c2("rb", a, b), ind(win, c2("lix", 64 * h, 64 * h + 64)), rr, A.add)
-            bk = (B4, B5)[h]; o = ps(bk, bk + 256); cc1 = c2("c1", 256 * h, 256 * h + 256)
-            if opt["c1_pe"]:
-                o1 = ps(B7, B7 + 256)
-                mm([(o1, I32, c2("rb", a + 1, b, 4), True, False), (o1, I32, c2("rb", a + 3, b, 4), False, True)])
-                act(cc1, o1, F.Copy)
+            cr = credit([c2("uw", G0, UE), c2("cc", C0 + NV, C0 + NV + NG), c2(other, 2 * NV, 4096)])
+        for c in range(4):
+            cl[0] = "l%d" % c
+            win = c2("tt", 2048 * c, 2048 * c + 2048); rr = c2("uu", 512 * c, 512 * c + 512)
+            mov(opt["rr"][c], rr, ind(win, c2("lix", 128 + 32 * c, 160 + 32 * c)))
+            mark["0123"[c]] = tt(rr, ind(win, c2("lix", 32 * c, 32 * c + 32)), rr, A.add)
+        for j, (qa, qb) in enumerate(opt["grp"]):
+            a, b = 512 * qa, 512 * qb; n = 128 * (qb - qa); cc1 = c2("c1", 128 * qa, 128 * qb); cl[0] = "w%d" % j
+            if opt["c1"][j] == "p":
+                h = H(); o1 = ps(h, 0, n)
+                mmg([(o1, I32, c2("uu", a + 1, b, 4)), (o1, I32, c2("uu", a + 3, b, 4))])
+                mov("s", cc1, o1)
             else:
-                tt(cc1, c2("rb", a + 1, b, 4), c2("rb", a + 3, b, 4), A.add)
-            if opt["lvl_pe"]:
-                mm([(o, I32, c2("rb", a, b, 4), True, False), (o, I32, c2("rb", a + 2, b, 4), False, False)])
-                mm([(o, I32, cc1, False, True)])
-            else:
-                tt(o, c2("rb", a, b, 4), c2("rb", a + 2, b, 4), A.add); tt(o, o, cc1, A.add)
-            act(o, o, F.Copy, 0.015625)
+                tt(cc1, c2("uu", a + 1, b, 4), c2("uu", a + 3, b, 4), A.add)
+            h = H(); o = ps(h, 0, n)
+            mmg([(o, I32, c2("uu", a, b, 4)), (o, I32, c2("uu", a + 2, b, 4)), (o, I32, cc1)], 2)
+            mov(opt["scale2"][j], o, o, 0.015625)
             for z in range(2):
-                w = c2("uw", W0 + 512 * h + 2 * par + z, W0 + 512 * h + 512, 4)
-                tt(w, ps(bk + z, bk + 256, 2), w, A.add)
+                w = c2("uw", 256 * qa + 2 * par + z, 256 * qb, 4)
+                tt(w, ps(h, z, n, 2), w, A.add)
         if last:
-            dma("y", V_("ys"), c2("uw", W0, W0 + 1024), 524288)
+            dma("y", V_("ys"), WW, 524288)
         cl[0] = "s3"
-        n0, n1 = c2("uw", W0 + 2 * par, W0 + 1024, 4), c2("uw", W0 + 2 * par + 1, W0 + 1024, 4)
-        if opt["dd_pe"]:
-            dd = ps(B7, B7 + 256)
-            mm([(dd, I32, n0, True, False), (dd, V_("n32m"), n1, False, True)])
+        n0, n1 = c2("uw", 2 * par, D0, 4), c2("uw", 2 * par + 1, D0, 4)
+        if opt["dd"] == "p":
+            dd = ps(H(), 0, 256)
+            mmg([(dd, I32, n0), (dd, V_("n32m"), n1)])
         else:
             dd = V_("dd"); tt(dd, n0, n1, A.subtract)
         ts(c2("ud", 0, 256), dd, c2("thr", 0, 1), A.is_gt, 0.5, A.subtract)
         ts(c2("ud", 256, 512), dd, c2("nth", 0, 1), A.is_lt, 0.5, A.subtract)
-        mm([(ps(B6, B6 + 512), V_("blk2k"), V_("ud"), True, True)])
-        tt(V_("rab"), ps(B6, B6 + 512), V_("cand"), A.min)
-        act(V_("cz", AL, 1, AL), ps(B6 + 256, B6 + 512), F.Sign); act(V_("zs"), ps(B6 + 256, B6 + 512), F.Sign)
+        hv = H(); up, dn = ps(hv, 0, 256), ps(hv, 256, 512)
+        mm([(ps(hv, 0, 512), V_("blk2k"), V_("ud"), True, True)])
+        tt(V_("rab"), ps(hv, 0, 512), V_("cand"), A.min)
         tt(V_("cz", AL, 0, AL), c2("rab", 0, 256), c2("rab", 256, 512), A.max)
-        mmg([(ps(B7, B7 + 16), sel("b16", i), V_("cz", AL, 0, S_(i, 256, 16))) for i in range(16)], 16)
-        cp(V_("cw"), ps(B7, B7 + 16))
-        mmg([(ps(B7, B7 + 16), c2("rowb", 0, 128), V_("t128h"))] + [(ps(B7, B7 + 16), sel("b16", i), V_("cz", AL, 1, S_(i, 256, 16))) for i in range(16)], 17)
-        mm([(ps(B6, B6 + 256), V_("z16"), c2("rowb", 0, 256), True, False)])
-        for a in range(16):
-            ts(c2("gg", 256 * a, 256 * a + 256 - 16 * a), V_("cz", AL, 0, S_(16 * a, 256)), c2("cw", a, a + 1), A.is_equal)
-            if a < 15:
-                mm([(ps(B6 + 16 * a + 16, B6 + 256), V_("blk"), c2("gg", 256 * a + 16, 256 * a + 256 - 16 * a), False, False)])
-        mm([(ps(B6 + i, B6 + 256, 16), c2("tri", 128 * i, 128 * i + 128), c2("gg", i, 4096, 256), False, i == 15) for i in range(1, 16)])
-        ts(V_("vlx"), ps(B7, B7 + 16), (ZV0, ZV1)[par], A.add, 0.5, A.mult)
-        act(V_("val"), ind(c2("uw", W0, W0 + 1024), V_("vlx")), F.Copy)
-        ts(V_("cwm"), V_("cw"), 0.0, A.is_gt, 4.0, A.mult); ts(V_("cwp"), V_("cw"), -1.0, A.mult, 0.0, A.min)
-        act(V_("neg"), ps(B6, B6 + 256), F.Sign, -1.0)
-        mmg([(ps(B7, B7 + 16), I16, V_("cwp")), (ps(B7, B7 + 16), V_("k16m"), V_("cwm"))] +
-            [(ps(B7, B7 + 16), sel("b4k", i), c2("neg", i, 256, 16)) for i in range(16)], 18)
-        tt(V_("tgf"), ps(B7, B7 + 16), V_("j2k"), A.max); ts(V_("tgx"), V_("tgf"), -2048.0, A.add)
-        tt(ind(c2("cc", 0, G0), V_("tgx")), V_("zs"), c2("tabs", 256 * par, 256 * par + 256), A.mult)
+        sign("s", V_("zs"), dn)
+        h = H()
+        mmg([(ps(h, 0, 16), sel("b16", i), V_("cz", AL, 0, S_(i, 256, 16))) for i in range(16)], 16)
+        mov("v", V_("cw"), ps(h, 0, 16))
+        if opt["val"] == "ab":
+            tt(c2("val", 0, 256), up, n0, A.min); tt(c2("val", 256, 512), dn, n1, A.min)
+        else:
+            sign("s", V_("cz", AL, 1, AL), dn)
+            h = H()
+            mmg([(ps(h, 0, 16), sel("b16h", i), V_("cz", AL, 1, S_(i, 256, 16))) for i in range(16)] + [(ps(h, 0, 16), ROW0, V_("t128h"))], 17)
+            ts(V_("vlx"), ps(h, 0, 16), ZV, A.add, 2.0 * par, A.add)
+            mov("s", c2("val", 0, 256), ind(WW, V_("vlx")))
+        h = H()
+        for a0 in range(0, 16, 4):
+            probe[0] = True
+            four = [ts(c2("gg", 256 * a, 256 * a + 256 - 16 * a), V_("cz", AL, 0, S_(16 * a, 256)), c2("cw", a, a + 1), A.is_equal) for a in range(a0, a0 + 4)]
+            probe[0] = False
+            add("v", lambda c, four=four: [x for f, k in four for x in f(c)], [V_("cz", AL, 0, AL), V_("cw")], [c2("gg", 256 * a0, 256 * a0 + 1024)],
+                sum(k for f, k in four))
+            mm(([(ps(h, 0, 256), V_("z16"), c2("rowb", 0, 256), True, False)] if a0 == 0 else []) +
+               [(ps(h, 16 * a + 16, 256), V_("blk"), c2("gg", 256 * a + 16, 256 * a + 256 - 16 * a), False, False) for a in range(a0, min(a0 + 4, 15))])
+        mm([(ps(h, i, 256, 16), c2("tri", 128 * i, 128 * i + 128), c2("gg", i, 4096, 256), False, i == 15) for i in range(1, 16)])
+        ts(V_("cwm"), V_("cw"), 0.0, A.is_le, -32768.0, A.mult); ts(V_("cwp"), V_("cw"), -1.0, A.mult, 1792.0, A.add)
+        sign("s", V_("neg"), ps(h, 0, 256), -1.0)
+        h = H(); o = ps(h, 0, 16)
+        mmg([(o, sel("b4k", i), c2("neg", i, 256, 16)) for i in range(16)] + [(o, I16, V_("cwp")), (o, I16, V_("cwm"))], 18)
+        tt(V_("tgf"), o, V_("jm"), A.max); ts(V_("tgx"), V_("tgf"), 256.0, A.add)
+        mark["c"] = tt(ind(c2("cc", 0, C0 + NV), V_("tgx")), V_("zs"), c2("tabs", 256 * par, 256 * par + 256), A.mult)
         if not last:
-            send_shifted("cc", "sc", B6, cr)
-            names(t + 1); cl[0] = "prep"; turn(t + 1)
-        cl[0] = "prep"
+            send_shifted("cc", C0, C0 + NV, "sc", cr)
+            cl[0] = "names"; names(t + 1); cl[0] = "turn"; turn(t + 1)
+        cl[0] = "host"
         hw = c2("hw", 16 * par, 16 * par + 16)
-        ts(V_("h1"), V_("tgf"), 2304.0, A.is_ge, -4096.0, A.mult); ts(V_("h2"), V_("tgf"), -2304.0, A.add)
-        tt(V_("h1"), V_("h1"), hw, A.add); tt(hw, V_("h1"), V_("h2"), A.max)
+        ts(V_("h1"), V_("tgf"), 0.0, A.is_ge, -4096.0, A.mult)
+        tt(V_("h1"), V_("h1"), hw, A.add); tt(hw, V_("h1"), V_("tgf"), A.max)
         if t < 2:
             cp(c2("hix", 16 * par, 16 * par + 16), hw)
+        cl[0] = "cch"; half_codes()
         if not last:
-            node_lists(t + 1); view_lists(t + 1); cl[0] = "sides"; sides(t + 1); cl[0] = "cand"; pair_lists(t + 1); candidates(t + 1)
+            lists(t + 1)
         else:
-            for j in range(2):
-                act(c2("cch", 896 * j, 896 * j + 896), c2("cc", U0 + 896 * j, U0 + 896 * j + 896), F.Copy)
-            mmg([(ps(B6, B6 + 112), sel("b162", i), c2("cch", 112 * i, 112 * i + 112)) for i in range(16)], 8)
-            ts(V_("yc1"), ps(B6, B6 + 112), -2047.0, A.add); ts(V_("yc2"), ps(B6, B6 + 112), -1.0, A.mult, -2048.0, A.add)
-            tt(V_("yc1"), V_("yc1"), V_("yc2"), A.max)
+            cl[0] = "vl"
+            h = H(); x = ps(h, 0, 112)
+            mmg([(x, sel("b162", i), c2("cch", 112 * i, 112 * i + 112)) for i in range(16)], 8)
+            ts(V_("yc1"), x, -1.0, A.mult, 2049.0, A.add); ts(V_("yc2"), x, 2048.0, A.add)
+            tt(V_("yc1"), V_("yc1"), V_("yc2"), A.min)
             dma("y", V_("yc"), V_("yc1"), 57344)
-            cp(V_("hw16"), V_("hw"))
-            mm([(V_("ps", S_(0, 8), S_(B7 + 2 * i + p2, B7 + 512, 32)), c2("rowb", 128 * i, 128 * i + 128, 16), c2("hw16", 16 * p2, 16 * p2 + 16), True, True)
+            cp(V_("hw16"), V_("hw")); h = H()
+            mm([(ps(h, 2 * i + p2, 512, 32, S_(0, 8)), c2("rowb", 128 * i, 128 * i + 128, 16), c2("hw16", 16 * p2, 16 * p2 + 16), True, True)
                 for i in range(16) for p2 in range(2)])
-            act(V_("cand", S_(0, 8), AL), V_("ps", S_(0, 8), S_(B7, B7 + 512)), F.Copy)
+            act(V_("cand", S_(0, 8), AL), ps(h, 0, 512, None, S_(0, 8)), F.Copy)
             dma("y", V_("yh"), V_("cand", S_(0, 8), AL), 16384)
-        cl[0] = "A"
         step1(t, 0)
-        cp(ind(c2("uw", 0, G0), V_("tgx")), V_("val"))
+        if O("once", t):
+            step1(t, 1)
+        claimed_values()
         if not last:
-            send_shifted("uw", "su", B5, cr)
+            send_shifted("uw", U0, G0, "su", cr)
+            ghost_views(t + 1, cr)
+            cl[0] = "vA"
+            if opt["vAearly"]:
+                views(t + 1, 256, 896, opt["vA"])
+            cl[0] = "ue"; old_values(t + 1, 0)
         else:
             dma("y", c2("yu", 0, 896), c2("uw", U0, U0 + 896), 458752)
-        cl[0] = "B"
-        step1(t, 1)
-        cp(ind(c2("uw", 0, G0), V_("tgx")), V_("val"))
+        if not O("once", t):
+            step1(t, 1)
+            claimed_values()
+        if not last:
+            cl[0] = "uf"; old_values(t + 1, 1)
     dma("y", c2("yu", 896, 1344), c2("uw", U0 + 896, U0 + 1344), 229376)
     dma("s", c2("yu", 1344, NV), c2("uw", U0 + 1344, G0), 229376)
-    return ops
+    return ops, pieces
 
 
-def plan(ops):
+def plan(ops, pieces, boost):
     n = len(ops); succ = [[] for _ in ops]
     for j, o in enumerate(ops):
         for d in o["deps"]:
@@ -606,9 +714,12 @@ def plan(ops):
     pri = [0.0] * n
     for j in range(n - 1, -1, -1):
         pri[j] = ops[j]["cost"] + max([gap(j, s) + pri[s] for s in succ[j]] + [ops[j]["lat"]])
-    left = [len(o["deps"]) for o in ops]; rdy = [0.0] * n; end = [0.0] * n; start = [0.0] * n
+    pri = [pri[j] + boost.get(o["cl"], 0.0) + boost.get("%s.%s" % (o["cl"], o["e"]), 0.0) for j, o in enumerate(ops)]
+    left = [len(o["deps"]) for o in ops]; rdy = [0.0] * n; end = [0.0] * n; start = [0.0] * n; done = [False] * n
     free = {e: 0.0 for e in "vspgy"}; pool = {e: [] for e in "vspgy"}; order = []
+    holder = [None] * 8; bank = [None] * len(pieces)
     def release(j):
+        done[j] = True
         for s in succ[j]:
             rdy[s] = max(rdy[s], end[j] + gap(j, s)); left[s] -= 1
             if left[s] == 0:
@@ -616,21 +727,37 @@ def plan(ops):
                     start[s] = end[s] = rdy[s]; order.append(s); release(s)
                 else:
                     pool[ops[s]["e"]].append(s)
+    def room(j):
+        if not ops[j]["new"]:
+            return rdy[j], None
+        best = None
+        for bs in pieces[ops[j]["new"][0]]["pool"]:
+            last = [x for b in bs if holder[b] is not None for x in pieces[holder[b]]["ops"]]
+            if all(done[x] for x in last):
+                tm = max([rdy[j]] + [end[x] + gap(x, j) for x in last])
+                if best is None or tm < best[0] - 1e-9:
+                    best = (tm, bs)
+        return best
     for j in range(n):
         if left[j] == 0:
             pool[ops[j]["e"]].append(j)
     while len(order) < n:
         best = None
         for e in pool:
-            if pool[e]:
-                tnow = max(free[e], min(rdy[j] for j in pool[e]))
+            can = [(x, room(x)) for x in pool[e]]; can = [(x, r) for x, r in can if r is not None]
+            if can:
+                tnow = max(free[e], min(r[0] for x, r in can))
                 if best is None or tnow < best[0]:
-                    best = (tnow, e)
-        tnow, e = best
-        j = max([x for x in pool[e] if rdy[x] <= tnow + 0.05], key=lambda x: (pri[x] + ops[x]["up"], -x))
-        soon = [x for x in pool[e] if rdy[x] <= tnow + LOOK * ops[j]["cost"]]
-        j = max(soon + [j], key=lambda x: (pri[x] + ops[x]["up"], -x))
-        pool[e].remove(j); start[j] = max(tnow, rdy[j]); end[j] = start[j] + ops[j]["cost"]; free[e] = end[j]
+                    best = (tnow, e, can)
+        tnow, e, can = best
+        j, r = max([c for c in can if c[1][0] <= tnow + boost.get("look", 0.05)], key=lambda c: (pri[c[0]], -c[0]))
+        if r[1] is not None:
+            for b in r[1]:
+                if holder[b] is not None:
+                    ops[j]["deps"].update(pieces[holder[b]]["ops"])
+                holder[b] = ops[j]["new"][0]
+            bank[ops[j]["new"][0]] = r[1][0]
+        pool[e].remove(j); start[j] = max(tnow, r[0]); end[j] = start[j] + ops[j]["cost"]; free[e] = end[j]
         order.append(j); release(j)
 
     def place(seq, links):
@@ -648,33 +775,327 @@ def plan(ops):
                 b.insert(k, (r, r + w))
             st[j] = r
         return st
+    rank = {j: k for k, j in enumerate(order)}
     fw = [[(d, gap(d, j)) for d in ops[j]["deps"]] for j in range(n)]
-    bw = [[(s, gap(j, s)) for s in succ[j]] for j in range(n)]
+    bw = [[] for _ in ops]
+    for j in range(n):
+        for d, gp in fw[j]:
+            bw[d].append((j, gp))
     span = lambda st: max(st[j] + ops[j]["cost"] + ops[j]["lat"] for j in range(n))
     best = span(start); st = start
     for it in range(PASSES):
-        sb = place(sorted(range(n), key=lambda j: (-(st[j] + ops[j]["cost"]), -j)), bw)
-        st = place(sorted(range(n), key=lambda j: (-(sb[j] + ops[j]["cost"]), j)), fw)
+        sb = place(sorted(range(n), key=lambda j: (-(st[j] + ops[j]["cost"]), -rank[j])), bw)
+        st = place(sorted(range(n), key=lambda j: (-(sb[j] + ops[j]["cost"]), rank[j])), fw)
         if span(st) < best:
             best = span(st); start = st
-    order = sorted(range(n), key=lambda j: (start[j], j))
-    return order, start, [start[j] + ops[j]["cost"] for j in range(n)]
+    order = sorted(range(n), key=lambda j: (start[j], rank[j]))
+    return order, start, [start[j] + ops[j]["cost"] for j in range(n)], bank
+
+
+def plan(ops, pieces, times):
+    n = len(ops); cost = [o["cost"] for o in ops]
+    def links():
+        fw = [[(d, 0.0 if (ops[d]["e"] == "p" and o["e"] == "p") else ops[d]["lat"]) for d in o["deps"]] for o in ops]
+        bw = [[] for o in ops]
+        for j in range(n):
+            for d, gp in fw[j]:
+                bw[d].append((j, gp))
+        return fw, bw
+    def place(key, fw, bw):
+        left = [len(x) for x in fw]; ready = sorted((key[j], j) for j in range(n) if not left[j])
+        st = [0.0] * n; busy = {e: [] for e in "vspgy"}; seq = []
+        while ready:
+            j = ready.pop(0)[1]; r = 0.0; w = cost[j]; seq.append(j)
+            for d, gp in fw[j]:
+                r = max(r, st[d] + cost[d] + gp)
+            if ops[j]["e"] is not None:
+                b = busy[ops[j]["e"]]; k = len(b)
+                while k > 0 and b[k - 1][1] > r:
+                    k -= 1
+                while k < len(b) and b[k][0] < r + w - 1e-9:
+                    r = max(r, b[k][1]); k += 1
+                b.insert(k, (r, r + w))
+            st[j] = r
+            new = False
+            for s, gp in bw[j]:
+                left[s] -= 1
+                if not left[s]:
+                    ready.append((key[s], s)); new = True
+            if new:
+                ready.sort()
+        assert len(seq) == n
+        return st, seq
+    def span(st):
+        return max(st[j] + cost[j] + ops[j]["lat"] for j in range(n))
+    def close(key, passes):
+        fw, bw = links(); st, seq = place(key, fw, bw); best = (span(st), st, seq)
+        for it in range(passes):
+            sb = place([-(st[j] + cost[j]) for j in range(n)], bw, fw)[0]
+            st, seq = place([-(sb[j] + cost[j]) for j in range(n)], fw, bw)
+            best = min(best, (span(st), st, seq))
+        return best[1:]
+    key = [0.0] * n; bw = links()[1]
+    for j in range(n - 1, -1, -1):
+        o = ops[j]
+        if o["cl"] in times:
+            key[j] = ROUND * o["rd"] + times[o["cl"]] + times.get("%s@%d" % (o["cl"][0], o["rd"]), 0.0)
+        else:
+            key[j] = min([key[s] - gp for s, gp in bw[j]] + [1e9]) - cost[j]
+    st, seq = close(key, PASSES[0])
+    bank = banks(pieces, [o["deps"] for o in ops], st, [st[j] + cost[j] for j in range(n)])
+    st, seq = close(st, PASSES[1])
+    rank = {j: k for k, j in enumerate(seq)}
+    return sorted(range(n), key=lambda j: (st[j], rank[j])), st, [st[j] + cost[j] for j in range(n)], bank
+
+
+def banks(pieces, deps, st, end):
+    holder = [None] * 8; bank = [None] * len(pieces)
+    for h in sorted(range(len(pieces)), key=lambda h: (st[pieces[h]["ops"][0]], h)):
+        j = pieces[h]["ops"][0]; ways = []
+        for k, bs in enumerate(pieces[h]["pool"]):
+            last = [x for b in bs if holder[b] is not None for x in pieces[holder[b]]["ops"]]
+            ways.append((max([0.0] + [end[x] for x in last]), k, bs, last))
+        for tm, k, bs, last in sorted(ways):
+            seen = set(); todo = list(last) if tm > st[j] else []
+            while todo and j not in seen:
+                x = todo.pop()
+                if x not in seen:
+                    seen.add(x); todo += [d for d in deps[x] if end[d] > st[j] - 30.0]
+            if j not in seen:
+                break
+        deps[j].update(last); bank[h] = bs[0]
+        for b in bs:
+            holder[b] = h
+    return bank
+
+
+QUEUES = ("v", "s", "p", "g", "y", None)
+
+
+def refine(ops, refs, order, steps, heat, seed):
+    n = len(ops); state = [seed]
+    def rnd():
+        state[0] = (state[0] * 1103515245 + 12345) % 2147483648
+        return state[0] / 2147483648.0
+    en = [QUEUES.index(o["e"]) for o in ops]; deps = [[] for o in ops]
+    pos = {j: k for k, j in enumerate(order)}; above = [0] * n
+    for j in order:
+        for d in sorted(ops[j]["deps"], key=lambda d: -pos[d]):
+            if not above[j] >> d & 1:
+                deps[j].append(d); above[j] |= above[d] | 1 << d
+    alt = [[QUEUES.index(e) for e in o["alt"]] if o["alt"] else None for o in ops]
+    figs = []
+    for ref in refs:
+        cost = [[o["alt"][e][1] if o["alt"] and e in o["alt"] else o["cost"] for o in ref] for e in QUEUES]
+        lat = [0.0 if o["xf"] else o["lat"] for o in ref]
+        figs.append((cost, lat, [(o["lat"] - o["xf"], o["xf"]) if o["xf"] else None for o in ref], [[(d, 0.0 if en[j] == 2 and en[d] == 2 else lat[d]) for d in deps[j]] for j in range(n)]))
+    def run(order, en, fig, k0, old):
+        cost, lat, xf, lk = fig; free = [0.0] * 6; last = [-1] * 6; top = 0.0; tj = -1; wire = 0.0; wj = -1
+        end = list(old[3]) if k0 else [0.0] * n; why = list(old[1]) if k0 else [-1] * n; out = list(old[4]) if k0 else [0.0] * n
+        for j in order[k0 - 1:max(k0 - 300, 0):-1] if k0 else ():
+            if last[en[j]] < 0:
+                last[en[j]] = j; free[en[j]] = out[j]
+            if wj < 0 and xf[j]:
+                wj = j; wire = end[j]
+        for j in order[k0:]:
+            r = 0.0; w = -1
+            for d, g in lk[j]:
+                x = end[d] + g
+                if x > r:
+                    r = x; w = d
+            e = en[j]
+            if e < 5:
+                if free[e] > r:
+                    r = free[e]; w = -2 - last[e]
+                r += cost[e][j]; free[e] = r; last[e] = j
+            out[j] = r
+            if xf[j]:
+                r += xf[j][0]
+                if wire > r:
+                    r = wire; w = -2 - wj
+                r += xf[j][1]; wire = r; wj = j
+            end[j] = r; why[j] = w; r += lat[j]
+            if r > top:
+                top = r; tj = j
+        return top, why, tj, end, out
+    def tails(order, en, fig, succ):
+        cost, lat, xf, lk = fig; tl = [0.0] * n; nxt = [0.0] * 6; wire = 0.0
+        for j in reversed(order):
+            a = lat[j]
+            for s, g in succ[j]:
+                x = g + tl[s]
+                if x > a:
+                    a = x
+            if xf[j]:
+                wire = xf[j][1] + (a if a > wire else wire); a = xf[j][0] + wire
+            e = en[j]
+            if e < 5:
+                a = cost[e][j] + (a if a > nxt[e] else nxt[e]); nxt[e] = a
+            tl[j] = a
+        return tl
+    def least(new, en, fig, succ, k0, k1, old, tl):
+        cost, lat, xf, lk = fig; end = {}; free = {}; oe = old[3]; top = 0.0
+        for j in new[k0:k1 + 1]:
+            r = 0.0
+            for d, g in lk[j]:
+                x = end.get(d, oe[d]) + g
+                if x > r:
+                    r = x
+            e = en[j]
+            if e < 5:
+                if e not in free:
+                    k = k0 - 1
+                    while k >= 0 and en[new[k]] != e:
+                        k -= 1
+                    free[e] = old[4][new[k]] if k >= 0 else 0.0
+                r = max(r, free[e]) + cost[e][j]; free[e] = r
+            if xf[j]:
+                r += xf[j][0] + xf[j][1]
+            end[j] = r
+            for s, g in succ[j]:
+                if pos[s] > k1 and r + g + tl[s] > top:
+                    top = r + g + tl[s]
+        for e in free:
+            k = k1 + 1
+            while k < n and en[new[k]] != e:
+                k += 1
+            if k < n and free[e] + tl[new[k]] > top:
+                top = free[e] + tl[new[k]]
+        return top
+    succ = []
+    for fig in figs:
+        succ.append([[] for o in ops])
+        for j in range(n):
+            for d, g in fig[3][j]:
+                succ[-1][d].append((j, g))
+    tl = None; free_calls = [j for j in range(n) if alt[j]]
+    rs = [run(order, en, f, 0, None) for f in figs]; wt = [200.0 / r[0] / len(figs) for r in rs]
+    cur = 200.0; best = (cur, order, en, rs); pos = {j: k for k, j in enumerate(order)}; arcs = [None] * len(figs)
+    for it in range(steps):
+        f = int(rnd() * len(figs))
+        if arcs[f] is None:
+            why = rs[f][1]; j = rs[f][2]; arcs[f] = []
+            while j != -1:
+                w = why[j]
+                if w <= -2:
+                    w = -2 - w; arcs[f].append((w, j))
+                j = w
+        a, b = arcs[f][int(rnd() * len(arcs[f]))]; u = rnd(); e2 = en; far = (0, 0, 1, 2, 4, 8)[int(rnd() * 6)]; ok = True; qn = set(); fee = 0.0
+        if u < 0.2:
+            x = a if u < 0.07 else b if u < 0.14 else free_calls[int(rnd() * len(free_calls))]
+            if not alt[x]:
+                continue
+            e2 = list(en); e2[x] = [e for e in alt[x] if e != en[x]][int(rnd() * (len(alt[x]) - 1))]; new = order; k0 = k1 = pos[x]
+            fee = LEAN * figs[0][0][0][x] * ((e2[x] == 0) - (en[x] == 0))
+        elif u < 0.6:
+            k0 = pos[a]; k1 = pos[b]
+            while far and k0 > 0:
+                k0 -= 1; far -= en[order[k0]] == en[a]
+            seg = order[k0:pos[b]]; need = set(deps[b]); mv = []
+            for x in reversed(seg):
+                if x in need or en[x] in qn:
+                    if en[x] == en[b]:
+                        ok = False
+                        break
+                    mv.append(x); need.update(deps[x])
+                    if en[x] < 5:
+                        qn.add(en[x])
+            if not ok:
+                continue
+            ms = set(mv); new = order[:k0] + mv[::-1] + [b] + [x for x in seg if x not in ms] + order[pos[b] + 1:]
+        else:
+            k = pos[b]; k0 = pos[a]
+            while far and k < n - 1:
+                k += 1; far -= en[order[k]] == en[a]
+            seg = order[k0:k + 1]; ms = {a}; mv = [a]; k1 = k
+            for x in seg[1:]:
+                if en[x] in qn or not ms.isdisjoint(deps[x]):
+                    if en[x] == en[a]:
+                        ok = False
+                        break
+                    mv.append(x); ms.add(x)
+                    if en[x] < 5:
+                        qn.add(en[x])
+            if not ok:
+                continue
+            new = order[:k0] + [x for x in seg if x not in ms] + mv + order[k + 1:]
+        bar = cur + heat * rnd() ** 3 * (1 - it / steps) - fee
+        if tl is None:
+            tl = [tails(order, en, fig, sc) for fig, sc in zip(figs, succ)]
+        if sum(least(new, e2, fig, sc, k0, k1, r, x) * w for fig, sc, r, x, w in zip(figs, succ, rs, tl, wt)) > bar + 1e-6:
+            continue
+        if k0 > n - 60:
+            k0 = 0
+        r2 = [run(new, e2, fig, k0, r) for fig, r in zip(figs, rs)]; t = sum(r[0] * w for r, w in zip(r2, wt))
+        if t <= bar:
+            cur, rs, en = t, r2, e2; arcs = [None] * len(figs); tl = None
+            if it % 8 == 0:
+                end = r2[0][4]; c0 = figs[0][0]; rk = {j: k for k, j in enumerate(new)}
+                new = sorted(new, key=lambda j: (end[j] - (c0[en[j]][j] if en[j] < 5 else 0.0), rk[j]))
+                r2 = rs = [run(new, en, fig, 0, None) for fig in figs]; t = cur = sum(r[0] * w for r, w in zip(r2, wt))
+            order = new; pos = {j: k for k, j in enumerate(order)}
+            if t < best[0]:
+                best = (t, order, en, r2)
+    for calls in [ops] + refs:
+        for o, e in zip(calls, best[2]):
+            if o["alt"]:
+                o["e"] = QUEUES[e]; o["f"], o["cost"] = o["alt"][o["e"]]
+    return best[1], best[3][0][4], [r[0] for r in best[3]]
+
+
+def rebank(ops, pieces, data, order, end):
+    n = len(ops); st = [end[j] - ops[j]["cost"] for j in range(n)]
+    deps = [set(d) for d in data]; bank = banks(pieces, deps, st, end)
+    placed = set(); out = []; rest = order
+    while rest:
+        late = []
+        for k, j in enumerate(rest):
+            if deps[j] <= placed:
+                out.append(j); placed.add(j)
+                if late:
+                    late += rest[k + 1:]
+                    break
+            else:
+                late.append(j)
+        if len(late) == len(rest):
+            return None
+        rest = late
+    for o, d in zip(ops, deps):
+        o["deps"] = d
+    return out, bank
+
+
+def schedule(opt, plans, phases):
+    ops, pieces = build(opt, plans[0]); refs = [build(opt, p)[0] for p in plans]
+    data = [set(o["deps"]) for o in ops]
+    order, st, end, bank = plan(ops, pieces, opt["boost"])
+    for k, (steps, heat) in enumerate(phases):
+        if k:
+            order, bank = rebank(ops, pieces, data, order, end) or (order, bank)
+        order, end, times = refine(ops, refs, order, steps, heat, k + 1)
+    return ops, order, end, bank
 
 
 CACHE = {}
+
+
+def prepare():
+    if "ops" not in CACHE:
+        ops, order, end, bank = schedule(OPT, PLANS, PHASES)
+        CACHE["ops"] = ops; CACHE["plan"] = (order, None, end, bank)
 
 
 def rank_program(g, core, T, topo):
     rank = T.rank_of(core)
     if rank is None:
         return
-    if "ops" not in CACHE:
-        CACHE["ops"] = build(OPT); CACHE["plan"] = plan(CACHE["ops"])
+    prepare()
     ops = CACHE["ops"]; order = CACHE["plan"][0]
     nr = len(T.cores); dst = T.cores[(rank - 1) % nr]; up = T.cores[(rank + 1) % nr]
     rid, pid = topo.addr(dst)[:2]
     en = topo.engines(core, dst); inn = len(topo.engines(up, core))
-    c = {"g": g, "T": T, "dst": DstId(rid=rid, pnc=pid), "en": en, "up": topo.addr(up)[:2], "upm": 1 << topo.engines(core, up)[0]}
+    c = {"g": g, "T": T, "dst": DstId(rid=rid, pnc=pid), "en": en, "up": topo.addr(up)[:2], "upm": 1 << topo.engines(core, up)[0],
+         "bank": CACHE["plan"][3]}
     queue = {"v": g.vector, "s": g.scalar, "p": g.tensor, "g": g, "y": g.sync}
     own = {"v": "v", "s": "s", "p": "p", "g": "gq"}
     count = {}; token = {}; known = {e: {} for e in queue}; total = {}
@@ -690,7 +1111,7 @@ def rank_program(g, core, T, topo):
             continue
         need = {}
         for d in o["deps"]:
-            if (e == "p" and ops[d]["e"] == "p") or (o["k"] == "r" and ops[d]["k"] == "r" and ops[d]["sem"][1] == 1):
+            if d in o["soft"] or (e == "p" and ops[d]["e"] == "p") or (o["k"] == "r" and ops[d]["k"] == "r" and ops[d]["sem"][1] == 1):
                 continue
             s, k = token[d]; need[s] = max(need.get(s, 0), k)
         if o["ext"]:

@@ -13,7 +13,7 @@ C0 = 256
 SLOT = (4, 0, 6, 2, 5, 1, 7, 3)
 OPT = {"pair": "pppp", "val": "ab", "dd": "p", "c1": "ppv", "scale2": "sss", "grp": ((0, 2), (2, 3), (3, 4)), "fine": (3,), "cch": "gggg", "ue": "g", "const": "g", "nm": "s", "cab": "p",
        "sides": "ssss", "ucol": "ssss", "rr": "ssss", "gv": "ss", "vA": "ss", "vB": "ss", "vAearly": True,
-       "treeA": "dddv", "treeB": "ddvv", "tail": "ps", "scale1": "ss", "eng": {}, "once": False, "wide": True, "peA": (), "peB": (), "dmaA": (), "dmaB": (),
+       "treeA": "dddv", "treeB": "ddvv", "tail": "ps", "scale1": "ss", "eng": {}, "qA": (), "qB": (), "sgn": False, "votes": ((0, 192), (192, 256)), "sfine": (), "once": False, "wide": True, "peA": (), "peB": (), "dmaA": (), "dmaB": (),
        "boost": {"uc0": -2, "uc1": 0, "uc2": 3, "uc3": 5, "x0": 0, "x1": 1.5, "x2": 4.5, "x3": 6.5, "vB": 1, "m0": 2, "m1": 4, "m2": 7, "m3": 9,
                  "l0": 7, "l1": 8, "l2": 11, "l3": 12, "w0": 10, "w1": 13, "w2": 14, "s3": 16, "A0": 8, "A1": 10, "A2": 14, "A3": 17, "At": 22,
                  "names": 18, "turn": 20, "host": 27, "cch": 26.5, "vl": 27.5, "nl": 38, "B0": 26, "B1": 28, "B2": 31, "B3": 33, "Bt": 36,
@@ -36,6 +36,16 @@ OPT.update({"dmaA": (), "dmaB": (), "peA": (3,), "peB": (2,), "dmaB@3": (), "peA
 OPT.update({"dmaA": (2, 3), "dmaB": (2,), "peA": (), "peB": (), "dmaB@3": (2, 3), "peA@3": (), "peB@3": (), "treeA": "dddd", "treeB": "dddv",
             "treeB@3": "ddvv", "wide": False, "pair": "ddxx", "pair@3": "ddxx",
             "dmaA": (0, 1, 3), "dmaB": (2,), "treeB": "ddvv", "c1": "vvv", "tail": "ss", "cab": "v"})
+OPT.update({"dmaA@3": (0, 1, 3), "dmaB@3": (2, 3), "sides": "svss", "ucol": "ssss",
+            "boost": {"s2": 18, 'vB': 5.0, 'uc0': -2.0, 'x0': 0.0, 'm0': 3.0, 'uc1': -4.0, 'x1': 0.5, 'm1': 5.0, 'uc2': 2.5, 'x2': 6.5, 'm2': 10.0, 'uc3': -0.5,
+                      'x3': 4.0, 'm3': 9.0, 'l0': 13.0, 'l1': 12.5, 'l2': 15.0, 'l3': 14.5, 'w0': 15.0, 'w1': 17.5, 'w2': 17.0, 's3': 22.0,
+                      'names': 12, 'turn': 20, 'host': 30.5, 'cch': 32.0, 'vl': 35.0, 'nl': 42.0, 'sd0': 38.0, 'sd1': 37.0, 'sd2': 40.0,
+                      'sd3': 37.0, 'pl': 46.5, 'cand': 56.5, 'A0': 10.5, 'A1': 15.5, 'A2': 11.0, 'A3': 16.5, 'At': 31.0, 'gv': 39.5,
+                      'vA': 39.0, 'ue': 35.5, 'B0': 26.0, 'B1': 25.0, 'B2': 22.0, 'B3': 30.5, 'Bt': 35.0, 'uf': 47.0,
+                      "ld0": 20, "ldw": 20.5, "ld1": 21, "ld2": 22, "sc0": 24, "su0": 25, "vl@-1": 26, "gv@-1": 27, "vA@-1": 29,
+                      "vB@0": -15, "nl@-1": 31}})
+OPT.update({"votes": ((0, 256),), "sides": "vsvs", "gv": "sv", "eng": {"Bt.ps": "v", "Bt.hi1": "v", "s3.cw": "s"}})
+OPT["boost"].update({'vB': 2.5, 'uc0': -3.0, 'x0': 0.0, 'm0': 3.5, 'uc1': -0.5, 'x1': 2.0, 'm1': 5.5, 'uc2': 4.5, 'x2': 6.5, 'm2': 9.5, 'uc3': -1.5, 'x3': 4.5, 'm3': 11.0, 'l0': 13.0, 'l1': 13.5, 'l2': 16.5, 'l3': 13.0, 'w0': 16.5, 'w1': 18.5, 'w2': 15.5, 's3': 23.5, 'names': 15, 'turn': 22, 'host': 33.0, 'cch': 30.0, 'vl': 33.5, 'nl': 45.5, 'sd0': 37.0, 'sd1': 39.5, 'sd2': 41.5, 'sd3': 37.5, 'pl': 47.5, 'cand': 51.5, 'A0': 10.0, 'A1': 11.5, 'A2': 10.0, 'A3': 15.0, 'At': 29.5, 'gv': 40.0, 'vA': 37.0, 'ue': 34.5, 'B0': 27.5, 'B1': 24.0, 'B2': 21.0, 'B3': 30.5, 'Bt': 35.0, 'uf': 48.0})
 f32, f16, i32, u16, bf = "float32", "float16", "int32", "uint16", "bfloat16"
 SB = {
     "uw": ([128, UE], f32), "cc": ([128, C0 + NV + NG], f32), "vw0": ([128, 4096], f32), "vw1": ([128, 4096], f32),
@@ -48,7 +58,7 @@ SB = {
     "hw": ([128, 32], f32), "hix": ([128, 32], u16), "hw16": ([128, 32], f16),
     "nmh": ([128, 256], f16), "nix": ([128, 2, 256], u16), "jm": ([128, 16], f32), "n32m": ([128, 128], f32), "n1": ([128, 256], f16),
     "uix": ([128, 256], u16), "sg": ([128, 256], f16), "lix": ([128, 256], u16), "cab": ([128, 512], f16),
-    "sel": ([128, 512], f16), "cand": ([128, 512], f32),
+    "sel": ([128, 512], f16), "sv16": ([128, 512], f16), "cand16": ([128, 512], f16), "cand": ([128, 512], f32),
     "dd": ([128, 256], f32), "ud": ([128, 512], f16), "rab": ([128, 512], f16), "cz": ([128, 2, 256], f16), "zs": ([128, 256], f32),
     "cw": ([128, 16], f32), "cwm": ([128, 16], f16), "cwp": ([128, 16], f16), "vlx": ([128, 16], u16),
     "neg": ([128, 256], f16), "tgf": ([128, 16], f32), "tgx": ([128, 16], u16), "val": ([128, 512], f32),
@@ -73,11 +83,11 @@ IO = {"tl": [128, NV], "sd": [8, NV], "nr": [8, NV], "hs": [8, NS], "u0": [128, 
 SEMAPHORES = (["v", "s", "p", "gq"] + ["d%d" % i for i in range(112)] + ["a%d" % i for i in range(16)] + ["l%d" % i for i in range(16)])
 
 PLAN = {"cy": 0.83e-3 * 1.1, "gam": 1.5, "sig": 3.5, "gi": 1.0, "dl": 2.0, "dr": 120e3, "hop": 0.1, "rl": 1.8, "rr": 80e3, "first": 3.0, "row": 0.03, "pe": 1.0}
-PLANS = [dict(PLAN, cy=0.87e-3, dr=180e3, rr=100e3), dict(PLAN, cy=0.9e-3, dl=2.3, dr=150e3, rl=2.3, rr=80e3, row=0.04, gi=1.1, hop=0.12, first=4.0, pe=2.0)]
-PHASES = ((22000, 1.5), (26000, 0.6), (14000, 0.3))
+PLANS = [dict(PLAN, cy=0.92e-3, gam=1.55, dr=180e3, rr=100e3), dict(PLAN, cy=0.9e-3, gam=1.5, dl=2.3, dr=150e3, rl=2.3, rr=80e3, row=0.04, gi=1.1, hop=0.12, first=4.0, pe=2.0)]
+PHASES = ((14000, 1.5, 1), (24000, 2.0, 4), (24000, 1.0, 5), (20000, 0.6, 6), (14000, 0.3, 5), (12000, 0.3, 8))
 PASSES = [1, 2]
-ROUND = 45.0
-LEAN = 0.1
+ROUND = 43.0
+TWINS = 0.6
 WIDE, NARROW, ANY = ((0, 1), (2, 3)), ((4,), (5,), (6,), (7,)), ((4,), (5,), (6,), (7,), (0,), (1,), (2,), (3,))
 
 
@@ -118,7 +128,7 @@ def two(v):
 
 
 def build(opt, P):
-    cl = ["setup", -1]; ops = []; hist = {}; nd = [0]; na = [0]; pieces = []; mark = {}; probe = [False]
+    cl = ["setup", -1]; ops = []; hist = {}; nd = [0]; na = [0]; pieces = []; mark = {}; probe = [False]; made = set()
     CY = P["cy"]; PCY = CY / 2 * P["pe"]; GAM = P["gam"]
 
     def O(name, t):
@@ -131,7 +141,7 @@ def build(opt, P):
     def add(eng, emit, rd, wr, cost, lat=None, kind="c", ninc=1, sem=None, after=(), ext=None, xf=0.0):
         if probe[0]:
             return emit, cost
-        me = len(ops); deps = set(after); acc = []; new = []
+        me = len(ops); deps = set(after); acc = []; new = []; reads = set(); firm = set(after)
         for v in rd:
             acc.append((v, v["n"] == "ps"))
             if v["off"] is not None:
@@ -155,6 +165,9 @@ def build(opt, P):
             for (o, m, box, p, w0, d0) in hist.get(v["key"], []):
                 if (w or w0) and o != me and p[0] < v["p"][1] and v["p"][0] < p[1] and ((box & v["box"]) if (dma or d0) else (m & v["m"])):
                     deps.add(o)
+                    both = v["n"] == "ps" and (v["key"], o) not in made and not any(v["key"] == x["key"] for x in wr)
+                    (reads if both else firm).add(o)
+        made.update((v["key"], me) for v in wr)
         for v, w in acc:
             if v["n"] in IO:
                 continue
@@ -163,7 +176,7 @@ def build(opt, P):
                 h[:] = [e for e in h if not (e[3][0] >= v["p"][0] and e[3][1] <= v["p"][1] and (e[1] & ~v["m"]) == 0)]
             h.append((me, v["m"], v["box"], v["p"], w, dma))
         ops.append({"cl": cl[0], "rd": cl[1], "tag": wr[0]["n"] if wr else "send", "e": eng, "f": emit, "deps": deps,
-                    "cost": cost, "lat": P["hop"] if lat is None else lat + xf, "xf": xf, "k": kind, "ninc": ninc, "sem": sem, "ext": ext, "new": new, "soft": set(), "alt": None})
+                    "cost": cost, "lat": P["hop"] if lat is None else lat + xf, "xf": xf, "k": kind, "ninc": ninc, "sem": sem, "ext": ext, "new": new, "soft": set(), "alt": None, "reads": reads - firm})
         return me
 
     def hold(j, d):
@@ -301,8 +314,11 @@ def build(opt, P):
 
     dma("y", V_("sdi"), V_("sd"), 57344); dma("s", V_("nri"), V_("nr"), 57344)
     dma("y", V_("hsi", S_(0, 8), AL), V_("hs"), 16384)
-    dma("s", V_("tli"), V_("tl"), 917504)
-    dma("g", c2("uw", U0, G0), V_("u0"), 917504); dma("g", WW, V_("w0"), 524288)
+    cl[0] = "ld0"; dma("g", c2("uw", U0, U0 + 256), c2("u0", 0, 256), 131072)
+    cl[0] = "ldw"; j = dma("g", WW, V_("w0"), 524288)
+    cl[0] = "ld1"; dma("s", V_("tli"), V_("tl"), 917504)
+    cl[0] = "ld2"; dma("g", c2("uw", U0 + 256, G0), c2("u0", 256, NV), 786432)
+    cl[0] = "setup"
     dma("y", c2("thr", 0, 1), V_("th"), 4096)
     iota(c2("pi", 0, 1), [[0, 1]], 0, 1)
     iota(V_("xr"), [[1, 152]], -16, 0); iota(V_("md"), [[1, 8], [0, 16]], 0, 0); iota(V_("x16"), [[1, 16]], 0, 0)
@@ -342,8 +358,8 @@ def build(opt, P):
         send([(c2(name, own, own + 128), c2(name, ghost, ghost + 128)), (c2(stage, 0, 128), c2(name, ghost + 128, ghost + 256))], cr)
         return j
 
-    first = send_shifted("cc", C0, C0 + NV, "sc", None)
-    send_shifted("uw", U0, G0, "su", None)
+    cl[0] = "sc0"; first = send_shifted("cc", C0, C0 + NV, "sc", None)
+    cl[0] = "su0"; send_shifted("uw", U0, G0, "su", None); cl[0] = "setup"
     cp(V_("hsf", S_(0, 8)), V_("hsi", S_(0, 8), AL))
     h = H()
     for par in range(2):
@@ -393,7 +409,7 @@ def build(opt, P):
 
     def turn(t):
         for h in range(2):
-            ts(V_("ftr", AL, AL, S_(16 * h, 16 * h + 16)), V_("lsw", AL, h, S_(t, 896, 4)), 4.0, A.mult)
+            mov("s", V_("ftr", AL, AL, S_(16 * h, 16 * h + 16)), V_("lsw", AL, h, S_(t, 896, 4)), 4.0)
         tr(V_("tlt"), V_("ftr"))
 
     def names(t):
@@ -432,12 +448,13 @@ def build(opt, P):
     def sides(t):
         for j, (part, hf) in enumerate(CH):
             cl[0] = "sd%d" % j
-            a = 128 * part + 64 * hf; h = H(); o = ps(h, 0, 64); gq = c2("gg", 16 * a, 16 * a + 1024)
-            x = ind(c2("cc", C0, C0 + NV + NG), V_("nix", AL, t % 2, S_(a, a + 64)))
-            sign(O("sides", t)[j], gq, x)
-            mmg([(o, sel("b16h", k), c2("gg", 16 * a + k, 16 * a + 1024, 16)) for k in range(16)] + [(o, ROW0, c2("tab8h", 64 * hf, 64 * hf + 64))], 17)
-            ts(c2("uix", a, a + 64), o, E4, A.add, 0.5 + 2 * (t % 2), A.add)
-            tt(c2("sg", a, a + 64), o, c2("tab8", 64 * hf, 64 * hf + 64), A.subtract)
+            w = 32 if j in opt["sfine"] else 64
+            for a in range(128 * part + 64 * hf, 128 * part + 64 * hf + 64, w):
+                h = H(); o = ps(h, 0, w); b = a % 128
+                sign(O("sides", t)[j], c2("gg", 16 * a, 16 * (a + w)), ind(c2("cc", C0, C0 + NV + NG), V_("nix", AL, t % 2, S_(a, a + w))))
+                mmg([(o, sel("b16h", k), c2("gg", 16 * a + k, 16 * (a + w), 16)) for k in range(16)] + [(o, ROW0, c2("tab8h", b, b + w))], 17)
+                ts(c2("uix", a, a + w), o, E4, A.add, 0.5 + 2 * (t % 2), A.add)
+                tt(c2("sg", a, a + w), o, c2("tab8", b, b + w), A.subtract)
 
     def pair_lists():
         h = H()
@@ -463,7 +480,7 @@ def build(opt, P):
         h = H()
         mm([(ps(h, 256 * z + e, 256 * z + 256, 2), V_("ee", AL, e, AL), c2("sel", 256 * z + 128 * part, 256 * z + 128 * part + 128), part == 0, part == 1)
             for z in range(2) for e in range(2) for part in range(2)])
-        mov("s", V_("cand"), ps(h, 0, 512))
+        mov("s", V_("cand16" if opt["sgn"] else "cand"), ps(h, 0, 512))
 
     def views(t, a, b, eng):
         for e, lo, hi in ((eng[0], a, (a + b) // 2), (eng[1], (a + b) // 2, b)):
@@ -482,7 +499,7 @@ def build(opt, P):
 
     def step1(t, r):
         win = c2("vw%d" % (t % 2), 0, 4096); ue = V_("uexp", AL, r, S_(0, 448))
-        m15, m37, m4, m26 = O("tree" + "AB"[r], t); onpe = O("pe" + "AB"[r], t); ondma = O("dma" + "AB"[r], t)
+        m15, m37, m4, m26 = O("tree" + "AB"[r], t); onpe = O("pe" + "AB"[r], t); ondma = O("dma" + "AB"[r], t); onq = O("q" + "AB"[r], t); up = []
         assert (0 in ondma) == (1 in ondma) or m4 == "v"
         def d(k, n=1): return c2("d2", 448 * k, 448 * (k + n))
         def q(k, n=1, a=0, b=448): return c2("q%d" % r, 448 * k + a, 448 * (k + n - 1) + b)
@@ -501,6 +518,11 @@ def build(opt, P):
                 if j // 2 in ondma:
                     act(d(j, 2), ind(win, c2("six%d" % (t % 2), 224 * r + 28 * j, 224 * r + 28 * j + 56)), F.Copy, -1.0)
                     dadd(d(j, 2), V_("uexp", AL, r, AL))
+                elif j // 2 in onq:
+                    act(d(j, 2), ind(win, c2("six%d" % (t % 2), 224 * r + 28 * j, 224 * r + 28 * j + 56)), F.Copy)
+                    if not up:
+                        up.append(ps(H(), 0, 448)); mov("s", up[0], ue)
+                    tt(d(j), d(j), up[0], A.subtract); tt(d(j + 1), d(j + 1), up[0], A.subtract)
                 else:
                     tt(d(j), x(j), ue, A.subtract); tt(d(j + 1), x(j + 1), ue, A.subtract)
                 act(ps(h, 0, 896), d(j, 2), F.Abs)
@@ -618,27 +640,35 @@ def build(opt, P):
             dma("y", V_("ys"), WW, 524288)
         cl[0] = "s3"
         n0, n1 = c2("uw", 2 * par, D0, 4), c2("uw", 2 * par + 1, D0, 4)
-        if opt["dd"] == "p":
-            dd = ps(H(), 0, 256)
-            mmg([(dd, I32, n0), (dd, V_("n32m"), n1)])
-        else:
-            dd = V_("dd"); tt(dd, n0, n1, A.subtract)
-        ts(c2("ud", 0, 256), dd, c2("thr", 0, 1), A.is_gt, 0.5, A.subtract)
-        ts(c2("ud", 256, 512), dd, c2("nth", 0, 1), A.is_lt, 0.5, A.subtract)
         hv = H(); up, dn = ps(hv, 0, 256), ps(hv, 256, 512)
-        mm([(ps(hv, 0, 512), V_("blk2k"), V_("ud"), True, True)])
-        tt(V_("rab"), ps(hv, 0, 512), V_("cand"), A.min)
-        tt(V_("cz", AL, 0, AL), c2("rab", 0, 256), c2("rab", 256, 512), A.max)
-        sign("s", V_("zs"), dn)
+        for a, b in opt["votes"]:
+            cl[0] = "s3" if b == 256 else "s2"
+            dd = c2("dd", a, b)
+            tt(dd, c2("uw", 4 * a + 2 * par, 4 * b, 4), c2("uw", 4 * a + 2 * par + 1, 4 * b, 4), A.subtract)
+            ts(c2("ud", a, b), dd, c2("thr", 0, 1), A.is_gt, 0.5, A.subtract)
+            ts(c2("ud", 256 + a, 256 + b), dd, c2("nth", 0, 1), A.is_lt, 0.5, A.subtract)
+            for lo, hi in ((0, 512),) if b - a == 256 else ((a, b), (256 + a, 256 + b)):
+                mm([(ps(hv, lo, hi), V_("blk2k"), c2("ud", lo, hi), True, True)])
+            for lo, hi in ((0, 512),) if b - a == 256 else ((a, b), (256 + a, 256 + b)):
+                if opt["sgn"]:
+                    sign("s", c2("sv16", lo, hi), ps(hv, lo, hi)); tt(c2("rab", lo, hi), c2("sv16", lo, hi), c2("cand16", lo, hi), A.mult)
+                else:
+                    tt(c2("rab", lo, hi), ps(hv, lo, hi), c2("cand", lo, hi), A.min)
+            tt(V_("cz", AL, 0, S_(a, b)), c2("rab", a, b), c2("rab", 256 + a, 256 + b), A.max)
+        if opt["sgn"]:
+            mov("g", V_("zs"), c2("sv16", 256, 512))
+        else:
+            sign("s", V_("zs"), dn)
         h = H()
         mmg([(ps(h, 0, 16), sel("b16", i), V_("cz", AL, 0, S_(i, 256, 16))) for i in range(16)], 16)
         mov("v", V_("cw"), ps(h, 0, 16))
         if opt["val"] == "ab":
             tt(c2("val", 0, 256), up, n0, A.min); tt(c2("val", 256, 512), dn, n1, A.min)
         else:
-            sign("s", V_("cz", AL, 1, AL), dn)
+            if not opt["sgn"]:
+                mov("g", c2("sv16", 256, 512), V_("zs"))
             h = H()
-            mmg([(ps(h, 0, 16), sel("b16h", i), V_("cz", AL, 1, S_(i, 256, 16))) for i in range(16)] + [(ps(h, 0, 16), ROW0, V_("t128h"))], 17)
+            mmg([(ps(h, 0, 16), sel("b16h", i), c2("sv16", 256 + i, 512, 16)) for i in range(16)] + [(ps(h, 0, 16), ROW0, V_("t128h"))], 17)
             ts(V_("vlx"), ps(h, 0, 16), ZV, A.add, 2.0 * par, A.add)
             mov("s", c2("val", 0, 256), ind(WW, V_("vlx")))
         h = H()
@@ -838,7 +868,7 @@ def plan(ops, pieces, times):
     for j in range(n - 1, -1, -1):
         o = ops[j]
         if o["cl"] in times:
-            key[j] = ROUND * o["rd"] + times[o["cl"]] + times.get("%s@%d" % (o["cl"][0], o["rd"]), 0.0)
+            key[j] = ROUND * o["rd"] + times.get("%s@%d" % (o["cl"], o["rd"]), times[o["cl"]])
         else:
             key[j] = min([key[s] - gp for s, gp in bw[j]] + [1e9]) - cost[j]
     st, seq = close(key, PASSES[0])
@@ -968,7 +998,41 @@ def refine(ops, refs, order, steps, heat, seed):
         for j in range(n):
             for d, g in fig[3][j]:
                 succ[-1][d].append((j, g))
-    tl = None; free_calls = [j for j in range(n) if alt[j]]
+    def move(order, en, a, b, far, ahead):
+        k0, k1 = pos[a], pos[b]; qn = set()
+        if ahead:
+            while far and k0 > 0:
+                k0 -= 1; far -= en[order[k0]] == en[a]
+            seg = order[k0:k1]; need = set(deps[b]); mv = []
+            for x in reversed(seg):
+                if x in need or en[x] in qn:
+                    if x == a:
+                        return None
+                    mv.append(x); need.update(deps[x])
+                    if en[x] < 5 and en[x] != en[b]:
+                        qn.add(en[x])
+            ms = set(mv)
+            return k0, mv[::-1] + [b] + [x for x in seg if x not in ms]
+        while far and k1 < n - 1:
+            k1 += 1; far -= en[order[k1]] == en[a]
+        seg = order[k0:k1 + 1]; ms = {a}; mv = [a]
+        for x in seg[1:]:
+            if en[x] in qn or not ms.isdisjoint(deps[x]):
+                if x == b:
+                    return None
+                mv.append(x); ms.add(x)
+                if en[x] < 5 and en[x] != en[a]:
+                    qn.add(en[x])
+        return k0, [x for x in seg if x not in ms] + mv
+    name = {}; seen = {}
+    for j, o in enumerate(ops):
+        k = (o["rd"], o["cl"], o["tag"], o["k"], o["e"] if not o["alt"] else "*"); seen[k] = seen.get(k, 0) + 1; name[k + (seen[k],)] = j
+    twin = [{} for o in ops]
+    for k, j in name.items():
+        for d in (-3, -2, -1, 1, 2, 3):
+            if (k[0] + d,) + k[1:] in name:
+                twin[j][d] = name[(k[0] + d,) + k[1:]]
+    free_calls = [j for j in range(n) if alt[j]]
     rs = [run(order, en, f, 0, None) for f in figs]; wt = [200.0 / r[0] / len(figs) for r in rs]
     cur = 200.0; best = (cur, order, en, rs); pos = {j: k for k, j in enumerate(order)}; arcs = [None] * len(figs)
     for it in range(steps):
@@ -980,55 +1044,31 @@ def refine(ops, refs, order, steps, heat, seed):
                 if w <= -2:
                     w = -2 - w; arcs[f].append((w, j))
                 j = w
-        a, b = arcs[f][int(rnd() * len(arcs[f]))]; u = rnd(); e2 = en; far = (0, 0, 1, 2, 4, 8)[int(rnd() * 6)]; ok = True; qn = set(); fee = 0.0
+        a, b = arcs[f][int(rnd() * len(arcs[f]))]; u = rnd(); e2 = en; far = (0, 0, 1, 2, 4, 8)[int(rnd() * 6)]; new = order; every = rnd() < TWINS
         if u < 0.2:
             x = a if u < 0.07 else b if u < 0.14 else free_calls[int(rnd() * len(free_calls))]
             if not alt[x]:
                 continue
-            e2 = list(en); e2[x] = [e for e in alt[x] if e != en[x]][int(rnd() * (len(alt[x]) - 1))]; new = order; k0 = k1 = pos[x]
-            fee = LEAN * figs[0][0][0][x] * ((e2[x] == 0) - (en[x] == 0))
-        elif u < 0.6:
-            k0 = pos[a]; k1 = pos[b]
-            while far and k0 > 0:
-                k0 -= 1; far -= en[order[k0]] == en[a]
-            seg = order[k0:pos[b]]; need = set(deps[b]); mv = []
-            for x in reversed(seg):
-                if x in need or en[x] in qn:
-                    if en[x] == en[b]:
-                        ok = False
-                        break
-                    mv.append(x); need.update(deps[x])
-                    if en[x] < 5:
-                        qn.add(en[x])
-            if not ok:
-                continue
-            ms = set(mv); new = order[:k0] + mv[::-1] + [b] + [x for x in seg if x not in ms] + order[pos[b] + 1:]
+            e2 = list(en); to = [e for e in alt[x] if e != en[x]][int(rnd() * (len(alt[x]) - 1))]; k0 = n
+            for y in [x] + (list(twin[x].values()) if every else []):
+                if alt[y] and to in alt[y]:
+                    e2[y] = to; k0 = min(k0, pos[y])
         else:
-            k = pos[b]; k0 = pos[a]
-            while far and k < n - 1:
-                k += 1; far -= en[order[k]] == en[a]
-            seg = order[k0:k + 1]; ms = {a}; mv = [a]; k1 = k
-            for x in seg[1:]:
-                if en[x] in qn or not ms.isdisjoint(deps[x]):
-                    if en[x] == en[a]:
-                        ok = False
-                        break
-                    mv.append(x); ms.add(x)
-                    if en[x] < 5:
-                        qn.add(en[x])
-            if not ok:
+            new = list(order); k0 = n; used = []
+            for x, y in [(a, b)] + ([(twin[a][d], twin[b][d]) for d in twin[a] if d in twin[b]] if every else []):
+                got = move(order, en, x, y, far, u < 0.6) if pos[x] < pos[y] else None
+                if got and all(got[0] > hi or got[0] + len(got[1]) <= lo for lo, hi in used):
+                    new[got[0]:got[0] + len(got[1])] = got[1]; k0 = min(k0, got[0]); used.append((got[0], got[0] + len(got[1]) - 1))
+                elif x == a:
+                    break
+            if k0 == n:
                 continue
-            new = order[:k0] + [x for x in seg if x not in ms] + mv + order[k + 1:]
-        bar = cur + heat * rnd() ** 3 * (1 - it / steps) - fee
-        if tl is None:
-            tl = [tails(order, en, fig, sc) for fig, sc in zip(figs, succ)]
-        if sum(least(new, e2, fig, sc, k0, k1, r, x) * w for fig, sc, r, x, w in zip(figs, succ, rs, tl, wt)) > bar + 1e-6:
-            continue
+        bar = cur + heat * rnd() ** 3 * (1 - it / steps)
         if k0 > n - 60:
             k0 = 0
         r2 = [run(new, e2, fig, k0, r) for fig, r in zip(figs, rs)]; t = sum(r[0] * w for r, w in zip(r2, wt))
         if t <= bar:
-            cur, rs, en = t, r2, e2; arcs = [None] * len(figs); tl = None
+            cur, rs, en = t, r2, e2; arcs = [None] * len(figs)
             if it % 8 == 0:
                 end = r2[0][4]; c0 = figs[0][0]; rk = {j: k for k, j in enumerate(new)}
                 new = sorted(new, key=lambda j: (end[j] - (c0[en[j]][j] if en[j] < 5 else 0.0), rk[j]))
@@ -1041,6 +1081,151 @@ def refine(ops, refs, order, steps, heat, seed):
             if o["alt"]:
                 o["e"] = QUEUES[e]; o["f"], o["cost"] = o["alt"][o["e"]]
     return best[1], best[3][0][4], [r[0] for r in best[3]]
+
+
+def refine(ops, refs, full, steps, heat, seed, lo, hi):
+    n = len(ops); state = [seed]
+    def rnd():
+        state[0] = (state[0] * 1103515245 + 12345) % 2147483648
+        return state[0] / 2147483648.0
+    en = [QUEUES.index(o["e"]) for o in ops]; deps = [[] for o in ops]
+    pos = {j: k for k, j in enumerate(full)}; above = [0] * n
+    for j in full:
+        for d in sorted(ops[j]["deps"], key=lambda d: -pos[d]):
+            if not above[j] >> d & 1:
+                deps[j].append(d); above[j] |= above[d] | 1 << d
+    alt = [[QUEUES.index(e) for e in o["alt"]] if o["alt"] else None for o in ops]
+    def run(order, en, fig, k0, old):
+        cost, xf, lk, rest, behind, start = fig
+        end, why, out = list(old[3]), list(old[1]), list(old[4]); free, last = list(start[0]), list(start[1]); left = {0, 1, 2, 3, 4, 6}
+        for j in order[k0 - 1::-1] if k0 else ():
+            if en[j] in left:
+                left.discard(en[j]); last[en[j]] = j; free[en[j]] = out[j]
+            if xf[j] and 6 in left:
+                left.discard(6); last[6] = j; free[6] = end[j]
+            if not left:
+                break
+        for j in order[k0:]:
+            r = 0.0; w = -1
+            for d, g in lk[j]:
+                x = end[d] + g
+                if x > r:
+                    r = x; w = d
+            e = en[j]
+            if e < 5:
+                if free[e] > r:
+                    r = free[e]; w = -2 - last[e]
+                r += cost[e][j]; free[e] = r; last[e] = j
+            out[j] = r
+            if xf[j]:
+                r += xf[j][0]
+                if free[6] > r:
+                    r = free[6]; w = -2 - last[6]
+                r += xf[j][1]; free[6] = r; last[6] = j
+            end[j] = r; why[j] = w
+        top, tj = max([(end[j] + rest[j], j) for j in order] + [(free[e] + behind[e], last[e]) for e in range(7)])
+        return top, why, tj, end, out, free, last
+    figs = []; rs = []; order = full[lo:hi]
+    for ref in refs:
+        cost = [[o["alt"][e][1] if o["alt"] and e in o["alt"] else o["cost"] for o in ref] for e in QUEUES]
+        lat = [0.0 if o["xf"] else o["lat"] for o in ref]; xf = [(o["lat"] - o["xf"], o["xf"]) if o["xf"] else None for o in ref]
+        lk = [[(d, 0.0 if en[j] == 2 and en[d] == 2 else lat[d]) for d in deps[j]] for j in range(n)]
+        rest = list(lat); behind = [0.0] * 7
+        for j in reversed(full[hi:]):
+            a = rest[j]
+            if xf[j]:
+                behind[6] = xf[j][1] + max(a, behind[6]); a = xf[j][0] + behind[6]
+            if en[j] < 5:
+                a = behind[en[j]] = cost[en[j]][j] + max(a, behind[en[j]])
+            for d, g in lk[j]:
+                rest[d] = max(rest[d], g + a)
+        zero = (0, [-1] * n, 0, [0.0] * n, [0.0] * n)
+        head = run(full[:lo], en, (cost, xf, lk, rest, behind, ([0.0] * 7, [-1] * 7)), 0, zero)
+        figs.append((cost, xf, lk, rest, behind, head[5:])); rs.append(run(order, en, figs[-1], 0, head))
+    n = len(order); pos = {j: k for k, j in enumerate(order)}
+    def move(a, b, far, ahead):
+        k0, k1 = pos[a], pos[b]; qn = set()
+        if ahead:
+            while far and k0 > 0:
+                k0 -= 1; far -= en[order[k0]] == en[a]
+            seg = order[k0:k1]; need = set(deps[b]); mv = []
+            for x in reversed(seg):
+                if x in need or en[x] in qn:
+                    if x == a:
+                        return None
+                    mv.append(x); need.update(deps[x])
+                    if en[x] < 5 and en[x] != en[b]:
+                        qn.add(en[x])
+            ms = set(mv)
+            return k0, mv[::-1] + [b] + [x for x in seg if x not in ms]
+        while far and k1 < n - 1:
+            k1 += 1; far -= en[order[k1]] == en[a]
+        seg = order[k0:k1 + 1]; ms = {a}; mv = [a]
+        for x in seg[1:]:
+            if en[x] in qn or not ms.isdisjoint(deps[x]):
+                if x == b:
+                    return None
+                mv.append(x); ms.add(x)
+                if en[x] < 5 and en[x] != en[a]:
+                    qn.add(en[x])
+        return k0, [x for x in seg if x not in ms] + mv
+    name = {}; seen = {}; twin = {j: {} for j in order}
+    for j in sorted(order):
+        o = ops[j]; k = (o["rd"], o["cl"], o["tag"], o["k"], "*" if o["alt"] else o["e"]); seen[k] = seen.get(k, 0) + 1; name[k + (seen[k],)] = j
+    for k, j in name.items():
+        for d in (-3, -2, -1, 1, 2, 3):
+            if (k[0] + d,) + k[1:] in name:
+                twin[j][d] = name[(k[0] + d,) + k[1:]]
+    either = [j for j in order if alt[j]]
+    wt = [200.0 / r[0] / len(figs) for r in rs]; cur = 200.0; best = (cur, order, en, rs); arcs = [None] * len(figs)
+    for it in range(steps):
+        f = int(rnd() * len(figs))
+        if arcs[f] is None:
+            why = rs[f][1]; j = rs[f][2]; arcs[f] = []
+            while j in pos:
+                w = why[j]
+                if w <= -2:
+                    w = -2 - w
+                    if w in pos:
+                        arcs[f].append((w, j))
+                j = w
+        if not arcs[f]:
+            continue
+        a, b = arcs[f][int(rnd() * len(arcs[f]))]; u = rnd(); e2 = en; far = (0, 0, 1, 2, 4, 8)[int(rnd() * 6)]; new = order; k0 = n
+        every = rnd() < TWINS
+        if u < 0.2:
+            x = a if u < 0.07 else b if u < 0.14 else either[int(rnd() * len(either))]
+            if not alt[x]:
+                continue
+            e2 = list(en); to = [e for e in alt[x] if e != en[x]][int(rnd() * (len(alt[x]) - 1))]
+            for y in [x] + (list(twin[x].values()) if every else []):
+                if to in alt[y]:
+                    e2[y] = to; k0 = min(k0, pos[y])
+        else:
+            new = list(order); used = []
+            for x, y in [(a, b)] + ([(twin[a][d], twin[b][d]) for d in twin[a] if d in twin[b]] if every else []):
+                got = move(x, y, far, u < 0.6) if pos[x] < pos[y] else None
+                if got and all(got[0] > q or got[0] + len(got[1]) <= p for p, q in used):
+                    new[got[0]:got[0] + len(got[1])] = got[1]; k0 = min(k0, got[0]); used.append((got[0], got[0] + len(got[1]) - 1))
+                elif x == a:
+                    break
+            if k0 == n:
+                continue
+        r2 = [run(new, e2, fig, k0, r) for fig, r in zip(figs, rs)]; t = sum(r[0] * w for r, w in zip(r2, wt))
+        if t <= cur + heat * rnd() ** 3 * (1 - it / steps):
+            cur, rs, en = t, r2, e2; arcs = [None] * len(figs)
+            if it % 8 == 0:
+                out = r2[0][4]; c0 = figs[0][0]; rk = {j: k for k, j in enumerate(new)}
+                new = sorted(new, key=lambda j: (out[j] - (c0[en[j]][j] if en[j] < 5 else 0.0), rk[j]))
+                r2 = rs = [run(new, en, fig, 0, r) for fig, r in zip(figs, rs)]; t = cur = sum(r[0] * w for r, w in zip(r2, wt))
+            order = new; pos = {j: k for k, j in enumerate(order)}
+            if t < best[0]:
+                best = (t, order, en, r2)
+    for calls in [ops] + refs:
+        for o, e in zip(calls, best[2]):
+            if o["alt"]:
+                o["e"] = QUEUES[e]; o["f"], o["cost"] = o["alt"][o["e"]]
+    return full[:lo] + best[1] + full[hi:], best[3][0][4]
 
 
 def rebank(ops, pieces, data, order, end):
@@ -1069,10 +1254,13 @@ def schedule(opt, plans, phases):
     ops, pieces = build(opt, plans[0]); refs = [build(opt, p)[0] for p in plans]
     data = [set(o["deps"]) for o in ops]
     order, st, end, bank = plan(ops, pieces, opt["boost"])
-    for k, (steps, heat) in enumerate(phases):
+    n = len(ops)
+    for k, (steps, heat, parts) in enumerate(phases):
         if k:
             order, bank = rebank(ops, pieces, data, order, end) or (order, bank)
-        order, end, times = refine(ops, refs, order, steps, heat, k + 1)
+        for j in range(parts):
+            order, end = refine(ops, refs, order, steps, heat, 7 * k + j + 1, max(0, n * j // parts - 40), min(n, n * (j + 1) // parts + 40))
+        order, end = refine(ops, refs, order, 0, heat, 1, 0, n)
     return ops, order, end, bank
 
 
@@ -1098,11 +1286,11 @@ def rank_program(g, core, T, topo):
          "bank": CACHE["plan"][3]}
     queue = {"v": g.vector, "s": g.scalar, "p": g.tensor, "g": g, "y": g.sync}
     own = {"v": "v", "s": "s", "p": "p", "g": "gq"}
-    count = {}; token = {}; known = {e: {} for e in queue}; total = {}
+    count = {}; token = {}; known = {e: {} for e in queue}; total = {}; seen = {}; when = {}; waited = {}
 
     def wait(e, s, k):
         if known[e].get(s, 0) < k:
-            queue[e].wait_ge(T.sem[s], k); known[e][s] = k
+            queue[e].wait_ge(T.sem[s], k); known[e][s] = k; waited[s] = max(waited.get(s, 0), k)
 
     for j in order:
         o = ops[j]; e = o["e"]
@@ -1113,11 +1301,18 @@ def rank_program(g, core, T, topo):
         for d in o["deps"]:
             if d in o["soft"] or (e == "p" and ops[d]["e"] == "p") or (o["k"] == "r" and ops[d]["k"] == "r" and ops[d]["sem"][1] == 1):
                 continue
-            s, k = token[d]; need[s] = max(need.get(s, 0), k)
+            s, k = token[d]
+            if s == own.get(e) and d in o["reads"]:
+                continue
+            need[s] = max(need.get(s, 0), k)
         if o["ext"]:
             need[o["ext"][0]] = o["ext"][1]; total[o["ext"][0]] = o["ext"][1]
-        for s in sorted(need):
-            wait(e, s, need[s])
+        for s in sorted(need, key=lambda s: -when.get((s, need[s]), -1)):
+            if known[e].get(s, 0) < need[s]:
+                wait(e, s, need[s])
+                for s2, k2 in seen.get((s, need[s]), {}).items():
+                    known[e][s2] = max(known[e].get(s2, 0), k2)
+        before = dict(known[e])
         ins = o["f"](c)
         if o["k"] == "c":
             s = own[e]
@@ -1129,6 +1324,7 @@ def rank_program(g, core, T, topo):
         else:
             k = len(en) if o["sem"][1] == "en" else 1
             token[j] = (o["sem"][0], k); total[o["sem"][0]] = k
+        seen[token[j]] = before; when[token[j]] = len(when)
     for s in sorted(total):
-        if max(known[e].get(s, 0) for e in known) < total[s]:
-            wait("y", s, total[s])
+        if waited.get(s, 0) < total[s]:
+            queue["y"].wait_ge(T.sem[s], total[s])

@@ -5,89 +5,86 @@ A = AluOpType
 F = ActivationFunctionType
 
 NV, NG, NS, RO = 1792, 256, 512, 4
-D0 = 1024
-U0 = D0 + 256
+W0 = 256
+U0 = W0 + 1024
 G0 = U0 + NV
 UE = G0 + NG
-C0 = 256
-SLOT = (4, 0, 6, 2, 5, 1, 7, 3)
-OPT = {"pair": "pppp", "val": "ab", "dd": "p", "c1": "ppv", "scale2": "sss", "grp": ((0, 2), (2, 3), (3, 4)), "fine": (3,), "cch": "gggg", "ue": "g", "const": "g", "nm": "s", "cab": "p",
-       "sides": "ssss", "ucol": "ssss", "rr": "ssss", "gv": "ss", "vA": "ss", "vB": "ss", "vAearly": True,
-       "treeA": "dddv", "treeB": "ddvv", "tail": "ps", "scale1": "ss", "eng": {}, "qA": (), "qB": (), "sgn": False, "votes": ((0, 192), (192, 256)), "sfine": (), "once": False, "wide": True, "peA": (), "peB": (), "dmaA": (), "dmaB": (),
-       "boost": {"uc0": -2, "uc1": 0, "uc2": 3, "uc3": 5, "x0": 0, "x1": 1.5, "x2": 4.5, "x3": 6.5, "vB": 1, "m0": 2, "m1": 4, "m2": 7, "m3": 9,
-                 "l0": 7, "l1": 8, "l2": 11, "l3": 12, "w0": 10, "w1": 13, "w2": 14, "s3": 16, "A0": 8, "A1": 10, "A2": 14, "A3": 17, "At": 22,
-                 "names": 18, "turn": 20, "host": 27, "cch": 26.5, "vl": 27.5, "nl": 38, "B0": 26, "B1": 28, "B2": 31, "B3": 33, "Bt": 36,
-                 "gv": 29, "vA": 30, "sd0": 31, "sd1": 32.5, "sd2": 34, "sd3": 35.5, "pl": 38, "cand": 40, "ue": 30, "uf": 44}}
-OPT.update({"pair": "pppx", "val": "g", "dd": "v", "treeA": "dddd", "treeB": "ddpv", "tail": "pp", "dmaA": (2, 3), "dmaB": (2,),
-            "sides@0": "svsv", "vA@0": "sv", "vB@0": "sv", "pair@3": "pppv", "dmaB@3": (2, 3), "treeB@3": "ddvv",
-            "boost": {'uc0': -3.0, 'uc1': -1.5, 'uc2': 3.0, 'uc3': 2.5, 'x0': -0.5, 'x1': 1.0, 'x2': 2.5, 'x3': 4.0, 'vB': 8.5, 'm0': 2.0, 'm1': 3.5,
-                      'm2': 10.0, 'm3': 10.5, 'l0': 7.5, 'l1': -2.0, 'l2': 14.0, 'l3': -4.0, 'w0': 10.5, 'w1': 11.0, 'w2': 17.0, 's3': -13.5,
-                      'A0': -23.5, 'A1': 13.0, 'A2': 16.0, 'A3': 20.0, 'At': 22.0, 'names': -18.5, 'turn': 15.0, 'host': 11.0, 'cch': 25.5,
-                      'vl': 27.0, 'nl': 57.5, 'B0': 22.0, 'B1': 28.5, 'B2': 32.0, 'B3': 29.5, 'Bt': 40.5, 'gv': 19.5, 'vA': 30.0, 'sd0': 9.0,
-                      'sd1': 11.5, 'sd2': 38.5, 'sd3': 36.0, 'pl': 23.0, 'cand': 23.0, 'ue': 16.0, 'uf': 43.0, 'B@3': -4.5, 'A@3': -2.0,
-                      'v@-1': -1.0, 's@-1': 6.5}})
-OPT.update({"dmaA": (), "dmaB": (), "peA": (3,), "peB": (2,), "dmaB@3": (), "peA@3": (2, 3), "peB@3": (0, 2), "treeA": "dddd", "treeB": "ddvv",
-            "ucol": "svss", "sides": "vsss", "gv": "vs", "eng": {"nl.sgw": "v", "Bt.ps": "v", "Bt.hi1": "v", "s3.cw": "s"},
-            "boost": {'vB': 4.5, 'uc0': -4.0, 'x0': 0.0, 'm0': 3.5, 'uc1': -5.0, 'x1': 1.5, 'm1': 4.5, 'uc2': 0.0, 'x2': 6.0, 'm2': 9.0, 'uc3': 0.0,
-                      'x3': 5.0, 'm3': 8.5, 'l0': 10.5, 'l1': 10.0, 'l2': 14.5, 'l3': 14.5, 'w0': 15.0, 'w1': 17.0, 'w2': 17.5, 's3': 23.5,
-                      'names': 12, 'turn': 5, 'host': 28.5, 'cch': 30.5, 'vl': 34.5, 'nl': 41.5, 'sd0': 36, 'sd1': 36.5, 'sd2': 41.0,
-                      'sd3': 37.0, 'pl': 46.5, 'cand': 50.0, 'A0': 12.0, 'A1': 14.5, 'A2': 17.5, 'A3': 17.0, 'At': 29.5, 'gv': 41.0,
-                      'vA': 40.0, 'ue': 36.0, 'B0': 26.5, 'B1': 26.0, 'B2': 31.0, 'B3': 30.5, 'Bt': 39.0, 'uf': 44.5}})
-OPT.update({"dmaA": (2, 3), "dmaB": (2,), "peA": (), "peB": (), "dmaB@3": (2, 3), "peA@3": (), "peB@3": (), "treeA": "dddd", "treeB": "dddv",
-            "treeB@3": "ddvv", "wide": False, "pair": "ddxx", "pair@3": "ddxx",
-            "dmaA": (0, 1, 3), "dmaB": (2,), "treeB": "ddvv", "c1": "vvv", "tail": "ss", "cab": "v"})
-OPT.update({"dmaA@3": (0, 1, 3), "dmaB@3": (2, 3), "sides": "svss", "ucol": "ssss",
-            "boost": {"s2": 18, 'vB': 5.0, 'uc0': -2.0, 'x0': 0.0, 'm0': 3.0, 'uc1': -4.0, 'x1': 0.5, 'm1': 5.0, 'uc2': 2.5, 'x2': 6.5, 'm2': 10.0, 'uc3': -0.5,
-                      'x3': 4.0, 'm3': 9.0, 'l0': 13.0, 'l1': 12.5, 'l2': 15.0, 'l3': 14.5, 'w0': 15.0, 'w1': 17.5, 'w2': 17.0, 's3': 22.0,
-                      'names': 12, 'turn': 20, 'host': 30.5, 'cch': 32.0, 'vl': 35.0, 'nl': 42.0, 'sd0': 38.0, 'sd1': 37.0, 'sd2': 40.0,
-                      'sd3': 37.0, 'pl': 46.5, 'cand': 56.5, 'A0': 10.5, 'A1': 15.5, 'A2': 11.0, 'A3': 16.5, 'At': 31.0, 'gv': 39.5,
-                      'vA': 39.0, 'ue': 35.5, 'B0': 26.0, 'B1': 25.0, 'B2': 22.0, 'B3': 30.5, 'Bt': 35.0, 'uf': 47.0,
-                      "ld0": 20, "ldw": 20.5, "ld1": 21, "ld2": 22, "sc0": 24, "su0": 25, "vl@-1": 26, "gv@-1": 27, "vA@-1": 29,
-                      "vB@0": -15, "nl@-1": 31}})
-OPT.update({"votes": ((0, 256),), "sides": "vsvs", "gv": "sv", "eng": {"Bt.ps": "v", "Bt.hi1": "v", "s3.cw": "s"}})
-OPT["boost"].update({'vB': 2.5, 'uc0': -3.0, 'x0': 0.0, 'm0': 3.5, 'uc1': -0.5, 'x1': 2.0, 'm1': 5.5, 'uc2': 4.5, 'x2': 6.5, 'm2': 9.5, 'uc3': -1.5, 'x3': 4.5, 'm3': 11.0, 'l0': 13.0, 'l1': 13.5, 'l2': 16.5, 'l3': 13.0, 'w0': 16.5, 'w1': 18.5, 'w2': 15.5, 's3': 23.5, 'names': 15, 'turn': 22, 'host': 33.0, 'cch': 30.0, 'vl': 33.5, 'nl': 45.5, 'sd0': 37.0, 'sd1': 39.5, 'sd2': 41.5, 'sd3': 37.5, 'pl': 47.5, 'cand': 51.5, 'A0': 10.0, 'A1': 11.5, 'A2': 10.0, 'A3': 15.0, 'At': 29.5, 'gv': 40.0, 'vA': 37.0, 'ue': 34.5, 'B0': 27.5, 'B1': 24.0, 'B2': 21.0, 'B3': 30.5, 'Bt': 35.0, 'uf': 48.0})
+C0 = U0
+MID, FAR = 1024, 960
+TOP = 49152
+SPINE = (4, 0, 6, 2, 5, 1, 7, 3)
+OPT = {"pair": "ddxx", "dd": "v", "c1": "vvv", "grp": ((0, 2), (2, 3), (3, 4)), "fine": (3,), "shift": "ppp", "direct": 0,
+       "treeA": "dddd", "treeB": "ddvv", "tail": "ss", "dmaA": (0, 1, 3), "dmaB": (2,), "once": False, "ftr": "g", "u16": "sv", "mask": True, "rep": "d", "cz": "v", "cut": NV, "cut@-1": NV,
+       "dmaB@3": (2, 3)}
+ROUND = 43.0
+TIMES = {'vB': 2.5, 'uc0': -3.0, 'x0': 0.0, 'm0': 3.5, 'uc1': -0.5, 'x1': 2.0, 'm1': 5.5, 'uc2': 4.5, 'x2': 6.5, 'm2': 9.5, 'uc3': -1.5, 'x3': 4.5,
+         'm3': 11.0, 'l0': 13.0, 'l1': 13.5, 'l2': 16.5, 'l3': 13.0, 'w0': 16.5, 'w1': 18.5, 'w2': 15.5, 's3': 23.5, 'names': 15, 'turn': 22,
+         'host': 33.0, 'cch': 30.0, 'vl': 33.5, 'nl': 45.5, 'sd0': 37.0, 'sd1': 39.5, 'sd2': 41.5, 'sd3': 37.5, 'pl': 47.5, 'cand': 51.5,
+         'A0': 10.0, 'A1': 11.5, 'A2': 10.0, 'A3': 15.0, 'At': 29.5, 'gv': 40.0, 'vA': 37.0, 'ue': 34.5, 'B0': 27.5, 'B1': 24.0, 'B2': 21.0,
+         'B3': 30.5, 'Bt': 35.0, 'uf': 48.0, 'put': 30.0, 'cred': 12.0, 'out': 36.0,
+         "ld0": 20, "ldw": 20.5, "ld1": 21, "ld2": 22, "sc0": 24, "su0": 25, "vl@-1": 26, "gv@-1": 27, "vA@-1": 29, "vB@0": -15, "nl@-1": 31,
+         "names@-1": 28, "turn@-1": 30}
+OPT.update({"dmaB": (0, 1, 2, 3), "dmaB@3": (0, 1, 2, 3), "dmaA": (1, 3), "direct": 448})
+ROUND = 43.3
+TIMES = {'out': 40, 'ld0@-1': (28.4,),'ldw@-1': (29.4,),'ld1@-1': (26.5,),'ld2@-1': (27.4,),'sc0@-1': (30.3,30.7,31,39.1),'su0@-1': (33.6,34.4,37.9,43),'names@-1': (33.2,35.1,35.2,37),'turn@-1': (42.5,42.7,43.5),'vl@-1': (32.7,33.1,33.7,34.1),'nl@-1': (34.6,43.7,44.4,45,45.5,46,48.7),'sd0@-1': (39.6,41.1,42.4,43,43.9),'sd1@-1': (41,42.5,43.4,43.6,47.3),'sd2@-1': (41,43.9,45.5,46.5,50.1),'sd3@-1': (39.6,41.6,42.4,43.1,51.3),'pl@-1': (52.1,52.3,55.5),'cand@-1': (51.5,51.7,51.9,52.5,55.2,55.8,56.1,56.9,57.5,62.1),'gv@-1': (36.6,36.2,36.7,37.3,41.7,48.1),'vA@-1': (36.5,34.4),'ue@-1': (44.1,44.7),'uf@-1': (37.4,49.3),'vB': (-3,-2),'uc0': (-1.7,),'x0': (0,2.2),'m0': (4.8,5.4,3.6,4.2),'uc1': (-0.1,),'x1': (1.4,4.7),'m1': (6.7,8.8,7.2,7.8),'uc2': (3.2,),'x2': (5.3,8.4),'m2': (10.6,10.1),'uc3': (-0.8,1.3),'x3': (2.8,5.7,4.1,6.7),'m3': (11.1,12,13,11.5,12.5,13.9),'cred': (12.1,),'l0': (14.4,15.7),'l1': (13.2,14.3),'l2': (15,16.4),'l3': (16.3,17.6),'w0': (17.2,16.5,17.7,19.3,20.5,20.8),'w1': (18.4,18.2,18.8,20.6,20.9,21.1),'w2': (19.4,19,19.8,20.8,21,21.2),'s3': (21.4,22.2,22,22.6,23,23.4,23.7,24.1,24.1,24.8,24.5,24.9,28.6,28.8,25,25.6,25.5,26.2,25.9,26.5,26.3,26.7,26.8,27.5,27.4,27.5,27.8,28.6,28.8,29,29.9,30.4,30.9,36),'names': (9.3,12.3,12.4,22.5),'turn': (-14.9,-13.7,22.7),'host': (29.8,31.1,31.8,32.6),'cch': (31.9,29.9,29.9,29.9),'vl': (31.7,32.2,33.9,34.4,31,31.4,32.4,32.8),'nl': (39.7,42.5,43.3,43.8,44.3,44.8,47.3),'sd0': (36.5,38,39.6,41.2,42.4),'sd1': (37.9,40.2,42.4,42.6,46.1),'sd2': (39.1,42.7,44,45.3,47.2),'sd3': (36.5,39.2,40.9,41.1,48.7),'pl': (49.4,49.6,53.9),'cand': (47.9,48.9,49.2,49.8,53.7,54.2,54.6,56.1,56.7,60.6),'A0': (7.7,11.8,13.4,14.4),'A1': (7.2,9.8,17.1,18.6,19.5,25.9),'A2': (8.9,18.4,19.7),'A3': (9.7,11.1,22.2,24,24.9),'At': (21,22.9,28.9,30.2,31.2,31.6,31.9,32.2),'put': (32.6,33.9,34.5,34.7,39.8),'gv': (35.5,34.9,37.1,39.3,39.7,46),'vA': (34.6,33.6),'ue': (36.8,37.5),'B0': (19.5,20.9,26,27.6,28.9),'B1': (15.1,16.4,23,26.6,27.9,35.3),'B2': (20.9,22.3,27.7,30.3),'B3': (24.8,26.9,31.8,33.5,34,34.5),'Bt': (33,34.1,35,36.2,37.9,38.2,32.7,36.1,38.5,38.9),'uf': (35.7,48.1)}
+ENGINES = {'sc0@-1': '.s','su0@-1': '.v','names@-1': 's..v','turn@-1': 'vg','vl@-1': '...s','nl@-1': '.v....s','sd0@-1': 'v.v.s','sd1@-1': 's.v.v','sd2@-1': 'v.s.s','sd3@-1': 's.s.s','pl@-1': '..s','cand@-1': '....ss.s.s','gv@-1': 'vv.v','vA@-1': 'ss','ue@-1': 'g','uf@-1': 'g','vB': 'sv','uc0': 's','uc1': 's','uc2': 's','uc3': 'vs','m3': '..v..s','l0': 's','l1': 's','l2': 'v','l3': 's','w0': '...s','w1': '...v','w2': '...s','s3': '.......s.vs.ss...........s..v..s','names': 's..v','turn': 'sg','host': '...s','cch': 'gvsg','vl': '...v...s','nl': '.v....s','sd0': 'v.s.s','sd1': 's.v.v','sd2': 'v.s.s','sd3': 's.s.s','pl': '..s','cand': '....ss.s.s','A1': 's','A3': 's','At': '....s.v','put': '..s','gv': 'sv.s','vA': 'ss','ue': 'g','B0': 's','B1': 's','B2': 's','B3': 's','Bt': '....v','uf': 'g'}
+for k in list(TIMES):
+    if k[:2] == "sd":
+        TIMES[k] = TIMES[k][:3] + TIMES[k][4:]
+TIMES.update({"s3": 21.4, "val": (24, 24.5, 25, 27, 27.5), "s4": 24.5, "sc": 28, "sc0@-1": 29, "sc1@-1": 36, "yh": 32})
+ENGINES["s3"] = ""
+OPT.update({"dmaA": (), "direct": 0, "rep": "g", "shift": "www"})
+ROUND = 41.7
+TIMES = {'out':40,'yh':34,'ld0@-1':(26.4,),'ldw@-1':(27.6,),'ld1@-1':(25.5,),'sc0@-1':(28.6,35.1),'sc1@-1':(35.6,36),'su0@-1':(32.8,33.8,32.7,36.2,40.8),'names@-1':(31.8,32.4,32.6,33.2),'turn@-1':(38.9,37.8,39.6),'vl@-1':(31.3,31.9,32.6,32.9),'nl@-1':(39.9,42.1,42.3,43,43.6,44.2,47),'sd0@-1':(36.4,37.9,39.1,39.9),'sd1@-1':(36.4,38.5,39.8,40),'sd2@-1':(37.8,39.2,41.2,45.5),'sd3@-1':(38,40.5,43.6,45.6),'pl@-1':(47,48,54),'cand@-1':(45.7,47.3,47.5,47.8,50.1,52,53.1,54.3,54.9,62.4,63,65.6),'gv@-1':(33.4,33.4,35.9,39.2,34.8,40.8,46.7),'vA@-1':(33.8,34),'ue@-1':(47.9,39.8),'uf@-1':(44.8,41.8,46.9,34.2),'vB':(5.9,-1.2),'uc0':(-2.3,),'x0':(0,2.2),'m0':(4.7,5.3,4.3,4.8),'uc1':(-0.8,),'x1':(1.4,3.8),'m1':(5.2,8.5,6.4,7.5),'uc2':(0.7,),'x2':(2.7,7.6),'m2':(9.3,10.8),'uc3':(3.1,5.2),'x3':(5.7,7.1,6.8,8.8),'m3':(8.8,10.4,11.1,11.3,13,14.7),'cred':(22.4,),'l0':(16.4,17.2),'l1':(13.9,15.6),'l2':(13.2,14.9),'l3':(17.1,17.9),'w0':(18.7,18,19.3,21.3,21.7,22),'w1':(16.3,15.7,16.7,17.8,19.1,20),'w2':(20.1,20.2,20.8,21.6,21.9,22.1),'s3':(22.3,22.9,23.1,23.5,23.8,24.2,24.5,24.9,24.8,25.1),'val':(25.8,26.2,27.9,28.8,31.5),'s4':(26.9,25.5,25.3,25.9,25.8,26.4,26.2,26.8,26.5,27,27.2,28.1,28.4,28.6),'sc':(29.7,30.4,30.2,30.6,35.2),'names':(10.8,11.2,11.4,21.7),'turn':(27.3,26.5,33.9),'host':(31.3,32.2,34.9,39),'cch':(29.6,30,30.4,29.6),'vl':(31.1,31.6,32.5,32.8),'nl':(40.4,42,42.2,42.8,43.5,44.1,46.9),'sd0':(35.7,37.3,38.7,39.8),'sd1':(35.9,39.1,40.1,40.4),'sd2':(37.9,39.7,41.9,45.8),'sd3':(37.3,41,43.5,45.9),'pl':(46.2,47.2,54),'cand':(46,46.5,46.7,47,50,51.9,53,54.3,54.8,62.3,62.9,64.4),'A0':(8.2,9.7,11.6,13.5,14.4),'A1':(7.6,14.3,18,19.2,20.1,25.3),'A2':(12.4,11.8,18.8,21),'A3':(20.3,16.6,22,23.4,24.3),'At':(22.1,24.4,28.6,30,31.3,31.6,31.9,32.3),'put':(32.7,33.6,34.9,33.6,35.1,39.7),'gv':(34.1,33.6,36.6,38.8,36.7,39.1,45),'vA':(35,34),'ue':(41.8,36.1),'B0':(9.3,10.6,25,29.5,31.6),'B1':(15.2,16.5,24.2,27,27.9,37.1),'B2':(20.1,21.4,27.9,30.5),'B3':(22.8,26.3,31.9,33.5,34.5,35),'Bt':(33.2,33.9,35.6,38,39.2,39.6,33.3,35.5,39.9,40.2),'uf':(40.7,51.2,41.2,40.1)}
+ENGINES = {'sc1@-1':'.s','su0@-1':'.ss','names@-1':'s..s','turn@-1':'gs','vl@-1':'...s','nl@-1':'.s....s','sd0@-1':'v.v','sd1@-1':'s.v','sd2@-1':'v.v','sd3@-1':'s.s','pl@-1':'..s','cand@-1':'....ss.s.s.s','gv@-1':'vs.vv','vA@-1':'vs','ue@-1':'gg','uf@-1':'gggg','vB':'sv','uc0':'s','uc1':'s','uc2':'s','uc3':'ss','m3':'..s..s','l0':'s','l1':'s','l2':'s','l3':'s','w0':'...s','w1':'...s','w2':'...s','val':'ss.ss','s4':'............v','sc':'.vv','names':'s..s','turn':'gs','host':'...s','cch':'sssg','vl':'...s','nl':'.s....s','sd0':'v.s','sd1':'s.v','sd2':'v.s','sd3':'s.s','pl':'..s','cand':'....ss.s.s.s','At':'....s.v','put':'..sg','gv':'vs.sg','vA':'ss','ue':'gg','B0':'s','B1':'s','B2':'s','B3':'s','Bt':'....v','uf':'gggg'}
+TIMES["val"] = (25, 25.2, 25.4, 26, 30); ENGINES.update({"val": "..sss", "s4": "............vs"})
+OPT.update({"fine": (), "grp": ((0, 2), (2, 4)), "cz": "p", "dmaB": (0, 1, 2), "cut": 896, "pair": "ddpp"})
+ROUND = 40.9
+TIMES = {'out':40,'yh':34,'ld0@-1':(25.8,),'ldw@-1':(26.8,),'ld1@-1':(24.8,),'sc0@-1':(27.8,34.3),'sc1@-1':(34.8,35.2),'su0@-1':(32.9,33.4,33.9,34.3,38.9),'names@-1':(31.9,32.5,32.7,33.1),'turn@-1':(36.9,38.5,41.9),'vl@-1':(31.5,32.7,33.3),'nl@-1':(39.7,43.7,43.9,44.5,45.2,46.4,48.2),'sd0@-1':(35.6,37,38.3,38.6),'sd1@-1':(35.6,37.7,39,43.4),'sd2@-1':(36.9,38.4,40.4,43.5),'sd3@-1':(37.2,39.1,43.6,46),'pl@-1':(47,47.8,52.2),'cand@-1':(45.8,46.2,47.3,47.5,48.7,49.9,51.4,53.7,54.4,55,61.4),'gv@-1':(33.7,34.9,35.4,38.4,35.9,39.6,45.5),'vA@-1':(34.1,34.2),'ue@-1':(39,33.7),'uf@-1':(43.9,46,35.3,32.7),'vB':(5.2,-1.2),'uc0':(-2.4,),'x0':(0,1.7),'m0':(3.4,3.9,2.9,3.5),'uc1':(-1,),'x1':(1.4,2.9),'m1':(5.7,7.2,5.3,6.2),'uc2':(0.4,),'x2':(3.8,6.4),'m2':(8.7,7.6),'uc3':(3.8,),'x3':(6.2,8),'m3':(10.4,9.4,11.1,13.3,11.5,8.1,12.3,15.2),'cred':(21.1,),'l0':(14.5,15.4),'l1':(13.8,14.6),'l2':(15.7,16.6),'l3':(16.4,17.3),'w0':(16.2,16.2,17.4,20.1,20.7,21),'w1':(18.9,18.2,19.4,20.5,20.9,21.2),'s3':(21.4,22.2,22,22.6,23.4,23.5,23.7,24.5,23.7),'val':(23.6,23.8,24.8,27.2,25.7),'s4':(26.5,24.9,24.9,25.5,25.4,26.1,25.8,26.4,26.2,26.7,26.8,27.8,28.2,28.4),'sc':(29.3,30,30.2,30.5,35.1),'names':(20.8,24.4,24.5,31.8),'turn':(26.9,14.6,30.6),'host':(30.1,30.8,32.1,60),'cch':(30.4,29.7,32.1,31.5),'vl':(31.8,33,33.3),'vm':(33.8,35.2,38.6),'nl':(40.1,43.7,43.9,44.6,45.2,46.5,48.3),'sd0':(35.6,37.4,38.3,39),'sd1':(35.6,38.1,39.3,43.6),'sd2':(37,38.8,39.6,43.7),'sd3':(36.9,39.4,43.6,46.1),'pl':(47.2,47.9,53.4),'cand':(45.8,46.3,47.4,47.7,48.7,49.9,51.5,53.7,54.5,55.1,61.6),'A0':(8,9.8,10.5,12.6,13.6),'A1':(13.4,10.9,17.1,18.1,19,24.4),'A2':(9.1,12,18,19.3),'A3':(14,20.1,21.2,22.5,23.4),'At':(20.2,21.3,27.5,29.6,30.9,31.2,31.5,31.9),'put':(32.2,33.5,34.3,33.1,34.6,39.1),'gv':(33.5,33.9,36.8,38.3,35.6,38.7,44.6),'vA':(34.5,34.4),'ue':(40.2,36.7),'B0':(9.2,10.5,24.9,28.1,29),'B1':(11.3,12.6,22,23.9,25.4,33.6),'B2':(18.8,20.1,26.1,28.9),'B3':(26.6,29.2,30.2,31.4,33.2),'B3@3':(21,22,29.2,30.2,31.4,33.2),'Bt':(30.7,32.4,34.6,35.7,38.4,38.7,34.3,35.4,39.1,39.4),'uf':(39.7,40.8,36.2,49.1)}
+ENGINES = {'sc1@-1':'.v','su0@-1':'.vv','names@-1':'s..s','turn@-1':'sg','vl@-1':'..s','nl@-1':'......s','sd0@-1':'v.v','sd1@-1':'s.v','sd2@-1':'v.v','sd3@-1':'s.s','pl@-1':'..s','cand@-1':'....ss.s..s','gv@-1':'ss.vg','vA@-1':'sv','ue@-1':'gv','uf@-1':'gggs','vB':'sv','uc0':'s','uc1':'s','uc2':'s','uc3':'s','m3':'...s...s','l0':'s','l1':'s','l2':'s','l3':'s','w0':'...s','w1':'...s','s3':'.......s','val':'..sss','s4':'............ss','sc':'.ss','names':'s..s','turn':'sg','host':'...s','cch':'svsg','vl':'..s','vm':'..v','nl':'......s','sd0':'v.v','sd1':'s.v','sd2':'v.v','sd3':'s.s','pl':'..s','cand':'....ss.s..s','At':'....v.s','put':'..sg','gv':'ss.sg','vA':'sv','ue':'gg','B0':'s','B1':'s','B2':'s','Bt':'....v','uf':'gggg'}
 f32, f16, i32, u16, bf = "float32", "float16", "int32", "uint16", "bfloat16"
 SB = {
     "uw": ([128, UE], f32), "cc": ([128, C0 + NV + NG], f32), "vw0": ([128, 4096], f32), "vw1": ([128, 4096], f32),
     "tli": ([128, NV], i32), "lsw": ([128, 2, 896], i32), "ftr": ([128, 14, 32], f16), "tlt": ([128, 14, 32], f16),
-    "tt": ([128, 8192], f32), "d2": ([128, 3584], f32), "uu": ([128, 4096], f32), "gg": ([128, 4096], f16),
+    "tt": ([128, 8192], f32), "uu": ([128, 4096], f32), "gg": ([128, 4096], f16),
     "q0": ([128, 3584], f32), "q1": ([128, 3584], f32), "c1": ([128, 512], f32), "hi1": ([128, 448], f32),
     "uexp": ([128, 2, 896], f32),
     "sdi": ([128, 112], i32), "nri": ([128, 112], i32), "sdf": ([128, 112], f32), "nrf": ([128, 112], f32), "cb": ([128, 112], f16),
     "hsi": ([128, 512], i32), "hsf": ([128, 16, 32], f16), "thr": ([128, 4], f32), "nth": ([128, 4], f32),
     "hw": ([128, 32], f32), "hix": ([128, 32], u16), "hw16": ([128, 32], f16),
-    "nmh": ([128, 256], f16), "nix": ([128, 2, 256], u16), "jm": ([128, 16], f32), "n32m": ([128, 128], f32), "n1": ([128, 256], f16),
+    "nmh": ([128, 256], f16), "nix": ([128, 2, 256], u16), "jm": ([128, 16], f32), "n32m": ([128, 128], f32), "mk": ([128, 224], f32),
     "uix": ([128, 256], u16), "sg": ([128, 256], f16), "lix": ([128, 256], u16), "cab": ([128, 512], f16),
-    "sel": ([128, 512], f16), "sv16": ([128, 512], f16), "cand16": ([128, 512], f16), "cand": ([128, 512], f32),
-    "dd": ([128, 256], f32), "ud": ([128, 512], f16), "rab": ([128, 512], f16), "cz": ([128, 2, 256], f16), "zs": ([128, 256], f32),
-    "cw": ([128, 16], f32), "cwm": ([128, 16], f16), "cwp": ([128, 16], f16), "vlx": ([128, 16], u16),
-    "neg": ([128, 256], f16), "tgf": ([128, 16], f32), "tgx": ([128, 16], u16), "val": ([128, 512], f32),
-    "h1": ([128, 16], f32),
+    "sel": ([128, 2, 2, 128], f16), "r8": ([128, 2, 144], f16), "cw16": ([128, 16], f16), "zl": ([128, 16], f32), "cand": ([128, 512], f16), "clw": ([128, 32], f32), "cv": ([128, 32], f32),
+    "dd": ([128, 256], f32), "ud": ([128, 512], f16), "rb": ([128, 256], f32), "cz": ([128, 256], f16), "zs": ([128, 256], f32),
+    "cw": ([128, 16], f32), "vlx": ([128, 16], u16), "cbg": ([128, 112], f16), "rowsh": ([128, 2, 128], f16),
+    "idl": ([128, 256], f16), "tg": ([128, 256], f32), "rs0": ([128, 256], f32), "cdg": ([128, 256], f16), "tgx": ([128, 16], u16), "val": ([128, 256], f32),
+    "h1": ([128, 16], f32), "eq": ([128, 4096], f16),
     "f0": ([128, 224], f32), "vix": ([128, 224], u16), "sgw": ([128, 28], f16), "six0": ([128, 448], u16), "six1": ([128, 448], u16),
-    "sc": ([128, 256], f32), "su": ([128, 256], f32), "sv": ([128, 256], f32),
+    "sc": ([128, 256], f32), "su": ([128, 256], f32), "sv": ([128, 512], f32),
     "yc1": ([128, 112], f32), "yc2": ([128, 112], f32),
     "pi": ([128, 4], i32), "pj": ([128, 4], i32), "col": ([128, 16], f32), "xr": ([128, 152], f32), "x16": ([128, 16], f32),
     "ce": ([128, 16], f32), "md": ([128, 128], f32), "tz": ([128, 256], f32), "c2k": ([128, 128], f32),
-    "i32m": ([128, 128], f32), "i16m": ([128, 128], f16), "bz": ([128, 144], f16), "pk": ([128, 4], i32), "pm": ([128, 128], f32), "b32": ([128, 144], f32),
-    "b162": ([128, 144], f16), "cch": ([128, NV], f16), "b16": ([128, 144], f16), "b16h": ([128, 144], f16), "b4k": ([128, 144], f16),
+    "i32m": ([128, 128], f32), "i16m": ([128, 128], f16), "i4": ([128, 128], f16), "bz": ([128, 144], f16),
+    "pk": ([128, 4], i32), "pm": ([128, 128], f32), "b32": ([128, 144], f32),
+    "b162": ([128, 144], f16), "cch0": ([128, NV], f16), "cch1": ([128, NV], f16), "i4k": ([128, 2, 128], f16), "tab8": ([128, 256], f32), "b16": ([128, 144], f16), "b16h": ([128, 144], f16), "bsum": ([128, 144], f16),
     "b8": ([128, 144], f16), "blk": ([128, 128], f16), "blk2k": ([128, 128], f16), "lo8": ([128, 152], f16), "hi8": ([128, 152], f16),
-    "y8": ([128, 6, 128], f16), "ee": ([128, 2, 128], f16), "t1": ([128, 128], f32), "t2": ([128, 128], f32), "z16": ([128, 128], f16),
+    "y8": ([128, 2, 128], f16), "ee": ([128, 2, 128], f16), "t1": ([128, 128], f32), "t2": ([128, 256], f32),
     "rowb": ([128, 2048], f16), "tri": ([128, 2048], f16), "mm": ([128, 4, 128], f16),
-    "tab8": ([128, 128], f32), "tab8h": ([128, 128], f16), "tab16": ([128, 128], f32), "tab16h": ([128, 128], f16),
-    "tabs": ([128, 512], f32), "jw": ([128, 224], f32), "t128": ([128, 16], f32), "t128h": ([128, 16], f16),
+    "tab8h": ([128, 256], f16), "tab16": ([128, 256], f32), "tab16h": ([128, 256], f16),
+    "jw": ([128, 224], f32), "t128": ([128, 32], f32),
 }
 SCRATCH = {k: ("sbuf", s, d) for k, (s, d) in SB.items()}
 SCRATCH["ps"] = ("psum", [128, 4096], f32)
 IO = {"tl": [128, NV], "sd": [8, NV], "nr": [8, NV], "hs": [8, NS], "u0": [128, NV], "w0": [128, 1024], "th": [128, 1],
       "yu": [128, NV], "ys": [128, 1024], "yc": [8, NV], "yh": [8, NS]}
-SEMAPHORES = (["v", "s", "p", "gq"] + ["d%d" % i for i in range(112)] + ["a%d" % i for i in range(16)] + ["l%d" % i for i in range(16)])
+SEMAPHORES = (["v", "s", "p", "gq"] + ["d%d" % i for i in range(114)] + ["a%d" % i for i in range(16)] + ["l%d" % i for i in range(16)])
 
-PLAN = {"cy": 0.83e-3 * 1.1, "gam": 1.5, "sig": 3.5, "gi": 1.0, "dl": 2.0, "dr": 120e3, "hop": 0.1, "rl": 1.8, "rr": 80e3, "first": 3.0, "row": 0.03, "pe": 1.0}
-PLANS = [dict(PLAN, cy=0.92e-3, gam=1.55, dr=180e3, rr=100e3), dict(PLAN, cy=0.9e-3, gam=1.5, dl=2.3, dr=150e3, rl=2.3, rr=80e3, row=0.04, gi=1.1, hop=0.12, first=4.0, pe=2.0)]
-PHASES = ((14000, 1.5, 1), (24000, 2.0, 4), (24000, 1.0, 5), (20000, 0.6, 6), (14000, 0.3, 5), (12000, 0.3, 8))
-PASSES = [1, 2]
-ROUND = 43.0
+PLAN = {"cy": 0.85e-3, "gam": 1.5, "sig": 3.5, "gi": 1.0, "dl": 2.0, "dr": 220e3, "hop": 0.1, "rl": 1.8, "rr": 100e3, "first": 3.0, "row": 0.03, "pe": 1.4, "load": 1.3}
+PLANS = [PLAN, dict(PLAN, cy=0.84e-3, gam=1.2, sig=2.5, pe=1.45, dl=2.3, dr=165e3, rl=2.3, rr=80e3, row=0.04, gi=1.1, hop=0.13, first=4.0),
+         dict(PLAN, cy=1.2e-3, gam=2.0, sig=5.0)]
+PHASES = ((6000, 0.5, 1), (14000, 0.5, 4), (14000, 0.4, 5), (12000, 0.3, 6), (10000, 0.2, 5))
 TWINS = 0.6
+SEED = 1
 WIDE, NARROW, ANY = ((0, 1), (2, 3)), ((4,), (5,), (6,), (7,)), ((4,), (5,), (6,), (7,), (0,), (1,), (2,), (3,))
 
 
@@ -127,8 +124,8 @@ def two(v):
     return v["n"] != "ps" and SB[v["n"]][1] in (f16, u16, bf)
 
 
-def build(opt, P):
-    cl = ["setup", -1]; ops = []; hist = {}; nd = [0]; na = [0]; pieces = []; mark = {}; probe = [False]; made = set()
+def build(opt, engines, P):
+    cl = ["setup", -1]; ops = []; hist = {}; nd = [0]; na = [0]; pieces = []; probe = [False]; made = set(); nth = {}
     CY = P["cy"]; PCY = CY / 2 * P["pe"]; GAM = P["gam"]
 
     def O(name, t):
@@ -138,10 +135,10 @@ def build(opt, P):
         pieces.append({"pool": pool, "ops": []})
         return len(pieces) - 1
 
-    def add(eng, emit, rd, wr, cost, lat=None, kind="c", ninc=1, sem=None, after=(), ext=None, xf=0.0):
+    def add(eng, emit, rd, wr, cost, lat=None, kind="c", sem=None, after=(), ext=None, xf=0.0):
         if probe[0]:
             return emit, cost
-        me = len(ops); deps = set(after); acc = []; new = []; reads = set(); firm = set(after)
+        me = len(ops); deps = set(after); acc = []; reads = set(); firm = set(after)
         for v in rd:
             acc.append((v, v["n"] == "ps"))
             if v["off"] is not None:
@@ -156,9 +153,7 @@ def build(opt, P):
                 continue
             if v["n"] == "ps":
                 po = pieces[v["key"]]["ops"]
-                if not po:
-                    new.append(v["key"])
-                elif po[0] != me:
+                if po and po[0] != me:
                     deps.add(po[0])
                 if me not in po:
                     po.append(me)
@@ -175,13 +170,10 @@ def build(opt, P):
             if w:
                 h[:] = [e for e in h if not (e[3][0] >= v["p"][0] and e[3][1] <= v["p"][1] and (e[1] & ~v["m"]) == 0)]
             h.append((me, v["m"], v["box"], v["p"], w, dma))
-        ops.append({"cl": cl[0], "rd": cl[1], "tag": wr[0]["n"] if wr else "send", "e": eng, "f": emit, "deps": deps,
-                    "cost": cost, "lat": P["hop"] if lat is None else lat + xf, "xf": xf, "k": kind, "ninc": ninc, "sem": sem, "ext": ext, "new": new, "soft": set(), "alt": None, "reads": reads - firm})
+        k = nth.get(tuple(cl), 0); nth[tuple(cl)] = k + 1
+        ops.append({"cl": cl[0], "rd": cl[1], "nth": k, "tag": wr[0]["n"] if wr else "send", "e": eng, "f": emit, "deps": deps, "cost": cost,
+                    "lat": P["hop"] if lat is None else lat + xf, "xf": xf, "k": kind, "sem": sem, "ext": ext, "alt": None, "reads": reads - firm})
         return me
-
-    def hold(j, d):
-        if d is not None and d not in ops[j]["deps"]:
-            ops[j]["deps"].add(d); ops[j]["soft"].add(d)
 
     def ap(c, v):
         if not isinstance(v, dict):
@@ -189,6 +181,8 @@ def build(opt, P):
         if v["n"] == "ps":
             p, a, b, s = v["i"]; o = 512 * c["bank"][v["key"]]
             return c["T"]["ps"][p, slice(o + a, o + b, s)]
+        if "by" in v and ops[v["by"][0]]["e"] == "v":
+            v = v["by"][1]
         a = c["T"][v["n"]][v["i"]]
         return a if v["off"] is None else a.indirect(ap(c, v["off"]))
 
@@ -200,15 +194,15 @@ def build(opt, P):
             return 0.06 + out["c"] * P["sig"] * CY
         if ins and ins[0]["off"] is not None:
             return 0.06 + out["c"] * GAM * CY
-        if all(two(x) for x in [out] + ins):
-            k = k * 0.5
+        if k == 1 and all(two(x) for x in [out] + ins):
+            k = 0.5
         return 0.03 + max(64, out["c"] * k) * CY
 
     def cp(out, a):
         return add("v", lambda c: [c["g"].vector.tensor_copy(ap(c, out), ap(c, a))], [a], [out], vcost(out, [a], 1))
 
     def tt(out, a, b, op):
-        k = 1 if "ps" in (a["n"], b["n"]) else 2
+        k = 1 if "ps" in (a["n"], b["n"]) else 1.5 if two(a) and two(b) and two(out) else 2
         return add("v", lambda c: [c["g"].vector.tensor_tensor(ap(c, out), ap(c, a), ap(c, b), op)], [a, b], [out], vcost(out, [a, b], k))
 
     def ts(out, a, s1, op0, s2=None, op1=None):
@@ -218,19 +212,31 @@ def build(opt, P):
             f = lambda c: [c["g"].vector.tensor_scalar(ap(c, out), ap(c, a), ap(c, s1), ap(c, s2), op0, op1)]
         return add("v", f, vs(a, s1, s2), [out], vcost(out, [a], 1))
 
-    def ms(out, x):
-        return add("v", lambda c: [c["g"].vector.memset(ap(c, out), x)], [], [out], vcost(out, [], 1))
+    def scan(out, a, b, first, op0, op1):
+        return add("v", lambda c: [c["g"].vector.tensor_tensor_scan(ap(c, out), ap(c, a), ap(c, b), first, op0, op1)], [a, b], [out], vcost(out, [a, b], 1))
 
     def tr(out, a):
         return add("v", lambda c: [c["g"].vector.transpose(ap(c, out), ap(c, a))], [a], [out], vcost(out, [a], 1))
 
-    def act(out, a, fn, scale=1.0, bias=0.0):
+    def act(out, a, fn, scale=1.0, bias=0.0, more=0.0):
         k = GAM if a["off"] is not None else 1
         return add("s", lambda c: [c["g"].scalar.activation(ap(c, out), ap(c, a), fn, bias=ap(c, bias), scale=ap(c, scale))],
-                   vs(a, scale, bias), [out], 0.06 + max(64, out["c"] * k) * CY)
+                   vs(a, scale, bias), [out], 0.06 + more + max(64, out["c"] * k) * CY)
+
+    def put_codes(out, a):
+        return either("s", {"v": lambda: cp(out, a),
+                            "s": lambda: add("s", lambda c: [c["g"].scalar.activation(ap(c, out), ap(c, a), F.Silu)], [a], [out], vcost(out, [a], 1))})
 
     def asel(out, a, pat, op, fill, base, cm):
         return add("g", lambda c: [c["g"].affine_select(ap(c, out), ap(c, a), pat, op, fill, base, cm)], [a], [out], 0.17 + 2 * out["c"] * CY)
+
+    def either(e, ways):
+        me = ways[e](); o = ops[me]; o["alt"] = {}
+        for k in ways:
+            probe[0] = True; o["alt"][k] = ways[k](); probe[0] = False
+        pick = engines.get("%s@%d" % (o["cl"], o["rd"]), engines.get(o["cl"], ""))[o["nth"]:o["nth"] + 1]
+        o["e"] = pick if pick in ways else e; o["f"], o["cost"] = o["alt"][o["e"]]
+        return me
 
     def mov(e, out, a, scale=None):
         ways = {"s": lambda: act(out, a, F.Copy, 1.0 if scale is None else scale),
@@ -239,16 +245,16 @@ def build(opt, P):
             ways["g"] = lambda: asel(out, a, [[0, out["c"]]], A.is_ge, 0.0, 0, 0)
         return either(e, ways)
 
-    def either(e, ways):
-        me = ways[e](); o = ops[me]; o["alt"] = {}
-        for k in ways:
-            probe[0] = True; o["alt"][k] = ways[k](); probe[0] = False
-        o["e"] = opt["eng"].get("%s.%s" % (o["cl"], o["tag"]), e); o["f"], o["cost"] = o["alt"][o["e"]]
-        return me
+    def lin(e, out, a, scale, bias, relu=False):
+        ways = {"s": lambda: act(out, a, F.Relu if relu else F.Identity, scale, bias),
+                "v": lambda: ts(out, a, bias, A.add, 0.0, A.max) if relu else ts(out, a, scale, A.mult, bias, A.add)}
+        if SB[out["n"]][1] == u16:
+            ways = {k: ways[k] for k in opt["u16"]}
+        return either(e if e in ways else "v", ways)
 
-    def sign(e, out, a, k=1.0):
-        return either(e, {"s": lambda: act(out, a, F.Sign, k),
-                          "v": lambda: ts(out, a, -1.0, A.max, 1.0, A.min) if k > 0 else ts(out, a, 0.0, A.is_gt, -1.0, A.mult)})
+    def side(e, out, a):
+        j = either(e, {"s": lambda: act(out, a, F.Sign, 1.0, -float(MID)), "v": lambda: ts(out, a, float(MID), A.is_gt, 0.5, A.subtract)})
+        return lambda k: dict(sel("b16h", k), by=(j, sel("b16", k)))
 
     def dadd(out, a):
         s = "d%d" % nd[0]; nd[0] += 1
@@ -260,7 +266,7 @@ def build(opt, P):
         for o, l, r, a, b in lst:
             cost += max(min(64, l["c"]), r["c"]) * (1 if two(r) else 4) * PCY
         return add("p", lambda c: [c["g"].tensor.matmul(ap(c, o), ap(c, l), ap(c, r), a, b) for o, l, r, a, b in lst],
-                   [x[1] for x in lst] + [x[2] for x in lst], [x[0] for x in lst], cost, lat=P["hop"] + 0.07, ninc=len(lst))
+                   [x[1] for x in lst] + [x[2] for x in lst] + [x[1]["by"][1] for x in lst if "by" in x[1]], [x[0] for x in lst], cost, lat=P["hop"] + 0.07)
 
     def mmg(lst, per=4):
         full = [(o, l, r, j == 0, j == len(lst) - 1) for j, (o, l, r) in enumerate(lst)]
@@ -274,12 +280,16 @@ def build(opt, P):
             f = lambda c: [c["g"].iota(ap(c, out), pat, base, cm)]
         return add("g", f, [], [out], 0.13 + 2 * out["c"] * CY)
 
-    def dma(q, out, a, nbytes, after=()):
+    def dmas(q, pairs, nbytes, after=()):
         s = "d%d" % nd[0]; nd[0] += 1
         def f(c):
             e = {"y": c["g"].sync, "s": c["g"].scalar, "g": c["g"]}[q]
-            return [e.dma_start(ap(c, out), ap(c, a))]
-        return add(q, f, [a], [out], P["gi"] if q == "g" else 0.1, lat=P["dl"], xf=nbytes / (2 * P["dr"]), kind="d", sem=(s, 16), after=after)
+            return [e.dma_start(ap(c, out), ap(c, a)) for out, a in pairs]
+        return add(q, f, [a for out, a in pairs], [out for out, a in pairs], len(pairs) * (P["gi"] if q == "g" else 0.1), lat=P["dl"],
+                   xf=nbytes / (2 * P["dr"]), kind="d", sem=(s, 16 * len(pairs)), after=after)
+
+    def dma(q, out, a, nbytes):
+        return dmas(q, [(out, a)], nbytes)
 
     def send(pairs, credit):
         k = na[0]; na[0] += 1
@@ -290,7 +300,7 @@ def build(opt, P):
                                              remote_sem=c["T"].sem["a%d" % k], src=ap(c, a), dst=ap(c, b)))
             c["g"].remote_dma_fused(trs, local_sem=c["T"].sem["l%d" % k])
             return []
-        nb = sum(a["c"] * 512 + 16 * P["row"] * P["rr"] for a, b in pairs)
+        nb = sum(a["c"] * (256 if two(a) else 512) + 16 * P["row"] * P["rr"] for a, b in pairs)
         o = add("g", f, [a for a, b in pairs], [], P["gi"], lat=P["rl"] + (P["first"] if k == 0 else 0.0), xf=nb / P["rr"], kind="r", sem=("l%d" % k, "en"),
                 after=[credit[0]] if credit else [], ext=credit[1] if credit else None)
         add(None, None, [], [b for a, b in pairs], 0.0, lat=0.5, kind="x", sem=("a%d" % k, "en"), after=[o])
@@ -310,19 +320,18 @@ def build(opt, P):
         return c2("col", j, j + 1)
 
     I32, I16, ROW0 = V_("i32m"), V_("i16m"), c2("rowb", 0, 128)
-    WW = c2("uw", 0, D0); CE = opt["const"]
+    WW = c2("uw", W0, U0)
 
     dma("y", V_("sdi"), V_("sd"), 57344); dma("s", V_("nri"), V_("nr"), 57344)
     dma("y", V_("hsi", S_(0, 8), AL), V_("hs"), 16384)
-    cl[0] = "ld0"; dma("g", c2("uw", U0, U0 + 256), c2("u0", 0, 256), 131072)
-    cl[0] = "ldw"; j = dma("g", WW, V_("w0"), 524288)
+    cl[0] = "ld0"; dma("g", c2("uw", U0, G0), V_("u0"), 917504)
+    cl[0] = "ldw"; dma("g", WW, V_("w0"), 524288)
     cl[0] = "ld1"; dma("s", V_("tli"), V_("tl"), 917504)
-    cl[0] = "ld2"; dma("g", c2("uw", U0 + 256, G0), c2("u0", 256, NV), 786432)
     cl[0] = "setup"
     dma("y", c2("thr", 0, 1), V_("th"), 4096)
-    iota(c2("pi", 0, 1), [[0, 1]], 0, 1)
+    iota(c2("pi", 0, 2), [[112, 2]], 0, 1)
     iota(V_("xr"), [[1, 152]], -16, 0); iota(V_("md"), [[1, 8], [0, 16]], 0, 0); iota(V_("x16"), [[1, 16]], 0, 0)
-    P_, PM, PD, P16, KV, E4, ZV, ZB, LO, HI, KQ, KZ, KR = [colv(j) for j in range(13)]
+    P_, PM, PD, P16, KV, E4, ZV, ZB, LO, HI, PB, KZ, KR, PS, PG = [colv(j) for j in range(15)]
     cp(P_, c2("pi", 0, 1))
     ts(c2("pj", 0, 1), c2("pi", 0, 1), 15, A.bitwise_and); cp(PM, c2("pj", 0, 1))
     ts(c2("pj", 1, 2), c2("pi", 0, 1), 4, A.arith_shift_right); cp(PD, c2("pj", 1, 2))
@@ -330,61 +339,77 @@ def build(opt, P):
     ts(V_("ce"), V_("x16"), PM, A.is_equal)
     for i in range(16):
         mov("vs"[i % 3 == 2], c2("rowb", 128 * i, 128 * i + 128), V_("blk"), c2("ce", i, i + 1))
-    ts(c2("pm", 0, 112), c2("xr", 32, 144), P_, A.is_equal); ts(c2("pm", 112, 128), c2("xr", 16, 32), P_, A.is_equal)
+    ts(c2("pk", 2, 3), c2("pi", 1, 2), 127, A.bitwise_and); cp(PS, c2("pk", 2, 3)); ts(V_("pm"), c2("xr", 16, 144), PS, A.is_equal)
+    ts(c2("pk", 3, 4), c2("pi", 1, 2), 4, A.arith_shift_right, 7, A.bitwise_and); cp(PG, c2("pk", 3, 4))
+    for i in range(2):
+        ts(V_("rowsh", AL, i, AL), V_("md"), PG, A.is_equal, c2("ce", i + 1, i + 2), A.mult)
     ts(P16, P_, 16.0, A.mult); ts(V_("b8"), c2("xr", 0, 144), P16, A.is_equal)
     ts(V_("b32"), c2("xr", 0, 144), P_, A.is_equal, c2("ce", 0, 1), A.mult)
-    for name, k in (("b16", 1.0), ("b16h", 0.5), ("b162", 2.0), ("b4k", 4096.0)):
-        act(V_(name), V_("b32"), F.Copy, k)
-    ts(HI, PM, 8.0, A.is_ge); ts(LO, PM, 8.0, A.is_lt); ts(E4, PM, 8.0, A.is_ge, 4.0, A.mult)
+    for name, k in (("b16", 1.0), ("b16h", 0.5), ("b162", 2.0)):
+        mov("s", V_(name), V_("b32"), k)
+    ts(HI, PM, 8.0, A.is_ge, -1.0, A.mult); ts(LO, PM, 8.0, A.is_lt, -1.0, A.mult); ts(E4, HI, -4.0, A.mult, 0.5, A.add)
     ts(V_("lo8"), V_("xr"), P_, A.is_equal, LO, A.mult); ts(V_("hi8"), V_("xr"), P_, A.is_equal, HI, A.mult)
-    ts(I32, c2("xr", 16, 144), P_, A.is_equal); act(I16, I32, F.Copy)
-    ts(V_("sdf"), V_("sdi"), 2.0, A.mult, -1.0, A.add); ts(V_("nrf"), V_("nri"), -1.0, A.mult, 1024.0, A.add)
-    tt(V_("cb"), V_("sdf"), V_("nrf"), A.mult)
+    ts(I32, c2("xr", 16, 144), P_, A.is_equal); mov("g", I16, I32); mov("s", V_("i4"), I32, 4.0)
+    mov("s", V_("i4k", AL, 0, AL), I32, 4096.0); mov("s", V_("i4k", AL, 1, AL), I32, -4096.0)
+    ts(V_("sdf"), V_("sdi"), 2.0, A.mult, -1.0, A.add); ts(V_("nrf"), V_("nri"), -1.0, A.mult, float(FAR), A.add)
+    first = tt(V_("cb"), V_("sdf"), V_("nrf"), A.mult)
+    cl[0] = "sc0"; send([(V_("cb"), V_("cbg"))], None); cl[0] = "setup"
     for b in range(4):
         h = H(ANY)
         mm([(ps(h, 112 * j, 112 * j + 112), c2("rowb", 128 * (4 * b + j), 128 * (4 * b + j) + 128), V_("cb"), True, True) for j in range(4)])
-        mov("sv"[b % 2], c2("cc", C0 + 448 * b, C0 + 448 * b + 448), ps(h, 0, 448))
-        mov("vs"[b % 2], c2("cch", 448 * b, 448 * b + 448), ps(h, 0, 448))
+        if b == 3:
+            act(c2("cc", C0 + 448 * b, C0 + 448 * b + 448), ps(h, 0, 448), F.Silu, 1.0, float(MID), P["load"])
+        else:
+            lin("sv"[b % 2], c2("cc", C0 + 448 * b, C0 + 448 * b + 448), ps(h, 0, 448), 1.0, float(MID))
+        lin("vs"[b % 2], c2("cch0", 448 * b, 448 * b + 448), ps(h, 0, 448), 1.0, float(MID))
 
-    def send_shifted(name, own, ghost, stage, cr):
-        h = H()
-        if opt["wide"]:
-            mm([(ps(h, 128 * k, 128 * k + 128), (I32, V_("pm"))[k], c2(name, own + 128 * k, own + 128 * k + 128), True, True) for k in range(2)])
-            j = mov("s", V_(stage), ps(h, 0, 256))
-            send([(V_(stage), c2(name, ghost, ghost + 256))], cr)
-            return j
-        mm([(ps(h, 0, 128), V_("pm"), c2(name, own + 128, own + 256), True, True)])
-        j = mov("s", c2(stage, 0, 128), ps(h, 0, 128))
-        send([(c2(name, own, own + 128), c2(name, ghost, ghost + 128)), (c2(stage, 0, 128), c2(name, ghost + 128, ghost + 256))], cr)
-        return j
+    def send_shifted(way, name, own, ghost, n, stage, cr):
+        h = H(); hi = c2(stage, n, 2 * n)
+        mm([(ps(h, 0, n), V_("pm"), c2(name, own + n, own + 2 * n), True, True)])
+        mov("s", hi, ps(h, 0, n))
+        if way == "w":
+            mov("g", c2(stage, 0, n), c2(name, own, own + n))
+            send([(V_(stage), c2(name, ghost, ghost + 2 * n))], cr)
+        else:
+            send([(c2(name, own, own + n), c2(name, ghost, ghost + n)), (hi, c2(name, ghost + n, ghost + 2 * n))], cr)
 
-    cl[0] = "sc0"; first = send_shifted("cc", C0, C0 + NV, "sc", None)
-    cl[0] = "su0"; send_shifted("uw", U0, G0, "su", None); cl[0] = "setup"
+    h = H(); cl[0] = "sc1"
+    mm([(ps(h, a, b), l, c2("cbg", a % 112, (b - 1) % 112 + 1), True, True) for a, b, l in
+        ((0, 112, ROW0), (112, 128, c2("rowb", 128, 256)), (128, 224, V_("rowsh", AL, 0, AL)), (224, 256, V_("rowsh", AL, 1, AL)))])
+    lin("s", c2("cc", C0 + NV, C0 + NV + NG), ps(h, 0, 256), 1.0, float(MID))
+    cl[0] = "su0"; send_shifted(O("shift", -1)[1], "uw", U0, G0, 128, "su", None); cl[0] = "setup"
     cp(V_("hsf", S_(0, 8)), V_("hsi", S_(0, 8), AL))
     h = H()
     for par in range(2):
         mmg([(ps(h, 16 * par, 16 * par + 16), V_("b8", S_(0, 8), S_(16 - i, 144 - i)), V_("hsf", S_(0, 8), AL, 2 * i + par)) for i in range(16)], 16)
-    cp(V_("hix"), ps(h, 0, 32)); cp(V_("hw"), ps(h, 0, 32))
-    iota(V_("t2"), [[8, 128]], 0, 0); mov(CE, V_("tab8h"), V_("t2")); ts(V_("tab8"), V_("t2"), -0.5, A.add)
-    iota(V_("jw"), [[-8, 224]], 2048 - U0, 0)
-    ts(c2("pk", 0, 1), c2("pi", 0, 1), 1, A.bitwise_and); ts(KZ, c2("pk", 0, 1), 2048.0, A.add)
-    ts(c2("pk", 1, 2), c2("pi", 0, 1), 1, A.arith_shift_right, 7, A.bitwise_and); ts(KR, c2("pk", 1, 2), 2048.0, A.add)
+    lin("v", V_("hix"), ps(h, 0, 32), 1.0, 0.0); lin("v", V_("hw"), ps(h, 0, 32), 1.0, float(TOP + U0))
+    iota(V_("t2"), [[2, 2], [8, 128]], 0, 0); mov("g", V_("tab8h"), V_("t2")); lin("s", V_("tab8"), V_("t2"), 1.0, -0.5)
+    iota(V_("jw"), [[-8, 224]], W0 - U0, 0)
+    ts(c2("pk", 0, 1), c2("pi", 0, 1), 1, A.bitwise_and); ts(KZ, c2("pk", 0, 1), 1.0 - 4 * MID, A.mult, 2.0 * (MID + FAR), A.add)
+    ts(c2("pk", 1, 2), c2("pi", 0, 1), 1, A.arith_shift_right, 7, A.bitwise_and); cp(KR, c2("pk", 1, 2))
     ts(V_("jw"), V_("jw"), KZ, A.add, KR, A.subtract)
     tt(c2("bz", 1, 144), c2("b162", 1, 144), c2("b162", 0, 143), A.subtract)
-    iota(V_("jm"), [[16, 16]], -256, 0); ts(V_("jm"), V_("jm"), PM, A.add)
-    iota(V_("tab16"), [[0, 4], [16, 32]], 0, 0); mov(CE, V_("tab16h"), V_("tab16"))
-    iota(V_("tabs"), [[-1, 2], [-2, 256]], 1024, 0)
-    iota(c2("uw", D0, U0), [[0, 256]], 0, 0); iota(c2("cc", 0, C0), [[0, 256]], 0, 0)
+    iota(V_("jm"), [[-16, 16]], TOP + 255, 0); iota(V_("rs0"), [[0, 256]], 1000000, 0); ts(c2("rs0", 0, 256, 16), V_("jm"), PM, A.subtract)
+    iota(V_("dd"), [[0, 16], [1, 16]], 0, 0); ts(V_("cdg"), V_("dd"), PM, A.is_equal, float(TOP + G0), A.mult)
+    ts(PB, PD, 16.0, A.mult); ts(V_("bsum"), c2("xr", 0, 144), PB, A.is_equal, -2048.0, A.mult)
+    iota(V_("tab16"), [[4, 2], [0, 4], [16, 32]], 1536, 0); mov("g", V_("tab16h"), V_("tab16"))
+    iota(c2("uw", 0, W0), [[0, 256]], 0, 0); iota(c2("cc", 0, W0), [[0, 256]], 0, 0)
+    iota(c2("cc", W0, U0, 2), [[1, 512]], MID - FAR, 0); iota(c2("cc", W0 + 1, U0, 2), [[-1, 512]], MID + FAR, 0)
     for j in range(4):
         iota(c2("tt", 2048 * j, 2048 * j + 512), [[0, 512]], 0, 0)
-    ms(V_("z16"), 0.0); ms(KQ, 1792.0)
-    act(V_("blk2k"), V_("blk"), F.Copy, 2048.0)
+    if opt["cz"] == "v":
+        mov("s", V_("blk2k"), V_("blk"), -2048.0)
+        asel(V_("ee", AL, 0, AL), V_("blk"), [[16, 8], [0, 16]], A.is_ge, 0.0, 7, -1)
+        asel(V_("ee", AL, 1, AL), V_("blk"), [[-16, 8], [0, 16]], A.is_ge, 0.0, -8, 1)
+    else:
+        for e, half in enumerate((LO, HI)):
+            ts(V_("r8", AL, e, AL), c2("xr", 0, 144), PB, A.is_equal, half, A.mult)
     ts(c2("nth", 0, 1), c2("thr", 0, 1), -1.0, A.mult)
     ts(c2("pj", 2, 3), c2("pi", 0, 1), 2, A.arith_shift_right, 1, A.bitwise_and); cp(ZB, c2("pj", 2, 3))
     ts(KV, ZB, -1540.0, A.mult, PM, A.add)
-    if opt["val"] == "g":
-        iota(V_("t128"), [[64, 16]], 0, 0); mov(CE, V_("t128h"), V_("t128")); ts(ZV, PM, 4.0, A.mult, 0.5, A.add)
-    act(V_("n32m"), I32, F.Copy, -1.0)
+    iota(V_("t128"), [[2, 2], [64, 16]], 0, 0); ts(ZV, PM, 4.0, A.mult)
+    if opt["dd"] == "p":
+        mov("s", V_("n32m"), I32, -1.0)
     for part in range(2):
         iota(c2("tz", 128 * part, 128 * part + 128), [[0, 16], [1024 << part, 2], [0, 4]], -(512 << part), 0)
         for L in range(2):
@@ -393,206 +418,192 @@ def build(opt, P):
     asel(V_("t1"), V_("c2k"), [[-8, 16], [0, 8]], A.is_ge, 0.0, 0, 1)
     asel(V_("y8", AL, 1, AL), V_("t1"), [[8, 16], [0, 8]], A.is_ge, 0.0, 7, -1)
     asel(V_("t1"), V_("t1"), [[1, 128]], A.is_gt, 0.0, 0, -1)
-    asel(V_("y8", AL, 4, AL), V_("t1"), [[-1, 128]], A.not_equal, 1.0, 0, 1)
-    if opt["cab"] == "p":
-        mov(CE, V_("y8", AL, 0, AL), V_("t1")); act(V_("y8", AL, 5, AL), I32, F.Copy, -1.0)
-        act(V_("y8", AL, S_(2, 4), AL), V_("y8", AL, S_(0, 2), AL), F.Copy, -1.0)
-    asel(V_("ee", AL, 0, AL), V_("blk"), [[16, 8], [0, 16]], A.is_ge, 0.0, 7, -1)
-    asel(V_("ee", AL, 1, AL), V_("blk"), [[-16, 8], [0, 16]], A.is_ge, 0.0, -8, 1)
+    asel(V_("y8", AL, 0, AL), V_("t1"), [[-1, 128]], A.not_equal, 1.0, 0, 1)
     for i in range(1, 16):
         asel(c2("tri", 128 * i, 128 * i + 128), V_("blk"), [[16, 8], [0, 16]], A.is_ge, 0.0, i - 1, -1)
     for a in range(4):
-        for r1 in range(2):
-            for h in range(2):
-                dma("y", V_("lsw", S_(32 * a + 16 * r1, 32 * a + 16 * r1 + 16), h, AL),
-                    V_("tl", S_(32 * a + 16 * h, 32 * a + 16 * h + 16), S_(896 * r1, 896 * r1 + 896)), 57344, [first])
+        dmas("y", [(V_("lsw", S_(32 * a + 16 * r1, 32 * a + 16 * r1 + 16), h, AL),
+                    V_("tl", S_(32 * a + 16 * h, 32 * a + 16 * h + 16), S_(896 * r1, 896 * r1 + 896))) for r1 in range(2) for h in range(2)], 229376, [first])
 
     def turn(t):
+        cl[0] = "turn"
         for h in range(2):
-            mov("s", V_("ftr", AL, AL, S_(16 * h, 16 * h + 16)), V_("lsw", AL, h, S_(t, 896, 4)), 4.0)
+            mov(opt["ftr"], V_("ftr", AL, AL, S_(16 * h, 16 * h + 16)), V_("lsw", AL, h, S_(t, 896, 4)))
         tr(V_("tlt"), V_("ftr"))
 
     def names(t):
-        par = t % 2; h = H()
-        mov(opt["nm"], V_("nmh"), ind(c2("tli", 0, NV), c2("hix", 16 * par, 16 * par + 16)))
+        par = t % 2; h = H(); cl[0] = "names"
+        mov("s", V_("nmh"), ind(c2("tli", 0, NV), c2("hix", 16 * par, 16 * par + 16)))
         for part in range(2):
-            mmg([(ps(h, 128 * part, 128 * part + 128), sel(("lo8", "hi8")[part], 8 * (e - part)), c2("nmh", e, 256, 2)) for e in range(2)])
-        cp(V_("nix", AL, par, AL), ps(h, 0, 256))
-        act(V_("n1"), ps(h, 0, 256), F.Relu, -1.0, KQ)
+            mmg(minus_names(h, 128 * part, part))
+        lin("v", V_("nix", AL, par, AL), ps(h, 0, 256), -1.0, 0.0)
 
-    def half_codes():
+    def minus_names(h, a, part):
+        return [(ps(h, a, a + 128), sel(("lo8", "hi8")[part], 8 * (e - part)), c2("nmh", e, 256, 2)) for e in range(2)]
+
+    def half_codes(t):
+        cl[0] = "cch"
         for j in range(4):
-            mov(opt["cch"][j], c2("cch", 448 * j, 448 * j + 448), c2("cc", C0 + 448 * j, C0 + 448 * j + 448))
+            mov("g", c2("cch%d" % (t % 2), 448 * j, 448 * j + 448), c2("cc", C0 + 448 * j, C0 + 448 * j + 448))
 
-    def view_lists():
-        h = H(); x = ps(h, 0, 224)
-        mmg([(x, sel("bz", 2 * i), c2("cch", i, NV, 8)) for i in range(8)], 4)
-        tt(V_("f0"), x, V_("jw"), A.max); ts(V_("vix"), V_("f0"), -1.0, A.mult, KZ, A.add)
+    def view_lists(t):
+        cut = O("cut", t - 1)
+        for name, a, b in (("vl", 0, cut), ("vm", cut, NV)):
+            if a < b:
+                cl[0] = name; x = ps(H(), 0, (b - a) // 8); f0 = c2("f0", a // 8, b // 8)
+                mmg([(x, sel("bz", 2 * i), c2("cch%d" % (t % 2), a + i, b, 8)) for i in range(8)], 8)
+                tt(f0, x, c2("jw", a // 8, b // 8), A.max); lin("v", c2("vix", a // 8, b // 8), f0, -1.0, KZ)
+
+    def slots(t, r):
+        return range(8) if O("tree" + "AB"[r], t)[0] == "X" else SPINE
 
     def node_lists(t):
-        h = H()
-        mmg([(ps(h, 0, 28), sel("b16", i), c2("cch", 4 * i + t, NV, 64)) for i in range(16)], 16)
-        sign("s", V_("sgw"), ps(h, 0, 28))
+        cl[0] = "nl"; h = H()
+        mmg([(ps(h, 0, 28), sel("b16", i), c2("cch%d" % (t % 2), 4 * i + t, NV, 64)) for i in range(16)], 16)
+        act(V_("sgw"), ps(h, 0, 28), F.Sign, 1.0, -float(MID))
         h = H(); lst = []
         for r in range(2):
             for k in range(16):
-                a = 224 * r + 28 * SLOT[k // 2] + 14 * (k % 2); o = ps(h, a, a + 14)
+                a = 224 * r + 28 * slots(t, r)[k // 2] + 14 * (k % 2); o = ps(h, a, a + 14)
                 lst.append((o, I16, c2("sgw", 14 * r, 14 * r + 14), True, False))
-                lst.append((o, I16, V_("tlt", AL, AL, 16 * r + k), False, True))
+                lst.append((o, V_("i4"), V_("tlt", AL, AL, 16 * r + k), False, True))
         for j in range(0, 64, 16):
             mm(lst[j:j + 16])
-        ts(V_("six%d" % (t % 2)), ps(h, 0, 448), 1.0, A.add, 0.5, A.mult)
+        lin("v", V_("six%d" % (t % 2)), ps(h, 0, 448), 0.5, 0.5)
 
     CH = ((0, 0), (1, 0), (0, 1), (1, 1))
 
     def sides(t):
         for j, (part, hf) in enumerate(CH):
             cl[0] = "sd%d" % j
-            w = 32 if j in opt["sfine"] else 64
-            for a in range(128 * part + 64 * hf, 128 * part + 64 * hf + 64, w):
-                h = H(); o = ps(h, 0, w); b = a % 128
-                sign(O("sides", t)[j], c2("gg", 16 * a, 16 * (a + w)), ind(c2("cc", C0, C0 + NV + NG), V_("nix", AL, t % 2, S_(a, a + w))))
-                mmg([(o, sel("b16h", k), c2("gg", 16 * a + k, 16 * (a + w), 16)) for k in range(16)] + [(o, ROW0, c2("tab8h", b, b + w))], 17)
-                ts(c2("uix", a, a + w), o, E4, A.add, 0.5 + 2 * (t % 2), A.add)
-                tt(c2("sg", a, a + w), o, c2("tab8", b, b + w), A.subtract)
+            a = 128 * part + 64 * hf; h = H(); o = ps(h, 0, 64); b = a % 128 + 128 * (t % 2)
+            half = side("vs"[j % 2], c2("gg", 16 * a, 16 * (a + 64)), ind(c2("cc", C0, C0 + NV + NG), V_("nix", AL, t % 2, S_(a, a + 64))))
+            mmg([(o, half(k), c2("gg", 16 * a + k, 16 * (a + 64), 16)) for k in range(16)] + [(o, ROW0, c2("tab8h", b, b + 64))], 17)
+            lin("v", c2("uix", a, a + 64), o, 1.0, E4)
+            tt(c2("sg", a, a + 64), o, c2("tab8", b, b + 64), A.subtract)
 
     def pair_lists():
-        h = H()
+        cl[0] = "pl"; h = H()
         for L in range(2):
             o = ps(h, 128 * L, 128 * L + 128)
-            mmg([(o, V_("mm", AL, 2 * L + part, AL), c2("sg", 128 * part, 128 * part + 128)) for part in range(2)] + [(o, ROW0, V_("tab16h"))])
-        for L in range(2):
-            ts(c2("lix", 128 * L, 128 * L + 128), ps(h, 128 * L, 128 * L + 128), KV, A.add, 1536.0 + 4 * L, A.add)
+            mmg([(o, V_("mm", AL, 2 * L + part, AL), c2("sg", 128 * part, 128 * part + 128)) for part in range(2)] + [(o, ROW0, c2("tab16h", 128 * L, 128 * L + 128))])
+        lin("v", V_("lix"), ps(h, 0, 256), 1.0, KV)
 
     def candidates():
-        cab = c2("cab", 0, 256)
-        tt(cab, V_("n1"), V_("sg"), A.mult)
-        h = H(); Y = [V_("y8", AL, j, AL) for j in range(6)]
-        if opt["cab"] == "v":
-            tt(c2("cab", 256, 512), V_("n1"), cab, A.subtract)
-            mmg([(ps(h, 0, 512), Y[4], V_("cab"))] + [(ps(h, 256 * z + 128, 256 * z + 256), Y[1], c2("cab", 256 * z, 256 * z + 128)) for z in range(2)])
-        else:
-            mmg([(ps(h, 0, 256), Y[4], cab), (ps(h, 128, 256), Y[1], c2("cab", 0, 128))])
-            mmg([(ps(h, 256, 512), Y[0], V_("n1")), (ps(h, 256, 512), Y[2], cab), (ps(h, 384, 512), Y[1], c2("n1", 0, 128)),
-                 (ps(h, 384, 512), Y[3], c2("cab", 0, 128)), (ps(h, 256, 512), I16, V_("n1")), (ps(h, 256, 512), Y[5], cab)], 6)
+        cl[0] = "cand"; h = H()
+        for z in range(2):
+            for part in range(2):
+                a = 256 * z + 128 * part
+                mmg(minus_names(h, a, part) + [(ps(h, a, a + 128), V_("i4k", AL, z, AL), c2("sg", 128 * part, 128 * part + 128))])
+        for z in range(2):
+            lin("s", c2("cab", 256 * z, 256 * z + 256), ps(h, 256 * z, 256 * z + 256), 1.0, 1792.0 - 4096.0 * (1 - z), True)
+        h = H(); Y = [V_("y8", AL, j, AL) for j in range(2)]
+        mmg([(ps(h, 0, 512), Y[0], V_("cab"))] + [(ps(h, 256 * z + 128, 256 * z + 256), Y[1], c2("cab", 256 * z, 256 * z + 128)) for z in range(2)])
         x = ps(h, 0, 512)
-        either("s", {"s": lambda: act(V_("sel"), x, F.Relu), "v": lambda: ts(V_("sel"), x, 0.0, A.max)})
+        lin("s", V_("sel"), x, 1.0, 0.0, True)
         h = H()
-        mm([(ps(h, 256 * z + e, 256 * z + 256, 2), V_("ee", AL, e, AL), c2("sel", 256 * z + 128 * part, 256 * z + 128 * part + 128), part == 0, part == 1)
+        if opt["cz"] == "p":
+            mmg([(ps(h, 0, 32), V_("r8", AL, i % 2, S_(16 - i, 144 - i)), V_("sel", AL, AL, part, S_(i // 2, 128, 8))) for i in range(16) for part in range(2)], 16)
+            return mov("s", V_("clw"), ps(h, 0, 32))
+        mm([(ps(h, 256 * z + e, 256 * z + 256, 2), V_("ee", AL, e, AL), V_("sel", AL, z, part, AL), part == 0, part == 1)
             for z in range(2) for e in range(2) for part in range(2)])
-        mov("s", V_("cand16" if opt["sgn"] else "cand"), ps(h, 0, 512))
+        mov("s", V_("cand"), ps(h, 0, 512), -1.0)
+        h = H()
+        mmg([(ps(h, 0, 32), sel("b16", i), c2("cand", i, 512, 16)) for i in range(16)], 16)
+        mov("s", V_("clw"), ps(h, 0, 32))
 
-    def views(t, a, b, eng):
-        for e, lo, hi in ((eng[0], a, (a + b) // 2), (eng[1], (a + b) // 2, b)):
-            mov(e, c2("vw%d" % (t % 2), 2 * lo, 2 * hi), ind(c2("uw", 0, U0 + b), c2("vix", lo // 8, hi // 8)))
+    def views(t, a, b):
+        for lo, hi in ((a, (a + b) // 2), ((a + b) // 2, b)):
+            mov("s", c2("vw%d" % (t % 2), 2 * lo, 2 * hi), ind(c2("uw", W0, U0 + b), c2("vix", lo // 8, hi // 8)), -1.0)
 
     def ghost_views(t, cr):
-        vw = "vw%d" % (t % 2); cl[0] = "gv"; h = H()
-        views(t, 0, 256, O("gv", t))
-        mm([(ps(h, 0, 256), V_("pm"), c2(vw, 256, 512), True, True)])
-        mov("s", V_("sv"), ps(h, 0, 256))
-        send([(c2(vw, 0, 256), c2(vw, 2 * NV, 2 * NV + 256)), (V_("sv"), c2(vw, 2 * NV + 256, 4096))], cr)
+        cl[0] = "gv"; views(t, 0, 256)
+        send_shifted(O("shift", t - 1)[2], "vw%d" % (t % 2), 0, 2 * NV, 256, "sv", cr)
 
     def old_values(t, r):
-        for j in range(4 if O("dma" + "AB"[r], t) else 2):
-            mov(opt["ue"], V_("uexp", AL, r, S_(224 * j, 224 * j + 224)), c2("uw", U0 + 896 * r + t, U0 + 896 * r + 896, 4))
+        cl[0] = "ue" if r == 0 else "uf"
+        n = 4 if O("dma" + "AB"[r], t) else 2; part = [V_("uexp", AL, r, S_(224 * j, 224 * j + 224)) for j in range(n)]
+        for j in range(n if O("rep", t) == "g" else 1):
+            mov("g", part[j], c2("uw", U0 + 896 * r + t, U0 + 896 * r + 896, 4))
+        if O("rep", t) == "d":
+            dmas("y", [(x, part[0]) for x in part[1:]], 114688 * (n - 1))
 
     def step1(t, r):
-        win = c2("vw%d" % (t % 2), 0, 4096); ue = V_("uexp", AL, r, S_(0, 448))
-        m15, m37, m4, m26 = O("tree" + "AB"[r], t); onpe = O("pe" + "AB"[r], t); ondma = O("dma" + "AB"[r], t); onq = O("q" + "AB"[r], t); up = []
-        assert (0 in ondma) == (1 in ondma) or m4 == "v"
-        def d(k, n=1): return c2("d2", 448 * k, 448 * (k + n))
+        win = c2("vw%d" % (t % 2), 0, 4096); tree = O("tree" + "AB"[r], t); ondma = O("dma" + "AB"[r], t)
         def q(k, n=1, a=0, b=448): return c2("q%d" % r, 448 * k + a, 448 * (k + n - 1) + b)
-        def x(k): return ind(win, c2("six%d" % (t % 2), 224 * r + 28 * k, 224 * r + 28 * k + 28))
-        def one(k): return V_("n32m") if k // 2 in ondma else I32
-        def pair(j, mode):
-            h = H(WIDE); cl[0] = "AB"[r] + str(j // 2)
-            if j // 2 in onpe:
-                a, b = ps(h, 0, 448), ps(h, 512, 960)
-                for i, o in ((j, a), (j + 1, b)):
-                    mov("s", d(i), x(i))
-                    mmg([(o, I32, d(i)), (o, V_("n32m"), ue)], 1)
-                    act(d(i), o, F.Abs)
+        def x(k, n): return ind(win, c2("six%d" % (t % 2), 224 * r + 28 * k, 224 * r + 28 * (k + n)))
+        def pair(i, j, mode):
+            h = H(WIDE); cl[0] = "AB"[r] + str(i); a, b = ps(h, 0, 448), ps(h, 448, 896)
+            if i in ondma:
+                mov("s", q(j, 2), x(j, 2)); dadd(q(j, 2), V_("uexp", AL, r, AL))
+            elif ondma:
+                tt(q(j, 2), x(j, 2), V_("uexp", AL, r, AL), A.add)
             else:
-                a, b = ps(h, 0, 448), ps(h, 448, 896)
-                if j // 2 in ondma:
-                    act(d(j, 2), ind(win, c2("six%d" % (t % 2), 224 * r + 28 * j, 224 * r + 28 * j + 56)), F.Copy, -1.0)
-                    dadd(d(j, 2), V_("uexp", AL, r, AL))
-                elif j // 2 in onq:
-                    act(d(j, 2), ind(win, c2("six%d" % (t % 2), 224 * r + 28 * j, 224 * r + 28 * j + 56)), F.Copy)
-                    if not up:
-                        up.append(ps(H(), 0, 448)); mov("s", up[0], ue)
-                    tt(d(j), d(j), up[0], A.subtract); tt(d(j + 1), d(j + 1), up[0], A.subtract)
-                else:
-                    tt(d(j), x(j), ue, A.subtract); tt(d(j + 1), x(j + 1), ue, A.subtract)
-                act(ps(h, 0, 896), d(j, 2), F.Abs)
+                for k in (j, j + 1):
+                    tt(q(k), x(k, 1), V_("uexp", AL, r, S_(0, 448)), A.add)
+            act(ps(h, 0, 896), q(j, 2), F.Abs)
             if mode == "v":
-                tt(q(j + 1), d(j + 1), b, A.mult); tt(a, d(j), a, A.mult); tt(q(j), a, q(j + 1), A.add)
-            elif j // 2 in onpe:
-                tt(q(j), d(j), a, A.mult); tt(q(j + 1), d(j + 1), b, A.mult)
+                tt(q(j + 1), q(j + 1), b, A.mult); tt(a, q(j), a, A.mult); tt(q(j), a, q(j + 1), A.add)
             else:
-                tt(q(j, 2), d(j, 2), ps(h, 0, 896), A.mult)
+                tt(q(j, 2), q(j, 2), ps(h, 0, 896), A.mult)
             if mode == "d":
                 dadd(q(j), q(j + 1))
-        def onpe_sum(slots):
-            h = H()
-            mmg([(ps(h, 0, 448), I32, q(k)) for k in slots], 1)
-            mov("s", q(slots[0]), ps(h, 0, 448))
-        pair(0, m15)
-        if m15 == "p" and m4 != "p":
-            onpe_sum((0, 1))
-        pair(2, m37)
-        if m37 == "p":
-            onpe_sum((2, 3))
-        if m4 == "d":
-            dadd(q(0), q(2))
-        elif m4 == "v":
-            tt(q(0), q(0), q(2), A.add if (0 in ondma) == (1 in ondma) else A.subtract)
+        hi = c2("hi1", 224 * r, 224 * r + 224)
+        if tree[0] == "X":
+            pair(0, 0, ""); pair(1, 4, ""); dadd(q(0, 2), q(4, 2))
+            pair(2, 2, ""); pair(3, 6, ""); dadd(q(2, 2), q(6, 2))
+            cl[0] = "AB"[r] + "t"; dadd(q(0, 2), q(2, 2)); lo = ps(H(), 0, 224)
+            if tree[1] == "d":
+                dadd(q(0), q(1)); dadd(q(0, 1, 0, 224), q(0, 1, 224, 448)); mov("s", lo, q(0, 1, 0, 224), -0.015625)
+            else:
+                h = H()
+                mmg([(ps(h, 0, 224), I32, q(k, 1, 224, 448)) for k in (0, 1)], 2); mov("s", hi, ps(h, 0, 224))
+                mmg([(lo, I32, q(k, 1, 0, 224)) for k in (0, 1)] + [(lo, I32, hi)], 2); mov("s", lo, lo, -0.015625)
         else:
-            onpe_sum((0, 1, 2) if m15 == "p" else (0, 2))
-        pair(4, "p"); pair(6, m26)
-        if m26 == "p":
-            onpe_sum((6, 7))
-        hi = c2("hi1", 224 * r, 224 * r + 224); cl[0] = "AB"[r] + "t"
-        if O("tail", t)[r] == "p":
+            m15, m37, m4, m26 = tree
+            pair(0, 0, m15); pair(1, 2, m37)
+            if m4 == "d":
+                dadd(q(0), q(2))
+            else:
+                tt(q(0), q(0), q(2), A.add)
+            pair(2, 4, ""); pair(3, 6, m26); cl[0] = "AB"[r] + "t"
             h = H()
-            mmg([(ps(h, 0, 224), one(k), q(k, 1, 224, 448)) for k in (4, 5, 6, 0)], 2)
-            mov("s", hi, ps(h, 0, 224))
-            h = H(); lo = ps(h, 0, 224)
-            mmg([(lo, one(k), q(k, 1, 0, 224)) for k in (4, 5, 6, 0)] + [(lo, I32, hi)], 2)
-        else:
-            h = H(); lo = ps(h, 0, 224)
-            mmg([(ps(h, 0, 448), one(k), q(k)) for k in (4, 5, 6, 0)], 1)
-            mov("s", hi, ps(h, 224, 448)); tt(lo, lo, hi, A.add)
-        mov(opt["scale1"][r], lo, lo, 0.015625)
+            if O("tail", t)[r] == "p":
+                mmg([(ps(h, 0, 224), I32, q(k, 1, 224, 448)) for k in (4, 5, 6, 0)], 2); mov("s", hi, ps(h, 0, 224))
+                lo = ps(H(), 0, 224)
+                mmg([(lo, I32, q(k, 1, 0, 224)) for k in (4, 5, 6, 0)] + [(lo, I32, hi)], 2)
+            else:
+                lo = ps(h, 0, 224)
+                mmg([(ps(h, 0, 448), I32, q(k)) for k in (4, 5, 6, 0)], 1)
+                mov("s", hi, ps(h, 224, 448)); tt(lo, lo, hi, A.add)
+            if r and O("mask", t):
+                h = H(); x = ps(h, 0, 224); u = c2("uw", U0 + 896 + t, G0, 4)
+                mmg([(x, V_("i4k", AL, k, AL), c2("cch%d" % ((t + k) % 2), 896 + t, NV, 4)) for k in range(2)])
+                ts(V_("mk"), x, 0.0, A.is_equal, -0.015625, A.mult); tt(lo, lo, V_("mk"), A.mult)
+                return tt(u, lo, u, A.add)
+            mov("s", lo, lo, -0.015625)
         tt(c2("uw", U0 + 896 * r + t, U0 + 896 * r + 896, 4), lo, V_("uexp", AL, r, S_(0, 224)), A.add)
 
     def claimed_values():
-        o = ind(c2("uw", D0, G0), V_("tgx"))
-        if opt["val"] == "ab":
-            tt(o, c2("val", 0, 256), c2("val", 256, 512), A.max)
-        else:
-            cp(o, c2("val", 0, 256))
+        cp(ind(c2("uw", 0, G0), V_("tgx")), V_("val"))
 
     def lists(t):
-        cl[0] = "vl"; view_lists(); cl[0] = "nl"; node_lists(t); sides(t); cl[0] = "pl"; pair_lists(); cl[0] = "cand"; candidates()
+        view_lists(t); node_lists(t); sides(t); pair_lists(); candidates()
 
     names(0); turn(0); lists(0)
-    ghost_views(0, None); cl[0] = "vA"; views(0, 256, 896, O("vA", 0)); cl[0] = "ue"; old_values(0, 0); old_values(0, 1)
+    ghost_views(0, None); cl[0] = "vA"; views(0, 256, 896); old_values(0, 0); old_values(0, 1)
     cr = None
     for t in range(RO):
         par = t % 2; last = t == RO - 1; cl[1] = t
-        if t and not opt["vAearly"]:
-            cl[0] = "vA"; views(t, 256, 896, opt["vA"])
-        cl[0] = "vB"; views(t, 896, NV, O("vB", t))
+        cl[0] = "vB"; views(t, 896, NV)
         for j, (part, hf) in enumerate(CH):
             a = 128 * part + 64 * hf; h = H(WIDE); w = 32 if j in opt["fine"] else 64
             for b in range(a, a + 64, w):
                 uu = c2("uu", 16 * b, 16 * (b + w))
                 cl[0] = "uc%d" % j
-                mov(O("ucol", t)[j], uu, ind(WW, c2("uix", b, b + w)))
+                mov("s", uu, ind(WW, c2("uix", b, b + w)))
                 cl[0] = "x%d" % j
-                mark["x"] = tt(uu, ind(c2("uw", U0, UE), V_("nix", AL, par, S_(b, b + w))), uu, A.subtract)
+                tt(uu, ind(c2("uw", U0, UE), V_("nix", AL, par, S_(b, b + w))), uu, A.subtract)
                 act(ps(h, 16 * (b - a), 16 * (b - a + w)), uu, F.Abs)
             for i in range(2):
                 t0 = 2048 * (2 * hf + i); mode = O("pair", t)[2 * hf + i]; cl[0] = "m%d" % j
@@ -602,29 +613,29 @@ def build(opt, P):
                     tt(lo, di, st, A.mult)
                     if mode == "d":
                         dma("y", sm, lo, 262144)
+                    elif mode == "g":
+                        mov("g", sm, lo)
                 elif mode == "x":
                     tt(st, di, st, A.mult); tt(sm, st, lo, A.add); mov("s", hi, st)
                 else:
                     tt(hi, di, st, A.mult)
-                    if mode == "v":
-                        tt(sm, lo, hi, A.add)
-                    elif mode == "d":
+                    if mode in "dg":
                         dadd(sm, hi)
                     else:
                         h2 = H(ANY)
                         mmg([(ps(h2, 0, 512), I32, lo), (ps(h2, 0, 512), I32, hi)], 1)
                         mov("s", sm, ps(h2, 0, 512))
         if not last:
-            other = "vw%d" % (1 - par)
-            cr = credit([c2("uw", G0, UE), c2("cc", C0 + NV, C0 + NV + NG), c2(other, 2 * NV, 4096)])
+            cl[0] = "cred"
+            cr = credit([c2("uw", G0, UE), c2("cc", C0 + NV, C0 + NV + NG), c2("vw%d" % (1 - par), 2 * NV, 4096)])
         for c in range(4):
             cl[0] = "l%d" % c
             win = c2("tt", 2048 * c, 2048 * c + 2048); rr = c2("uu", 512 * c, 512 * c + 512)
-            mov(opt["rr"][c], rr, ind(win, c2("lix", 128 + 32 * c, 160 + 32 * c)))
-            mark["0123"[c]] = tt(rr, ind(win, c2("lix", 32 * c, 32 * c + 32)), rr, A.add)
+            mov("s", rr, ind(win, c2("lix", 128 + 32 * c, 160 + 32 * c)))
+            tt(rr, ind(win, c2("lix", 32 * c, 32 * c + 32)), rr, A.add)
         for j, (qa, qb) in enumerate(opt["grp"]):
             a, b = 512 * qa, 512 * qb; n = 128 * (qb - qa); cc1 = c2("c1", 128 * qa, 128 * qb); cl[0] = "w%d" % j
-            if opt["c1"][j] == "p":
+            if O("c1", t)[j] == "p":
                 h = H(); o1 = ps(h, 0, n)
                 mmg([(o1, I32, c2("uu", a + 1, b, 4)), (o1, I32, c2("uu", a + 3, b, 4))])
                 mov("s", cc1, o1)
@@ -632,197 +643,102 @@ def build(opt, P):
                 tt(cc1, c2("uu", a + 1, b, 4), c2("uu", a + 3, b, 4), A.add)
             h = H(); o = ps(h, 0, n)
             mmg([(o, I32, c2("uu", a, b, 4)), (o, I32, c2("uu", a + 2, b, 4)), (o, I32, cc1)], 2)
-            mov(opt["scale2"][j], o, o, 0.015625)
+            mov("s", o, o, 0.015625)
             for z in range(2):
-                w = c2("uw", 256 * qa + 2 * par + z, 256 * qb, 4)
+                w = c2("uw", W0 + 256 * qa + 2 * par + z, W0 + 256 * qb, 4)
                 tt(w, ps(h, z, n, 2), w, A.add)
         if last:
-            dma("y", V_("ys"), WW, 524288)
+            cl[0] = "out"; dma("y", V_("ys"), WW, 524288)
         cl[0] = "s3"
-        n0, n1 = c2("uw", 2 * par, D0, 4), c2("uw", 2 * par + 1, D0, 4)
-        hv = H(); up, dn = ps(hv, 0, 256), ps(hv, 256, 512)
-        for a, b in opt["votes"]:
-            cl[0] = "s3" if b == 256 else "s2"
-            dd = c2("dd", a, b)
-            tt(dd, c2("uw", 4 * a + 2 * par, 4 * b, 4), c2("uw", 4 * a + 2 * par + 1, 4 * b, 4), A.subtract)
-            ts(c2("ud", a, b), dd, c2("thr", 0, 1), A.is_gt, 0.5, A.subtract)
-            ts(c2("ud", 256 + a, 256 + b), dd, c2("nth", 0, 1), A.is_lt, 0.5, A.subtract)
-            for lo, hi in ((0, 512),) if b - a == 256 else ((a, b), (256 + a, 256 + b)):
-                mm([(ps(hv, lo, hi), V_("blk2k"), c2("ud", lo, hi), True, True)])
-            for lo, hi in ((0, 512),) if b - a == 256 else ((a, b), (256 + a, 256 + b)):
-                if opt["sgn"]:
-                    sign("s", c2("sv16", lo, hi), ps(hv, lo, hi)); tt(c2("rab", lo, hi), c2("sv16", lo, hi), c2("cand16", lo, hi), A.mult)
-                else:
-                    tt(c2("rab", lo, hi), ps(hv, lo, hi), c2("cand", lo, hi), A.min)
-            tt(V_("cz", AL, 0, S_(a, b)), c2("rab", a, b), c2("rab", 256 + a, 256 + b), A.max)
-        if opt["sgn"]:
-            mov("g", V_("zs"), c2("sv16", 256, 512))
+        n0, n1 = c2("uw", W0 + 2 * par, U0, 4), c2("uw", W0 + 2 * par + 1, U0, 4)
+        if opt["dd"] == "p":
+            dd = ps(H(), 0, 256); mmg([(dd, I32, n0), (dd, V_("n32m"), n1)])
         else:
-            sign("s", V_("zs"), dn)
+            dd = V_("dd"); tt(dd, n0, n1, A.subtract)
+        ts(c2("ud", 0, 256), dd, c2("thr", 0, 1), A.is_gt, 0.5, A.subtract)
+        ts(c2("ud", 256, 512), dd, c2("nth", 0, 1), A.is_lt, 0.5, A.subtract)
+        if opt["cz"] == "v":
+            hv = H(); up, dn = ps(hv, 0, 256), ps(hv, 256, 512)
+            mm([(ps(hv, 0, 512), V_("blk2k"), V_("ud"), True, True)])
         h = H()
-        mmg([(ps(h, 0, 16), sel("b16", i), V_("cz", AL, 0, S_(i, 256, 16))) for i in range(16)], 16)
-        mov("v", V_("cw"), ps(h, 0, 16))
-        if opt["val"] == "ab":
-            tt(c2("val", 0, 256), up, n0, A.min); tt(c2("val", 256, 512), dn, n1, A.min)
+        mmg([(ps(h, 0, 32), sel("bsum", i), c2("ud", i, 512, 16)) for i in range(16)], 16)
+        tt(V_("cv"), ps(h, 0, 32), V_("clw"), A.max)
+        if opt["cz"] == "v":
+            tt(V_("rb"), dn, c2("cand", 256, 512), A.max); tt(up, up, c2("cand", 0, 256), A.max); tt(V_("cz"), up, V_("rb"), A.min)
         else:
-            if not opt["sgn"]:
-                mov("g", c2("sv16", 256, 512), V_("zs"))
-            h = H()
-            mmg([(ps(h, 0, 16), sel("b16h", i), c2("sv16", 256 + i, 512, 16)) for i in range(16)] + [(ps(h, 0, 16), ROW0, V_("t128h"))], 17)
-            ts(V_("vlx"), ps(h, 0, 16), ZV, A.add, 2.0 * par, A.add)
-            mov("s", c2("val", 0, 256), ind(WW, V_("vlx")))
-        h = H()
+            tt(V_("cw16"), c2("cv", 0, 16), c2("cv", 16, 32), A.min); hz = H()
+            mm([(ps(hz, i, 256, 16), c2("rowb", 128 * i, 128 * i + 128), V_("cw16"), True, True) for i in range(16)])
+            mov("s", V_("cz"), ps(hz, 0, 256))
+        tt(V_("cw"), c2("cv", 0, 16), c2("cv", 16, 32), A.min)
+        cl[0] = "val"
+        ts(V_("zl"), ps(h, 16, 32), 0.0, A.is_lt, ZV, A.add); tt(V_("zl"), V_("zl"), c2("t128", 16 * par, 16 * par + 16), A.add)
+        lin("s", V_("vlx"), V_("zl"), 1.0, 0.0)
+        mov("s", V_("zs"), ind(c2("cc", W0, U0), V_("vlx"))); mov("s", V_("val"), ind(WW, V_("vlx")))
+        cl[0] = "s4"; h = H(); y = ps(h, 0, 256)
+        ts(V_("idl"), V_("cz"), 0.0, A.is_ge, -32768.0, A.mult)
+        mm([(y, I16, V_("cdg"), True, False), (y, I16, V_("cz"), False, False)])
         for a0 in range(0, 16, 4):
             probe[0] = True
-            four = [ts(c2("gg", 256 * a, 256 * a + 256 - 16 * a), V_("cz", AL, 0, S_(16 * a, 256)), c2("cw", a, a + 1), A.is_equal) for a in range(a0, a0 + 4)]
+            four = [ts(c2("eq", 256 * a, 256 * a + 256 - 16 * a), c2("cz", 16 * a, 256), c2("cw", a, a + 1), A.is_equal, -4096.0, A.mult)
+                    for a in range(a0, a0 + 4)]
             probe[0] = False
-            add("v", lambda c, four=four: [x for f, k in four for x in f(c)], [V_("cz", AL, 0, AL), V_("cw")], [c2("gg", 256 * a0, 256 * a0 + 1024)],
+            add("v", lambda c, four=four: [x for f, k in four for x in f(c)], [V_("cz"), V_("cw")], [c2("eq", 256 * a0, 256 * a0 + 1024)],
                 sum(k for f, k in four))
-            mm(([(ps(h, 0, 256), V_("z16"), c2("rowb", 0, 256), True, False)] if a0 == 0 else []) +
-               [(ps(h, 16 * a + 16, 256), V_("blk"), c2("gg", 256 * a + 16, 256 * a + 256 - 16 * a), False, False) for a in range(a0, min(a0 + 4, 15))])
-        mm([(ps(h, i, 256, 16), c2("tri", 128 * i, 128 * i + 128), c2("gg", i, 4096, 256), False, i == 15) for i in range(1, 16)])
-        ts(V_("cwm"), V_("cw"), 0.0, A.is_le, -32768.0, A.mult); ts(V_("cwp"), V_("cw"), -1.0, A.mult, 1792.0, A.add)
-        sign("s", V_("neg"), ps(h, 0, 256), -1.0)
-        h = H(); o = ps(h, 0, 16)
-        mmg([(o, sel("b4k", i), c2("neg", i, 256, 16)) for i in range(16)] + [(o, I16, V_("cwp")), (o, I16, V_("cwm"))], 18)
-        tt(V_("tgf"), o, V_("jm"), A.max); ts(V_("tgx"), V_("tgf"), 256.0, A.add)
-        mark["c"] = tt(ind(c2("cc", 0, C0 + NV), V_("tgx")), V_("zs"), c2("tabs", 256 * par, 256 * par + 256), A.mult)
+            mm([(ps(h, 16 * a + 16, 256), V_("blk"), c2("eq", 256 * a + 16, 256 * a + 256 - 16 * a), False, False) for a in range(a0, min(a0 + 4, 15))])
+        mm([(y, I16, V_("idl"), False, False)] +
+           [(ps(h, i, 256, 16), c2("tri", 128 * i, 128 * i + 128), c2("eq", i, 4096, 256), False, i == 15) for i in range(1, 16)])
+        scan(V_("tg"), V_("rs0"), y, 1e6, A.min, A.max)
+        tgf = c2("tg", 15, 256, 16); lin("v", V_("tgx"), tgf, 1.0, -float(TOP))
+        put_codes(ind(c2("cc", 0, C0 + NV), V_("tgx")), V_("zs"))
         if not last:
-            send_shifted("cc", C0, C0 + NV, "sc", cr)
-            cl[0] = "names"; names(t + 1); cl[0] = "turn"; turn(t + 1)
+            cl[0] = "sc"; send_shifted(O("shift", t)[0], "cc", C0, C0 + NV, 128, "sc", cr)
+            names(t + 1); turn(t + 1)
         cl[0] = "host"
         hw = c2("hw", 16 * par, 16 * par + 16)
-        ts(V_("h1"), V_("tgf"), 0.0, A.is_ge, -4096.0, A.mult)
-        tt(V_("h1"), V_("h1"), hw, A.add); tt(hw, V_("h1"), V_("tgf"), A.max)
+        ts(V_("h1"), tgf, float(TOP + U0), A.is_ge, -65536.0, A.mult)
+        tt(V_("h1"), V_("h1"), hw, A.add); tt(hw, V_("h1"), tgf, A.max)
         if t < 2:
-            cp(c2("hix", 16 * par, 16 * par + 16), hw)
-        cl[0] = "cch"; half_codes()
+            lin("v", c2("hix", 16 * par, 16 * par + 16), hw, 1.0, -float(TOP + U0))
+        half_codes(t + 1)
         if not last:
             lists(t + 1)
         else:
             cl[0] = "vl"
             h = H(); x = ps(h, 0, 112)
-            mmg([(x, sel("b162", i), c2("cch", 112 * i, 112 * i + 112)) for i in range(16)], 8)
-            ts(V_("yc1"), x, -1.0, A.mult, 2049.0, A.add); ts(V_("yc2"), x, 2048.0, A.add)
+            mmg([(x, sel("b162", i), c2("cch0", 112 * i, 112 * i + 112)) for i in range(16)], 8)
+            lin("v", V_("yc1"), x, -1.0, 2.0 * (MID + FAR) + 1); lin("v", V_("yc2"), x, 1.0, 2.0 * (FAR - MID))
             tt(V_("yc1"), V_("yc1"), V_("yc2"), A.min)
             dma("y", V_("yc"), V_("yc1"), 57344)
-            cp(V_("hw16"), V_("hw")); h = H()
+            cl[0] = "yh"; lin("v", V_("hw16"), V_("hw"), 1.0, -float(TOP + U0)); h = H()
             mm([(ps(h, 2 * i + p2, 512, 32, S_(0, 8)), c2("rowb", 128 * i, 128 * i + 128, 16), c2("hw16", 16 * p2, 16 * p2 + 16), True, True)
                 for i in range(16) for p2 in range(2)])
-            act(V_("cand", S_(0, 8), AL), ps(h, 0, 512, None, S_(0, 8)), F.Copy)
-            dma("y", V_("yh"), V_("cand", S_(0, 8), AL), 16384)
+            mov("s", V_("c1", S_(0, 8), AL), ps(h, 0, 512, None, S_(0, 8)))
+            dma("y", V_("yh"), V_("c1", S_(0, 8), AL), 16384)
+        once = O("once", t)
         step1(t, 0)
-        if O("once", t):
+        if once:
             step1(t, 1)
-        claimed_values()
+        cl[0] = "put"; claimed_values()
         if not last:
-            send_shifted("uw", U0, G0, "su", cr)
+            send_shifted(O("shift", t)[1], "uw", U0, G0, 128, "su", cr)
             ghost_views(t + 1, cr)
-            cl[0] = "vA"
-            if opt["vAearly"]:
-                views(t + 1, 256, 896, opt["vA"])
-            cl[0] = "ue"; old_values(t + 1, 0)
+            cl[0] = "vA"; views(t + 1, 256, 896); old_values(t + 1, 0)
         else:
-            dma("y", c2("yu", 0, 896), c2("uw", U0, U0 + 896), 458752)
-        if not O("once", t):
+            cl[0] = "out"
+            dma("y", c2("yu", 0, 448), c2("uw", U0, U0 + 448), 229376); dma("s", c2("yu", 448, 896), c2("uw", U0 + 448, U0 + 896), 229376)
+        if not once:
             step1(t, 1)
-            claimed_values()
+            if not O("mask", t):
+                claimed_values()
         if not last:
-            cl[0] = "uf"; old_values(t + 1, 1)
+            old_values(t + 1, 1)
+    cl[0] = "out"
     dma("y", c2("yu", 896, 1344), c2("uw", U0 + 896, U0 + 1344), 229376)
     dma("s", c2("yu", 1344, NV), c2("uw", U0 + 1344, G0), 229376)
     return ops, pieces
 
 
-def plan(ops, pieces, boost):
-    n = len(ops); succ = [[] for _ in ops]
-    for j, o in enumerate(ops):
-        for d in o["deps"]:
-            succ[d].append(j)
-    def gap(d, j):
-        return 0.0 if (ops[d]["e"] == "p" and ops[j]["e"] == "p") else ops[d]["lat"]
-    pri = [0.0] * n
-    for j in range(n - 1, -1, -1):
-        pri[j] = ops[j]["cost"] + max([gap(j, s) + pri[s] for s in succ[j]] + [ops[j]["lat"]])
-    pri = [pri[j] + boost.get(o["cl"], 0.0) + boost.get("%s.%s" % (o["cl"], o["e"]), 0.0) for j, o in enumerate(ops)]
-    left = [len(o["deps"]) for o in ops]; rdy = [0.0] * n; end = [0.0] * n; start = [0.0] * n; done = [False] * n
-    free = {e: 0.0 for e in "vspgy"}; pool = {e: [] for e in "vspgy"}; order = []
-    holder = [None] * 8; bank = [None] * len(pieces)
-    def release(j):
-        done[j] = True
-        for s in succ[j]:
-            rdy[s] = max(rdy[s], end[j] + gap(j, s)); left[s] -= 1
-            if left[s] == 0:
-                if ops[s]["e"] is None:
-                    start[s] = end[s] = rdy[s]; order.append(s); release(s)
-                else:
-                    pool[ops[s]["e"]].append(s)
-    def room(j):
-        if not ops[j]["new"]:
-            return rdy[j], None
-        best = None
-        for bs in pieces[ops[j]["new"][0]]["pool"]:
-            last = [x for b in bs if holder[b] is not None for x in pieces[holder[b]]["ops"]]
-            if all(done[x] for x in last):
-                tm = max([rdy[j]] + [end[x] + gap(x, j) for x in last])
-                if best is None or tm < best[0] - 1e-9:
-                    best = (tm, bs)
-        return best
-    for j in range(n):
-        if left[j] == 0:
-            pool[ops[j]["e"]].append(j)
-    while len(order) < n:
-        best = None
-        for e in pool:
-            can = [(x, room(x)) for x in pool[e]]; can = [(x, r) for x, r in can if r is not None]
-            if can:
-                tnow = max(free[e], min(r[0] for x, r in can))
-                if best is None or tnow < best[0]:
-                    best = (tnow, e, can)
-        tnow, e, can = best
-        j, r = max([c for c in can if c[1][0] <= tnow + boost.get("look", 0.05)], key=lambda c: (pri[c[0]], -c[0]))
-        if r[1] is not None:
-            for b in r[1]:
-                if holder[b] is not None:
-                    ops[j]["deps"].update(pieces[holder[b]]["ops"])
-                holder[b] = ops[j]["new"][0]
-            bank[ops[j]["new"][0]] = r[1][0]
-        pool[e].remove(j); start[j] = max(tnow, r[0]); end[j] = start[j] + ops[j]["cost"]; free[e] = end[j]
-        order.append(j); release(j)
-
-    def place(seq, links):
-        st = [0.0] * n; busy = {e: [] for e in "vspgy"}
-        for j in seq:
-            o = ops[j]; r = 0.0; w = o["cost"]
-            for d, gp in links[j]:
-                r = max(r, st[d] + ops[d]["cost"] + gp)
-            if o["e"] is not None:
-                b = busy[o["e"]]; k = len(b)
-                while k > 0 and b[k - 1][1] > r:
-                    k -= 1
-                while k < len(b) and b[k][0] < r + w - 1e-9:
-                    r = max(r, b[k][1]); k += 1
-                b.insert(k, (r, r + w))
-            st[j] = r
-        return st
-    rank = {j: k for k, j in enumerate(order)}
-    fw = [[(d, gap(d, j)) for d in ops[j]["deps"]] for j in range(n)]
-    bw = [[] for _ in ops]
-    for j in range(n):
-        for d, gp in fw[j]:
-            bw[d].append((j, gp))
-    span = lambda st: max(st[j] + ops[j]["cost"] + ops[j]["lat"] for j in range(n))
-    best = span(start); st = start
-    for it in range(PASSES):
-        sb = place(sorted(range(n), key=lambda j: (-(st[j] + ops[j]["cost"]), -rank[j])), bw)
-        st = place(sorted(range(n), key=lambda j: (-(sb[j] + ops[j]["cost"]), rank[j])), fw)
-        if span(st) < best:
-            best = span(st); start = st
-    order = sorted(range(n), key=lambda j: (start[j], rank[j]))
-    return order, start, [start[j] + ops[j]["cost"] for j in range(n)], bank
-
-
-def plan(ops, pieces, times):
+def plan(ops, pieces, times, period):
     n = len(ops); cost = [o["cost"] for o in ops]
     def links():
         fw = [[(d, 0.0 if (ops[d]["e"] == "p" and o["e"] == "p") else ops[d]["lat"]) for d in o["deps"]] for o in ops]
@@ -831,7 +747,8 @@ def plan(ops, pieces, times):
             for d, gp in fw[j]:
                 bw[d].append((j, gp))
         return fw, bw
-    def place(key, fw, bw):
+    def place(key):
+        fw, bw = links()
         left = [len(x) for x in fw]; ready = sorted((key[j], j) for j in range(n) if not left[j])
         st = [0.0] * n; busy = {e: [] for e in "vspgy"}; seq = []
         while ready:
@@ -846,36 +763,24 @@ def plan(ops, pieces, times):
                     r = max(r, b[k][1]); k += 1
                 b.insert(k, (r, r + w))
             st[j] = r
-            new = False
             for s, gp in bw[j]:
                 left[s] -= 1
                 if not left[s]:
-                    ready.append((key[s], s)); new = True
-            if new:
-                ready.sort()
-        assert len(seq) == n
+                    ready.append((key[s], s))
+            ready.sort()
         return st, seq
-    def span(st):
-        return max(st[j] + cost[j] + ops[j]["lat"] for j in range(n))
-    def close(key, passes):
-        fw, bw = links(); st, seq = place(key, fw, bw); best = (span(st), st, seq)
-        for it in range(passes):
-            sb = place([-(st[j] + cost[j]) for j in range(n)], bw, fw)[0]
-            st, seq = place([-(sb[j] + cost[j]) for j in range(n)], fw, bw)
-            best = min(best, (span(st), st, seq))
-        return best[1:]
     key = [0.0] * n; bw = links()[1]
     for j in range(n - 1, -1, -1):
-        o = ops[j]
-        if o["cl"] in times:
-            key[j] = ROUND * o["rd"] + times.get("%s@%d" % (o["cl"], o["rd"]), times[o["cl"]])
-        else:
+        o = ops[j]; tm = times.get("%s@%d" % (o["cl"], o["rd"]), times.get(o["cl"]))
+        if tm is None:
             key[j] = min([key[s] - gp for s, gp in bw[j]] + [1e9]) - cost[j]
-    st, seq = close(key, PASSES[0])
+        else:
+            key[j] = period * o["rd"] + (tm[min(o["nth"], len(tm) - 1)] if isinstance(tm, tuple) else tm)
+    st, seq = place(key)
     bank = banks(pieces, [o["deps"] for o in ops], st, [st[j] + cost[j] for j in range(n)])
-    st, seq = close(st, PASSES[1])
+    st, seq = place(st)
     rank = {j: k for k, j in enumerate(seq)}
-    return sorted(range(n), key=lambda j: (st[j], rank[j])), st, [st[j] + cost[j] for j in range(n)], bank
+    return sorted(range(n), key=lambda j: (st[j], rank[j])), [st[j] + cost[j] for j in range(n)], bank
 
 
 def banks(pieces, deps, st, end):
@@ -902,187 +807,6 @@ def banks(pieces, deps, st, end):
 QUEUES = ("v", "s", "p", "g", "y", None)
 
 
-def refine(ops, refs, order, steps, heat, seed):
-    n = len(ops); state = [seed]
-    def rnd():
-        state[0] = (state[0] * 1103515245 + 12345) % 2147483648
-        return state[0] / 2147483648.0
-    en = [QUEUES.index(o["e"]) for o in ops]; deps = [[] for o in ops]
-    pos = {j: k for k, j in enumerate(order)}; above = [0] * n
-    for j in order:
-        for d in sorted(ops[j]["deps"], key=lambda d: -pos[d]):
-            if not above[j] >> d & 1:
-                deps[j].append(d); above[j] |= above[d] | 1 << d
-    alt = [[QUEUES.index(e) for e in o["alt"]] if o["alt"] else None for o in ops]
-    figs = []
-    for ref in refs:
-        cost = [[o["alt"][e][1] if o["alt"] and e in o["alt"] else o["cost"] for o in ref] for e in QUEUES]
-        lat = [0.0 if o["xf"] else o["lat"] for o in ref]
-        figs.append((cost, lat, [(o["lat"] - o["xf"], o["xf"]) if o["xf"] else None for o in ref], [[(d, 0.0 if en[j] == 2 and en[d] == 2 else lat[d]) for d in deps[j]] for j in range(n)]))
-    def run(order, en, fig, k0, old):
-        cost, lat, xf, lk = fig; free = [0.0] * 6; last = [-1] * 6; top = 0.0; tj = -1; wire = 0.0; wj = -1
-        end = list(old[3]) if k0 else [0.0] * n; why = list(old[1]) if k0 else [-1] * n; out = list(old[4]) if k0 else [0.0] * n
-        for j in order[k0 - 1:max(k0 - 300, 0):-1] if k0 else ():
-            if last[en[j]] < 0:
-                last[en[j]] = j; free[en[j]] = out[j]
-            if wj < 0 and xf[j]:
-                wj = j; wire = end[j]
-        for j in order[k0:]:
-            r = 0.0; w = -1
-            for d, g in lk[j]:
-                x = end[d] + g
-                if x > r:
-                    r = x; w = d
-            e = en[j]
-            if e < 5:
-                if free[e] > r:
-                    r = free[e]; w = -2 - last[e]
-                r += cost[e][j]; free[e] = r; last[e] = j
-            out[j] = r
-            if xf[j]:
-                r += xf[j][0]
-                if wire > r:
-                    r = wire; w = -2 - wj
-                r += xf[j][1]; wire = r; wj = j
-            end[j] = r; why[j] = w; r += lat[j]
-            if r > top:
-                top = r; tj = j
-        return top, why, tj, end, out
-    def tails(order, en, fig, succ):
-        cost, lat, xf, lk = fig; tl = [0.0] * n; nxt = [0.0] * 6; wire = 0.0
-        for j in reversed(order):
-            a = lat[j]
-            for s, g in succ[j]:
-                x = g + tl[s]
-                if x > a:
-                    a = x
-            if xf[j]:
-                wire = xf[j][1] + (a if a > wire else wire); a = xf[j][0] + wire
-            e = en[j]
-            if e < 5:
-                a = cost[e][j] + (a if a > nxt[e] else nxt[e]); nxt[e] = a
-            tl[j] = a
-        return tl
-    def least(new, en, fig, succ, k0, k1, old, tl):
-        cost, lat, xf, lk = fig; end = {}; free = {}; oe = old[3]; top = 0.0
-        for j in new[k0:k1 + 1]:
-            r = 0.0
-            for d, g in lk[j]:
-                x = end.get(d, oe[d]) + g
-                if x > r:
-                    r = x
-            e = en[j]
-            if e < 5:
-                if e not in free:
-                    k = k0 - 1
-                    while k >= 0 and en[new[k]] != e:
-                        k -= 1
-                    free[e] = old[4][new[k]] if k >= 0 else 0.0
-                r = max(r, free[e]) + cost[e][j]; free[e] = r
-            if xf[j]:
-                r += xf[j][0] + xf[j][1]
-            end[j] = r
-            for s, g in succ[j]:
-                if pos[s] > k1 and r + g + tl[s] > top:
-                    top = r + g + tl[s]
-        for e in free:
-            k = k1 + 1
-            while k < n and en[new[k]] != e:
-                k += 1
-            if k < n and free[e] + tl[new[k]] > top:
-                top = free[e] + tl[new[k]]
-        return top
-    succ = []
-    for fig in figs:
-        succ.append([[] for o in ops])
-        for j in range(n):
-            for d, g in fig[3][j]:
-                succ[-1][d].append((j, g))
-    def move(order, en, a, b, far, ahead):
-        k0, k1 = pos[a], pos[b]; qn = set()
-        if ahead:
-            while far and k0 > 0:
-                k0 -= 1; far -= en[order[k0]] == en[a]
-            seg = order[k0:k1]; need = set(deps[b]); mv = []
-            for x in reversed(seg):
-                if x in need or en[x] in qn:
-                    if x == a:
-                        return None
-                    mv.append(x); need.update(deps[x])
-                    if en[x] < 5 and en[x] != en[b]:
-                        qn.add(en[x])
-            ms = set(mv)
-            return k0, mv[::-1] + [b] + [x for x in seg if x not in ms]
-        while far and k1 < n - 1:
-            k1 += 1; far -= en[order[k1]] == en[a]
-        seg = order[k0:k1 + 1]; ms = {a}; mv = [a]
-        for x in seg[1:]:
-            if en[x] in qn or not ms.isdisjoint(deps[x]):
-                if x == b:
-                    return None
-                mv.append(x); ms.add(x)
-                if en[x] < 5 and en[x] != en[a]:
-                    qn.add(en[x])
-        return k0, [x for x in seg if x not in ms] + mv
-    name = {}; seen = {}
-    for j, o in enumerate(ops):
-        k = (o["rd"], o["cl"], o["tag"], o["k"], o["e"] if not o["alt"] else "*"); seen[k] = seen.get(k, 0) + 1; name[k + (seen[k],)] = j
-    twin = [{} for o in ops]
-    for k, j in name.items():
-        for d in (-3, -2, -1, 1, 2, 3):
-            if (k[0] + d,) + k[1:] in name:
-                twin[j][d] = name[(k[0] + d,) + k[1:]]
-    free_calls = [j for j in range(n) if alt[j]]
-    rs = [run(order, en, f, 0, None) for f in figs]; wt = [200.0 / r[0] / len(figs) for r in rs]
-    cur = 200.0; best = (cur, order, en, rs); pos = {j: k for k, j in enumerate(order)}; arcs = [None] * len(figs)
-    for it in range(steps):
-        f = int(rnd() * len(figs))
-        if arcs[f] is None:
-            why = rs[f][1]; j = rs[f][2]; arcs[f] = []
-            while j != -1:
-                w = why[j]
-                if w <= -2:
-                    w = -2 - w; arcs[f].append((w, j))
-                j = w
-        a, b = arcs[f][int(rnd() * len(arcs[f]))]; u = rnd(); e2 = en; far = (0, 0, 1, 2, 4, 8)[int(rnd() * 6)]; new = order; every = rnd() < TWINS
-        if u < 0.2:
-            x = a if u < 0.07 else b if u < 0.14 else free_calls[int(rnd() * len(free_calls))]
-            if not alt[x]:
-                continue
-            e2 = list(en); to = [e for e in alt[x] if e != en[x]][int(rnd() * (len(alt[x]) - 1))]; k0 = n
-            for y in [x] + (list(twin[x].values()) if every else []):
-                if alt[y] and to in alt[y]:
-                    e2[y] = to; k0 = min(k0, pos[y])
-        else:
-            new = list(order); k0 = n; used = []
-            for x, y in [(a, b)] + ([(twin[a][d], twin[b][d]) for d in twin[a] if d in twin[b]] if every else []):
-                got = move(order, en, x, y, far, u < 0.6) if pos[x] < pos[y] else None
-                if got and all(got[0] > hi or got[0] + len(got[1]) <= lo for lo, hi in used):
-                    new[got[0]:got[0] + len(got[1])] = got[1]; k0 = min(k0, got[0]); used.append((got[0], got[0] + len(got[1]) - 1))
-                elif x == a:
-                    break
-            if k0 == n:
-                continue
-        bar = cur + heat * rnd() ** 3 * (1 - it / steps)
-        if k0 > n - 60:
-            k0 = 0
-        r2 = [run(new, e2, fig, k0, r) for fig, r in zip(figs, rs)]; t = sum(r[0] * w for r, w in zip(r2, wt))
-        if t <= bar:
-            cur, rs, en = t, r2, e2; arcs = [None] * len(figs)
-            if it % 8 == 0:
-                end = r2[0][4]; c0 = figs[0][0]; rk = {j: k for k, j in enumerate(new)}
-                new = sorted(new, key=lambda j: (end[j] - (c0[en[j]][j] if en[j] < 5 else 0.0), rk[j]))
-                r2 = rs = [run(new, en, fig, 0, None) for fig in figs]; t = cur = sum(r[0] * w for r, w in zip(r2, wt))
-            order = new; pos = {j: k for k, j in enumerate(order)}
-            if t < best[0]:
-                best = (t, order, en, r2)
-    for calls in [ops] + refs:
-        for o, e in zip(calls, best[2]):
-            if o["alt"]:
-                o["e"] = QUEUES[e]; o["f"], o["cost"] = o["alt"][o["e"]]
-    return best[1], best[3][0][4], [r[0] for r in best[3]]
-
-
 def refine(ops, refs, full, steps, heat, seed, lo, hi):
     n = len(ops); state = [seed]
     def rnd():
@@ -1094,7 +818,7 @@ def refine(ops, refs, full, steps, heat, seed, lo, hi):
         for d in sorted(ops[j]["deps"], key=lambda d: -pos[d]):
             if not above[j] >> d & 1:
                 deps[j].append(d); above[j] |= above[d] | 1 << d
-    alt = [[QUEUES.index(e) for e in o["alt"]] if o["alt"] else None for o in ops]
+    alt = [[QUEUES.index(e) for e in o["alt"]] if o["alt"] and len(o["alt"]) > 1 else None for o in ops]
     def run(order, en, fig, k0, old):
         cost, xf, lk, rest, behind, start = fig
         end, why, out = list(old[3]), list(old[1]), list(old[4]); free, last = list(start[0]), list(start[1]); left = {0, 1, 2, 3, 4, 6}
@@ -1169,13 +893,12 @@ def refine(ops, refs, full, steps, heat, seed, lo, hi):
                 if en[x] < 5 and en[x] != en[a]:
                     qn.add(en[x])
         return k0, [x for x in seg if x not in ms] + mv
-    name = {}; seen = {}; twin = {j: {} for j in order}
-    for j in sorted(order):
-        o = ops[j]; k = (o["rd"], o["cl"], o["tag"], o["k"], "*" if o["alt"] else o["e"]); seen[k] = seen.get(k, 0) + 1; name[k + (seen[k],)] = j
+    name = {(ops[j]["rd"], ops[j]["cl"], ops[j]["nth"]): j for j in order}; twin = {j: {} for j in order}
     for k, j in name.items():
         for d in (-3, -2, -1, 1, 2, 3):
-            if (k[0] + d,) + k[1:] in name:
-                twin[j][d] = name[(k[0] + d,) + k[1:]]
+            x = name.get((k[0] + d,) + k[1:])
+            if x is not None and ops[x]["tag"] == ops[j]["tag"] and ops[x]["k"] == ops[j]["k"]:
+                twin[j][d] = x
     either = [j for j in order if alt[j]]
     wt = [200.0 / r[0] / len(figs) for r in rs]; cur = 200.0; best = (cur, order, en, rs); arcs = [None] * len(figs)
     for it in range(steps):
@@ -1199,7 +922,7 @@ def refine(ops, refs, full, steps, heat, seed, lo, hi):
                 continue
             e2 = list(en); to = [e for e in alt[x] if e != en[x]][int(rnd() * (len(alt[x]) - 1))]
             for y in [x] + (list(twin[x].values()) if every else []):
-                if to in alt[y]:
+                if alt[y] and to in alt[y]:
                     e2[y] = to; k0 = min(k0, pos[y])
         else:
             new = list(order); used = []
@@ -1225,7 +948,7 @@ def refine(ops, refs, full, steps, heat, seed, lo, hi):
         for o, e in zip(calls, best[2]):
             if o["alt"]:
                 o["e"] = QUEUES[e]; o["f"], o["cost"] = o["alt"][o["e"]]
-    return full[:lo] + best[1] + full[hi:], best[3][0][4]
+    return full[:lo] + best[1] + full[hi:], best[3][0][4], [r[0] for r in best[3]]
 
 
 def rebank(ops, pieces, data, order, end):
@@ -1250,40 +973,34 @@ def rebank(ops, pieces, data, order, end):
     return out, bank
 
 
-def schedule(opt, plans, phases):
-    ops, pieces = build(opt, plans[0]); refs = [build(opt, p)[0] for p in plans]
+def schedule(opt, times, engines, period, plans, phases, seed):
+    ops, pieces = build(opt, engines, plans[0]); refs = [build(opt, engines, p)[0] for p in plans]
     data = [set(o["deps"]) for o in ops]
-    order, st, end, bank = plan(ops, pieces, opt["boost"])
-    n = len(ops)
+    order, end, bank = plan(ops, pieces, times, period)
+    n = len(ops); spans = None
     for k, (steps, heat, parts) in enumerate(phases):
         if k:
             order, bank = rebank(ops, pieces, data, order, end) or (order, bank)
         for j in range(parts):
-            order, end = refine(ops, refs, order, steps, heat, 7 * k + j + 1, max(0, n * j // parts - 40), min(n, n * (j + 1) // parts + 40))
-        order, end = refine(ops, refs, order, 0, heat, 1, 0, n)
-    return ops, order, end, bank
+            order, end, spans = refine(ops, refs, order, steps, heat, 7 * k + j + seed, max(0, n * j // parts - 40), min(n, n * (j + 1) // parts + 40))
+        order, end, spans = refine(ops, refs, order, 0, heat, 1, 0, n)
+    return ops, order, end, bank, spans
 
 
 CACHE = {}
-
-
-def prepare():
-    if "ops" not in CACHE:
-        ops, order, end, bank = schedule(OPT, PLANS, PHASES)
-        CACHE["ops"] = ops; CACHE["plan"] = (order, None, end, bank)
 
 
 def rank_program(g, core, T, topo):
     rank = T.rank_of(core)
     if rank is None:
         return
-    prepare()
-    ops = CACHE["ops"]; order = CACHE["plan"][0]
+    if not CACHE:
+        CACHE["plan"] = schedule(OPT, TIMES, ENGINES, ROUND, PLANS, PHASES, SEED)
+    ops, order, end, bank, spans = CACHE["plan"]
     nr = len(T.cores); dst = T.cores[(rank - 1) % nr]; up = T.cores[(rank + 1) % nr]
     rid, pid = topo.addr(dst)[:2]
     en = topo.engines(core, dst); inn = len(topo.engines(up, core))
-    c = {"g": g, "T": T, "dst": DstId(rid=rid, pnc=pid), "en": en, "up": topo.addr(up)[:2], "upm": 1 << topo.engines(core, up)[0],
-         "bank": CACHE["plan"][3]}
+    c = {"g": g, "T": T, "dst": DstId(rid=rid, pnc=pid), "en": en, "up": topo.addr(up)[:2], "upm": 1 << topo.engines(core, up)[0], "bank": bank}
     queue = {"v": g.vector, "s": g.scalar, "p": g.tensor, "g": g, "y": g.sync}
     own = {"v": "v", "s": "s", "p": "p", "g": "gq"}
     count = {}; token = {}; known = {e: {} for e in queue}; total = {}; seen = {}; when = {}; waited = {}
@@ -1299,7 +1016,7 @@ def rank_program(g, core, T, topo):
             continue
         need = {}
         for d in o["deps"]:
-            if d in o["soft"] or (e == "p" and ops[d]["e"] == "p") or (o["k"] == "r" and ops[d]["k"] == "r" and ops[d]["sem"][1] == 1):
+            if (e == "p" and ops[d]["e"] == "p") or (o["k"] == "r" and ops[d]["k"] == "r" and ops[d]["sem"][1] == 1):
                 continue
             s, k = token[d]
             if s == own.get(e) and d in o["reads"]:
@@ -1320,7 +1037,9 @@ def rank_program(g, core, T, topo):
                 x.then_inc(T.sem[s], 1)
             count[s] = count.get(s, 0) + len(ins); token[j] = (s, count[s]); total[s] = count[s]
         elif o["k"] == "d":
-            ins[0].then_inc(T.sem[o["sem"][0]], 16); token[j] = o["sem"]; total[o["sem"][0]] = 16
+            for x in ins:
+                x.then_inc(T.sem[o["sem"][0]], 16)
+            token[j] = o["sem"]; total[o["sem"][0]] = o["sem"][1]
         else:
             k = len(en) if o["sem"][1] == "en" else 1
             token[j] = (o["sem"][0], k); total[o["sem"][0]] = k

@@ -12,53 +12,42 @@ UE = G0 + NG
 C0 = U0
 MID, FAR = 1024, 960
 TOP = 49152
-SPINE = (4, 0, 6, 2, 5, 1, 7, 3)
-OPT = {"pair": "ddxx", "dd": "v", "c1": "vvv", "grp": ((0, 2), (2, 3), (3, 4)), "fine": (3,), "shift": "ppp", "direct": 0,
-       "treeA": "dddd", "treeB": "ddvv", "tail": "ss", "dmaA": (0, 1, 3), "dmaB": (2,), "once": False, "ftr": "g", "u16": "sv", "mask": True, "rep": "d", "cz": "v", "cut": NV, "cut@-1": NV,
-       "dmaB@3": (2, 3)}
-ROUND = 43.0
-TIMES = {'vB': 2.5, 'uc0': -3.0, 'x0': 0.0, 'm0': 3.5, 'uc1': -0.5, 'x1': 2.0, 'm1': 5.5, 'uc2': 4.5, 'x2': 6.5, 'm2': 9.5, 'uc3': -1.5, 'x3': 4.5,
-         'm3': 11.0, 'l0': 13.0, 'l1': 13.5, 'l2': 16.5, 'l3': 13.0, 'w0': 16.5, 'w1': 18.5, 'w2': 15.5, 's3': 23.5, 'names': 15, 'turn': 22,
-         'host': 33.0, 'cch': 30.0, 'vl': 33.5, 'nl': 45.5, 'sd0': 37.0, 'sd1': 39.5, 'sd2': 41.5, 'sd3': 37.5, 'pl': 47.5, 'cand': 51.5,
-         'A0': 10.0, 'A1': 11.5, 'A2': 10.0, 'A3': 15.0, 'At': 29.5, 'gv': 40.0, 'vA': 37.0, 'ue': 34.5, 'B0': 27.5, 'B1': 24.0, 'B2': 21.0,
-         'B3': 30.5, 'Bt': 35.0, 'uf': 48.0, 'put': 30.0, 'cred': 12.0, 'out': 36.0,
-         "ld0": 20, "ldw": 20.5, "ld1": 21, "ld2": 22, "sc0": 24, "su0": 25, "vl@-1": 26, "gv@-1": 27, "vA@-1": 29, "vB@0": -15, "nl@-1": 31,
-         "names@-1": 28, "turn@-1": 30}
-OPT.update({"dmaB": (0, 1, 2, 3), "dmaB@3": (0, 1, 2, 3), "dmaA": (1, 3), "direct": 448})
-ROUND = 43.3
-TIMES = {'out': 40, 'ld0@-1': (28.4,),'ldw@-1': (29.4,),'ld1@-1': (26.5,),'ld2@-1': (27.4,),'sc0@-1': (30.3,30.7,31,39.1),'su0@-1': (33.6,34.4,37.9,43),'names@-1': (33.2,35.1,35.2,37),'turn@-1': (42.5,42.7,43.5),'vl@-1': (32.7,33.1,33.7,34.1),'nl@-1': (34.6,43.7,44.4,45,45.5,46,48.7),'sd0@-1': (39.6,41.1,42.4,43,43.9),'sd1@-1': (41,42.5,43.4,43.6,47.3),'sd2@-1': (41,43.9,45.5,46.5,50.1),'sd3@-1': (39.6,41.6,42.4,43.1,51.3),'pl@-1': (52.1,52.3,55.5),'cand@-1': (51.5,51.7,51.9,52.5,55.2,55.8,56.1,56.9,57.5,62.1),'gv@-1': (36.6,36.2,36.7,37.3,41.7,48.1),'vA@-1': (36.5,34.4),'ue@-1': (44.1,44.7),'uf@-1': (37.4,49.3),'vB': (-3,-2),'uc0': (-1.7,),'x0': (0,2.2),'m0': (4.8,5.4,3.6,4.2),'uc1': (-0.1,),'x1': (1.4,4.7),'m1': (6.7,8.8,7.2,7.8),'uc2': (3.2,),'x2': (5.3,8.4),'m2': (10.6,10.1),'uc3': (-0.8,1.3),'x3': (2.8,5.7,4.1,6.7),'m3': (11.1,12,13,11.5,12.5,13.9),'cred': (12.1,),'l0': (14.4,15.7),'l1': (13.2,14.3),'l2': (15,16.4),'l3': (16.3,17.6),'w0': (17.2,16.5,17.7,19.3,20.5,20.8),'w1': (18.4,18.2,18.8,20.6,20.9,21.1),'w2': (19.4,19,19.8,20.8,21,21.2),'s3': (21.4,22.2,22,22.6,23,23.4,23.7,24.1,24.1,24.8,24.5,24.9,28.6,28.8,25,25.6,25.5,26.2,25.9,26.5,26.3,26.7,26.8,27.5,27.4,27.5,27.8,28.6,28.8,29,29.9,30.4,30.9,36),'names': (9.3,12.3,12.4,22.5),'turn': (-14.9,-13.7,22.7),'host': (29.8,31.1,31.8,32.6),'cch': (31.9,29.9,29.9,29.9),'vl': (31.7,32.2,33.9,34.4,31,31.4,32.4,32.8),'nl': (39.7,42.5,43.3,43.8,44.3,44.8,47.3),'sd0': (36.5,38,39.6,41.2,42.4),'sd1': (37.9,40.2,42.4,42.6,46.1),'sd2': (39.1,42.7,44,45.3,47.2),'sd3': (36.5,39.2,40.9,41.1,48.7),'pl': (49.4,49.6,53.9),'cand': (47.9,48.9,49.2,49.8,53.7,54.2,54.6,56.1,56.7,60.6),'A0': (7.7,11.8,13.4,14.4),'A1': (7.2,9.8,17.1,18.6,19.5,25.9),'A2': (8.9,18.4,19.7),'A3': (9.7,11.1,22.2,24,24.9),'At': (21,22.9,28.9,30.2,31.2,31.6,31.9,32.2),'put': (32.6,33.9,34.5,34.7,39.8),'gv': (35.5,34.9,37.1,39.3,39.7,46),'vA': (34.6,33.6),'ue': (36.8,37.5),'B0': (19.5,20.9,26,27.6,28.9),'B1': (15.1,16.4,23,26.6,27.9,35.3),'B2': (20.9,22.3,27.7,30.3),'B3': (24.8,26.9,31.8,33.5,34,34.5),'Bt': (33,34.1,35,36.2,37.9,38.2,32.7,36.1,38.5,38.9),'uf': (35.7,48.1)}
-ENGINES = {'sc0@-1': '.s','su0@-1': '.v','names@-1': 's..v','turn@-1': 'vg','vl@-1': '...s','nl@-1': '.v....s','sd0@-1': 'v.v.s','sd1@-1': 's.v.v','sd2@-1': 'v.s.s','sd3@-1': 's.s.s','pl@-1': '..s','cand@-1': '....ss.s.s','gv@-1': 'vv.v','vA@-1': 'ss','ue@-1': 'g','uf@-1': 'g','vB': 'sv','uc0': 's','uc1': 's','uc2': 's','uc3': 'vs','m3': '..v..s','l0': 's','l1': 's','l2': 'v','l3': 's','w0': '...s','w1': '...v','w2': '...s','s3': '.......s.vs.ss...........s..v..s','names': 's..v','turn': 'sg','host': '...s','cch': 'gvsg','vl': '...v...s','nl': '.v....s','sd0': 'v.s.s','sd1': 's.v.v','sd2': 'v.s.s','sd3': 's.s.s','pl': '..s','cand': '....ss.s.s','A1': 's','A3': 's','At': '....s.v','put': '..s','gv': 'sv.s','vA': 'ss','ue': 'g','B0': 's','B1': 's','B2': 's','B3': 's','Bt': '....v','uf': 'g'}
-for k in list(TIMES):
-    if k[:2] == "sd":
-        TIMES[k] = TIMES[k][:3] + TIMES[k][4:]
-TIMES.update({"s3": 21.4, "val": (24, 24.5, 25, 27, 27.5), "s4": 24.5, "sc": 28, "sc0@-1": 29, "sc1@-1": 36, "yh": 32})
-ENGINES["s3"] = ""
-OPT.update({"dmaA": (), "direct": 0, "rep": "g", "shift": "www"})
-ROUND = 41.7
-TIMES = {'out':40,'yh':34,'ld0@-1':(26.4,),'ldw@-1':(27.6,),'ld1@-1':(25.5,),'sc0@-1':(28.6,35.1),'sc1@-1':(35.6,36),'su0@-1':(32.8,33.8,32.7,36.2,40.8),'names@-1':(31.8,32.4,32.6,33.2),'turn@-1':(38.9,37.8,39.6),'vl@-1':(31.3,31.9,32.6,32.9),'nl@-1':(39.9,42.1,42.3,43,43.6,44.2,47),'sd0@-1':(36.4,37.9,39.1,39.9),'sd1@-1':(36.4,38.5,39.8,40),'sd2@-1':(37.8,39.2,41.2,45.5),'sd3@-1':(38,40.5,43.6,45.6),'pl@-1':(47,48,54),'cand@-1':(45.7,47.3,47.5,47.8,50.1,52,53.1,54.3,54.9,62.4,63,65.6),'gv@-1':(33.4,33.4,35.9,39.2,34.8,40.8,46.7),'vA@-1':(33.8,34),'ue@-1':(47.9,39.8),'uf@-1':(44.8,41.8,46.9,34.2),'vB':(5.9,-1.2),'uc0':(-2.3,),'x0':(0,2.2),'m0':(4.7,5.3,4.3,4.8),'uc1':(-0.8,),'x1':(1.4,3.8),'m1':(5.2,8.5,6.4,7.5),'uc2':(0.7,),'x2':(2.7,7.6),'m2':(9.3,10.8),'uc3':(3.1,5.2),'x3':(5.7,7.1,6.8,8.8),'m3':(8.8,10.4,11.1,11.3,13,14.7),'cred':(22.4,),'l0':(16.4,17.2),'l1':(13.9,15.6),'l2':(13.2,14.9),'l3':(17.1,17.9),'w0':(18.7,18,19.3,21.3,21.7,22),'w1':(16.3,15.7,16.7,17.8,19.1,20),'w2':(20.1,20.2,20.8,21.6,21.9,22.1),'s3':(22.3,22.9,23.1,23.5,23.8,24.2,24.5,24.9,24.8,25.1),'val':(25.8,26.2,27.9,28.8,31.5),'s4':(26.9,25.5,25.3,25.9,25.8,26.4,26.2,26.8,26.5,27,27.2,28.1,28.4,28.6),'sc':(29.7,30.4,30.2,30.6,35.2),'names':(10.8,11.2,11.4,21.7),'turn':(27.3,26.5,33.9),'host':(31.3,32.2,34.9,39),'cch':(29.6,30,30.4,29.6),'vl':(31.1,31.6,32.5,32.8),'nl':(40.4,42,42.2,42.8,43.5,44.1,46.9),'sd0':(35.7,37.3,38.7,39.8),'sd1':(35.9,39.1,40.1,40.4),'sd2':(37.9,39.7,41.9,45.8),'sd3':(37.3,41,43.5,45.9),'pl':(46.2,47.2,54),'cand':(46,46.5,46.7,47,50,51.9,53,54.3,54.8,62.3,62.9,64.4),'A0':(8.2,9.7,11.6,13.5,14.4),'A1':(7.6,14.3,18,19.2,20.1,25.3),'A2':(12.4,11.8,18.8,21),'A3':(20.3,16.6,22,23.4,24.3),'At':(22.1,24.4,28.6,30,31.3,31.6,31.9,32.3),'put':(32.7,33.6,34.9,33.6,35.1,39.7),'gv':(34.1,33.6,36.6,38.8,36.7,39.1,45),'vA':(35,34),'ue':(41.8,36.1),'B0':(9.3,10.6,25,29.5,31.6),'B1':(15.2,16.5,24.2,27,27.9,37.1),'B2':(20.1,21.4,27.9,30.5),'B3':(22.8,26.3,31.9,33.5,34.5,35),'Bt':(33.2,33.9,35.6,38,39.2,39.6,33.3,35.5,39.9,40.2),'uf':(40.7,51.2,41.2,40.1)}
-ENGINES = {'sc1@-1':'.s','su0@-1':'.ss','names@-1':'s..s','turn@-1':'gs','vl@-1':'...s','nl@-1':'.s....s','sd0@-1':'v.v','sd1@-1':'s.v','sd2@-1':'v.v','sd3@-1':'s.s','pl@-1':'..s','cand@-1':'....ss.s.s.s','gv@-1':'vs.vv','vA@-1':'vs','ue@-1':'gg','uf@-1':'gggg','vB':'sv','uc0':'s','uc1':'s','uc2':'s','uc3':'ss','m3':'..s..s','l0':'s','l1':'s','l2':'s','l3':'s','w0':'...s','w1':'...s','w2':'...s','val':'ss.ss','s4':'............v','sc':'.vv','names':'s..s','turn':'gs','host':'...s','cch':'sssg','vl':'...s','nl':'.s....s','sd0':'v.s','sd1':'s.v','sd2':'v.s','sd3':'s.s','pl':'..s','cand':'....ss.s.s.s','At':'....s.v','put':'..sg','gv':'vs.sg','vA':'ss','ue':'gg','B0':'s','B1':'s','B2':'s','B3':'s','Bt':'....v','uf':'gggg'}
-TIMES["val"] = (25, 25.2, 25.4, 26, 30); ENGINES.update({"val": "..sss", "s4": "............vs"})
-OPT.update({"fine": (), "grp": ((0, 2), (2, 4)), "cz": "p", "dmaB": (0, 1, 2), "cut": 896, "pair": "ddpp"})
-ROUND = 40.9
-TIMES = {'out':40,'yh':34,'ld0@-1':(25.8,),'ldw@-1':(26.8,),'ld1@-1':(24.8,),'sc0@-1':(27.8,34.3),'sc1@-1':(34.8,35.2),'su0@-1':(32.9,33.4,33.9,34.3,38.9),'names@-1':(31.9,32.5,32.7,33.1),'turn@-1':(36.9,38.5,41.9),'vl@-1':(31.5,32.7,33.3),'nl@-1':(39.7,43.7,43.9,44.5,45.2,46.4,48.2),'sd0@-1':(35.6,37,38.3,38.6),'sd1@-1':(35.6,37.7,39,43.4),'sd2@-1':(36.9,38.4,40.4,43.5),'sd3@-1':(37.2,39.1,43.6,46),'pl@-1':(47,47.8,52.2),'cand@-1':(45.8,46.2,47.3,47.5,48.7,49.9,51.4,53.7,54.4,55,61.4),'gv@-1':(33.7,34.9,35.4,38.4,35.9,39.6,45.5),'vA@-1':(34.1,34.2),'ue@-1':(39,33.7),'uf@-1':(43.9,46,35.3,32.7),'vB':(5.2,-1.2),'uc0':(-2.4,),'x0':(0,1.7),'m0':(3.4,3.9,2.9,3.5),'uc1':(-1,),'x1':(1.4,2.9),'m1':(5.7,7.2,5.3,6.2),'uc2':(0.4,),'x2':(3.8,6.4),'m2':(8.7,7.6),'uc3':(3.8,),'x3':(6.2,8),'m3':(10.4,9.4,11.1,13.3,11.5,8.1,12.3,15.2),'cred':(21.1,),'l0':(14.5,15.4),'l1':(13.8,14.6),'l2':(15.7,16.6),'l3':(16.4,17.3),'w0':(16.2,16.2,17.4,20.1,20.7,21),'w1':(18.9,18.2,19.4,20.5,20.9,21.2),'s3':(21.4,22.2,22,22.6,23.4,23.5,23.7,24.5,23.7),'val':(23.6,23.8,24.8,27.2,25.7),'s4':(26.5,24.9,24.9,25.5,25.4,26.1,25.8,26.4,26.2,26.7,26.8,27.8,28.2,28.4),'sc':(29.3,30,30.2,30.5,35.1),'names':(20.8,24.4,24.5,31.8),'turn':(26.9,14.6,30.6),'host':(30.1,30.8,32.1,60),'cch':(30.4,29.7,32.1,31.5),'vl':(31.8,33,33.3),'vm':(33.8,35.2,38.6),'nl':(40.1,43.7,43.9,44.6,45.2,46.5,48.3),'sd0':(35.6,37.4,38.3,39),'sd1':(35.6,38.1,39.3,43.6),'sd2':(37,38.8,39.6,43.7),'sd3':(36.9,39.4,43.6,46.1),'pl':(47.2,47.9,53.4),'cand':(45.8,46.3,47.4,47.7,48.7,49.9,51.5,53.7,54.5,55.1,61.6),'A0':(8,9.8,10.5,12.6,13.6),'A1':(13.4,10.9,17.1,18.1,19,24.4),'A2':(9.1,12,18,19.3),'A3':(14,20.1,21.2,22.5,23.4),'At':(20.2,21.3,27.5,29.6,30.9,31.2,31.5,31.9),'put':(32.2,33.5,34.3,33.1,34.6,39.1),'gv':(33.5,33.9,36.8,38.3,35.6,38.7,44.6),'vA':(34.5,34.4),'ue':(40.2,36.7),'B0':(9.2,10.5,24.9,28.1,29),'B1':(11.3,12.6,22,23.9,25.4,33.6),'B2':(18.8,20.1,26.1,28.9),'B3':(26.6,29.2,30.2,31.4,33.2),'B3@3':(21,22,29.2,30.2,31.4,33.2),'Bt':(30.7,32.4,34.6,35.7,38.4,38.7,34.3,35.4,39.1,39.4),'uf':(39.7,40.8,36.2,49.1)}
-ENGINES = {'sc1@-1':'.v','su0@-1':'.vv','names@-1':'s..s','turn@-1':'sg','vl@-1':'..s','nl@-1':'......s','sd0@-1':'v.v','sd1@-1':'s.v','sd2@-1':'v.v','sd3@-1':'s.s','pl@-1':'..s','cand@-1':'....ss.s..s','gv@-1':'ss.vg','vA@-1':'sv','ue@-1':'gv','uf@-1':'gggs','vB':'sv','uc0':'s','uc1':'s','uc2':'s','uc3':'s','m3':'...s...s','l0':'s','l1':'s','l2':'s','l3':'s','w0':'...s','w1':'...s','s3':'.......s','val':'..sss','s4':'............ss','sc':'.ss','names':'s..s','turn':'sg','host':'...s','cch':'svsg','vl':'..s','vm':'..v','nl':'......s','sd0':'v.v','sd1':'s.v','sd2':'v.v','sd3':'s.s','pl':'..s','cand':'....ss.s..s','At':'....v.s','put':'..sg','gv':'ss.sg','vA':'sv','ue':'gg','B0':'s','B1':'s','B2':'s','Bt':'....v','uf':'gggg'}
+SLOTS = ((9, 11, 13, 15, 1, 3, 5, 7, 2, 6, 10, 14, 4, 12, 0, 8), (3, 7, 11, 15, 2, 6, 10, 14, 5, 4, 13, 12, 1, 9, 0, 8))
+NB = 14
+PER = (4, 4)
+OPT = {"pair": "ddyy", "dd": "g", "c1": "vvv", "grp": ((0, 2), (2, 3), (3, 4)), "fine": (0,), "sdf": (0,), "shift": "wdd", "once": False, "once@3": True,
+       "rep": "g", "cz": "p", "fold": 2, "cch": "h", "cch0": "g", "wayA": "vv", "wayB": "ssssvvvv", "a4": "vv", "treeA": "ddd", "treeB": "ddd", "fin": "vv", "diag": True,
+       "cut": 256, "parts": (256, 768, 1280, NV), "vcut": (768, 1280, NV)}
+OPT = {'pair': 'ddpp', 'dd': 'g', 'c1': 'vvv', 'grp': ((0, 2), (2, 4)), 'fine': (0,), 'sdf': (0,), 'shift': 'www', 'once': False, 'rep': 'd', 'cz': 'p', 'fold': 2,
+       'cch': 'h', 'cch0': 'g', 'wayA': 'vvvv', 'wayB': 'sssv', 'a4': 'vv', 'treeA': 'ddddd', 'treeB': 'ddddv', 'fin': 'vv', 'diag': True, 'cut': 896,
+       'parts': (448, 896, 1344, 1792), 'vcut': (576, 896, 1344, 1792), 'cut@-1': 1792}
+START = (0, 148, 541, 960, 1363)
+TIMES = {
+    -1: "setup:0,0,2,1,0,6,1,5,9,3,6,2,5,7,8,12s,21s,16s,24s,17s,14s,25v,22s,11s,14v,11v,31v,16v,19s,29v,26s,4,15,48,10,60,82,67,30,32,11,88v,69s,27s,30,28,50,65,70,13,134g,77s,75s,65s,22,24,26,34,40,46,64s,76s,40,65g,60,46,17,49,18,47,61,52,195,267,364,71,106,51,68,196,203g,150,188,348,283,64,59,63,18,79,138,368,38,138,146,142,164,168,172,100,109,179,247,304,9s,239,300,293,160,328,392,264,81,176,297,243,396,191,183,187,37,41,33,29 ld0:10 ldw:20 ld1:2 sc0:30,96 code:35,39v,51g,29,33s,55v,37,43v,55s,32,38,59s sc1:101,105s su0:75,80s,77g,85,130 names:71s,79,80,101v turn:129g,123g,136 vl:65,77,80v nl:103,145,149,156,162,168,227s sd0:108v,116,136s,139,115v,123,135s,140 sd1:108s,130,144s,147 sd2:122s,136,165s,187 sd3:122v,143,180v,186 pl:210,212,264s cand:188,191,193,215,297s,318,353s,359,365,381s gv:92s,84v,89,103v,103g,113,177 vA:96s,83s ue:95g,101 uf:67s,85",
+    0: "vB:-59v,68s uc0:-8v,-11s x0:0,12,7,18 m0:28,33,33,39 uc1:-1s x1:14,49 m1:66,71,70,81 uc2:23s x2:39,59 m2:80,75 uc3:36s x3:53,84 m3:113,114,126,159s,96,81,102,154s cred:170 l0:127s,137 l1:134s,144 l2:171s,183 l3:164s,175 w0:159,152,164,182,190,196,222,218 w1:192,191,203,214,217,219,223,224 s3:227,235,237,238,246s,238s val:237,244,249s,255s,251s s4:250,252,245,252,257,255,263,260,268,263,272,267,274,277,280s,283s sc:301,306v,300s,308,354 names:229s,234,235,269s turn:267s,210s,307 host:314,324,327,610s cch:296s,292s,306s,302s vl:310,323,325s vm:318,334,336v nl:401,421,424,430,442,449,484s sd0:359s,367,382v,392,359v,374,393s,400 sd1:366s,381,402s,444 sd2:380s,394,424v,438 sd3:366v,407,444v,459 pl:468,470,488s cand:440,460,463,465,585s,598,605s,611,617,627s A0:85,119,129 A1:117,141,151,160,222,262 A2:101,189,198,210,252 A3:163,221,238,245,269 At:275,291,304,311 put:315,324,335v,324s,337,383 gv:340v,328s,333,343v,358g,365,424 vA:332s,340s ue:347g,365 B0:105s,125,197,206 B1:93s,106,213,226,234,285,326 B2:178s,190,259,279,295,348 B3:287,311,328,337,346 Bt:339,344,350,355,361,315,325,380,383 uf:353g,359",
+    1: "vB:8v,79s uc0:-8v,2s x0:0,10,19,30 m0:26,32,46,52 uc1:15s x1:32,48 m1:66,72,71,82 uc2:34s x2:52,70 m2:93,89 uc3:57s x3:76,110 m3:121,107,127,166s,126,94,139,161s cred:142 l0:131s,142 l1:154s,165 l2:177s,185 l3:170s,178 w0:173,173,185,206,219,222,225,229 w1:201,193,210,220,224,227,232,230 s3:234,242,244,246,254s,256s val:267,274,276s,278s,282s s4:258,261,252,260,265,262,271,268,276,275,280,271,282,286,289s,291s sc:305,310v,309s,314,363 names:235s,315,317,327s turn:209s,232g,312 host:290,305,311,319v cch:311s,300s,315s,305s vl:318,328,330s vm:324,350,390v nl:405,436,438,444,466,472,489s sd0:368v,385,394v,455,368s,392,408s,418 sd1:375s,398,409s,458 sd2:388s,411,437s,457 sd3:375v,418,443s,456 pl:461,464,493s cand:459,478,481,483,583s,589,607s,615,621,636s A0:131,146,157 A1:110,138,149,166,222,274 A2:98,184,193,202,243 A3:207,239,252,288,291 At:284,295,310,317 put:320,329,336s,329g,355,401 gv:347s,333s,337,350s,381g,388,447 vA:338s,339v ue:365g,371 B0:98s,111,218,233 B1:119s,132,226,245,253,304,345 B2:197s,212,263,278,287,329 B3:294,319,333,348,351 Bt:344,349,354,360,380,332,353,388,391 uf:370g,377",
+    2: "vB:-24v,-13v uc0:-18s,-8s x0:0,12,7,19 m0:27,33,32,37 uc1:-1s x1:14,38 m1:53,60,57,70 uc2:25s x2:40,61 m2:75,80 uc3:47s x3:62,77 m3:101,81,106,140s,96,93,118,145s cred:191 l0:126s,137 l1:133s,144 l2:150s,163 l3:157s,170 w0:158,152,164,193s,202,205,207,215,212 w1:178,178,190,198s,203,206,210,213,216 s3:219,226,228,230,238s,230s val:237,239,241s,247s,243s s4:242,244,236,244,249,246,254,251,260,255,263,258,266,269,272s,274s sc:283,288v,288s,299,347 names:218s,267,269,318s turn:80g,-43g,290 host:273,305,654 cch:297s,283s,309g,314s vl:310,317,321s vm:338,369,385v nl:394,421,423,429,435,448,483v sd0:352s,360,373v,389,372s,381,389v,402 sd1:359s,388,400s,417 sd2:379s,400,420s,435 sd3:352v,407,436v,442 pl:444,459,516s cand:446,455,457,537,601s,609,616s,622,628,640s A0:105,118,151 A1:84,98,117,159,213,258 A2:125,180,194,203,248 A3:182,221,261,271,274 At:270,294,304,312s,315 put:318,329,334s,328g,342,388 gv:329v,327s,332,371v,352g,374,433 vA:335s,332v ue:384g,444 B0:86s,99,208,229 B1:106s,119,200,218,238,289,332 B2:169s,181,250,292,318,365 B3:276,289,299,326,341 Bt:315,323,344,370,376,321,374,383,386 uf:358g,447",
+    3: "vB:-13v,69s uc0:-27v,-10s x0:0,12,7,19 m0:28,33,34,40 uc1:-1s x1:15,37 m1:53,60,57,70 uc2:24s x2:40,60 m2:75,84 uc3:46s x3:62,81 m3:112,81,137,163s,116,93,122,158s l0:124s,152 l1:139s,159 l2:174s,185 l3:168s,179 w0:174,167,180,210s,220,223,226,235,231 w1:200,193,210,218s,222,225,228,232,233 out:284,340,361 s3:237,250,252,254,262s,265s val:264,281,283s,285s,289s s4:266,268,260,268,273,270,278,277,284,284,298,287,301,304,307s,309s host:307,310,313 cch:318v,332s,323g,327s yc:339,353,356,359,363v,365v,368,371 yh:336s,362,366s,372 A0:88,131,166 A1:100,116,145,175,231,283 A2:121,181,192,201,242 A3:133,221,236,275,282 At:243,288,318,325s,328 put:331 B0:102s,114,189,205 B1:90s,103,202,212,221,272,313 B2:146s,159,229,242,252,314 B3:252,266,290,308,311 Bt:302,323,329,334,348,342,347,355,358",
+}
+BANKS = "4657446675767426466670020754776676464776456446660002756200077020075477660664757674234666200475402005600205747766267674746756644402042710204060202576764656720027200047"
 f32, f16, i32, u16, bf = "float32", "float16", "int32", "uint16", "bfloat16"
+NN = (16 * NB, 448 - 16 * NB)
 SB = {
     "uw": ([128, UE], f32), "cc": ([128, C0 + NV + NG], f32), "vw0": ([128, 4096], f32), "vw1": ([128, 4096], f32),
     "tli": ([128, NV], i32), "lsw": ([128, 2, 896], i32), "ftr": ([128, 14, 32], f16), "tlt": ([128, 14, 32], f16),
     "tt": ([128, 8192], f32), "uu": ([128, 4096], f32), "gg": ([128, 4096], f16),
-    "q0": ([128, 3584], f32), "q1": ([128, 3584], f32), "c1": ([128, 512], f32), "hi1": ([128, 448], f32),
-    "uexp": ([128, 2, 896], f32),
+    "q0": ([128, 4, 4 * NN[0]], f32), "q1": ([128, 4, 4 * NN[1]], f32), "ue0": ([128, PER[0] * NN[0]], f32), "ue1": ([128, PER[1] * NN[1]], f32),
+    "oc": ([128, NN[1]], f32), "mk": ([128, NN[1]], f32), "bz32": ([128, 144], f32), "yci": ([128, 112], i32), "c1": ([128, 512], f32),
     "sdi": ([128, 112], i32), "nri": ([128, 112], i32), "sdf": ([128, 112], f32), "nrf": ([128, 112], f32), "cb": ([128, 112], f16),
     "hsi": ([128, 512], i32), "hsf": ([128, 16, 32], f16), "thr": ([128, 4], f32), "nth": ([128, 4], f32),
     "hw": ([128, 32], f32), "hix": ([128, 32], u16), "hw16": ([128, 32], f16),
-    "nmh": ([128, 256], f16), "nix": ([128, 2, 256], u16), "jm": ([128, 16], f32), "n32m": ([128, 128], f32), "mk": ([128, 224], f32),
+    "nmh": ([128, 256], f16), "nix": ([128, 2, 256], u16), "jm": ([128, 16], f32), "n32m": ([128, 128], f32),
     "uix": ([128, 256], u16), "sg": ([128, 256], f16), "lix": ([128, 256], u16), "cab": ([128, 512], f16),
     "sel": ([128, 2, 2, 128], f16), "r8": ([128, 2, 144], f16), "cw16": ([128, 16], f16), "zl": ([128, 16], f32), "cand": ([128, 512], f16), "clw": ([128, 32], f32), "cv": ([128, 32], f32),
     "dd": ([128, 256], f32), "ud": ([128, 512], f16), "rb": ([128, 256], f32), "cz": ([128, 256], f16), "zs": ([128, 256], f32),
     "cw": ([128, 16], f32), "vlx": ([128, 16], u16), "cbg": ([128, 112], f16), "rowsh": ([128, 2, 128], f16),
     "idl": ([128, 256], f16), "tg": ([128, 256], f32), "rs0": ([128, 256], f32), "cdg": ([128, 256], f16), "tgx": ([128, 16], u16), "val": ([128, 256], f32),
-    "h1": ([128, 16], f32), "eq": ([128, 4096], f16),
+    "h1": ([128, 16], f32), "eq": ([128, 4096], f16), "eqd": ([128, 256], f16),
     "f0": ([128, 224], f32), "vix": ([128, 224], u16), "sgw": ([128, 28], f16), "six0": ([128, 448], u16), "six1": ([128, 448], u16),
     "sc": ([128, 256], f32), "su": ([128, 256], f32), "sv": ([128, 512], f32),
     "yc1": ([128, 112], f32), "yc2": ([128, 112], f32),
@@ -67,25 +56,22 @@ SB = {
     "i32m": ([128, 128], f32), "i16m": ([128, 128], f16), "i4": ([128, 128], f16), "bz": ([128, 144], f16),
     "pk": ([128, 4], i32), "pm": ([128, 128], f32), "b32": ([128, 144], f32),
     "b162": ([128, 144], f16), "cch0": ([128, NV], f16), "cch1": ([128, NV], f16), "i4k": ([128, 2, 128], f16), "tab8": ([128, 256], f32), "b16": ([128, 144], f16), "b16h": ([128, 144], f16), "bsum": ([128, 144], f16),
-    "b8": ([128, 144], f16), "blk": ([128, 128], f16), "blk2k": ([128, 128], f16), "lo8": ([128, 152], f16), "hi8": ([128, 152], f16),
+    "b8": ([128, 144], f16), "blk": ([128, 128], f16), "blk2k": ([128, 128], f16), "blk4k": ([128, 128], f16), "lo8": ([128, 152], f16), "hi8": ([128, 152], f16),
     "y8": ([128, 2, 128], f16), "ee": ([128, 2, 128], f16), "t1": ([128, 128], f32), "t2": ([128, 256], f32),
     "rowb": ([128, 2048], f16), "tri": ([128, 2048], f16), "mm": ([128, 4, 128], f16),
     "tab8h": ([128, 256], f16), "tab16": ([128, 256], f32), "tab16h": ([128, 256], f16),
     "jw": ([128, 224], f32), "t128": ([128, 32], f32),
 }
-SCRATCH = {k: ("sbuf", s, d) for k, (s, d) in SB.items()}
+SPARE = ("rb", "cand", "blk2k", "ee", "oc", "bz32", "yci", "n32m")
+SCRATCH = {k: ("sbuf", s, d) for k, (s, d) in SB.items() if k not in SPARE}
 SCRATCH["ps"] = ("psum", [128, 4096], f32)
 IO = {"tl": [128, NV], "sd": [8, NV], "nr": [8, NV], "hs": [8, NS], "u0": [128, NV], "w0": [128, 1024], "th": [128, 1],
       "yu": [128, NV], "ys": [128, 1024], "yc": [8, NV], "yh": [8, NS]}
 SEMAPHORES = (["v", "s", "p", "gq"] + ["d%d" % i for i in range(114)] + ["a%d" % i for i in range(16)] + ["l%d" % i for i in range(16)])
 
-PLAN = {"cy": 0.85e-3, "gam": 1.5, "sig": 3.5, "gi": 1.0, "dl": 2.0, "dr": 220e3, "hop": 0.1, "rl": 1.8, "rr": 100e3, "first": 3.0, "row": 0.03, "pe": 1.4, "load": 1.3}
-PLANS = [PLAN, dict(PLAN, cy=0.84e-3, gam=1.2, sig=2.5, pe=1.45, dl=2.3, dr=165e3, rl=2.3, rr=80e3, row=0.04, gi=1.1, hop=0.13, first=4.0),
-         dict(PLAN, cy=1.2e-3, gam=2.0, sig=5.0)]
-PHASES = ((6000, 0.5, 1), (14000, 0.5, 4), (14000, 0.4, 5), (12000, 0.3, 6), (10000, 0.2, 5))
-TWINS = 0.6
-SEED = 1
-WIDE, NARROW, ANY = ((0, 1), (2, 3)), ((4,), (5,), (6,), (7,)), ((4,), (5,), (6,), (7,), (0,), (1,), (2,), (3,))
+PLAN = {"cy": 0.83e-3, "gam": 1.5, "sig": 3.5, "gi": 1.0, "dl": 2.0, "dr": 220e3, "hop": 0.1, "rl": 1.8, "rr": 100e3, "first": 3.0, "row": 0.03,
+        "pe": 1.4, "load": 1.3, "ov": 0.0}
+WIDE, NARROW = ((0, 1), (2, 3), (4, 5)), ((6,), (7,), (4,), (5,), (0,), (1,), (2,), (3,))
 
 
 def V_(name, *idx):
@@ -96,8 +82,8 @@ def V_(name, *idx):
     pr = range(shape[0])[idx[0]]
     bits = np.zeros(int(np.prod(shape[1:])), np.uint8); bits[ar] = 1
     m = int.from_bytes(np.packbits(bits, bitorder="little").tobytes(), "little")
-    lo, hi = int(ar.min()) // 8 * 8, int(ar.max()) // 8 * 8 + 8
-    return {"n": name, "key": name, "i": idx, "m": m, "box": ((1 << (hi - lo)) - 1) << lo, "p": (pr[0], pr[-1] + 1), "c": int(ar.size), "off": None}
+    wide = np.zeros((bits.size + 7) // 8, np.uint8); wide[ar // 8] = 255
+    return {"n": name, "key": name, "i": idx, "m": m, "box": int.from_bytes(wide.tobytes(), "little"), "p": (pr[0], pr[-1] + 1), "c": int(ar.size), "off": None}
 
 
 S_ = slice
@@ -136,6 +122,8 @@ def build(opt, engines, P):
         return len(pieces) - 1
 
     def add(eng, emit, rd, wr, cost, lat=None, kind="c", sem=None, after=(), ext=None, xf=0.0):
+        if eng in ("v", "s") and kind == "c":
+            cost += P["ov"]
         if probe[0]:
             return emit, cost
         me = len(ops); deps = set(after); acc = []; reads = set(); firm = set(after)
@@ -202,7 +190,7 @@ def build(opt, engines, P):
         return add("v", lambda c: [c["g"].vector.tensor_copy(ap(c, out), ap(c, a))], [a], [out], vcost(out, [a], 1))
 
     def tt(out, a, b, op):
-        k = 1 if "ps" in (a["n"], b["n"]) else 1.5 if two(a) and two(b) and two(out) else 2
+        k = 1 if "ps" in (a["n"], b["n"]) else 2
         return add("v", lambda c: [c["g"].vector.tensor_tensor(ap(c, out), ap(c, a), ap(c, b), op)], [a, b], [out], vcost(out, [a, b], k))
 
     def ts(out, a, s1, op0, s2=None, op1=None):
@@ -246,11 +234,8 @@ def build(opt, engines, P):
         return either(e, ways)
 
     def lin(e, out, a, scale, bias, relu=False):
-        ways = {"s": lambda: act(out, a, F.Relu if relu else F.Identity, scale, bias),
-                "v": lambda: ts(out, a, bias, A.add, 0.0, A.max) if relu else ts(out, a, scale, A.mult, bias, A.add)}
-        if SB[out["n"]][1] == u16:
-            ways = {k: ways[k] for k in opt["u16"]}
-        return either(e if e in ways else "v", ways)
+        return either(e, {"s": lambda: act(out, a, F.Relu if relu else F.Identity, scale, bias),
+                          "v": lambda: ts(out, a, bias, A.add, 0.0, A.max) if relu else ts(out, a, scale, A.mult, bias, A.add)})
 
     def side(e, out, a):
         j = either(e, {"s": lambda: act(out, a, F.Sign, 1.0, -float(MID)), "v": lambda: ts(out, a, float(MID), A.is_gt, 0.5, A.subtract)})
@@ -321,6 +306,11 @@ def build(opt, engines, P):
 
     I32, I16, ROW0 = V_("i32m"), V_("i16m"), c2("rowb", 0, 128)
     WW = c2("uw", W0, U0)
+    CF = opt["cch"] == "f"
+    LATE = 4 * NN[0]
+
+    def cch(t, a, b, s=None):
+        return c2("cc", C0 + a, C0 + b, s) if CF else c2("cch%d" % (t % 2), a, b, s)
 
     dma("y", V_("sdi"), V_("sd"), 57344); dma("s", V_("nri"), V_("nr"), 57344)
     dma("y", V_("hsi", S_(0, 8), AL), V_("hs"), 16384)
@@ -353,18 +343,29 @@ def build(opt, engines, P):
     mov("s", V_("i4k", AL, 0, AL), I32, 4096.0); mov("s", V_("i4k", AL, 1, AL), I32, -4096.0)
     ts(V_("sdf"), V_("sdi"), 2.0, A.mult, -1.0, A.add); ts(V_("nrf"), V_("nri"), -1.0, A.mult, float(FAR), A.add)
     first = tt(V_("cb"), V_("sdf"), V_("nrf"), A.mult)
-    cl[0] = "sc0"; send([(V_("cb"), V_("cbg"))], None); cl[0] = "setup"
+    cl[0] = "sc0"; send([(V_("cb"), V_("cbg"))], None); cl[0] = "code"
     for b in range(4):
-        h = H(ANY)
+        h = H()
         mm([(ps(h, 112 * j, 112 * j + 112), c2("rowb", 128 * (4 * b + j), 128 * (4 * b + j) + 128), V_("cb"), True, True) for j in range(4)])
         if b == 3:
             act(c2("cc", C0 + 448 * b, C0 + 448 * b + 448), ps(h, 0, 448), F.Silu, 1.0, float(MID), P["load"])
         else:
             lin("sv"[b % 2], c2("cc", C0 + 448 * b, C0 + 448 * b + 448), ps(h, 0, 448), 1.0, float(MID))
-        lin("vs"[b % 2], c2("cch0", 448 * b, 448 * b + 448), ps(h, 0, 448), 1.0, float(MID))
+        if CF:
+            continue
+        if opt["cch0"] == "g":
+            mov("g", c2("cch0", 448 * b, 448 * b + 448), c2("cc", C0 + 448 * b, C0 + 448 * b + 448))
+        else:
+            lin("vs"[b % 2], c2("cch0", 448 * b, 448 * b + 448), ps(h, 0, 448), 1.0, float(MID))
 
     def send_shifted(way, name, own, ghost, n, stage, cr):
-        h = H(); hi = c2(stage, n, 2 * n)
+        hi = c2(stage, n, 2 * n)
+        if way == "d":
+            dmas("y", [(V_(stage, S_(0, 112), S_(n, 2 * n)), V_(name, S_(16, 128), S_(own + n, own + 2 * n))),
+                       (V_(stage, S_(112, 128), S_(n, 2 * n)), V_(name, S_(0, 16), S_(own + n, own + 2 * n))),
+                       (c2(stage, 0, n), c2(name, own, own + n))], 1024 * n)
+            return send([(V_(stage), c2(name, ghost, ghost + 2 * n))], cr)
+        h = H()
         mm([(ps(h, 0, n), V_("pm"), c2(name, own + n, own + 2 * n), True, True)])
         mov("s", hi, ps(h, 0, n))
         if way == "w":
@@ -383,20 +384,19 @@ def build(opt, engines, P):
     for par in range(2):
         mmg([(ps(h, 16 * par, 16 * par + 16), V_("b8", S_(0, 8), S_(16 - i, 144 - i)), V_("hsf", S_(0, 8), AL, 2 * i + par)) for i in range(16)], 16)
     lin("v", V_("hix"), ps(h, 0, 32), 1.0, 0.0); lin("v", V_("hw"), ps(h, 0, 32), 1.0, float(TOP + U0))
-    iota(V_("t2"), [[2, 2], [8, 128]], 0, 0); mov("g", V_("tab8h"), V_("t2")); lin("s", V_("tab8"), V_("t2"), 1.0, -0.5)
+    iota(V_("t2"), [[2, 2], [8, 128]], 0, 0); mov("g", V_("tab8h"), V_("t2")); iota(V_("tab8"), [[2, 2], [8, 128]], 0, 0)
     iota(V_("jw"), [[-8, 224]], W0 - U0, 0)
     ts(c2("pk", 0, 1), c2("pi", 0, 1), 1, A.bitwise_and); ts(KZ, c2("pk", 0, 1), 1.0 - 4 * MID, A.mult, 2.0 * (MID + FAR), A.add)
     ts(c2("pk", 1, 2), c2("pi", 0, 1), 1, A.arith_shift_right, 7, A.bitwise_and); cp(KR, c2("pk", 1, 2))
     ts(V_("jw"), V_("jw"), KZ, A.add, KR, A.subtract)
-    tt(c2("bz", 1, 144), c2("b162", 1, 144), c2("b162", 0, 143), A.subtract)
+    tt(c2("bz32" if CF else "bz", 1, 144), c2("b162", 1, 144), c2("b162", 0, 143), A.subtract)
     iota(V_("jm"), [[-16, 16]], TOP + 255, 0); iota(V_("rs0"), [[0, 256]], 1000000, 0); ts(c2("rs0", 0, 256, 16), V_("jm"), PM, A.subtract)
     iota(V_("dd"), [[0, 16], [1, 16]], 0, 0); ts(V_("cdg"), V_("dd"), PM, A.is_equal, float(TOP + G0), A.mult)
     ts(PB, PD, 16.0, A.mult); ts(V_("bsum"), c2("xr", 0, 144), PB, A.is_equal, -2048.0, A.mult)
-    iota(V_("tab16"), [[4, 2], [0, 4], [16, 32]], 1536, 0); mov("g", V_("tab16h"), V_("tab16"))
-    iota(c2("uw", 0, W0), [[0, 256]], 0, 0); iota(c2("cc", 0, W0), [[0, 256]], 0, 0)
+    iota(V_("tab16"), [[4, 2], [0, 4], [16, 32]], 768, 0); mov("g", V_("tab16h"), V_("tab16"))
+    iota(c2("tt", 0, 512), [[0, 512]], 0, 0)
+    dmas("y", [(c2("tt", a, a + 512), c2("tt", 0, 512)) for a in (2048, 4096, 6144)] + [(c2(k, 0, W0), c2("tt", 0, W0)) for k in ("uw", "cc")], 1048576)
     iota(c2("cc", W0, U0, 2), [[1, 512]], MID - FAR, 0); iota(c2("cc", W0 + 1, U0, 2), [[-1, 512]], MID + FAR, 0)
-    for j in range(4):
-        iota(c2("tt", 2048 * j, 2048 * j + 512), [[0, 512]], 0, 0)
     if opt["cz"] == "v":
         mov("s", V_("blk2k"), V_("blk"), -2048.0)
         asel(V_("ee", AL, 0, AL), V_("blk"), [[16, 8], [0, 16]], A.is_ge, 0.0, 7, -1)
@@ -406,9 +406,9 @@ def build(opt, engines, P):
             ts(V_("r8", AL, e, AL), c2("xr", 0, 144), PB, A.is_equal, half, A.mult)
     ts(c2("nth", 0, 1), c2("thr", 0, 1), -1.0, A.mult)
     ts(c2("pj", 2, 3), c2("pi", 0, 1), 2, A.arith_shift_right, 1, A.bitwise_and); cp(ZB, c2("pj", 2, 3))
-    ts(KV, ZB, -1540.0, A.mult, PM, A.add)
+    ts(KV, ZB, -4.0, A.mult, PM, A.add)
     iota(V_("t128"), [[2, 2], [64, 16]], 0, 0); ts(ZV, PM, 4.0, A.mult)
-    if opt["dd"] == "p":
+    if CF or opt["dd"] == "p" or "p" in opt["fin"]:
         mov("s", V_("n32m"), I32, -1.0)
     for part in range(2):
         iota(c2("tz", 128 * part, 128 * part + 128), [[0, 16], [1024 << part, 2], [0, 4]], -(512 << part), 0)
@@ -419,8 +419,10 @@ def build(opt, engines, P):
     asel(V_("y8", AL, 1, AL), V_("t1"), [[8, 16], [0, 8]], A.is_ge, 0.0, 7, -1)
     asel(V_("t1"), V_("t1"), [[1, 128]], A.is_gt, 0.0, 0, -1)
     asel(V_("y8", AL, 0, AL), V_("t1"), [[-1, 128]], A.not_equal, 1.0, 0, 1)
+    if opt["diag"]:
+        mov("s", V_("blk4k"), V_("blk"), -4096.0)
     for i in range(1, 16):
-        asel(c2("tri", 128 * i, 128 * i + 128), V_("blk"), [[16, 8], [0, 16]], A.is_ge, 0.0, i - 1, -1)
+        asel(c2("tri", 128 * i, 128 * i + 128), V_("blk4k" if opt["diag"] else "blk"), [[16, 8], [0, 16]], A.is_ge, 0.0, i - 1, -1)
     for a in range(4):
         dmas("y", [(V_("lsw", S_(32 * a + 16 * r1, 32 * a + 16 * r1 + 16), h, AL),
                     V_("tl", S_(32 * a + 16 * h, 32 * a + 16 * h + 16), S_(896 * r1, 896 * r1 + 896))) for r1 in range(2) for h in range(2)], 229376, [first])
@@ -428,7 +430,7 @@ def build(opt, engines, P):
     def turn(t):
         cl[0] = "turn"
         for h in range(2):
-            mov(opt["ftr"], V_("ftr", AL, AL, S_(16 * h, 16 * h + 16)), V_("lsw", AL, h, S_(t, 896, 4)))
+            mov("g", V_("ftr", AL, AL, S_(16 * h, 16 * h + 16)), V_("lsw", AL, h, S_(t, 896, 4)))
         tr(V_("tlt"), V_("ftr"))
 
     def names(t):
@@ -442,45 +444,45 @@ def build(opt, engines, P):
         return [(ps(h, a, a + 128), sel(("lo8", "hi8")[part], 8 * (e - part)), c2("nmh", e, 256, 2)) for e in range(2)]
 
     def half_codes(t):
-        cl[0] = "cch"
-        for j in range(4):
-            mov("g", c2("cch%d" % (t % 2), 448 * j, 448 * j + 448), c2("cc", C0 + 448 * j, C0 + 448 * j + 448))
+        cl[0] = "cch"; cuts = (0,) + O("parts", t - 1)
+        for a, b in zip(cuts, () if CF else cuts[1:]):
+            mov("g", c2("cch%d" % (t % 2), a, b), c2("cc", C0 + a, C0 + b))
 
     def view_lists(t):
         cut = O("cut", t - 1)
         for name, a, b in (("vl", 0, cut), ("vm", cut, NV)):
             if a < b:
                 cl[0] = name; x = ps(H(), 0, (b - a) // 8); f0 = c2("f0", a // 8, b // 8)
-                mmg([(x, sel("bz", 2 * i), c2("cch%d" % (t % 2), a + i, b, 8)) for i in range(8)], 8)
+                mmg([(x, sel("bz32" if CF else "bz", 2 * i), cch(t, a + i, b, 8)) for i in range(8)], 8)
                 tt(f0, x, c2("jw", a // 8, b // 8), A.max); lin("v", c2("vix", a // 8, b // 8), f0, -1.0, KZ)
-
-    def slots(t, r):
-        return range(8) if O("tree" + "AB"[r], t)[0] == "X" else SPINE
 
     def node_lists(t):
         cl[0] = "nl"; h = H()
-        mmg([(ps(h, 0, 28), sel("b16", i), c2("cch%d" % (t % 2), 4 * i + t, NV, 64)) for i in range(16)], 16)
+        mmg([(ps(h, 0, 28), sel("b32" if CF else "b16", i), cch(t, 4 * i + t, NV, 64)) for i in range(16)], 16)
         act(V_("sgw"), ps(h, 0, 28), F.Sign, 1.0, -float(MID))
-        h = H(); lst = []
-        for r in range(2):
-            for k in range(16):
-                a = 224 * r + 28 * slots(t, r)[k // 2] + 14 * (k % 2); o = ps(h, a, a + 14)
-                lst.append((o, I16, c2("sgw", 14 * r, 14 * r + 14), True, False))
-                lst.append((o, V_("i4"), V_("tlt", AL, AL, 16 * r + k), False, True))
-        for j in range(0, 64, 16):
-            mm(lst[j:j + 16])
+        h = H()
+        for r, b0, b1, base in ((0, 0, NB, 0), (1, NB, 28, 16 * NB)):
+            lst = []
+            for j, k in enumerate(SLOTS[O("a4", t)[r] in "23"]):
+                a = base + (b1 - b0) * j - b0; runs = [(x, y) for x, y in ((b0, min(b1, 14)), (max(b0, 14), b1)) if x < y]
+                lst.append((ps(h, a + b0, a + b1), I16, c2("sgw", b0, b1), True, False))
+                for x, y in runs:
+                    lst.append((ps(h, a + x, a + y), V_("i4"), V_("tlt", AL, S_(x % 14, (y - 1) % 14 + 1), 16 * (x // 14) + k), False, y == b1))
+            n = len(lst) // 2
+            mm(lst[:n]); mm(lst[n:])
         lin("v", V_("six%d" % (t % 2)), ps(h, 0, 448), 0.5, 0.5)
 
     CH = ((0, 0), (1, 0), (0, 1), (1, 1))
 
     def sides(t):
         for j, (part, hf) in enumerate(CH):
-            cl[0] = "sd%d" % j
-            a = 128 * part + 64 * hf; h = H(); o = ps(h, 0, 64); b = a % 128 + 128 * (t % 2)
-            half = side("vs"[j % 2], c2("gg", 16 * a, 16 * (a + 64)), ind(c2("cc", C0, C0 + NV + NG), V_("nix", AL, t % 2, S_(a, a + 64))))
-            mmg([(o, half(k), c2("gg", 16 * a + k, 16 * (a + 64), 16)) for k in range(16)] + [(o, ROW0, c2("tab8h", b, b + 64))], 17)
-            lin("v", c2("uix", a, a + 64), o, 1.0, E4)
-            tt(c2("sg", a, a + 64), o, c2("tab8", b, b + 64), A.subtract)
+            cl[0] = "sd%d" % j; w = 32 if j in O("sdf", t) else 64
+            for a in range(128 * part + 64 * hf, 128 * part + 64 * hf + 64, w):
+                h = H(); o = ps(h, 0, w); b = a % 128 + 128 * (t % 2)
+                half = side("vs"[(j + a // 32) % 2], c2("gg", 16 * a, 16 * (a + w)), ind(c2("cc", C0, C0 + NV + NG), V_("nix", AL, t % 2, S_(a, a + w))))
+                mmg([(o, half(k), c2("gg", 16 * a + k, 16 * (a + w), 16)) for k in range(16)] + [(o, ROW0, c2("tab8h", b, b + w))], 17)
+                lin("v", c2("uix", a, a + w), o, 1.0, E4)
+                tt(c2("sg", a, a + w), o, c2("tab8", b, b + w), A.subtract)
 
     def pair_lists():
         cl[0] = "pl"; h = H()
@@ -495,8 +497,7 @@ def build(opt, engines, P):
             for part in range(2):
                 a = 256 * z + 128 * part
                 mmg(minus_names(h, a, part) + [(ps(h, a, a + 128), V_("i4k", AL, z, AL), c2("sg", 128 * part, 128 * part + 128))])
-        for z in range(2):
-            lin("s", c2("cab", 256 * z, 256 * z + 256), ps(h, 256 * z, 256 * z + 256), 1.0, 1792.0 - 4096.0 * (1 - z), True)
+        lin("s", V_("cab"), ps(h, 0, 512), 1.0, 1792.0 - 2048.0, True)
         h = H(); Y = [V_("y8", AL, j, AL) for j in range(2)]
         mmg([(ps(h, 0, 512), Y[0], V_("cab"))] + [(ps(h, 256 * z + 128, 256 * z + 256), Y[1], c2("cab", 256 * z, 256 * z + 128)) for z in range(2)])
         x = ps(h, 0, 512)
@@ -512,117 +513,155 @@ def build(opt, engines, P):
         mmg([(ps(h, 0, 32), sel("b16", i), c2("cand", i, 512, 16)) for i in range(16)], 16)
         mov("s", V_("clw"), ps(h, 0, 32))
 
-    def views(t, a, b):
-        for lo, hi in ((a, (a + b) // 2), ((a + b) // 2, b)):
-            mov("s", c2("vw%d" % (t % 2), 2 * lo, 2 * hi), ind(c2("uw", W0, U0 + b), c2("vix", lo // 8, hi // 8)), -1.0)
+    def views(t, cuts):
+        for lo, hi in zip(cuts, cuts[1:]):
+            mov("s", c2("vw%d" % (t % 2), 2 * lo, 2 * hi), ind(c2("uw", W0, U0 + hi), c2("vix", lo // 8, hi // 8)), -1.0)
 
-    def ghost_views(t, cr):
-        cl[0] = "gv"; views(t, 0, 256)
+    def early_views(t, cr):
+        cl[0] = "gv"; views(t, (0, 128, 256))
         send_shifted(O("shift", t - 1)[2], "vw%d" % (t % 2), 0, 2 * NV, 256, "sv", cr)
+        cl[0] = "vA"; views(t, (256,) + tuple(x for x in opt["vcut"] if x < LATE) + (LATE,) if LATE > 256 else ())
+
+    def nodes(t, r):
+        return c2("uw", U0 + (LATE if r else 0) + t, G0 if r else U0 + LATE, 4)
 
     def old_values(t, r):
-        cl[0] = "ue" if r == 0 else "uf"
-        n = 4 if O("dma" + "AB"[r], t) else 2; part = [V_("uexp", AL, r, S_(224 * j, 224 * j + 224)) for j in range(n)]
-        for j in range(n if O("rep", t) == "g" else 1):
-            mov("g", part[j], c2("uw", U0 + 896 * r + t, U0 + 896 * r + 896, 4))
-        if O("rep", t) == "d":
-            dmas("y", [(x, part[0]) for x in part[1:]], 114688 * (n - 1))
+        cl[0] = "ue" if r == 0 else "uf"; n = NN[r]; ue = "ue%d" % r
+        mov("g", c2(ue, 0, n), nodes(t, r))
+        if O("rep", t) == "d" and PER[r] < 8:
+            return dmas("y", [(c2(ue, n * j, n * j + n), c2(ue, 0, n)) for j in range(1, PER[r])], 512 * n * (PER[r] - 1))
+        mov("g", c2(ue, n, 2 * n), nodes(t, r)); k = 2 * n
+        while k < PER[r] * n:
+            mov("g", c2(ue, k, 2 * k), c2(ue, 0, k)); k *= 2
 
     def step1(t, r):
-        win = c2("vw%d" % (t % 2), 0, 4096); tree = O("tree" + "AB"[r], t); ondma = O("dma" + "AB"[r], t)
-        def q(k, n=1, a=0, b=448): return c2("q%d" % r, 448 * k + a, 448 * (k + n - 1) + b)
-        def x(k, n): return ind(win, c2("six%d" % (t % 2), 224 * r + 28 * k, 224 * r + 28 * (k + n)))
-        def pair(i, j, mode):
-            h = H(WIDE); cl[0] = "AB"[r] + str(i); a, b = ps(h, 0, 448), ps(h, 448, 896)
-            if i in ondma:
-                mov("s", q(j, 2), x(j, 2)); dadd(q(j, 2), V_("uexp", AL, r, AL))
-            elif ondma:
-                tt(q(j, 2), x(j, 2), V_("uexp", AL, r, AL), A.add)
-            else:
-                for k in (j, j + 1):
-                    tt(q(k), x(k, 1), V_("uexp", AL, r, S_(0, 448)), A.add)
-            act(ps(h, 0, 896), q(j, 2), F.Abs)
-            if mode == "v":
-                tt(q(j + 1), q(j + 1), b, A.mult); tt(a, q(j), a, A.mult); tt(q(j), a, q(j + 1), A.add)
-            else:
-                tt(q(j, 2), q(j, 2), ps(h, 0, 896), A.mult)
-            if mode == "d":
-                dadd(q(j), q(j + 1))
-        hi = c2("hi1", 224 * r, 224 * r + 224)
-        if tree[0] == "X":
-            pair(0, 0, ""); pair(1, 4, ""); dadd(q(0, 2), q(4, 2))
-            pair(2, 2, ""); pair(3, 6, ""); dadd(q(2, 2), q(6, 2))
-            cl[0] = "AB"[r] + "t"; dadd(q(0, 2), q(2, 2)); lo = ps(H(), 0, 224)
-            if tree[1] == "d":
-                dadd(q(0), q(1)); dadd(q(0, 1, 0, 224), q(0, 1, 224, 448)); mov("s", lo, q(0, 1, 0, 224), -0.015625)
-            else:
-                h = H()
-                mmg([(ps(h, 0, 224), I32, q(k, 1, 224, 448)) for k in (0, 1)], 2); mov("s", hi, ps(h, 0, 224))
-                mmg([(lo, I32, q(k, 1, 0, 224)) for k in (0, 1)] + [(lo, I32, hi)], 2); mov("s", lo, lo, -0.015625)
+        win = c2("vw%d" % (t % 2), 0, 4096); way = O("way" + "AB"[r], t); a4 = O("a4", t)[r]; fold = t < opt["fold"]
+        n = NN[r]; per = PER[r]; ue = V_("ue%d" % r)
+        def q(a, b, regions=1):
+            if b - a > 4:
+                return V_("q%d" % r, AL, S_(a // 4, b // 4), AL)
+            cols = S_(a % 4 * n, ((b - 1) % 4 + 1) * n)
+            return V_("q%d" % r, AL, S_(a // 4, a // 4 + regions), cols) if regions > 1 else V_("q%d" % r, AL, a // 4, cols)
+        tree = O("tree" + "AB"[r], t); sums = [(8, q(4, 8), q(0, 4), tree[0])]
+        if len(tree) == 3:
+            sums += [(12, q(4, 6, 2), q(6, 8, 2), tree[1])]
+            sums += [(14, q(4, 5, 3), q(5, 6, 3), tree[2])] if a4 == "m" else [(12, q(4, 5, 2), q(5, 6, 2), tree[2])]
         else:
-            m15, m37, m4, m26 = tree
-            pair(0, 0, m15); pair(1, 2, m37)
-            if m4 == "d":
-                dadd(q(0), q(2))
+            sums += [(8, q(4, 6), q(6, 8), tree[1]), (8, q(4, 5), q(5, 6), tree[2]), (12, q(8, 10), q(10, 12), tree[3]), (12, q(8, 9), q(9, 10), tree[4])]
+        sums += [(14, q(12, 13), q(13, 14), "d")] if a4 == "d" else []
+        if a4 == "2":
+            sums = [(8, q(0, 2, 2), q(2, 4, 2), "d"), (8, q(0, 1, 2), q(1, 2, 2), "d"), (12, q(8, 10), q(10, 12), "d")]
+        if a4 == "3":
+            sums = [(4, q(0, 2), q(2, 4), "d"), (4, q(0, 1), q(1, 2), "d"), (8, q(4, 6), q(6, 8), "d"), (8, q(4, 5), q(5, 6), "d"), (12, q(8, 10), q(10, 12), "d")]
+        for j, a in enumerate(range(0, 16, per)):
+            b = a + per; h = H(WIDE if per * n > 512 else NARROW); cl[0] = "AB"[r] + str(j); k = 16 * NB * r + n // 16 * a
+            x = ind(win, c2("six%d" % (t % 2), k, k + n // 16 * per))
+            if way[j] == "p":
+                cuts = [(y, min(y + 512, per * n)) for y in range(0, per * n, 512)]; c0 = a % 4 * n
+                for y, z in cuts:
+                    mm([(ps(h, y, z), I32, c2("ue%d" % r, y, z), True, False)])
+                mov("s", q(a, b), x)
+                for y, z in cuts:
+                    mm([(ps(h, y, z), I32, V_("q%d" % r, AL, a // 4, S_(c0 + y, c0 + z)), False, True)])
+                act(q(a, b), ps(h, 0, per * n), F.Abs, 0.015625 if fold else 1.0)
             else:
-                tt(q(0), q(0), q(2), A.add)
-            pair(2, 4, ""); pair(3, 6, m26); cl[0] = "AB"[r] + "t"
-            h = H()
-            if O("tail", t)[r] == "p":
-                mmg([(ps(h, 0, 224), I32, q(k, 1, 224, 448)) for k in (4, 5, 6, 0)], 2); mov("s", hi, ps(h, 0, 224))
-                lo = ps(H(), 0, 224)
-                mmg([(lo, I32, q(k, 1, 0, 224)) for k in (4, 5, 6, 0)] + [(lo, I32, hi)], 2)
+                if way[j] == "s":
+                    mov("s", q(a, b), x); dadd(q(a, b), ue)
+                else:
+                    tt(q(a, b), x, ue, A.add)
+                act(ps(h, 0, per * n), q(a, b), F.Abs, 0.015625 if fold else 1.0)
+            if tree[0] == "x" and a == 0:
+                x = ps(h, 0, 4 * n)
+                tt(q(4, 8), q(4, 8), ps(h, 4 * n, 8 * n), A.mult); tt(x, q(0, 4), x, A.mult); tt(q(4, 8), x, q(4, 8), A.add); sums.pop(0)
+            elif a4 == "v" and a <= 12 < b:
+                for x, y in ((a, 12), (13, b)):
+                    if x < y:
+                        tt(q(x, y), q(x, y), ps(h, (x - a) * n, (y - a) * n), A.mult)
+                x = ps(h, (12 - a) * n, (13 - a) * n)
+                tt(x, q(12, 13), x, A.mult); tt(q(12, 13), x, q(13, 14), A.add)
             else:
-                lo = ps(h, 0, 224)
-                mmg([(ps(h, 0, 448), I32, q(k)) for k in (4, 5, 6, 0)], 1)
-                mov("s", hi, ps(h, 224, 448)); tt(lo, lo, hi, A.add)
-            if r and O("mask", t):
-                h = H(); x = ps(h, 0, 224); u = c2("uw", U0 + 896 + t, G0, 4)
-                mmg([(x, V_("i4k", AL, k, AL), c2("cch%d" % ((t + k) % 2), 896 + t, NV, 4)) for k in range(2)])
-                ts(V_("mk"), x, 0.0, A.is_equal, -0.015625, A.mult); tt(lo, lo, V_("mk"), A.mult)
-                return tt(u, lo, u, A.add)
-            mov("s", lo, lo, -0.015625)
-        tt(c2("uw", U0 + 896 * r + t, U0 + 896 * r + 896, 4), lo, V_("uexp", AL, r, S_(0, 224)), A.add)
-
-    def claimed_values():
-        cp(ind(c2("uw", 0, G0), V_("tgx")), V_("val"))
+                tt(q(a, b), q(a, b), ps(h, 0, per * n), A.mult)
+            while sums and sums[0][0] <= b:
+                k, x, y, mode = sums.pop(0)
+                if mode == "d":
+                    dadd(x, y)
+                elif mode == "D":
+                    dadd(q(4, 6), q(0, 2)); dadd(q(6, 8), q(2, 4))
+                elif mode == "p":
+                    z = ps(H(), 0, x["c"]); mmg([(z, I32, x), (z, I32, y)], 1); mov("s", x, z)
+                else:
+                    tt(x, x, y, A.add)
+        cl[0] = "AB"[r] + "t"; lo = ps(H(), 0, n); u = nodes(t, r); old = c2("ue%d" % r, 0, n)
+        spine = [q(k, k + 1) for k in (14, 15, 12, 8, 4)]
+        if a4 in "23":
+            x = ps(H(), 0, n); mmg([(x, I32, q(k, k + 1)) for k in (12, 13, 8, 0)], 2 - r); mov("s", q(1, 2), x)
+            spine = [q(k, k + 1) for k in (14, 15, 9, 4, 1)]
+        if r and not O("once", t):
+            mmg([(lo, I32, x) for x in spine], 1)
+            x = ps(H(), 0, n)
+            if CF:
+                mmg([(x, I32, V_("oc")), (x, V_("n32m"), cch(t + 1, LATE + t, NV, 4))])
+            else:
+                mmg([(x, V_("i4k", AL, k, AL), cch(t + k, LATE + t, NV, 4)) for k in range(2)])
+            ts(V_("mk"), x, 0.0, A.is_equal, -1.0 if fold else -0.015625, A.mult); tt(lo, lo, V_("mk"), A.mult)
+            tt(u, lo, u, A.add)
+        elif fold and O("fin", t)[r] == "p":
+            mmg([(lo, V_("n32m"), x) for x in spine] + [(lo, I32, old)], 2 - r); mov("s", u, lo)
+        elif fold:
+            mmg([(lo, I32, x) for x in spine], 2 - r); tt(u, old, lo, A.subtract)
+        else:
+            mmg([(lo, I32, x) for x in spine], 2 - r); mov("s", lo, lo, -0.015625); tt(u, lo, old, A.add)
 
     def lists(t):
         view_lists(t); node_lists(t); sides(t); pair_lists(); candidates()
 
+    def votes(a, b, par):
+        n0, n1 = [c2("uw", W0 + 4 * a + 2 * par + z, W0 + 4 * b, 4) for z in range(2)]
+        if opt["dd"] == "p":
+            dd = ps(H(), 0, b - a); mmg([(dd, I32, n0), (dd, V_("n32m"), n1)])
+        else:
+            dd = c2("dd", a, b); tt(dd, n0, n1, A.subtract)
+        ts(c2("ud", a, b), dd, c2("thr", 0, 1), A.is_gt, 0.5, A.subtract)
+        ts(c2("ud", 256 + a, 256 + b), dd, c2("nth", 0, 1), A.is_lt, 0.5, A.subtract)
+
     names(0); turn(0); lists(0)
-    ghost_views(0, None); cl[0] = "vA"; views(0, 256, 896); old_values(0, 0); old_values(0, 1)
+    early_views(0, None); old_values(0, 0); old_values(0, 1)
     cr = None
     for t in range(RO):
-        par = t % 2; last = t == RO - 1; cl[1] = t
-        cl[0] = "vB"; views(t, 896, NV)
+        par = t % 2; last = t == RO - 1; cl[1] = t; fold = t < opt["fold"]; once = O("once", t)
+        cl[0] = "vB"; views(t, (LATE,) + tuple(x for x in opt["vcut"] if x > LATE))
+        if CF and not once:
+            cl[0] = "oc"; mov("g", V_("oc"), c2("cc", C0 + LATE + t, C0 + NV, 4))
+        held = {}
         for j, (part, hf) in enumerate(CH):
-            a = 128 * part + 64 * hf; h = H(WIDE); w = 32 if j in opt["fine"] else 64
+            a = 128 * part + 64 * hf; h = H(WIDE); w = 32 if j in O("fine", t) else 64
             for b in range(a, a + 64, w):
                 uu = c2("uu", 16 * b, 16 * (b + w))
                 cl[0] = "uc%d" % j
                 mov("s", uu, ind(WW, c2("uix", b, b + w)))
                 cl[0] = "x%d" % j
                 tt(uu, ind(c2("uw", U0, UE), V_("nix", AL, par, S_(b, b + w))), uu, A.subtract)
-                act(ps(h, 16 * (b - a), 16 * (b - a + w)), uu, F.Abs)
+                act(ps(h, 16 * (b - a), 16 * (b - a + w)), uu, F.Abs, 0.015625 if fold else 1.0)
             for i in range(2):
                 t0 = 2048 * (2 * hf + i); mode = O("pair", t)[2 * hf + i]; cl[0] = "m%d" % j
                 lo, hi, sm = [c2("tt", t0 + 512 * k, t0 + 512 * k + 512) for k in (1, 2, 3)]
                 st = ps(h, 512 * i, 512 * i + 512); di = c2("uu", 16 * a + 512 * i, 16 * a + 512 * i + 512)
-                if part == 0:
+                if part == 0 and mode == "y":
+                    tt(st, di, st, A.mult); mov("s", lo, st); held[i] = st
+                elif part == 0:
                     tt(lo, di, st, A.mult)
                     if mode == "d":
                         dma("y", sm, lo, 262144)
-                    elif mode == "g":
-                        mov("g", sm, lo)
                 elif mode == "x":
                     tt(st, di, st, A.mult); tt(sm, st, lo, A.add); mov("s", hi, st)
                 else:
                     tt(hi, di, st, A.mult)
-                    if mode in "dg":
+                    if mode == "d":
                         dadd(sm, hi)
+                    elif mode == "y":
+                        tt(sm, held[i], hi, A.add)
                     else:
-                        h2 = H(ANY)
+                        h2 = H()
                         mmg([(ps(h2, 0, 512), I32, lo), (ps(h2, 0, 512), I32, hi)], 1)
                         mov("s", sm, ps(h2, 0, 512))
         if not last:
@@ -643,50 +682,55 @@ def build(opt, engines, P):
                 tt(cc1, c2("uu", a + 1, b, 4), c2("uu", a + 3, b, 4), A.add)
             h = H(); o = ps(h, 0, n)
             mmg([(o, I32, c2("uu", a, b, 4)), (o, I32, c2("uu", a + 2, b, 4)), (o, I32, cc1)], 2)
-            mov("s", o, o, 0.015625)
+            if not fold:
+                mov("s", o, o, 0.015625)
             for z in range(2):
                 w = c2("uw", W0 + 256 * qa + 2 * par + z, W0 + 256 * qb, 4)
                 tt(w, ps(h, z, n, 2), w, A.add)
+            if opt["dd"] == "g":
+                votes(64 * qa, 64 * qb, par)
         if last:
             cl[0] = "out"; dma("y", V_("ys"), WW, 524288)
         cl[0] = "s3"
-        n0, n1 = c2("uw", W0 + 2 * par, U0, 4), c2("uw", W0 + 2 * par + 1, U0, 4)
-        if opt["dd"] == "p":
-            dd = ps(H(), 0, 256); mmg([(dd, I32, n0), (dd, V_("n32m"), n1)])
-        else:
-            dd = V_("dd"); tt(dd, n0, n1, A.subtract)
-        ts(c2("ud", 0, 256), dd, c2("thr", 0, 1), A.is_gt, 0.5, A.subtract)
-        ts(c2("ud", 256, 512), dd, c2("nth", 0, 1), A.is_lt, 0.5, A.subtract)
+        if opt["dd"] != "g":
+            votes(0, 256, par)
         if opt["cz"] == "v":
             hv = H(); up, dn = ps(hv, 0, 256), ps(hv, 256, 512)
             mm([(ps(hv, 0, 512), V_("blk2k"), V_("ud"), True, True)])
         h = H()
         mmg([(ps(h, 0, 32), sel("bsum", i), c2("ud", i, 512, 16)) for i in range(16)], 16)
         tt(V_("cv"), ps(h, 0, 32), V_("clw"), A.max)
+        tt(V_("cw16"), c2("cv", 0, 16), c2("cv", 16, 32), A.min)
         if opt["cz"] == "v":
             tt(V_("rb"), dn, c2("cand", 256, 512), A.max); tt(up, up, c2("cand", 0, 256), A.max); tt(V_("cz"), up, V_("rb"), A.min)
         else:
-            tt(V_("cw16"), c2("cv", 0, 16), c2("cv", 16, 32), A.min); hz = H()
+            hz = H()
             mm([(ps(hz, i, 256, 16), c2("rowb", 128 * i, 128 * i + 128), V_("cw16"), True, True) for i in range(16)])
             mov("s", V_("cz"), ps(hz, 0, 256))
-        tt(V_("cw"), c2("cv", 0, 16), c2("cv", 16, 32), A.min)
+        mov("v", V_("cw"), V_("cw16"))
         cl[0] = "val"
         ts(V_("zl"), ps(h, 16, 32), 0.0, A.is_lt, ZV, A.add); tt(V_("zl"), V_("zl"), c2("t128", 16 * par, 16 * par + 16), A.add)
         lin("s", V_("vlx"), V_("zl"), 1.0, 0.0)
         mov("s", V_("zs"), ind(c2("cc", W0, U0), V_("vlx"))); mov("s", V_("val"), ind(WW, V_("vlx")))
-        cl[0] = "s4"; h = H(); y = ps(h, 0, 256)
+        cl[0] = "s4"; h = H(); y = ps(h, 0, 256); d0 = 16 if opt["diag"] else 0
         ts(V_("idl"), V_("cz"), 0.0, A.is_ge, -32768.0, A.mult)
-        mm([(y, I16, V_("cdg"), True, False), (y, I16, V_("cz"), False, False)])
-        for a0 in range(0, 16, 4):
+        mm([(y, I16, V_("cdg"), True, False), (y, I16, V_("cz"), False, False), (y, I16, V_("idl"), False, False)])
+        def same_block(src, step, stop):
+            mm([(ps(h, i, 256, 16), c2("tri", 128 * i, 128 * i + 128), c2(src, i, 16 * step, step), False, stop and i == 15) for i in range(1, 16)])
+        if d0:
+            hd = H()
+            mm([(ps(hd, i, 256, 16), I16, V_("cw16"), True, True) for i in range(16)])
+            tt(V_("eqd"), ps(hd, 0, 256), V_("cz"), A.is_equal); same_block("eqd", 16, False)
+        for a0, a1 in ((0, 4), (4, 8), (8, 12), (12, 16 - d0 // 16)):
             probe[0] = True
-            four = [ts(c2("eq", 256 * a, 256 * a + 256 - 16 * a), c2("cz", 16 * a, 256), c2("cw", a, a + 1), A.is_equal, -4096.0, A.mult)
-                    for a in range(a0, a0 + 4)]
+            four = [ts(c2("eq", 256 * a + d0, 256 * a + 256 - 16 * a), c2("cz", 16 * a + d0, 256), c2("cw", a, a + 1), A.is_equal, -4096.0, A.mult)
+                    for a in range(a0, a1)]
             probe[0] = False
             add("v", lambda c, four=four: [x for f, k in four for x in f(c)], [V_("cz"), V_("cw")], [c2("eq", 256 * a0, 256 * a0 + 1024)],
                 sum(k for f, k in four))
-            mm([(ps(h, 16 * a + 16, 256), V_("blk"), c2("eq", 256 * a + 16, 256 * a + 256 - 16 * a), False, False) for a in range(a0, min(a0 + 4, 15))])
-        mm([(y, I16, V_("idl"), False, False)] +
-           [(ps(h, i, 256, 16), c2("tri", 128 * i, 128 * i + 128), c2("eq", i, 4096, 256), False, i == 15) for i in range(1, 16)])
+            mm([(ps(h, 16 * a + 16, 256), V_("blk"), c2("eq", 256 * a + 16, 256 * a + 256 - 16 * a), False, d0 > 0 and a == 14) for a in range(a0, min(a1, 15))])
+        if not d0:
+            same_block("eq", 256, True)
         scan(V_("tg"), V_("rs0"), y, 1e6, A.min, A.max)
         tgf = c2("tg", 15, 256, 16); lin("v", V_("tgx"), tgf, 1.0, -float(TOP))
         put_codes(ind(c2("cc", 0, C0 + NV), V_("tgx")), V_("zs"))
@@ -703,288 +747,52 @@ def build(opt, engines, P):
         if not last:
             lists(t + 1)
         else:
-            cl[0] = "vl"
+            cl[0] = "yc"
             h = H(); x = ps(h, 0, 112)
-            mmg([(x, sel("b162", i), c2("cch0", 112 * i, 112 * i + 112)) for i in range(16)], 8)
-            lin("v", V_("yc1"), x, -1.0, 2.0 * (MID + FAR) + 1); lin("v", V_("yc2"), x, 1.0, 2.0 * (FAR - MID))
-            tt(V_("yc1"), V_("yc1"), V_("yc2"), A.min)
+            mmg([(x, sel("b32" if CF else "b16", i), cch(0, 112 * i, 112 * i + 112)) for i in range(16)], 4)
+            lin("v", V_("yc1"), x, -2.0, 2.0 * (MID + FAR) + 1); lin("v", V_("yc2"), x, 2.0, 2.0 * (FAR - MID))
+            if CF:
+                tt(V_("yci"), V_("yc1"), V_("yc2"), A.min); cp(V_("yc1"), V_("yci"))
+            else:
+                tt(V_("yc1"), V_("yc1"), V_("yc2"), A.min)
             dma("y", V_("yc"), V_("yc1"), 57344)
             cl[0] = "yh"; lin("v", V_("hw16"), V_("hw"), 1.0, -float(TOP + U0)); h = H()
             mm([(ps(h, 2 * i + p2, 512, 32, S_(0, 8)), c2("rowb", 128 * i, 128 * i + 128, 16), c2("hw16", 16 * p2, 16 * p2 + 16), True, True)
                 for i in range(16) for p2 in range(2)])
             mov("s", V_("c1", S_(0, 8), AL), ps(h, 0, 512, None, S_(0, 8)))
             dma("y", V_("yh"), V_("c1", S_(0, 8), AL), 16384)
-        once = O("once", t)
         step1(t, 0)
         if once:
             step1(t, 1)
-        cl[0] = "put"; claimed_values()
+        cl[0] = "put"; cp(ind(c2("uw", 0, G0), V_("tgx")), V_("val"))
         if not last:
             send_shifted(O("shift", t)[1], "uw", U0, G0, 128, "su", cr)
-            ghost_views(t + 1, cr)
-            cl[0] = "vA"; views(t + 1, 256, 896); old_values(t + 1, 0)
-        else:
-            cl[0] = "out"
-            dma("y", c2("yu", 0, 448), c2("uw", U0, U0 + 448), 229376); dma("s", c2("yu", 448, 896), c2("uw", U0 + 448, U0 + 896), 229376)
+            early_views(t + 1, cr); old_values(t + 1, 0)
         if not once:
             step1(t, 1)
-            if not O("mask", t):
-                claimed_values()
         if not last:
             old_values(t + 1, 1)
     cl[0] = "out"
-    dma("y", c2("yu", 896, 1344), c2("uw", U0 + 896, U0 + 1344), 229376)
-    dma("s", c2("yu", 1344, NV), c2("uw", U0 + 1344, G0), 229376)
+    for j in range(2):
+        dma("ys"[j], c2("yu", 896 * j, 896 * j + 896), c2("uw", U0 + 896 * j, U0 + 896 * j + 896), 458752)
     return ops, pieces
 
 
-def plan(ops, pieces, times, period):
-    n = len(ops); cost = [o["cost"] for o in ops]
-    def links():
-        fw = [[(d, 0.0 if (ops[d]["e"] == "p" and o["e"] == "p") else ops[d]["lat"]) for d in o["deps"]] for o in ops]
-        bw = [[] for o in ops]
-        for j in range(n):
-            for d, gp in fw[j]:
-                bw[d].append((j, gp))
-        return fw, bw
-    def place(key):
-        fw, bw = links()
-        left = [len(x) for x in fw]; ready = sorted((key[j], j) for j in range(n) if not left[j])
-        st = [0.0] * n; busy = {e: [] for e in "vspgy"}; seq = []
-        while ready:
-            j = ready.pop(0)[1]; r = 0.0; w = cost[j]; seq.append(j)
-            for d, gp in fw[j]:
-                r = max(r, st[d] + cost[d] + gp)
-            if ops[j]["e"] is not None:
-                b = busy[ops[j]["e"]]; k = len(b)
-                while k > 0 and b[k - 1][1] > r:
-                    k -= 1
-                while k < len(b) and b[k][0] < r + w - 1e-9:
-                    r = max(r, b[k][1]); k += 1
-                b.insert(k, (r, r + w))
-            st[j] = r
-            for s, gp in bw[j]:
-                left[s] -= 1
-                if not left[s]:
-                    ready.append((key[s], s))
-            ready.sort()
-        return st, seq
-    key = [0.0] * n; bw = links()[1]
-    for j in range(n - 1, -1, -1):
-        o = ops[j]; tm = times.get("%s@%d" % (o["cl"], o["rd"]), times.get(o["cl"]))
-        if tm is None:
-            key[j] = min([key[s] - gp for s, gp in bw[j]] + [1e9]) - cost[j]
-        else:
-            key[j] = period * o["rd"] + (tm[min(o["nth"], len(tm) - 1)] if isinstance(tm, tuple) else tm)
-    st, seq = place(key)
-    bank = banks(pieces, [o["deps"] for o in ops], st, [st[j] + cost[j] for j in range(n)])
-    st, seq = place(st)
-    rank = {j: k for k, j in enumerate(seq)}
-    return sorted(range(n), key=lambda j: (st[j], rank[j])), [st[j] + cost[j] for j in range(n)], bank
-
-
-def banks(pieces, deps, st, end):
-    holder = [None] * 8; bank = [None] * len(pieces)
-    for h in sorted(range(len(pieces)), key=lambda h: (st[pieces[h]["ops"][0]], h)):
-        j = pieces[h]["ops"][0]; ways = []
-        for k, bs in enumerate(pieces[h]["pool"]):
-            last = [x for b in bs if holder[b] is not None for x in pieces[holder[b]]["ops"]]
-            ways.append((max([0.0] + [end[x] for x in last]), k, bs, last))
-        for tm, k, bs, last in sorted(ways):
-            seen = set(); todo = list(last) if tm > st[j] else []
-            while todo and j not in seen:
-                x = todo.pop()
-                if x not in seen:
-                    seen.add(x); todo += [d for d in deps[x] if end[d] > st[j] - 30.0]
-            if j not in seen:
-                break
-        deps[j].update(last); bank[h] = bs[0]
-        for b in bs:
+def arrange():
+    time = {}; engines = {}
+    for t, line in TIMES.items():
+        for name, calls in [x.split(":") for x in line.split()]:
+            calls = calls.split(","); key = "%s@%d" % (name, t)
+            time[key] = [START[t + 1] + int(x.rstrip("vsg")) for x in calls]; engines[key] = "".join(x[-1] for x in calls)
+    ops, pieces = build(OPT, engines, PLAN)
+    order = sorted(range(len(ops)), key=lambda j: time["%s@%d" % (ops[j]["cl"], ops[j]["rd"])][ops[j]["nth"]])
+    pos = {j: k for k, j in enumerate(order)}; bank = [int(b) for b in BANKS]; holder = [None] * 8
+    for h in sorted(range(len(pieces)), key=lambda h: pos[pieces[h]["ops"][0]]):
+        for b in [x for x in pieces[h]["pool"] if x[0] == bank[h]][0]:
+            if holder[b] is not None:
+                ops[pieces[h]["ops"][0]]["deps"].update(pieces[holder[b]]["ops"])
             holder[b] = h
-    return bank
-
-
-QUEUES = ("v", "s", "p", "g", "y", None)
-
-
-def refine(ops, refs, full, steps, heat, seed, lo, hi):
-    n = len(ops); state = [seed]
-    def rnd():
-        state[0] = (state[0] * 1103515245 + 12345) % 2147483648
-        return state[0] / 2147483648.0
-    en = [QUEUES.index(o["e"]) for o in ops]; deps = [[] for o in ops]
-    pos = {j: k for k, j in enumerate(full)}; above = [0] * n
-    for j in full:
-        for d in sorted(ops[j]["deps"], key=lambda d: -pos[d]):
-            if not above[j] >> d & 1:
-                deps[j].append(d); above[j] |= above[d] | 1 << d
-    alt = [[QUEUES.index(e) for e in o["alt"]] if o["alt"] and len(o["alt"]) > 1 else None for o in ops]
-    def run(order, en, fig, k0, old):
-        cost, xf, lk, rest, behind, start = fig
-        end, why, out = list(old[3]), list(old[1]), list(old[4]); free, last = list(start[0]), list(start[1]); left = {0, 1, 2, 3, 4, 6}
-        for j in order[k0 - 1::-1] if k0 else ():
-            if en[j] in left:
-                left.discard(en[j]); last[en[j]] = j; free[en[j]] = out[j]
-            if xf[j] and 6 in left:
-                left.discard(6); last[6] = j; free[6] = end[j]
-            if not left:
-                break
-        for j in order[k0:]:
-            r = 0.0; w = -1
-            for d, g in lk[j]:
-                x = end[d] + g
-                if x > r:
-                    r = x; w = d
-            e = en[j]
-            if e < 5:
-                if free[e] > r:
-                    r = free[e]; w = -2 - last[e]
-                r += cost[e][j]; free[e] = r; last[e] = j
-            out[j] = r
-            if xf[j]:
-                r += xf[j][0]
-                if free[6] > r:
-                    r = free[6]; w = -2 - last[6]
-                r += xf[j][1]; free[6] = r; last[6] = j
-            end[j] = r; why[j] = w
-        top, tj = max([(end[j] + rest[j], j) for j in order] + [(free[e] + behind[e], last[e]) for e in range(7)])
-        return top, why, tj, end, out, free, last
-    figs = []; rs = []; order = full[lo:hi]
-    for ref in refs:
-        cost = [[o["alt"][e][1] if o["alt"] and e in o["alt"] else o["cost"] for o in ref] for e in QUEUES]
-        lat = [0.0 if o["xf"] else o["lat"] for o in ref]; xf = [(o["lat"] - o["xf"], o["xf"]) if o["xf"] else None for o in ref]
-        lk = [[(d, 0.0 if en[j] == 2 and en[d] == 2 else lat[d]) for d in deps[j]] for j in range(n)]
-        rest = list(lat); behind = [0.0] * 7
-        for j in reversed(full[hi:]):
-            a = rest[j]
-            if xf[j]:
-                behind[6] = xf[j][1] + max(a, behind[6]); a = xf[j][0] + behind[6]
-            if en[j] < 5:
-                a = behind[en[j]] = cost[en[j]][j] + max(a, behind[en[j]])
-            for d, g in lk[j]:
-                rest[d] = max(rest[d], g + a)
-        zero = (0, [-1] * n, 0, [0.0] * n, [0.0] * n)
-        head = run(full[:lo], en, (cost, xf, lk, rest, behind, ([0.0] * 7, [-1] * 7)), 0, zero)
-        figs.append((cost, xf, lk, rest, behind, head[5:])); rs.append(run(order, en, figs[-1], 0, head))
-    n = len(order); pos = {j: k for k, j in enumerate(order)}
-    def move(a, b, far, ahead):
-        k0, k1 = pos[a], pos[b]; qn = set()
-        if ahead:
-            while far and k0 > 0:
-                k0 -= 1; far -= en[order[k0]] == en[a]
-            seg = order[k0:k1]; need = set(deps[b]); mv = []
-            for x in reversed(seg):
-                if x in need or en[x] in qn:
-                    if x == a:
-                        return None
-                    mv.append(x); need.update(deps[x])
-                    if en[x] < 5 and en[x] != en[b]:
-                        qn.add(en[x])
-            ms = set(mv)
-            return k0, mv[::-1] + [b] + [x for x in seg if x not in ms]
-        while far and k1 < n - 1:
-            k1 += 1; far -= en[order[k1]] == en[a]
-        seg = order[k0:k1 + 1]; ms = {a}; mv = [a]
-        for x in seg[1:]:
-            if en[x] in qn or not ms.isdisjoint(deps[x]):
-                if x == b:
-                    return None
-                mv.append(x); ms.add(x)
-                if en[x] < 5 and en[x] != en[a]:
-                    qn.add(en[x])
-        return k0, [x for x in seg if x not in ms] + mv
-    name = {(ops[j]["rd"], ops[j]["cl"], ops[j]["nth"]): j for j in order}; twin = {j: {} for j in order}
-    for k, j in name.items():
-        for d in (-3, -2, -1, 1, 2, 3):
-            x = name.get((k[0] + d,) + k[1:])
-            if x is not None and ops[x]["tag"] == ops[j]["tag"] and ops[x]["k"] == ops[j]["k"]:
-                twin[j][d] = x
-    either = [j for j in order if alt[j]]
-    wt = [200.0 / r[0] / len(figs) for r in rs]; cur = 200.0; best = (cur, order, en, rs); arcs = [None] * len(figs)
-    for it in range(steps):
-        f = int(rnd() * len(figs))
-        if arcs[f] is None:
-            why = rs[f][1]; j = rs[f][2]; arcs[f] = []
-            while j in pos:
-                w = why[j]
-                if w <= -2:
-                    w = -2 - w
-                    if w in pos:
-                        arcs[f].append((w, j))
-                j = w
-        if not arcs[f]:
-            continue
-        a, b = arcs[f][int(rnd() * len(arcs[f]))]; u = rnd(); e2 = en; far = (0, 0, 1, 2, 4, 8)[int(rnd() * 6)]; new = order; k0 = n
-        every = rnd() < TWINS
-        if u < 0.2:
-            x = a if u < 0.07 else b if u < 0.14 else either[int(rnd() * len(either))]
-            if not alt[x]:
-                continue
-            e2 = list(en); to = [e for e in alt[x] if e != en[x]][int(rnd() * (len(alt[x]) - 1))]
-            for y in [x] + (list(twin[x].values()) if every else []):
-                if alt[y] and to in alt[y]:
-                    e2[y] = to; k0 = min(k0, pos[y])
-        else:
-            new = list(order); used = []
-            for x, y in [(a, b)] + ([(twin[a][d], twin[b][d]) for d in twin[a] if d in twin[b]] if every else []):
-                got = move(x, y, far, u < 0.6) if pos[x] < pos[y] else None
-                if got and all(got[0] > q or got[0] + len(got[1]) <= p for p, q in used):
-                    new[got[0]:got[0] + len(got[1])] = got[1]; k0 = min(k0, got[0]); used.append((got[0], got[0] + len(got[1]) - 1))
-                elif x == a:
-                    break
-            if k0 == n:
-                continue
-        r2 = [run(new, e2, fig, k0, r) for fig, r in zip(figs, rs)]; t = sum(r[0] * w for r, w in zip(r2, wt))
-        if t <= cur + heat * rnd() ** 3 * (1 - it / steps):
-            cur, rs, en = t, r2, e2; arcs = [None] * len(figs)
-            if it % 8 == 0:
-                out = r2[0][4]; c0 = figs[0][0]; rk = {j: k for k, j in enumerate(new)}
-                new = sorted(new, key=lambda j: (out[j] - (c0[en[j]][j] if en[j] < 5 else 0.0), rk[j]))
-                r2 = rs = [run(new, en, fig, 0, r) for fig, r in zip(figs, rs)]; t = cur = sum(r[0] * w for r, w in zip(r2, wt))
-            order = new; pos = {j: k for k, j in enumerate(order)}
-            if t < best[0]:
-                best = (t, order, en, r2)
-    for calls in [ops] + refs:
-        for o, e in zip(calls, best[2]):
-            if o["alt"]:
-                o["e"] = QUEUES[e]; o["f"], o["cost"] = o["alt"][o["e"]]
-    return full[:lo] + best[1] + full[hi:], best[3][0][4], [r[0] for r in best[3]]
-
-
-def rebank(ops, pieces, data, order, end):
-    n = len(ops); st = [end[j] - ops[j]["cost"] for j in range(n)]
-    deps = [set(d) for d in data]; bank = banks(pieces, deps, st, end)
-    placed = set(); out = []; rest = order
-    while rest:
-        late = []
-        for k, j in enumerate(rest):
-            if deps[j] <= placed:
-                out.append(j); placed.add(j)
-                if late:
-                    late += rest[k + 1:]
-                    break
-            else:
-                late.append(j)
-        if len(late) == len(rest):
-            return None
-        rest = late
-    for o, d in zip(ops, deps):
-        o["deps"] = d
-    return out, bank
-
-
-def schedule(opt, times, engines, period, plans, phases, seed):
-    ops, pieces = build(opt, engines, plans[0]); refs = [build(opt, engines, p)[0] for p in plans]
-    data = [set(o["deps"]) for o in ops]
-    order, end, bank = plan(ops, pieces, times, period)
-    n = len(ops); spans = None
-    for k, (steps, heat, parts) in enumerate(phases):
-        if k:
-            order, bank = rebank(ops, pieces, data, order, end) or (order, bank)
-        for j in range(parts):
-            order, end, spans = refine(ops, refs, order, steps, heat, 7 * k + j + seed, max(0, n * j // parts - 40), min(n, n * (j + 1) // parts + 40))
-        order, end, spans = refine(ops, refs, order, 0, heat, 1, 0, n)
-    return ops, order, end, bank, spans
+    return ops, order, bank
 
 
 CACHE = {}
@@ -995,8 +803,8 @@ def rank_program(g, core, T, topo):
     if rank is None:
         return
     if not CACHE:
-        CACHE["plan"] = schedule(OPT, TIMES, ENGINES, ROUND, PLANS, PHASES, SEED)
-    ops, order, end, bank, spans = CACHE["plan"]
+        CACHE["plan"] = arrange()
+    ops, order, bank = CACHE["plan"]
     nr = len(T.cores); dst = T.cores[(rank - 1) % nr]; up = T.cores[(rank + 1) % nr]
     rid, pid = topo.addr(dst)[:2]
     en = topo.engines(core, dst); inn = len(topo.engines(up, core))

import numpy as np
from concourse.bass import DstId, RemoteDMATransfer
from concourse.mybir import dt, AluOpType, AxisListType, ActivationFunctionType
A = AluOpType
F = ActivationFunctionType

NV, NG, NS, RO = 1792, 256, 512, 4
W0 = 256
U0 = W0 + 1024
G0 = U0 + NV
UE = G0 + NG
C0 = U0
MID, FAR = 1024, 960
TOP = 49152
SLOTS = ((9, 11, 13, 15, 1, 3, 5, 7, 2, 6, 10, 14, 4, 12, 0, 8), (3, 7, 11, 15, 2, 6, 10, 14, 5, 4, 13, 12, 1, 9, 0, 8))
NB = 14
PER = (4, 4)
OPT = {"pair": "ddyy", "dd": "g", "c1": "vvv", "grp": ((0, 2), (2, 3), (3, 4)), "fine": (0,), "sdf": (0,), "shift": "wdd", "once": False, "once@3": True,
       "rep": "g", "cz": "p", "fold": 2, "cch": "h", "cch0": "g", "wayA": "vv", "wayB": "ssssvvvv", "a4": "vv", "treeA": "ddd", "treeB": "ddd", "fin": "vv", "diag": True,
       "cut": 256, "parts": (256, 768, 1280, NV), "vcut": (768, 1280, NV)}
OPT = {'pair': 'ddpp', 'dd': 'g', 'c1': 'vvv', 'grp': ((0, 2), (2, 4)), 'fine': (0,), 'sdf': (0,), 'shift': 'www', 'once': False, 'rep': 'd', 'cz': 'p', 'fold': 2,
       'cch': 'h', 'cch0': 'g', 'wayA': 'vvvv', 'wayB': 'sssv', 'a4': 'vv', 'treeA': 'ddddd', 'treeB': 'ddddv', 'fin': 'vv', 'diag': True, 'cut': 896,
       'parts': (448, 896, 1344, 1792), 'vcut': (576, 896, 1344, 1792), 'cut@-1': 1792}
START = (0, 148, 541, 960, 1363)
TIMES = {
    -1: "setup:0,0,2,1,0,6,1,5,9,3,6,2,5,7,8,12s,21s,16s,24s,17s,14s,25v,22s,11s,14v,11v,31v,16v,19s,29v,26s,4,15,48,10,60,82,67,30,32,11,88v,69s,27s,30,28,50,65,70,13,134g,77s,75s,65s,22,24,26,34,40,46,64s,76s,40,65g,60,46,17,49,18,47,61,52,195,267,364,71,106,51,68,196,203g,150,188,348,283,64,59,63,18,79,138,368,38,138,146,142,164,168,172,100,109,179,247,304,9s,239,300,293,160,328,392,264,81,176,297,243,396,191,183,187,37,41,33,29 ld0:10 ldw:20 ld1:2 sc0:30,96 code:35,39v,51g,29,33s,55v,37,43v,55s,32,38,59s sc1:101,105s su0:75,80s,77g,85,130 names:71s,79,80,101v turn:129g,123g,136 vl:65,77,80v nl:103,145,149,156,162,168,227s sd0:108v,116,136s,139,115v,123,135s,140 sd1:108s,130,144s,147 sd2:122s,136,165s,187 sd3:122v,143,180v,186 pl:210,212,264s cand:188,191,193,215,297s,318,353s,359,365,381s gv:92s,84v,89,103v,103g,113,177 vA:96s,83s ue:95g,101 uf:67s,85",
    0: "vB:-59v,68s uc0:-8v,-11s x0:0,12,7,18 m0:28,33,33,39 uc1:-1s x1:14,49 m1:66,71,70,81 uc2:23s x2:39,59 m2:80,75 uc3:36s x3:53,84 m3:113,114,126,159s,96,81,102,154s cred:170 l0:127s,137 l1:134s,144 l2:171s,183 l3:164s,175 w0:159,152,164,182,190,196,222,218 w1:192,191,203,214,217,219,223,224 s3:227,235,237,238,246s,238s val:237,244,249s,255s,251s s4:250,252,245,252,257,255,263,260,268,263,272,267,274,277,280s,283s sc:301,306v,300s,308,354 names:229s,234,235,269s turn:267s,210s,307 host:314,324,327,610s cch:296s,292s,306s,302s vl:310,323,325s vm:318,334,336v nl:401,421,424,430,442,449,484s sd0:359s,367,382v,392,359v,374,393s,400 sd1:366s,381,402s,444 sd2:380s,394,424v,438 sd3:366v,407,444v,459 pl:468,470,488s cand:440,460,463,465,585s,598,605s,611,617,627s A0:85,119,129 A1:117,141,151,160,222,262 A2:101,189,198,210,252 A3:163,221,238,245,269 At:275,291,304,311 put:315,324,335v,324s,337,383 gv:340v,328s,333,343v,358g,365,424 vA:332s,340s ue:347g,365 B0:105s,125,197,206 B1:93s,106,213,226,234,285,326 B2:178s,190,259,279,295,348 B3:287,311,328,337,346 Bt:339,344,350,355,361,315,325,380,383 uf:353g,359",
    1: "vB:8v,79s uc0:-8v,2s x0:0,10,19,30 m0:26,32,46,52 uc1:15s x1:32,48 m1:66,72,71,82 uc2:34s x2:52,70 m2:93,89 uc3:57s x3:76,110 m3:121,107,127,166s,126,94,139,161s cred:142 l0:131s,142 l1:154s,165 l2:177s,185 l3:170s,178 w0:173,173,185,206,219,222,225,229 w1:201,193,210,220,224,227,232,230 s3:234,242,244,246,254s,256s val:267,274,276s,278s,282s s4:258,261,252,260,265,262,271,268,276,275,280,271,282,286,289s,291s sc:305,310v,309s,314,363 names:235s,315,317,327s turn:209s,232g,312 host:290,305,311,319v cch:311s,300s,315s,305s vl:318,328,330s vm:324,350,390v nl:405,436,438,444,466,472,489s sd0:368v,385,394v,455,368s,392,408s,418 sd1:375s,398,409s,458 sd2:388s,411,437s,457 sd3:375v,418,443s,456 pl:461,464,493s cand:459,478,481,483,583s,589,607s,615,621,636s A0:131,146,157 A1:110,138,149,166,222,274 A2:98,184,193,202,243 A3:207,239,252,288,291 At:284,295,310,317 put:320,329,336s,329g,355,401 gv:347s,333s,337,350s,381g,388,447 vA:338s,339v ue:365g,371 B0:98s,111,218,233 B1:119s,132,226,245,253,304,345 B2:197s,212,263,278,287,329 B3:294,319,333,348,351 Bt:344,349,354,360,380,332,353,388,391 uf:370g,377",
    2: "vB:-24v,-13v uc0:-18s,-8s x0:0,12,7,19 m0:27,33,32,37 uc1:-1s x1:14,38 m1:53,60,57,70 uc2:25s x2:40,61 m2:75,80 uc3:47s x3:62,77 m3:101,81,106,140s,96,93,118,145s cred:191 l0:126s,137 l1:133s,144 l2:150s,163 l3:157s,170 w0:158,152,164,193s,202,205,207,215,212 w1:178,178,190,198s,203,206,210,213,216 s3:219,226,228,230,238s,230s val:237,239,241s,247s,243s s4:242,244,236,244,249,246,254,251,260,255,263,258,266,269,272s,274s sc:283,288v,288s,299,347 names:218s,267,269,318s turn:80g,-43g,290 host:273,305,654 cch:297s,283s,309g,314s vl:310,317,321s vm:338,369,385v nl:394,421,423,429,435,448,483v sd0:352s,360,373v,389,372s,381,389v,402 sd1:359s,388,400s,417 sd2:379s,400,420s,435 sd3:352v,407,436v,442 pl:444,459,516s cand:446,455,457,537,601s,609,616s,622,628,640s A0:105,118,151 A1:84,98,117,159,213,258 A2:125,180,194,203,248 A3:182,221,261,271,274 At:270,294,304,312s,315 put:318,329,334s,328g,342,388 gv:329v,327s,332,371v,352g,374,433 vA:335s,332v ue:384g,444 B0:86s,99,208,229 B1:106s,119,200,218,238,289,332 B2:169s,181,250,292,318,365 B3:276,289,299,326,341 Bt:315,323,344,370,376,321,374,383,386 uf:358g,447",
    3: "vB:-13v,69s uc0:-27v,-10s x0:0,12,7,19 m0:28,33,34,40 uc1:-1s x1:15,37 m1:53,60,57,70 uc2:24s x2:40,60 m2:75,84 uc3:46s x3:62,81 m3:112,81,137,163s,116,93,122,158s l0:124s,152 l1:139s,159 l2:174s,185 l3:168s,179 w0:174,167,180,210s,220,223,226,235,231 w1:200,193,210,218s,222,225,228,232,233 out:284,340,361 s3:237,250,252,254,262s,265s val:264,281,283s,285s,289s s4:266,268,260,268,273,270,278,277,284,284,298,287,301,304,307s,309s host:307,310,313 cch:318v,332s,323g,327s yc:339,353,356,359,363v,365v,368,371 yh:336s,362,366s,372 A0:88,131,166 A1:100,116,145,175,231,283 A2:121,181,192,201,242 A3:133,221,236,275,282 At:243,288,318,325s,328 put:331 B0:102s,114,189,205 B1:90s,103,202,212,221,272,313 B2:146s,159,229,242,252,314 B3:252,266,290,308,311 Bt:302,323,329,334,348,342,347,355,358",
}
BANKS = "4657446675767426466670020754776676464776456446660002756200077020075477660664757674234666200475402005600205747766267674746756644402042710204060202576764656720027200047"
f32, f16, i32, u16, bf = "float32", "float16", "int32", "uint16", "bfloat16"
NN = (16 * NB, 448 - 16 * NB)
SB = {
    "uw": ([128, UE], f32), "cc": ([128, C0 + NV + NG], f32), "vw0": ([128, 4096], f32), "vw1": ([128, 4096], f32),
    "tli": ([128, NV], i32), "lsw": ([128, 2, 896], i32), "ftr": ([128, 14, 32], f16), "tlt": ([128, 14, 32], f16),
    "tt": ([128, 8192], f32), "uu": ([128, 4096], f32), "gg": ([128, 4096], f16),
    "q0": ([128, 4, 4 * NN[0]], f32), "q1": ([128, 4, 4 * NN[1]], f32), "ue0": ([128, PER[0] * NN[0]], f32), "ue1": ([128, PER[1] * NN[1]], f32),
    "oc": ([128, NN[1]], f32), "mk": ([128, NN[1]], f32), "bz32": ([128, 144], f32), "yci": ([128, 112], i32), "c1": ([128, 512], f32),
    "sdi": ([128, 112], i32), "nri": ([128, 112], i32), "sdf": ([128, 112], f32), "nrf": ([128, 112], f32), "cb": ([128, 112], f16),
    "hsi": ([128, 512], i32), "hsf": ([128, 16, 32], f16), "thr": ([128, 4], f32), "nth": ([128, 4], f32),
    "hw": ([128, 32], f32), "hix": ([128, 32], u16), "hw16": ([128, 32], f16),
    "nmh": ([128, 256], f16), "nix": ([128, 2, 256], u16), "jm": ([128, 16], f32), "n32m": ([128, 128], f32),
    "uix": ([128, 256], u16), "sg": ([128, 256], f16), "lix": ([128, 256], u16), "cab": ([128, 512], f16),
    "sel": ([128, 2, 2, 128], f16), "r8": ([128, 2, 144], f16), "cw16": ([128, 16], f16), "zl": ([128, 16], f32), "cand": ([128, 512], f16), "clw": ([128, 32], f32), "cv": ([128, 32], f32),
    "dd": ([128, 256], f32), "ud": ([128, 512], f16), "rb": ([128, 256], f32), "cz": ([128, 256], f16), "zs": ([128, 256], f32),
    "cw": ([128, 16], f32), "vlx": ([128, 16], u16), "cbg": ([128, 112], f16), "rowsh": ([128, 2, 128], f16),
    "idl": ([128, 256], f16), "tg": ([128, 256], f32), "rs0": ([128, 256], f32), "cdg": ([128, 256], f16), "tgx": ([128, 16], u16), "val": ([128, 256], f32),
    "h1": ([128, 16], f32), "eq": ([128, 4096], f16), "eqd": ([128, 256], f16),
    "f0": ([128, 224], f32), "vix": ([128, 224], u16), "sgw": ([128, 28], f16), "six0": ([128, 448], u16), "six1": ([128, 448], u16),
    "sc": ([128, 256], f32), "su": ([128, 256], f32), "sv": ([128, 512], f32),
    "yc1": ([128, 112], f32), "yc2": ([128, 112], f32),
    "pi": ([128, 4], i32), "pj": ([128, 4], i32), "col": ([128, 16], f32), "xr": ([128, 152], f32), "x16": ([128, 16], f32),
    "ce": ([128, 16], f32), "md": ([128, 128], f32), "tz": ([128, 256], f32), "c2k": ([128, 128], f32),
    "i32m": ([128, 128], f32), "i16m": ([128, 128], f16), "i4": ([128, 128], f16), "bz": ([128, 144], f16),
    "pk": ([128, 4], i32), "pm": ([128, 128], f32), "b32": ([128, 144], f32),
    "b162": ([128, 144], f16), "cch0": ([128, NV], f16), "cch1": ([128, NV], f16), "i4k": ([128, 2, 128], f16), "tab8": ([128, 256], f32), "b16": ([128, 144], f16), "b16h": ([128, 144], f16), "bsum": ([128, 144], f16),
    "b8": ([128, 144], f16), "blk": ([128, 128], f16), "blk2k": ([128, 128], f16), "blk4k": ([128, 128], f16), "lo8": ([128, 152], f16), "hi8": ([128, 152], f16),
    "y8": ([128, 2, 128], f16), "ee": ([128, 2, 128], f16), "t1": ([128, 128], f32), "t2": ([128, 256], f32),
    "rowb": ([128, 2048], f16), "tri": ([128, 2048], f16), "mm": ([128, 4, 128], f16),
    "tab8h": ([128, 256], f16), "tab16": ([128, 256], f32), "tab16h": ([128, 256], f16),
    "jw": ([128, 224], f32), "t128": ([128, 32], f32),
}
SPARE = ("rb", "cand", "blk2k", "ee", "oc", "bz32", "yci", "n32m")
SCRATCH = {k: ("sbuf", s, d) for k, (s, d) in SB.items() if k not in SPARE}
SCRATCH["ps"] = ("psum", [128, 4096], f32)
IO = {"tl": [128, NV], "sd": [8, NV], "nr": [8, NV], "hs": [8, NS], "u0": [128, NV], "w0": [128, 1024], "th": [128, 1],
      "yu": [128, NV], "ys": [128, 1024], "yc": [8, NV], "yh": [8, NS]}
SEMAPHORES = (["v", "s", "p", "gq"] + ["d%d" % i for i in range(114)] + ["a%d" % i for i in range(16)] + ["l%d" % i for i in range(16)])

PLAN = {"cy": 0.83e-3, "gam": 1.5, "sig": 3.5, "gi": 1.0, "dl": 2.0, "dr": 220e3, "hop": 0.1, "rl": 1.8, "rr": 100e3, "first": 3.0, "row": 0.03,
        "pe": 1.4, "load": 1.3, "ov": 0.0}
WIDE, NARROW = ((0, 1), (2, 3), (4, 5)), ((6,), (7,), (4,), (5,), (0,), (1,), (2,), (3,))


def V_(name, *idx):
    shape = SB[name][0] if name in SB else IO[name]
    if not idx:
        idx = (slice(None),)
    ar = np.arange(int(np.prod(shape[1:]))).reshape(shape[1:])[idx[1:]].ravel()
    pr = range(shape[0])[idx[0]]
    bits = np.zeros(int(np.prod(shape[1:])), np.uint8); bits[ar] = 1
    m = int.from_bytes(np.packbits(bits, bitorder="little").tobytes(), "little")
    wide = np.zeros((bits.size + 7) // 8, np.uint8); wide[ar // 8] = 255
    return {"n": name, "key": name, "i": idx, "m": m, "box": int.from_bytes(wide.tobytes(), "little"), "p": (pr[0], pr[-1] + 1), "c": int(ar.size), "off": None}


S_ = slice
AL = slice(None)


def c2(name, a, b, s=None):
    return V_(name, AL, slice(a, b, s))


def ps(h, a, b, s=None, p=AL):
    cols = range(a, b, s or 1); m = 0
    for k in range(cols[0] // 512, cols[-1] // 512 + 1):
        m |= 1 << k
    return {"n": "ps", "key": h, "i": (p, a, b, s), "m": m, "box": m, "p": (0, 128), "c": len(cols), "off": None}


def ind(win, off):
    w = dict(win); w["off"] = off; w["c"] = off["c"] * 16
    return w


def two(v):
    return v["n"] != "ps" and SB[v["n"]][1] in (f16, u16, bf)


def build(opt, engines, P):
    cl = ["setup", -1]; ops = []; hist = {}; nd = [0]; na = [0]; pieces = []; probe = [False]; made = set(); nth = {}
    CY = P["cy"]; PCY = CY / 2 * P["pe"]; GAM = P["gam"]

    def O(name, t):
        return opt.get("%s@%d" % (name, t), opt[name])

    def H(pool=NARROW):
        pieces.append({"pool": pool, "ops": []})
        return len(pieces) - 1

    def add(eng, emit, rd, wr, cost, lat=None, kind="c", sem=None, after=(), ext=None, xf=0.0):
        if eng in ("v", "s") and kind == "c":
            cost += P["ov"]
        if probe[0]:
            return emit, cost
        me = len(ops); deps = set(after); acc = []; reads = set(); firm = set(after)
        for v in rd:
            acc.append((v, v["n"] == "ps"))
            if v["off"] is not None:
                acc.append((v["off"], False))
        for v in wr:
            acc.append((v, True))
            if v["off"] is not None:
                acc.append((v["off"], False))
        dma = kind != "c"
        for v, w in acc:
            if v["n"] in IO:
                continue
            if v["n"] == "ps":
                po = pieces[v["key"]]["ops"]
                if po and po[0] != me:
                    deps.add(po[0])
                if me not in po:
                    po.append(me)
            for (o, m, box, p, w0, d0) in hist.get(v["key"], []):
                if (w or w0) and o != me and p[0] < v["p"][1] and v["p"][0] < p[1] and ((box & v["box"]) if (dma or d0) else (m & v["m"])):
                    deps.add(o)
                    both = v["n"] == "ps" and (v["key"], o) not in made and not any(v["key"] == x["key"] for x in wr)
                    (reads if both else firm).add(o)
        made.update((v["key"], me) for v in wr)
        for v, w in acc:
            if v["n"] in IO:
                continue
            h = hist.setdefault(v["key"], [])
            if w:
                h[:] = [e for e in h if not (e[3][0] >= v["p"][0] and e[3][1] <= v["p"][1] and (e[1] & ~v["m"]) == 0)]
            h.append((me, v["m"], v["box"], v["p"], w, dma))
        k = nth.get(tuple(cl), 0); nth[tuple(cl)] = k + 1
        ops.append({"cl": cl[0], "rd": cl[1], "nth": k, "tag": wr[0]["n"] if wr else "send", "e": eng, "f": emit, "deps": deps, "cost": cost,
                    "lat": P["hop"] if lat is None else lat + xf, "xf": xf, "k": kind, "sem": sem, "ext": ext, "alt": None, "reads": reads - firm})
        return me

    def ap(c, v):
        if not isinstance(v, dict):
            return v
        if v["n"] == "ps":
            p, a, b, s = v["i"]; o = 512 * c["bank"][v["key"]]
            return c["T"]["ps"][p, slice(o + a, o + b, s)]
        if "by" in v and ops[v["by"][0]]["e"] == "v":
            v = v["by"][1]
        a = c["T"][v["n"]][v["i"]]
        return a if v["off"] is None else a.indirect(ap(c, v["off"]))

    def vs(*xs):
        return [x for x in xs if isinstance(x, dict)]

    def vcost(out, ins, k):
        if out["off"] is not None:
            return 0.06 + out["c"] * P["sig"] * CY
        if ins and ins[0]["off"] is not None:
            return 0.06 + out["c"] * GAM * CY
        if k == 1 and all(two(x) for x in [out] + ins):
            k = 0.5
        return 0.03 + max(64, out["c"] * k) * CY

    def cp(out, a):
        return add("v", lambda c: [c["g"].vector.tensor_copy(ap(c, out), ap(c, a))], [a], [out], vcost(out, [a], 1))

    def tt(out, a, b, op):
        k = 1 if "ps" in (a["n"], b["n"]) else 2
        return add("v", lambda c: [c["g"].vector.tensor_tensor(ap(c, out), ap(c, a), ap(c, b), op)], [a, b], [out], vcost(out, [a, b], k))

    def ts(out, a, s1, op0, s2=None, op1=None):
        if op1 is None:
            f = lambda c: [c["g"].vector.tensor_scalar(ap(c, out), ap(c, a), ap(c, s1), None, op0)]
        else:
            f = lambda c: [c["g"].vector.tensor_scalar(ap(c, out), ap(c, a), ap(c, s1), ap(c, s2), op0, op1)]
        return add("v", f, vs(a, s1, s2), [out], vcost(out, [a], 1))

    def scan(out, a, b, first, op0, op1):
        return add("v", lambda c: [c["g"].vector.tensor_tensor_scan(ap(c, out), ap(c, a), ap(c, b), first, op0, op1)], [a, b], [out], vcost(out, [a, b], 1))

    def tr(out, a):
        return add("v", lambda c: [c["g"].vector.transpose(ap(c, out), ap(c, a))], [a], [out], vcost(out, [a], 1))

    def act(out, a, fn, scale=1.0, bias=0.0, more=0.0):
        k = GAM if a["off"] is not None else 1
        return add("s", lambda c: [c["g"].scalar.activation(ap(c, out), ap(c, a), fn, bias=ap(c, bias), scale=ap(c, scale))],
                   vs(a, scale, bias), [out], 0.06 + more + max(64, out["c"] * k) * CY)

    def put_codes(out, a):
        return either("s", {"v": lambda: cp(out, a),
                            "s": lambda: add("s", lambda c: [c["g"].scalar.activation(ap(c, out), ap(c, a), F.Silu)], [a], [out], vcost(out, [a], 1))})

    def asel(out, a, pat, op, fill, base, cm):
        return add("g", lambda c: [c["g"].affine_select(ap(c, out), ap(c, a), pat, op, fill, base, cm)], [a], [out], 0.17 + 2 * out["c"] * CY)

    def either(e, ways):
        me = ways[e](); o = ops[me]; o["alt"] = {}
        for k in ways:
            probe[0] = True; o["alt"][k] = ways[k](); probe[0] = False
        pick = engines.get("%s@%d" % (o["cl"], o["rd"]), engines.get(o["cl"], ""))[o["nth"]:o["nth"] + 1]
        o["e"] = pick if pick in ways else e; o["f"], o["cost"] = o["alt"][o["e"]]
        return me

    def mov(e, out, a, scale=None):
        ways = {"s": lambda: act(out, a, F.Copy, 1.0 if scale is None else scale),
                "v": lambda: cp(out, a) if scale is None else ts(out, a, scale, A.mult)}
        if e == "g":
            ways["g"] = lambda: asel(out, a, [[0, out["c"]]], A.is_ge, 0.0, 0, 0)
        return either(e, ways)

    def lin(e, out, a, scale, bias, relu=False):
        return either(e, {"s": lambda: act(out, a, F.Relu if relu else F.Identity, scale, bias),
                          "v": lambda: ts(out, a, bias, A.add, 0.0, A.max) if relu else ts(out, a, scale, A.mult, bias, A.add)})

    def side(e, out, a):
        j = either(e, {"s": lambda: act(out, a, F.Sign, 1.0, -float(MID)), "v": lambda: ts(out, a, float(MID), A.is_gt, 0.5, A.subtract)})
        return lambda k: dict(sel("b16h", k), by=(j, sel("b16", k)))

    def dadd(out, a):
        s = "d%d" % nd[0]; nd[0] += 1
        return add("g", lambda c: [c["g"].dma_start(ap(c, out), ap(c, a), accum_op=A.add)], [a, out], [out], P["gi"],
                   lat=P["dl"], xf=out["c"] * 512 / P["dr"], kind="d", sem=(s, 16))

    def mm(lst):
        cost = 0.02
        for o, l, r, a, b in lst:
            cost += max(min(64, l["c"]), r["c"]) * (1 if two(r) else 4) * PCY
        return add("p", lambda c: [c["g"].tensor.matmul(ap(c, o), ap(c, l), ap(c, r), a, b) for o, l, r, a, b in lst],
                   [x[1] for x in lst] + [x[2] for x in lst] + [x[1]["by"][1] for x in lst if "by" in x[1]], [x[0] for x in lst], cost, lat=P["hop"] + 0.07)

    def mmg(lst, per=4):
        full = [(o, l, r, j == 0, j == len(lst) - 1) for j, (o, l, r) in enumerate(lst)]
        for j in range(0, len(full), per):
            mm(full[j:j + per])

    def iota(out, pat, base, cm):
        if SB[out["n"]][1] != i32:
            f = lambda c: [c["g"].iota(ap(c, out), pat, base, cm, allow_small_or_imprecise_dtypes=True)]
        else:
            f = lambda c: [c["g"].iota(ap(c, out), pat, base, cm)]
        return add("g", f, [], [out], 0.13 + 2 * out["c"] * CY)

    def dmas(q, pairs, nbytes, after=()):
        s = "d%d" % nd[0]; nd[0] += 1
        def f(c):
            e = {"y": c["g"].sync, "s": c["g"].scalar, "g": c["g"]}[q]
            return [e.dma_start(ap(c, out), ap(c, a)) for out, a in pairs]
        return add(q, f, [a for out, a in pairs], [out for out, a in pairs], len(pairs) * (P["gi"] if q == "g" else 0.1), lat=P["dl"],
                   xf=nbytes / (2 * P["dr"]), kind="d", sem=(s, 16 * len(pairs)), after=after)

    def dma(q, out, a, nbytes):
        return dmas(q, [(out, a)], nbytes)

    def send(pairs, credit):
        k = na[0]; na[0] += 1
        def f(c):
            en = c["en"]; per = len(en) // len(pairs); trs = []
            for j, (a, b) in enumerate(pairs):
                trs.append(RemoteDMATransfer(dst_ids=[c["dst"]], dma_engine_mask=sum(1 << e for e in en[j * per:(j + 1) * per]),
                                             remote_sem=c["T"].sem["a%d" % k], src=ap(c, a), dst=ap(c, b)))
            c["g"].remote_dma_fused(trs, local_sem=c["T"].sem["l%d" % k])
            return []
        nb = sum(a["c"] * (256 if two(a) else 512) + 16 * P["row"] * P["rr"] for a, b in pairs)
        o = add("g", f, [a for a, b in pairs], [], P["gi"], lat=P["rl"] + (P["first"] if k == 0 else 0.0), xf=nb / P["rr"], kind="r", sem=("l%d" % k, "en"),
                after=[credit[0]] if credit else [], ext=credit[1] if credit else None)
        add(None, None, [], [b for a, b in pairs], 0.0, lat=0.5, kind="x", sem=("a%d" % k, "en"), after=[o])

    def credit(views):
        k = na[0]; na[0] += 1
        def f(c):
            c["g"].remote_sem_update(c["T"].sem["a%d" % k], c["T"].sem["l%d" % k], c["up"][1], c["up"][0], c["upm"])
            return []
        o = add("g", f, [], views, P["gi"], lat=P["rl"], kind="r", sem=("l%d" % k, 1))
        return (o, ("a%d" % k, 1))

    def sel(name, i):
        return c2(name, 16 - i, 144 - i)

    def colv(j):
        return c2("col", j, j + 1)

    I32, I16, ROW0 = V_("i32m"), V_("i16m"), c2("rowb", 0, 128)
    WW = c2("uw", W0, U0)
    CF = opt["cch"] == "f"
    LATE = 4 * NN[0]

    def cch(t, a, b, s=None):
        return c2("cc", C0 + a, C0 + b, s) if CF else c2("cch%d" % (t % 2), a, b, s)

    dma("y", V_("sdi"), V_("sd"), 57344); dma("s", V_("nri"), V_("nr"), 57344)
    dma("y", V_("hsi", S_(0, 8), AL), V_("hs"), 16384)
    cl[0] = "ld0"; dma("g", c2("uw", U0, G0), V_("u0"), 917504)
    cl[0] = "ldw"; dma("g", WW, V_("w0"), 524288)
    cl[0] = "ld1"; dma("s", V_("tli"), V_("tl"), 917504)
    cl[0] = "setup"
    dma("y", c2("thr", 0, 1), V_("th"), 4096)
    iota(c2("pi", 0, 2), [[112, 2]], 0, 1)
    iota(V_("xr"), [[1, 152]], -16, 0); iota(V_("md"), [[1, 8], [0, 16]], 0, 0); iota(V_("x16"), [[1, 16]], 0, 0)
    P_, PM, PD, P16, KV, E4, ZV, ZB, LO, HI, PB, KZ, KR, PS, PG = [colv(j) for j in range(15)]
    cp(P_, c2("pi", 0, 1))
    ts(c2("pj", 0, 1), c2("pi", 0, 1), 15, A.bitwise_and); cp(PM, c2("pj", 0, 1))
    ts(c2("pj", 1, 2), c2("pi", 0, 1), 4, A.arith_shift_right); cp(PD, c2("pj", 1, 2))
    ts(V_("blk"), V_("md"), PD, A.is_equal)
    ts(V_("ce"), V_("x16"), PM, A.is_equal)
    for i in range(16):
        mov("vs"[i % 3 == 2], c2("rowb", 128 * i, 128 * i + 128), V_("blk"), c2("ce", i, i + 1))
    ts(c2("pk", 2, 3), c2("pi", 1, 2), 127, A.bitwise_and); cp(PS, c2("pk", 2, 3)); ts(V_("pm"), c2("xr", 16, 144), PS, A.is_equal)
    ts(c2("pk", 3, 4), c2("pi", 1, 2), 4, A.arith_shift_right, 7, A.bitwise_and); cp(PG, c2("pk", 3, 4))
    for i in range(2):
        ts(V_("rowsh", AL, i, AL), V_("md"), PG, A.is_equal, c2("ce", i + 1, i + 2), A.mult)
    ts(P16, P_, 16.0, A.mult); ts(V_("b8"), c2("xr", 0, 144), P16, A.is_equal)
    ts(V_("b32"), c2("xr", 0, 144), P_, A.is_equal, c2("ce", 0, 1), A.mult)
    for name, k in (("b16", 1.0), ("b16h", 0.5), ("b162", 2.0)):
        mov("s", V_(name), V_("b32"), k)
    ts(HI, PM, 8.0, A.is_ge, -1.0, A.mult); ts(LO, PM, 8.0, A.is_lt, -1.0, A.mult); ts(E4, HI, -4.0, A.mult, 0.5, A.add)
    ts(V_("lo8"), V_("xr"), P_, A.is_equal, LO, A.mult); ts(V_("hi8"), V_("xr"), P_, A.is_equal, HI, A.mult)
    ts(I32, c2("xr", 16, 144), P_, A.is_equal); mov("g", I16, I32); mov("s", V_("i4"), I32, 4.0)
    mov("s", V_("i4k", AL, 0, AL), I32, 4096.0); mov("s", V_("i4k", AL, 1, AL), I32, -4096.0)
    ts(V_("sdf"), V_("sdi"), 2.0, A.mult, -1.0, A.add); ts(V_("nrf"), V_("nri"), -1.0, A.mult, float(FAR), A.add)
    first = tt(V_("cb"), V_("sdf"), V_("nrf"), A.mult)
    cl[0] = "sc0"; send([(V_("cb"), V_("cbg"))], None); cl[0] = "code"
    for b in range(4):
        h = H()
        mm([(ps(h, 112 * j, 112 * j + 112), c2("rowb", 128 * (4 * b + j), 128 * (4 * b + j) + 128), V_("cb"), True, True) for j in range(4)])
        if b == 3:
            act(c2("cc", C0 + 448 * b, C0 + 448 * b + 448), ps(h, 0, 448), F.Silu, 1.0, float(MID), P["load"])
        else:
            lin("sv"[b % 2], c2("cc", C0 + 448 * b, C0 + 448 * b + 448), ps(h, 0, 448), 1.0, float(MID))
        if CF:
            continue
        if opt["cch0"] == "g":
            mov("g", c2("cch0", 448 * b, 448 * b + 448), c2("cc", C0 + 448 * b, C0 + 448 * b + 448))
        else:
            lin("vs"[b % 2], c2("cch0", 448 * b, 448 * b + 448), ps(h, 0, 448), 1.0, float(MID))

    def send_shifted(way, name, own, ghost, n, stage, cr):
        hi = c2(stage, n, 2 * n)
        if way == "d":
            dmas("y", [(V_(stage, S_(0, 112), S_(n, 2 * n)), V_(name, S_(16, 128), S_(own + n, own + 2 * n))),
                       (V_(stage, S_(112, 128), S_(n, 2 * n)), V_(name, S_(0, 16), S_(own + n, own + 2 * n))),
                       (c2(stage, 0, n), c2(name, own, own + n))], 1024 * n)
            return send([(V_(stage), c2(name, ghost, ghost + 2 * n))], cr)
        h = H()
        mm([(ps(h, 0, n), V_("pm"), c2(name, own + n, own + 2 * n), True, True)])
        mov("s", hi, ps(h, 0, n))
        if way == "w":
            mov("g", c2(stage, 0, n), c2(name, own, own + n))
            send([(V_(stage), c2(name, ghost, ghost + 2 * n))], cr)
        else:
            send([(c2(name, own, own + n), c2(name, ghost, ghost + n)), (hi, c2(name, ghost + n, ghost + 2 * n))], cr)

    h = H(); cl[0] = "sc1"
    mm([(ps(h, a, b), l, c2("cbg", a % 112, (b - 1) % 112 + 1), True, True) for a, b, l in
        ((0, 112, ROW0), (112, 128, c2("rowb", 128, 256)), (128, 224, V_("rowsh", AL, 0, AL)), (224, 256, V_("rowsh", AL, 1, AL)))])
    lin("s", c2("cc", C0 + NV, C0 + NV + NG), ps(h, 0, 256), 1.0, float(MID))
    cl[0] = "su0"; send_shifted(O("shift", -1)[1], "uw", U0, G0, 128, "su", None); cl[0] = "setup"
    cp(V_("hsf", S_(0, 8)), V_("hsi", S_(0, 8), AL))
    h = H()
    for par in range(2):
        mmg([(ps(h, 16 * par, 16 * par + 16), V_("b8", S_(0, 8), S_(16 - i, 144 - i)), V_("hsf", S_(0, 8), AL, 2 * i + par)) for i in range(16)], 16)
    lin("v", V_("hix"), ps(h, 0, 32), 1.0, 0.0); lin("v", V_("hw"), ps(h, 0, 32), 1.0, float(TOP + U0))
    iota(V_("t2"), [[2, 2], [8, 128]], 0, 0); mov("g", V_("tab8h"), V_("t2")); iota(V_("tab8"), [[2, 2], [8, 128]], 0, 0)
    iota(V_("jw"), [[-8, 224]], W0 - U0, 0)
    ts(c2("pk", 0, 1), c2("pi", 0, 1), 1, A.bitwise_and); ts(KZ, c2("pk", 0, 1), 1.0 - 4 * MID, A.mult, 2.0 * (MID + FAR), A.add)
    ts(c2("pk", 1, 2), c2("pi", 0, 1), 1, A.arith_shift_right, 7, A.bitwise_and); cp(KR, c2("pk", 1, 2))
    ts(V_("jw"), V_("jw"), KZ, A.add, KR, A.subtract)
    tt(c2("bz32" if CF else "bz", 1, 144), c2("b162", 1, 144), c2("b162", 0, 143), A.subtract)
    iota(V_("jm"), [[-16, 16]], TOP + 255, 0); iota(V_("rs0"), [[0, 256]], 1000000, 0); ts(c2("rs0", 0, 256, 16), V_("jm"), PM, A.subtract)
    iota(V_("dd"), [[0, 16], [1, 16]], 0, 0); ts(V_("cdg"), V_("dd"), PM, A.is_equal, float(TOP + G0), A.mult)
    ts(PB, PD, 16.0, A.mult); ts(V_("bsum"), c2("xr", 0, 144), PB, A.is_equal, -2048.0, A.mult)
    iota(V_("tab16"), [[4, 2], [0, 4], [16, 32]], 768, 0); mov("g", V_("tab16h"), V_("tab16"))
    iota(c2("tt", 0, 512), [[0, 512]], 0, 0)
    dmas("y", [(c2("tt", a, a + 512), c2("tt", 0, 512)) for a in (2048, 4096, 6144)] + [(c2(k, 0, W0), c2("tt", 0, W0)) for k in ("uw", "cc")], 1048576)
    iota(c2("cc", W0, U0, 2), [[1, 512]], MID - FAR, 0); iota(c2("cc", W0 + 1, U0, 2), [[-1, 512]], MID + FAR, 0)
    if opt["cz"] == "v":
        mov("s", V_("blk2k"), V_("blk"), -2048.0)
        asel(V_("ee", AL, 0, AL), V_("blk"), [[16, 8], [0, 16]], A.is_ge, 0.0, 7, -1)
        asel(V_("ee", AL, 1, AL), V_("blk"), [[-16, 8], [0, 16]], A.is_ge, 0.0, -8, 1)
    else:
        for e, half in enumerate((LO, HI)):
            ts(V_("r8", AL, e, AL), c2("xr", 0, 144), PB, A.is_equal, half, A.mult)
    ts(c2("nth", 0, 1), c2("thr", 0, 1), -1.0, A.mult)
    ts(c2("pj", 2, 3), c2("pi", 0, 1), 2, A.arith_shift_right, 1, A.bitwise_and); cp(ZB, c2("pj", 2, 3))
    ts(KV, ZB, -4.0, A.mult, PM, A.add)
    iota(V_("t128"), [[2, 2], [64, 16]], 0, 0); ts(ZV, PM, 4.0, A.mult)
    if CF or opt["dd"] == "p" or "p" in opt["fin"]:
        mov("s", V_("n32m"), I32, -1.0)
    for part in range(2):
        iota(c2("tz", 128 * part, 128 * part + 128), [[0, 16], [1024 << part, 2], [0, 4]], -(512 << part), 0)
        for L in range(2):
            asel(V_("mm", AL, 2 * L + part, AL), c2("tz", 128 * part, 128 * part + 128), [[-8, 16], [0, 2], [-1, 4]], A.is_equal, 0.0, -4 * L, 1)
    iota(V_("c2k"), [[0, 128]], -2048, 0)
    asel(V_("t1"), V_("c2k"), [[-8, 16], [0, 8]], A.is_ge, 0.0, 0, 1)
    asel(V_("y8", AL, 1, AL), V_("t1"), [[8, 16], [0, 8]], A.is_ge, 0.0, 7, -1)
    asel(V_("t1"), V_("t1"), [[1, 128]], A.is_gt, 0.0, 0, -1)
    asel(V_("y8", AL, 0, AL), V_("t1"), [[-1, 128]], A.not_equal, 1.0, 0, 1)
    if opt["diag"]:
        mov("s", V_("blk4k"), V_("blk"), -4096.0)
    for i in range(1, 16):
        asel(c2("tri", 128 * i, 128 * i + 128), V_("blk4k" if opt["diag"] else "blk"), [[16, 8], [0, 16]], A.is_ge, 0.0, i - 1, -1)
    for a in range(4):
        dmas("y", [(V_("lsw", S_(32 * a + 16 * r1, 32 * a + 16 * r1 + 16), h, AL),
                    V_("tl", S_(32 * a + 16 * h, 32 * a + 16 * h + 16), S_(896 * r1, 896 * r1 + 896))) for r1 in range(2) for h in range(2)], 229376, [first])

    def turn(t):
        cl[0] = "turn"
        for h in range(2):
            mov("g", V_("ftr", AL, AL, S_(16 * h, 16 * h + 16)), V_("lsw", AL, h, S_(t, 896, 4)))
        tr(V_("tlt"), V_("ftr"))

    def names(t):
        par = t % 2; h = H(); cl[0] = "names"
        mov("s", V_("nmh"), ind(c2("tli", 0, NV), c2("hix", 16 * par, 16 * par + 16)))
        for part in range(2):
            mmg(minus_names(h, 128 * part, part))
        lin("v", V_("nix", AL, par, AL), ps(h, 0, 256), -1.0, 0.0)

    def minus_names(h, a, part):
        return [(ps(h, a, a + 128), sel(("lo8", "hi8")[part], 8 * (e - part)), c2("nmh", e, 256, 2)) for e in range(2)]

    def half_codes(t):
        cl[0] = "cch"; cuts = (0,) + O("parts", t - 1)
        for a, b in zip(cuts, () if CF else cuts[1:]):
            mov("g", c2("cch%d" % (t % 2), a, b), c2("cc", C0 + a, C0 + b))

    def view_lists(t):
        cut = O("cut", t - 1)
        for name, a, b in (("vl", 0, cut), ("vm", cut, NV)):
            if a < b:
                cl[0] = name; x = ps(H(), 0, (b - a) // 8); f0 = c2("f0", a // 8, b // 8)
                mmg([(x, sel("bz32" if CF else "bz", 2 * i), cch(t, a + i, b, 8)) for i in range(8)], 8)
                tt(f0, x, c2("jw", a // 8, b // 8), A.max); lin("v", c2("vix", a // 8, b // 8), f0, -1.0, KZ)

    def node_lists(t):
        cl[0] = "nl"; h = H()
        mmg([(ps(h, 0, 28), sel("b32" if CF else "b16", i), cch(t, 4 * i + t, NV, 64)) for i in range(16)], 16)
        act(V_("sgw"), ps(h, 0, 28), F.Sign, 1.0, -float(MID))
        h = H()
        for r, b0, b1, base in ((0, 0, NB, 0), (1, NB, 28, 16 * NB)):
            lst = []
            for j, k in enumerate(SLOTS[O("a4", t)[r] in "23"]):
                a = base + (b1 - b0) * j - b0; runs = [(x, y) for x, y in ((b0, min(b1, 14)), (max(b0, 14), b1)) if x < y]
                lst.append((ps(h, a + b0, a + b1), I16, c2("sgw", b0, b1), True, False))
                for x, y in runs:
                    lst.append((ps(h, a + x, a + y), V_("i4"), V_("tlt", AL, S_(x % 14, (y - 1) % 14 + 1), 16 * (x // 14) + k), False, y == b1))
            n = len(lst) // 2
            mm(lst[:n]); mm(lst[n:])
        lin("v", V_("six%d" % (t % 2)), ps(h, 0, 448), 0.5, 0.5)

    CH = ((0, 0), (1, 0), (0, 1), (1, 1))

    def sides(t):
        for j, (part, hf) in enumerate(CH):
            cl[0] = "sd%d" % j; w = 32 if j in O("sdf", t) else 64
            for a in range(128 * part + 64 * hf, 128 * part + 64 * hf + 64, w):
                h = H(); o = ps(h, 0, w); b = a % 128 + 128 * (t % 2)
                half = side("vs"[(j + a // 32) % 2], c2("gg", 16 * a, 16 * (a + w)), ind(c2("cc", C0, C0 + NV + NG), V_("nix", AL, t % 2, S_(a, a + w))))
                mmg([(o, half(k), c2("gg", 16 * a + k, 16 * (a + w), 16)) for k in range(16)] + [(o, ROW0, c2("tab8h", b, b + w))], 17)
                lin("v", c2("uix", a, a + w), o, 1.0, E4)
                tt(c2("sg", a, a + w), o, c2("tab8", b, b + w), A.subtract)

    def pair_lists():
        cl[0] = "pl"; h = H()
        for L in range(2):
            o = ps(h, 128 * L, 128 * L + 128)
            mmg([(o, V_("mm", AL, 2 * L + part, AL), c2("sg", 128 * part, 128 * part + 128)) for part in range(2)] + [(o, ROW0, c2("tab16h", 128 * L, 128 * L + 128))])
        lin("v", V_("lix"), ps(h, 0, 256), 1.0, KV)

    def candidates():
        cl[0] = "cand"; h = H()
        for z in range(2):
            for part in range(2):
                a = 256 * z + 128 * part
                mmg(minus_names(h, a, part) + [(ps(h, a, a + 128), V_("i4k", AL, z, AL), c2("sg", 128 * part, 128 * part + 128))])
        lin("s", V_("cab"), ps(h, 0, 512), 1.0, 1792.0 - 2048.0, True)
        h = H(); Y = [V_("y8", AL, j, AL) for j in range(2)]
        mmg([(ps(h, 0, 512), Y[0], V_("cab"))] + [(ps(h, 256 * z + 128, 256 * z + 256), Y[1], c2("cab", 256 * z, 256 * z + 128)) for z in range(2)])
        x = ps(h, 0, 512)
        lin("s", V_("sel"), x, 1.0, 0.0, True)
        h = H()
        if opt["cz"] == "p":
            mmg([(ps(h, 0, 32), V_("r8", AL, i % 2, S_(16 - i, 144 - i)), V_("sel", AL, AL, part, S_(i // 2, 128, 8))) for i in range(16) for part in range(2)], 16)
            return mov("s", V_("clw"), ps(h, 0, 32))
        mm([(ps(h, 256 * z + e, 256 * z + 256, 2), V_("ee", AL, e, AL), V_("sel", AL, z, part, AL), part == 0, part == 1)
            for z in range(2) for e in range(2) for part in range(2)])
        mov("s", V_("cand"), ps(h, 0, 512), -1.0)
        h = H()
        mmg([(ps(h, 0, 32), sel("b16", i), c2("cand", i, 512, 16)) for i in range(16)], 16)
        mov("s", V_("clw"), ps(h, 0, 32))

    def views(t, cuts):
        for lo, hi in zip(cuts, cuts[1:]):
            mov("s", c2("vw%d" % (t % 2), 2 * lo, 2 * hi), ind(c2("uw", W0, U0 + hi), c2("vix", lo // 8, hi // 8)), -1.0)

    def early_views(t, cr):
        cl[0] = "gv"; views(t, (0, 128, 256))
        send_shifted(O("shift", t - 1)[2], "vw%d" % (t % 2), 0, 2 * NV, 256, "sv", cr)
        cl[0] = "vA"; views(t, (256,) + tuple(x for x in opt["vcut"] if x < LATE) + (LATE,) if LATE > 256 else ())

    def nodes(t, r):
        return c2("uw", U0 + (LATE if r else 0) + t, G0 if r else U0 + LATE, 4)

    def old_values(t, r):
        cl[0] = "ue" if r == 0 else "uf"; n = NN[r]; ue = "ue%d" % r
        mov("g", c2(ue, 0, n), nodes(t, r))
        if O("rep", t) == "d" and PER[r] < 8:
            return dmas("y", [(c2(ue, n * j, n * j + n), c2(ue, 0, n)) for j in range(1, PER[r])], 512 * n * (PER[r] - 1))
        mov("g", c2(ue, n, 2 * n), nodes(t, r)); k = 2 * n
        while k < PER[r] * n:
            mov("g", c2(ue, k, 2 * k), c2(ue, 0, k)); k *= 2

    def step1(t, r):
        win = c2("vw%d" % (t % 2), 0, 4096); way = O("way" + "AB"[r], t); a4 = O("a4", t)[r]; fold = t < opt["fold"]
        n = NN[r]; per = PER[r]; ue = V_("ue%d" % r)
        def q(a, b, regions=1):
            if b - a > 4:
                return V_("q%d" % r, AL, S_(a // 4, b // 4), AL)
            cols = S_(a % 4 * n, ((b - 1) % 4 + 1) * n)
            return V_("q%d" % r, AL, S_(a // 4, a // 4 + regions), cols) if regions > 1 else V_("q%d" % r, AL, a // 4, cols)
        tree = O("tree" + "AB"[r], t); sums = [(8, q(4, 8), q(0, 4), tree[0])]
        if len(tree) == 3:
            sums += [(12, q(4, 6, 2), q(6, 8, 2), tree[1])]
            sums += [(14, q(4, 5, 3), q(5, 6, 3), tree[2])] if a4 == "m" else [(12, q(4, 5, 2), q(5, 6, 2), tree[2])]
        else:
            sums += [(8, q(4, 6), q(6, 8), tree[1]), (8, q(4, 5), q(5, 6), tree[2]), (12, q(8, 10), q(10, 12), tree[3]), (12, q(8, 9), q(9, 10), tree[4])]
        sums += [(14, q(12, 13), q(13, 14), "d")] if a4 == "d" else []
        if a4 == "2":
            sums = [(8, q(0, 2, 2), q(2, 4, 2), "d"), (8, q(0, 1, 2), q(1, 2, 2), "d"), (12, q(8, 10), q(10, 12), "d")]
        if a4 == "3":
            sums = [(4, q(0, 2), q(2, 4), "d"), (4, q(0, 1), q(1, 2), "d"), (8, q(4, 6), q(6, 8), "d"), (8, q(4, 5), q(5, 6), "d"), (12, q(8, 10), q(10, 12), "d")]
        for j, a in enumerate(range(0, 16, per)):
            b = a + per; h = H(WIDE if per * n > 512 else NARROW); cl[0] = "AB"[r] + str(j); k = 16 * NB * r + n // 16 * a
            x = ind(win, c2("six%d" % (t % 2), k, k + n // 16 * per))
            if way[j] == "p":
                cuts = [(y, min(y + 512, per * n)) for y in range(0, per * n, 512)]; c0 = a % 4 * n
                for y, z in cuts:
                    mm([(ps(h, y, z), I32, c2("ue%d" % r, y, z), True, False)])
                mov("s", q(a, b), x)
                for y, z in cuts:
                    mm([(ps(h, y, z), I32, V_("q%d" % r, AL, a // 4, S_(c0 + y, c0 + z)), False, True)])
                act(q(a, b), ps(h, 0, per * n), F.Abs, 0.015625 if fold else 1.0)
            else:
                if way[j] == "s":
                    mov("s", q(a, b), x); dadd(q(a, b), ue)
                else:
                    tt(q(a, b), x, ue, A.add)
                act(ps(h, 0, per * n), q(a, b), F.Abs, 0.015625 if fold else 1.0)
            if tree[0] == "x" and a == 0:
                x = ps(h, 0, 4 * n)
                tt(q(4, 8), q(4, 8), ps(h, 4 * n, 8 * n), A.mult); tt(x, q(0, 4), x, A.mult); tt(q(4, 8), x, q(4, 8), A.add); sums.pop(0)
            elif a4 == "v" and a <= 12 < b:
                for x, y in ((a, 12), (13, b)):
                    if x < y:
                        tt(q(x, y), q(x, y), ps(h, (x - a) * n, (y - a) * n), A.mult)
                x = ps(h, (12 - a) * n, (13 - a) * n)
                tt(x, q(12, 13), x, A.mult); tt(q(12, 13), x, q(13, 14), A.add)
            else:
                tt(q(a, b), q(a, b), ps(h, 0, per * n), A.mult)
            while sums and sums[0][0] <= b:
                k, x, y, mode = sums.pop(0)
                if mode == "d":
                    dadd(x, y)
                elif mode == "D":
                    dadd(q(4, 6), q(0, 2)); dadd(q(6, 8), q(2, 4))
                elif mode == "p":
                    z = ps(H(), 0, x["c"]); mmg([(z, I32, x), (z, I32, y)], 1); mov("s", x, z)
                else:
                    tt(x, x, y, A.add)
        cl[0] = "AB"[r] + "t"; lo = ps(H(), 0, n); u = nodes(t, r); old = c2("ue%d" % r, 0, n)
        spine = [q(k, k + 1) for k in (14, 15, 12, 8, 4)]
        if a4 in "23":
            x = ps(H(), 0, n); mmg([(x, I32, q(k, k + 1)) for k in (12, 13, 8, 0)], 2 - r); mov("s", q(1, 2), x)
            spine = [q(k, k + 1) for k in (14, 15, 9, 4, 1)]
        if r and not O("once", t):
            mmg([(lo, I32, x) for x in spine], 1)
            x = ps(H(), 0, n)
            if CF:
                mmg([(x, I32, V_("oc")), (x, V_("n32m"), cch(t + 1, LATE + t, NV, 4))])
            else:
                mmg([(x, V_("i4k", AL, k, AL), cch(t + k, LATE + t, NV, 4)) for k in range(2)])
            ts(V_("mk"), x, 0.0, A.is_equal, -1.0 if fold else -0.015625, A.mult); tt(lo, lo, V_("mk"), A.mult)
            tt(u, lo, u, A.add)
        elif fold and O("fin", t)[r] == "p":
            mmg([(lo, V_("n32m"), x) for x in spine] + [(lo, I32, old)], 2 - r); mov("s", u, lo)
        elif fold:
            mmg([(lo, I32, x) for x in spine], 2 - r); tt(u, old, lo, A.subtract)
        else:
            mmg([(lo, I32, x) for x in spine], 2 - r); mov("s", lo, lo, -0.015625); tt(u, lo, old, A.add)

    def lists(t):
        view_lists(t); node_lists(t); sides(t); pair_lists(); candidates()

    def votes(a, b, par):
        n0, n1 = [c2("uw", W0 + 4 * a + 2 * par + z, W0 + 4 * b, 4) for z in range(2)]
        if opt["dd"] == "p":
            dd = ps(H(), 0, b - a); mmg([(dd, I32, n0), (dd, V_("n32m"), n1)])
        else:
            dd = c2("dd", a, b); tt(dd, n0, n1, A.subtract)
        ts(c2("ud", a, b), dd, c2("thr", 0, 1), A.is_gt, 0.5, A.subtract)
        ts(c2("ud", 256 + a, 256 + b), dd, c2("nth", 0, 1), A.is_lt, 0.5, A.subtract)

    names(0); turn(0); lists(0)
    early_views(0, None); old_values(0, 0); old_values(0, 1)
    cr = None
    for t in range(RO):
        par = t % 2; last = t == RO - 1; cl[1] = t; fold = t < opt["fold"]; once = O("once", t)
        cl[0] = "vB"; views(t, (LATE,) + tuple(x for x in opt["vcut"] if x > LATE))
        if CF and not once:
            cl[0] = "oc"; mov("g", V_("oc"), c2("cc", C0 + LATE + t, C0 + NV, 4))
        held = {}
        for j, (part, hf) in enumerate(CH):
            a = 128 * part + 64 * hf; h = H(WIDE); w = 32 if j in O("fine", t) else 64
            for b in range(a, a + 64, w):
                uu = c2("uu", 16 * b, 16 * (b + w))
                cl[0] = "uc%d" % j
                mov("s", uu, ind(WW, c2("uix", b, b + w)))
                cl[0] = "x%d" % j
                tt(uu, ind(c2("uw", U0, UE), V_("nix", AL, par, S_(b, b + w))), uu, A.subtract)
                act(ps(h, 16 * (b - a), 16 * (b - a + w)), uu, F.Abs, 0.015625 if fold else 1.0)
            for i in range(2):
                t0 = 2048 * (2 * hf + i); mode = O("pair", t)[2 * hf + i]; cl[0] = "m%d" % j
                lo, hi, sm = [c2("tt", t0 + 512 * k, t0 + 512 * k + 512) for k in (1, 2, 3)]
                st = ps(h, 512 * i, 512 * i + 512); di = c2("uu", 16 * a + 512 * i, 16 * a + 512 * i + 512)
                if part == 0 and mode == "y":
                    tt(st, di, st, A.mult); mov("s", lo, st); held[i] = st
                elif part == 0:
                    tt(lo, di, st, A.mult)
                    if mode == "d":
                        dma("y", sm, lo, 262144)
                elif mode == "x":
                    tt(st, di, st, A.mult); tt(sm, st, lo, A.add); mov("s", hi, st)
                else:
                    tt(hi, di, st, A.mult)
                    if mode == "d":
                        dadd(sm, hi)
                    elif mode == "y":
                        tt(sm, held[i], hi, A.add)
                    else:
                        h2 = H()
                        mmg([(ps(h2, 0, 512), I32, lo), (ps(h2, 0, 512), I32, hi)], 1)
                        mov("s", sm, ps(h2, 0, 512))
        if not last:
            cl[0] = "cred"
            cr = credit([c2("uw", G0, UE), c2("cc", C0 + NV, C0 + NV + NG), c2("vw%d" % (1 - par), 2 * NV, 4096)])
        for c in range(4):
            cl[0] = "l%d" % c
            win = c2("tt", 2048 * c, 2048 * c + 2048); rr = c2("uu", 512 * c, 512 * c + 512)
            mov("s", rr, ind(win, c2("lix", 128 + 32 * c, 160 + 32 * c)))
            tt(rr, ind(win, c2("lix", 32 * c, 32 * c + 32)), rr, A.add)
        for j, (qa, qb) in enumerate(opt["grp"]):
            a, b = 512 * qa, 512 * qb; n = 128 * (qb - qa); cc1 = c2("c1", 128 * qa, 128 * qb); cl[0] = "w%d" % j
            if O("c1", t)[j] == "p":
                h = H(); o1 = ps(h, 0, n)
                mmg([(o1, I32, c2("uu", a + 1, b, 4)), (o1, I32, c2("uu", a + 3, b, 4))])
                mov("s", cc1, o1)
            else:
                tt(cc1, c2("uu", a + 1, b, 4), c2("uu", a + 3, b, 4), A.add)
            h = H(); o = ps(h, 0, n)
            mmg([(o, I32, c2("uu", a, b, 4)), (o, I32, c2("uu", a + 2, b, 4)), (o, I32, cc1)], 2)
            if not fold:
                mov("s", o, o, 0.015625)
            for z in range(2):
                w = c2("uw", W0 + 256 * qa + 2 * par + z, W0 + 256 * qb, 4)
                tt(w, ps(h, z, n, 2), w, A.add)
            if opt["dd"] == "g":
                votes(64 * qa, 64 * qb, par)
        if last:
            cl[0] = "out"; dma("y", V_("ys"), WW, 524288)
        cl[0] = "s3"
        if opt["dd"] != "g":
            votes(0, 256, par)
        if opt["cz"] == "v":
            hv = H(); up, dn = ps(hv, 0, 256), ps(hv, 256, 512)
            mm([(ps(hv, 0, 512), V_("blk2k"), V_("ud"), True, True)])
        h = H()
        mmg([(ps(h, 0, 32), sel("bsum", i), c2("ud", i, 512, 16)) for i in range(16)], 16)
        tt(V_("cv"), ps(h, 0, 32), V_("clw"), A.max)
        tt(V_("cw16"), c2("cv", 0, 16), c2("cv", 16, 32), A.min)
        if opt["cz"] == "v":
            tt(V_("rb"), dn, c2("cand", 256, 512), A.max); tt(up, up, c2("cand", 0, 256), A.max); tt(V_("cz"), up, V_("rb"), A.min)
        else:
            hz = H()
            mm([(ps(hz, i, 256, 16), c2("rowb", 128 * i, 128 * i + 128), V_("cw16"), True, True) for i in range(16)])
            mov("s", V_("cz"), ps(hz, 0, 256))
        mov("v", V_("cw"), V_("cw16"))
        cl[0] = "val"
        ts(V_("zl"), ps(h, 16, 32), 0.0, A.is_lt, ZV, A.add); tt(V_("zl"), V_("zl"), c2("t128", 16 * par, 16 * par + 16), A.add)
        lin("s", V_("vlx"), V_("zl"), 1.0, 0.0)
        mov("s", V_("zs"), ind(c2("cc", W0, U0), V_("vlx"))); mov("s", V_("val"), ind(WW, V_("vlx")))
        cl[0] = "s4"; h = H(); y = ps(h, 0, 256); d0 = 16 if opt["diag"] else 0
        ts(V_("idl"), V_("cz"), 0.0, A.is_ge, -32768.0, A.mult)
        mm([(y, I16, V_("cdg"), True, False), (y, I16, V_("cz"), False, False), (y, I16, V_("idl"), False, False)])
        def same_block(src, step, stop):
            mm([(ps(h, i, 256, 16), c2("tri", 128 * i, 128 * i + 128), c2(src, i, 16 * step, step), False, stop and i == 15) for i in range(1, 16)])
        if d0:
            hd = H()
            mm([(ps(hd, i, 256, 16), I16, V_("cw16"), True, True) for i in range(16)])
            tt(V_("eqd"), ps(hd, 0, 256), V_("cz"), A.is_equal); same_block("eqd", 16, False)
        for a0, a1 in ((0, 4), (4, 8), (8, 12), (12, 16 - d0 // 16)):
            probe[0] = True
            four = [ts(c2("eq", 256 * a + d0, 256 * a + 256 - 16 * a), c2("cz", 16 * a + d0, 256), c2("cw", a, a + 1), A.is_equal, -4096.0, A.mult)
                    for a in range(a0, a1)]
            probe[0] = False
            add("v", lambda c, four=four: [x for f, k in four for x in f(c)], [V_("cz"), V_("cw")], [c2("eq", 256 * a0, 256 * a0 + 1024)],
                sum(k for f, k in four))
            mm([(ps(h, 16 * a + 16, 256), V_("blk"), c2("eq", 256 * a + 16, 256 * a + 256 - 16 * a), False, d0 > 0 and a == 14) for a in range(a0, min(a1, 15))])
        if not d0:
            same_block("eq", 256, True)
        scan(V_("tg"), V_("rs0"), y, 1e6, A.min, A.max)
        tgf = c2("tg", 15, 256, 16); lin("v", V_("tgx"), tgf, 1.0, -float(TOP))
        put_codes(ind(c2("cc", 0, C0 + NV), V_("tgx")), V_("zs"))
        if not last:
            cl[0] = "sc"; send_shifted(O("shift", t)[0], "cc", C0, C0 + NV, 128, "sc", cr)
            names(t + 1); turn(t + 1)
        cl[0] = "host"
        hw = c2("hw", 16 * par, 16 * par + 16)
        ts(V_("h1"), tgf, float(TOP + U0), A.is_ge, -65536.0, A.mult)
        tt(V_("h1"), V_("h1"), hw, A.add); tt(hw, V_("h1"), tgf, A.max)
        if t < 2:
            lin("v", c2("hix", 16 * par, 16 * par + 16), hw, 1.0, -float(TOP + U0))
        half_codes(t + 1)
        if not last:
            lists(t + 1)
        else:
            cl[0] = "yc"
            h = H(); x = ps(h, 0, 112)
            mmg([(x, sel("b32" if CF else "b16", i), cch(0, 112 * i, 112 * i + 112)) for i in range(16)], 4)
            lin("v", V_("yc1"), x, -2.0, 2.0 * (MID + FAR) + 1); lin("v", V_("yc2"), x, 2.0, 2.0 * (FAR - MID))
            if CF:
                tt(V_("yci"), V_("yc1"), V_("yc2"), A.min); cp(V_("yc1"), V_("yci"))
            else:
                tt(V_("yc1"), V_("yc1"), V_("yc2"), A.min)
            dma("y", V_("yc"), V_("yc1"), 57344)
            cl[0] = "yh"; lin("v", V_("hw16"), V_("hw"), 1.0, -float(TOP + U0)); h = H()
            mm([(ps(h, 2 * i + p2, 512, 32, S_(0, 8)), c2("rowb", 128 * i, 128 * i + 128, 16), c2("hw16", 16 * p2, 16 * p2 + 16), True, True)
                for i in range(16) for p2 in range(2)])
            mov("s", V_("c1", S_(0, 8), AL), ps(h, 0, 512, None, S_(0, 8)))
            dma("y", V_("yh"), V_("c1", S_(0, 8), AL), 16384)
        step1(t, 0)
        if once:
            step1(t, 1)
        cl[0] = "put"; cp(ind(c2("uw", 0, G0), V_("tgx")), V_("val"))
        if not last:
            send_shifted(O("shift", t)[1], "uw", U0, G0, 128, "su", cr)
            early_views(t + 1, cr); old_values(t + 1, 0)
        if not once:
            step1(t, 1)
        if not last:
            old_values(t + 1, 1)
    cl[0] = "out"
    for j in range(2):
        dma("ys"[j], c2("yu", 896 * j, 896 * j + 896), c2("uw", U0 + 896 * j, U0 + 896 * j + 896), 458752)
    return ops, pieces


def arrange():
    time = {}; engines = {}
    for t, line in TIMES.items():
        for name, calls in [x.split(":") for x in line.split()]:
            calls = calls.split(","); key = "%s@%d" % (name, t)
            time[key] = [START[t + 1] + int(x.rstrip("vsg")) for x in calls]; engines[key] = "".join(x[-1] for x in calls)
    ops, pieces = build(OPT, engines, PLAN)
    order = sorted(range(len(ops)), key=lambda j: time["%s@%d" % (ops[j]["cl"], ops[j]["rd"])][ops[j]["nth"]])
    pos = {j: k for k, j in enumerate(order)}; bank = [int(b) for b in BANKS]; holder = [None] * 8
    for h in sorted(range(len(pieces)), key=lambda h: pos[pieces[h]["ops"][0]]):
        for b in [x for x in pieces[h]["pool"] if x[0] == bank[h]][0]:
            if holder[b] is not None:
                ops[pieces[h]["ops"][0]]["deps"].update(pieces[holder[b]]["ops"])
            holder[b] = h
    return ops, order, bank


CACHE = {}


def rank_program(g, core, T, topo):
    rank = T.rank_of(core)
    if rank is None:
        return
    if not CACHE:
        CACHE["plan"] = arrange()
    ops, order, bank = CACHE["plan"]
    nr = len(T.cores); dst = T.cores[(rank - 1) % nr]; up = T.cores[(rank + 1) % nr]
    rid, pid = topo.addr(dst)[:2]
    en = topo.engines(core, dst); inn = len(topo.engines(up, core))
    c = {"g": g, "T": T, "dst": DstId(rid=rid, pnc=pid), "en": en, "up": topo.addr(up)[:2], "upm": 1 << topo.engines(core, up)[0], "bank": bank}
    queue = {"v": g.vector, "s": g.scalar, "p": g.tensor, "g": g, "y": g.sync}
    own = {"v": "v", "s": "s", "p": "p", "g": "gq"}
    count = {}; token = {}; known = {e: {} for e in queue}; total = {}; seen = {}; when = {}; waited = {}

    def wait(e, s, k):
        if known[e].get(s, 0) < k:
            queue[e].wait_ge(T.sem[s], k); known[e][s] = k; waited[s] = max(waited.get(s, 0), k)

    for j in order:
        o = ops[j]; e = o["e"]
        if o["k"] == "x":
            token[j] = (o["sem"][0], inn); total[o["sem"][0]] = inn
            continue
        need = {}
        for d in o["deps"]:
            if (e == "p" and ops[d]["e"] == "p") or (o["k"] == "r" and ops[d]["k"] == "r" and ops[d]["sem"][1] == 1):
                continue
            s, k = token[d]
            if s == own.get(e) and d in o["reads"]:
                continue
            need[s] = max(need.get(s, 0), k)
        if o["ext"]:
            need[o["ext"][0]] = o["ext"][1]; total[o["ext"][0]] = o["ext"][1]
        for s in sorted(need, key=lambda s: -when.get((s, need[s]), -1)):
            if known[e].get(s, 0) < need[s]:
                wait(e, s, need[s])
                for s2, k2 in seen.get((s, need[s]), {}).items():
                    known[e][s2] = max(known[e].get(s2, 0), k2)
        before = dict(known[e])
        ins = o["f"](c)
        if o["k"] == "c":
            s = own[e]
            for x in ins:
                x.then_inc(T.sem[s], 1)
            count[s] = count.get(s, 0) + len(ins); token[j] = (s, count[s]); total[s] = count[s]
        elif o["k"] == "d":
            for x in ins:
                x.then_inc(T.sem[o["sem"][0]], 16)
            token[j] = o["sem"]; total[o["sem"][0]] = o["sem"][1]
        else:
            k = len(en) if o["sem"][1] == "en" else 1
            token[j] = (o["sem"][0], k); total[o["sem"][0]] = k
        seen[token[j]] = before; when[token[j]] = len(when)
    for s in sorted(total):
        if waited.get(s, 0) < total[s]:
            queue["y"].wait_ge(T.sem[s], total[s])
